import numpy as np, ml_dtypes
CORES = [113,118,241,246]
N = 4
BF = ml_dtypes.bfloat16
def gentries(a):
    return np.ascontiguousarray(a.reshape(8, 16, -1).transpose(0, 2, 1)).reshape(8, -1)
def gtable(e):
    e = np.asarray(e); return np.ascontiguousarray(e.reshape(8, -1, 16).transpose(0, 2, 1)).reshape(128, -1).astype(np.int32)
S, M, CAP, RO = 2048, 512, 48, 4
W = N * S
def look(x, k, p, wt):
    n, m = p.shape[0], p.shape[3]; gi = np.arange(8)[None, :, None]
    q = np.stack([k[gi, 3 - t, p[:, :, t]] for t in range(4)], axis=2)
    xt = np.ascontiguousarray(x.transpose(0, 2, 1))
    c = [xt[gi, q[:, :, t]].reshape(n, 8, m, 4, 4) for t in range(4)]
    board = np.concatenate([np.concatenate([c[0], c[1]], axis=4), np.concatenate([c[2], c[3]], axis=4)], axis=3)
    hot = (board == 15).astype(np.int64); near = np.zeros((n, 8, m, 4, 4), np.int64)
    for i in range(3):
        for j in range(3):
            if (i, j) != (1, 1): near = near + hot[..., 1 + i:5 + i, 1 + j:5 + j]
    mid = board[..., 2:6, 2:6]
    y = np.where(mid == 0, np.where(near == 2, 15, 0), np.maximum(mid - 1, 0)).reshape(n, 8, m, 16)
    h = np.add.reduce(y * wt[None, :, None, :], axis=3) & (W - 1)
    r0 = xt[gi, h]; r1 = xt[gi, h ^ 1]
    return q, y, h, np.all(r0 == y, axis=3), np.all(r1 == y, axis=3), r0[..., 0] < 0, r1[..., 0] < 0
def content(rng, n):
    u = rng.random((n, 16)); lo = 0.6 * rng.random((n, 1)); hi = 1 - 0.4 * rng.random((n, 1))
    return np.where(u < lo, 0, np.where(u > hi, 15, rng.integers(0, 16, (n, 16))))
def world(rng, share, few, ends=0):
    x = np.full((8, 16, W), -1, np.int64); k = np.zeros((8, 4, W), np.int64); pools = []
    for g in range(8):
        o = rng.permutation(W)
        if ends == 1: o = np.concatenate([np.array([0, W - 1]), o[(o > 0) & (o < W - 1)]])
        if ends == 2: o = o[(o > 1) & (o < W - 16)]
        n = min(int(W * float(share[g])), len(o)); a = n // 2
        c = content(rng, n); pal = content(rng, int(few[g])); c[:a] = pal[rng.integers(0, len(pal), a)]
        x[g][:, o[:n]] = c.T
        k[g][:, o[:a]] = rng.choice(o[:a], (4, a)); k[g][:, o[a:n]] = rng.choice(o[a:n], (4, n - a))
        pools.append((o[:a], o[a:n]))
    return x, k, pools
def start(rng, pools, share, m=M, pw=1.0):
    p = np.zeros((N, 8, 4, m), np.int64)
    for g in range(8):
        a, b = pools[g]
        pa = a[(len(a) * rng.random((N, 4, m)) ** pw).astype(np.int64)]; pb = b[(len(b) * rng.random((N, 4, m)) ** pw).astype(np.int64)]
        p[:, g] = np.where(rng.random((N, 1, m)) < share[:, g, None, None], pa, pb)
    return p
def plant(rng, x, k, p, wt, pools, share, flip=0.3, wrong=0.1, odd=False):
    q, y, h = look(x, k, p, wt)[:3]
    for g in range(8):
        yy = y[:, g].reshape(-1, 16); hh = h[:, g].reshape(-1); hh = hh ^ (rng.random(len(hh)) < flip).astype(np.int64)
        i = rng.permutation(len(hh))[:int(share * len(hh))]; i = i[x[g, 0, hh[i]] < 0]
        u, j = np.unique(hh[i], return_index=True); v = yy[i[j]].copy(); off = v.copy()
        rows = np.arange(len(u)); col = rng.integers(0, 16, len(u)); err = rng.random(len(u)) < wrong
        off[rows, col] = (v[rows, col] + 1) & 15
        if odd:
            sort = rng.integers(0, 4, len(u)); e = np.flatnonzero(sort == 1); off[e, col[e]] = (v[e, col[e]] + 8) & 15
            off[sort == 2] = 0
            a, b = v[:, :15], v[:, 1:]; up = (a == 15) & (b < 15)
            can = (up | ((a == 0) & (b > 0))) & (np.arange(15) % 4 < 3)
            c = np.argmax(can * (1 - rng.random(can.shape)), axis=1)
            e = np.flatnonzero((sort == 3) & np.any(can, axis=1)); c = c[e]
            off[e] = v[e]; off[e, c] = 15 - v[e, c]; off[e, c + 1] = v[e, c + 1] + np.where(up[e, c], 1, -1)
        v = np.where(err[:, None], off, v)
        kk = rng.choice(np.concatenate(pools[g]), (4, len(u)))
        if odd: kk[:, rng.random(len(u)) < 0.25] = 0
        x[g][:, u] = v.T; k[g][:, u] = kk
def pack(x, k, p, wt):
    return {"cells": np.ascontiguousarray(x.reshape(8, 16, N, S).transpose(2, 0, 1, 3)).reshape(N, 128, S).astype(np.float32).astype(BF),
            "kids": np.ascontiguousarray(k.reshape(8, 4, N, S).transpose(2, 0, 1, 3)).reshape(N, 32, S).astype(np.int32),
            "nodes": np.stack([gtable(a.reshape(8, 4 * M)) for a in p]),
            "wt": np.ascontiguousarray(np.tile(wt.reshape(1, 128, 1), (N, 1, 1))).astype(np.int32)}
def setup_inputs(rng):
    wt = rng.integers(0, W, (8, 16)); few = rng.permutation(np.array([2, 2, 3, 3, 4, 5, 6, 6]))
    x, k, pools = world(rng, 0.35 + 0.2 * rng.random(8), few)
    p = start(rng, pools, rng.choice(np.array([0.3, 0.6, 0.9]), (N, 8)))
    plant(rng, x, k, p, wt, pools, 0.3)
    return pack(x, k, p, wt)
def setup_inputs_room(rng):
    wt = rng.integers(0, W, (8, 16)); x, k, pools = world(rng, 0.35 + 0.15 * rng.random(8), rng.integers(3, 7, 8))
    cand = start(rng, pools, np.full((N, 8), 0.1), 2 * M)
    plant(rng, x, k, cand, wt, pools, 0.15)
    q, y, h, hit0, hit1, free0, free1 = look(x, k, cand, wt)
    own = np.where(hit0 | hit1 | ~(free0 | free1), -1, h // S); p = np.zeros((N, 8, 4, M), np.int64)
    want = np.where(free0, h, h ^ 1); taken = np.zeros(W, bool)
    for r in range(N):
        for g in range(8):
            sel = []
            for o in range(N):
                n = int(rng.choice(np.array([0, 1, CAP - 1, CAP, CAP + 1, 2 * CAP])))
                if r == 0 and o == 1: n = (CAP, CAP + 1, 2 * CAP, CAP - 1, 1, 0, CAP, CAP + 1)[g]
                f = rng.permutation(np.flatnonzero(own[r, g] == o))
                if g == 6 and o == 1:
                    n = CAP; f = f[np.unique(want[r, g, f], return_index=True)[1]]
                    f = rng.permutation(f[~taken[want[r, g, f]]]); taken[want[r, g, f[:n]]] = True
                sel.append(f[:n])
            sel = np.concatenate(sel); rest = np.flatnonzero(own[r, g] < 0)
            sel = rng.permutation(np.concatenate([sel, rng.choice(rest, M - len(sel))]))
            if r == 1 and g == 2:
                last = rng.permutation(np.flatnonzero(own[r, g] == 2))[:CAP]
                sel = np.concatenate([rng.choice(np.flatnonzero((own[r, g] >= 0) & (own[r, g] != 2)), M - len(last)), last])
            p[r, g] = cand[r, g][:, sel]
    return pack(x, k, p, wt)
def setup_inputs_clash(rng):
    wt = (2 * rng.integers(0, W // 2, (8, 1)) + 1) * rng.integers(0, 3, (8, 16)) & (W - 1)
    z = rng.permutation(8); wt[z[0]] = 0; wt[z[1]] = 0; wt[z[1], rng.integers(0, 16)] = W - 1
    x, k, pools = world(rng, 0.25 + 0.2 * rng.random(8), rng.integers(2, 9, 8), 2)
    p = start(rng, pools, rng.choice(np.array([0.2, 0.5, 0.8]), (N, 8)))
    return pack(x, k, p, wt)
def setup_inputs_near(rng):
    wt = rng.integers(0, W, (8, 16)); wt[rng.integers(0, 8)] = rng.integers(W - W // 8, W, 16)
    x, k, pools = world(rng, 0.15 + 0.2 * rng.random(8), rng.integers(2, 9, 8), 1)
    p = start(rng, pools, rng.choice(np.array([0.2, 0.5, 0.8]), (N, 8)))
    plant(rng, x, k, p, wt, pools, 0.5, 0.0, 0.5, True); plant(rng, x, k, p, wt, pools, 0.7, 1.0, 0.3, True)
    return pack(x, k, p, wt)
def setup_inputs_alike(rng):
    wt = rng.integers(0, W, (8, 16)); x, k, pools = world(rng, np.array([0.4, 0.98, 0.3, 0.05, 0.5, 0.4, 1.0, 0.6]), np.array([1, 3, 2, 2, 1, 4, 2, 12]), 1)
    a = pools[2][0]; k[2][:, a] = rng.choice(np.array([0, W - 1]), (4, len(a)))
    share = rng.random((N, 8)); share[:, [0, 2]] = 1.0
    p = start(rng, pools, share); p[:, 2] = rng.choice(np.array([0, W - 1]), (N, 4, M))
    for g in (3, 5, 7): p[:, g] = p[:, g][:, :, rng.integers(0, 8, M)]
    return pack(x, k, p, wt)
def setup_inputs_spread(rng):
    wt = np.minimum(np.exp2(rng.random((8, 16)) * np.log2(W)).astype(np.int64), W - 1) * (rng.random((8, 16)) > 0.0625)
    x, k, pools = world(rng, rng.permutation(np.linspace(0.08, 0.92, 8)), rng.integers(1, 41, 8))
    p = start(rng, pools, rng.random((N, 8)), M, 4.0)
    plant(rng, x, k, p, wt, pools, 0.2)
    return pack(x, k, p, wt)
def check_inputs(d):
    bad = []
    c = np.asarray(d["cells"]).astype(np.float32).reshape(N, 8, 16, S); e = c == -1
    if not np.all(e | ((c >= 0) & (c <= 15) & (c == np.floor(c)))): bad.append("numbers of cells")
    if np.any(np.any(e, axis=2) != np.all(e, axis=2)): bad.append("places of cells empty in part")
    ok = True
    for name in ("kids", "nodes", "wt"):
        if np.min(d[name]) < 0 or np.max(d[name]) > W - 1: bad.append("range of " + name); ok = False
    if np.any(d["wt"] != d["wt"][:1]): bad.append("wt alike on all ranks")
    full = ~np.any(e, axis=2).transpose(1, 0, 2).reshape(8, W)
    kd = np.asarray(d["kids"]).astype(np.int64).reshape(N, 8, 4, S).transpose(1, 2, 0, 3).reshape(8, 4, W)
    if np.any((kd != 0) & ~full[:, None, :]): bad.append("children of empty places")
    if ok:
        to = np.take_along_axis(full, kd.reshape(8, -1), 1).reshape(8, 4, W)
        if np.any(full[:, None, :] & ~to): bad.append("children name full places")
        if not all(np.all(np.take_along_axis(full, gentries(a).astype(np.int64), 1)) for a in d["nodes"]): bad.append("nodes name full places")
    return bad
def reference(cells, kids, nodes, wt):
    x = np.concatenate([a.astype(np.float32).astype(np.int64).reshape(8, 16, S) for a in cells], axis=2)
    k = np.concatenate([a.astype(np.int64).reshape(8, 4, S) for a in kids], axis=2)
    p = np.stack([gentries(a).astype(np.int64).reshape(8, 4, M) for a in nodes])
    w = wt[0].astype(np.int64).reshape(8, 16); gi = np.arange(8)[None, :, None]
    for rnd in range(RO):
        q, y, h, hit0, hit1, free0, free1 = look(x, k, p, w)
        at = np.where(hit0, h, np.where(hit1, h ^ 1, -1))
        got = np.stack([k[gi, t, np.maximum(at, 0)] for t in range(4)], axis=2)
        p = np.where(at[:, :, None] >= 0, got, q)
        want = np.where(at >= 0, -1, np.where(free0, h, np.where(free1, h ^ 1, -1)))
        keep = np.zeros(want.shape, bool)
        for o in range(N):
            mine = (want >= 0) & (want // S == o)
            keep = keep | (mine & (np.add.accumulate(mine.astype(np.int64), axis=2) <= CAP))
        for g in range(8):
            i = np.flatnonzero(keep[:, g].reshape(-1))
            u, first = np.unique(want[:, g].reshape(-1)[i], return_index=True); win = i[first]
            x[g][:, u] = y[:, g].reshape(-1, 16)[win].T
            k[g][:, u] = q[:, g].transpose(1, 0, 2).reshape(4, -1)[:, win]
    return {"ycells": np.stack([x[:, :, r * S:(r + 1) * S].reshape(128, S) for r in range(N)]).astype(np.float32).astype(BF),
            "ykids": np.stack([k[:, :, r * S:(r + 1) * S].reshape(32, S) for r in range(N)]).astype(np.float32),
            "ynodes": np.stack([gtable(a.reshape(8, 4 * M)) for a in p]).astype(np.float32)}

@@ -1,0 +1,688 @@
+from concourse.bass import DstId, RemoteDMATransfer
+from concourse.mybir import AluOpType as A, ActivationFunctionType as F, AxisListType as X
+
+N, S, RO = 4, 2048, 4
+DW = 11008
+TW = 102
+CUT = 316
+f32, bf, i32, u16 = "float32", "bfloat16", "int32", "uint16"
+SB = {
+    "CS": (2048, bf), "LC": (2048, bf), "KS": (640, i32), "LK": (640, i32), "YC": (DW, bf), "YK": (DW, f32),
+    "KT": (512, i32), "KI": (1024, i32), "KB": (1024, bf), "KF": (512, f32), "NN": (2048, bf), "DS": (2048, bf),
+    "B": (8192, bf), "CC": (8192, bf), "D": (512 + DW, bf), "KL": (512, u16), "WI": (8, i32), "WJ": (8, i32),
+    "PI": (8, i32), "BI": (16, i32), "COL": (128, f32), "IF": (256, f32), "RM": (256, f32),
+    "R5": (128, f32), "RE": (128, f32), "RC": (32, f32), "EU": (512, bf), "IDT": (512, bf), "IDL": (128, bf), "BB": (16, f32),
+    "AU": (224, bf), "TM": (80, f32), "RY": (128, bf), "NG": (128, bf), "GW": (224, bf), "KP": (544, bf),
+    "KR": (272, bf), "OB": (128, bf), "O1": (128, bf), "TR": (128, bf), "RX": (128, bf), "WX": (128, bf), "SH": (256, bf), "ONE": (256, bf),
+    "BC": (128, bf), "SK": (256, bf), "RA": (256, bf), "RP": (512, f32), "NI": (576, f32), "NO": (704, f32), "LW": (720, bf),
+    "EQ": (16, f32), "PW": (128, f32), "HZ": (128, f32), "D16": (16, f32), "FQ": (32, f32), "TH": (192, f32), "WC": (16, f32),
+    "CW": (576 + 2560, i32), "CI": (384, i32), "CT": (768, f32), "DL": (16, f32), "DM": (96, f32), "RT": (128, f32), "CA": (256, bf),
+    "DI": (16, i32), "DF": (8, f32),
+    "NA": (256, i32), "NF": (256, f32), "PL": (128, u16), "G": (2048, bf), "AB": (1024, bf), "UA": (512, bf), "DD": (1024, bf),
+    "HI": (256, i32), "HF": (192, f32), "HL": (64, u16), "PN": (128, f32), "CL": (512, f32), "PG": (512, bf),
+    "FB": (128, bf), "SC": (384, f32), "WL": (32, u16), "AT": (32, u16), "OL": (32, u16), "WG": (512, bf), "RQ": (512, f32), "YX": (384, bf),
+    "OY": (384, bf), "KU": (192, u16), "KC": (64, f32), "E": (12 * 192, bf), "WN": (192, bf), "AL": (48, u16), "RL": (768, bf),
+    "OH": (32, bf), "TS": (RO * N * TW, bf), "TL": (RO * N * TW, bf), "RBY": (192, bf), "RBK": (192, f32), "XL": (16, u16),
+    "NS": (128, f32), "NL": (128, f32),
+}
+SCRATCH = {n: ("sbuf", [128, w], d) for n, (w, d) in SB.items()}
+SCRATCH.update({"P%d" % k: ("psum", [128, 512], f32) for k in range(8)})
+SCRATCH.update({"DSD": ("dram", [4, 128, 512], bf), "DLD": ("dram", [4, 128, 512], bf), "KD": ("dram", [32, 2048], f32)})
+SEMAPHORES = (["eg", "ev", "es", "et", "sent", "ak", "an"] + ["ac%d" % k for k in range(N)] + ["ad%d" % k for k in range(N)]
+              + ["ar%d" % k for k in range(RO)] + ["d%d" % k for k in range(24)])
+
+
+def rank_program(g, core, T, topo):
+    rank = T.rank_of(core)
+    if rank is None:
+        return
+    Q = {"g": g, "v": g.vector, "s": g.scalar, "t": g.tensor, "y": g.sync}
+    V, SE, PE = g.vector, g.scalar, g.tensor
+    count = {"g": 0, "v": 0, "s": 0, "t": 0}
+    seen = {e: {} for e in Q}
+    total, wrote, read = {}, {}, {}
+    ndma = [0]
+
+    def need(e, tok):
+        if seen[e].get(tok[0], 0) < tok[1]:
+            Q[e].wait_ge(T.sem[tok[0]], tok[1])
+            seen[e][tok[0]] = tok[1]
+
+    def order(e, r, w, who):
+        for k in r:
+            if k in wrote:
+                need(e, wrote[k])
+            if k[0] == "P" and k[1].isdigit():
+                for tok in read.get(k, []):
+                    if tok[2] != who:
+                        need(e, tok)
+        for k in w:
+            for tok in read.get(k, []):
+                need(e, tok)
+            if k in wrote and (wrote[k][2] != who or who == "dma"):
+                need(e, wrote[k])
+
+    def note(tok, r, w):
+        total[tok[0]] = tok[1]
+        for k in r:
+            read.setdefault(k, []).append(tok)
+        for k in w:
+            wrote[k] = tok
+            read[k] = []
+
+    def op(e, fn, r, w):
+        r, w = r.split(), w.split()
+        order(e, r, w, e)
+        count[e] += 1
+        fn().then_inc(T.sem["e" + e], 1)
+        note(("e" + e, count[e], e), r, w)
+
+    def dma(e, pairs, r, w):
+        r, w = r.split(), w.split()
+        order(e, r, w, "dma")
+        sem = "d%d" % ndma[0]
+        ndma[0] += 1
+        for o, i in pairs:
+            Q[e].dma_start(o, i).then_inc(T.sem[sem], 16)
+        note((sem, 16 * len(pairs), "dma"), r, w)
+
+    def masks(src):
+        others = [o for o in range(N) if o != src]
+        en = {o: topo.engines(T.cores[src], T.cores[o]) for o in others}
+        least = min(len(v) for v in en.values())
+        far = [o for o in others if len(en[o]) == least]
+        near_ = [o for o in others if o not in far]
+        out, used = {}, set()
+        for grp in (far, near_):
+            for n_, o in enumerate(grp):
+                free = [x for x in en[o] if x not in used]
+                k = 1
+                while 2 * k <= len(free) // (len(grp) - n_):
+                    k *= 2
+                out[o] = free[:k]
+                used.update(free[:k])
+        return out
+    eng = {o: masks(o) for o in range(N)}
+    peers = [o for o in range(N) if o != rank]
+    sent = [0]
+
+    def send(src, dst, sem, r):
+        order("g", r.split(), [], "dma")
+        trs = []
+        for o in peers:
+            rid, pid = topo.addr(T.cores[o], core)
+            trs.append(RemoteDMATransfer(dst_ids=[DstId(rid=rid, pnc=pid)], dma_engine_mask=sum(1 << x for x in eng[rank][o]),
+                                         remote_sem=T.sem[sem], src=src(o), dst=dst(rank)))
+            sent[0] += len(eng[rank][o])
+        g.remote_dma_fused(trs, local_sem=T.sem.sent)
+        total["sent"] = sent[0]
+
+    def arrival(key, sem, from_):
+        n_ = sum(len(eng[o][rank]) for o in from_)
+        wrote[key] = (sem, n_, "dma")
+        total[sem] = n_
+
+    def ts(o, a, s1, s2, o0, o1, r, w):
+        if o1 is None:
+            op("v", lambda: V.tensor_scalar(o, a, s1, None, o0), r, w)
+        else:
+            op("v", lambda: V.tensor_scalar(o, a, s1, s2, o0, o1), r, w)
+
+    def tt(o, a, b, o0, r, w):
+        op("v", lambda: V.tensor_tensor(o, a, b, o0), r, w)
+
+    def cp(o, a, r, w):
+        op("v", lambda: V.tensor_copy(o, a), r, w)
+
+    def ms(o, c, w, r=""):
+        op("v", lambda: V.memset(o, c), r, w)
+
+    def act(o, a, fn, r, w, **kw):
+        op("s", lambda: SE.activation(o, a, fn, **kw), r, w)
+
+    def mm(items, r, w, first=True, last=True):
+        def run():
+            ins = None
+            for o, prs in items:
+                for n_, (l, x) in enumerate(prs):
+                    ins = PE.matmul(o, l, x, first and n_ == 0, last and n_ == len(prs) - 1)
+            return ins
+        op("t", run, r, w)
+
+    def quarters(parts, r, w):
+        for items in parts:
+            mm(items, r + " " + w, w)
+
+    def iota(o, pat, base, cm, w, r=""):
+        op("g", lambda: g.iota(o, pat, base, cm, allow_small_or_imprecise_dtypes=True), r, w)
+
+    def sel(o, a, pat, cmp, fill, base, cm, r, w):
+        op("g", lambda: g.affine_select(o, a, pat, cmp, fill, base, cm), r, w)
+
+    cols = {}
+
+    def col(name):
+        if name not in cols:
+            cols[name] = len(cols)
+        return T.COL[:, cols[name]:cols[name] + 1]
+
+    def lins(specs):
+        for n_ in range(3):
+            for name, terms, const in specs:
+                if n_ < len(terms):
+                    c, k = terms[n_]
+                    dst = name if n_ == len(terms) - 1 else name + "~%d" % n_
+                    if n_ == 0 and not const:
+                        act(col(dst), col(c), F.Identity, "c" + c, "c" + dst, scale=float(k))
+                    elif n_ == 0:
+                        act(col(dst), col(c), F.Identity, "c" + c, "c" + dst, scale=float(k), bias=float(const))
+                    else:
+                        prev = name + "~%d" % (n_ - 1)
+                        act(col(dst), col(c), F.Identity, "c%s c%s" % (c, prev), "c" + dst, scale=float(k), bias=col(prev))
+
+    def cts(name, c, s1, s2, o0, o1=None):
+        r = " ".join("c" + x for x in (c, s1, s2) if isinstance(x, str))
+        ts(col(name), col(c), col(s1) if isinstance(s1, str) else s1, col(s2) if isinstance(s2, str) else s2, o0, o1, r, "c" + name)
+
+    def onehot(out, row, rk, tc, wc, key):
+        if isinstance(wc, str):
+            ts(out, row, col(tc), col(wc), A.is_equal, A.mult, "%s c%s c%s" % (rk, tc, wc), key)
+        else:
+            ts(out, row, col(tc), wc, A.is_equal, A.mult, "%s c%s EQ" % (rk, tc), key)
+
+    def scaled(out, a, ak, c, key):
+        act(out, a, F.Identity, "%s c%s" % (ak, c), key, scale=col(c))
+
+    P = [T["P%d" % k] for k in range(8)]
+    blk = lambda t, o, w: t[:, o * w:(o + 1) * w]
+    srcs = [rank] + sorted(peers, key=lambda o: -len(eng[o][rank]))
+    ID, REC = T.SH[:, 0:128], T.D[:, 0:512]
+    shift = lambda m, d: m[:, 128 - 32 * (d % 4):256 - 32 * (d % 4)]
+    qshift = lambda m, q, d: m[32 * q:32 * q + 32, 128 - 32 * (d % 4):256 - 32 * (d % 4)]
+
+    dma("y", [(blk(T.CS, o, 512), T.cells[32 * o:32 * o + 32, :]) for o in peers], "", "CS")
+    dma("y", [(T.KT[:], T.kids[:])], "", "KT")
+    dma("y", [(blk(T.LC, rank, 512), T.cells[32 * rank:32 * rank + 32, :])], "", "LC%d" % rank)
+    dma("y", [(T.YC[:, 0:S], T.cells[:])], "", "YC")
+    dma("y", [(T.KS[:, 160 * o:160 * o + 128], T.kids[8 * o:8 * o + 8, :]) for o in peers]
+        + [(T.KS[:, 160 * o + 128:160 * o + 160], T.nodes[32 * o:32 * o + 32, :]) for o in peers], "", "KS")
+    dma("y", [(T.LK[:, 160 * rank:160 * rank + 128], T.kids[8 * rank:8 * rank + 8, :]),
+              (T.LK[:, 160 * rank + 128:160 * rank + 160], T.nodes[32 * rank:32 * rank + 32, :])]
+        + [(T.WI[32 * q:32 * q + 32, 0:1], T.wt[32 * rank:32 * rank + 32, :]) for q in range(4)], "", "LKo WI")
+    iota(T.PI[:, 0:1], [[0, 1]], 0, 1, "PI")
+    iota(T.IF[:], [[1, 256]], 0, 0, "IF")
+    ms(T.RE[:], 1000.0, "RE")
+    ms(T.IDT[0:64, :], 0.0, "IDT")
+    ms(T.IDL[0:64, :], 0.0, "IDL")
+    ms(T.ONE[:], 1.0, "ONE")
+    for a in range(3):
+        for b in range(3):
+            iota(T.RE[:, 4 * a + b::16], [[64, 2], [16, 2], [4, 2]], 4 * (4 * a + b), -1, "RE0", "RE")
+    for a in range(2):
+        for b in range(2):
+            iota(T.RE[:, 12 + 2 * a + b::16], [[64, 2], [32, 2], [8, 2]], 4 * (4 * a + b), -1, "RE0")
+    iota(T.IDT[0:1, :], [[0, 4], [1, 128]], 0, 0, "IDT0", "IDT")
+    send(lambda o: blk(T.CS, o, 512), lambda o: blk(T.LC, o, 512), "ac%d" % rank, "CS")
+    for o in peers:
+        arrival("LC%d" % o, "ac%d" % o, [o])
+    sel(T.SH[:], T.ONE[:], [[0, 2], [-1, 128]], A.is_equal, 0.0, 0, 1, "ONE", "SH")
+    iota(T.RC[:, 0:16], [[1, 4], [0, 4]], 0, 0, "RC")
+    iota(T.RC[:, 16:32], [[0, 4], [1, 4]], 0, 0, "RC")
+    sel(T.O1[:], T.ONE[:, 0:128], [[-16, 8], [0, 16]], A.is_ge, 0.0, 0, 1, "ONE", "O1")
+    sel(T.OB[:], T.O1[:], [[16, 8], [0, 16]], A.is_ge, 0.0, 15, -1, "O1", "OB")
+    send(lambda o: blk(T.KS, o, 160), lambda o: blk(T.LK, o, 160), "ak", "KS")
+    arrival("LK", "ak", peers)
+    iota(T.CT[:, 0:192], [[0, 48], [1, 4]], 0, 0, "CT0")
+    iota(T.CT[:, 192:384], [[1, 48], [0, 4]], 0, 0, "CT0")
+    iota(T.R5[:], [[0, 4], [1, 32]], 0, 0, "R5")
+    iota(T.RM[:], [[0, 2], [1, 128]], 0, 0, "RM")
+    sel(T.TR[:], T.OB[:], [[-1, 128]], A.is_gt, 0.0, 0, 1, "OB", "TR")
+    iota(T.CA[:, 0:128], [[0, 4], [16, 32]], 2048, 0, "CA")
+    iota(T.FQ[:, 0:4], [[0, 4]], 1, 0, "FQ0")
+    for n_, thr in enumerate((-96, -64, -32, 0, 32, 64, 96)):
+        sel(T.FQ[:, 4 * n_ + 4:4 * n_ + 8], T.FQ[:, 4 * n_:4 * n_ + 4], [[32, 4]], A.is_gt, 2.0 ** (96 - 48 * ((n_ + 1) % 4)), thr, -1,
+            "FQ%d" % n_, "FQ%d" % (n_ + 1))
+    FQ = lambda d: T.FQ[:, 28 + d:29 + d]
+
+    fields = [("p", 0, 127), ("j", 0, 15), ("lo2", 0, 3), ("a2", 2, 3), ("b0", 0, 1), ("b1", 1, 1), ("b3", 3, 1), ("b4", 4, 1), ("b5", 5, 1),
+              ("b6", 6, 1), ("grp", 4, 7), ("q", 5, 3), ("k2", 4, 3), ("m2", 1, 3), ("h3", 1, 7), ("p31", 0, 31)]
+    for n_, (name, sh, mk) in enumerate(fields):
+        col(name)
+        ts(T.BI[:, n_:n_ + 1], T.PI[:, 0:1], sh, mk, A.logical_shift_right, A.bitwise_and, "PI", "BI")
+    ms(T.IDL[0:1, 3::16], 1.0, "IDL", "IDL")
+    ms(T.IDL[32:33, 7::16], 1.0, "IDL")
+    cp(T.COL[:, 0:16], T.BI[:, 0:16], "BI", " ".join("c" + x[0] for x in fields))
+    lins([("tRY", [("grp", 16), ("h3", 1)], 0), ("w16", [("b0", 15)], 1), ("tKP", [("grp", 16), ("a2", 2)], 9), ("nb3", [("b3", -1)], 1)])
+    lins([("nR", [("a2", -1), ("b5", 3)], -2), ("dR", [("b1", -1), ("a2", 1), ("b5", -1)], 0), ("nC", [("lo2", -1), ("b4", 3)], -2),
+          ("dC", [("b0", -1), ("lo2", 1), ("b4", -1)], 0), ("tNI", [("b6", 64), ("lo2", -16), ("a2", 1)], 60),
+          ("tKR", [("b4", 64), ("q", 4), ("m2", -16)], 51), ("wp0", [("b0", 63)], 1), ("wn0", [("b0", -127)], 128),
+          ("na", [("p", 0)], -(1.0 + 2.0 ** -10)), ("j512", [("j", -1)], 512)])
+    cts("hb", "lo2", 2.5, -14.0, A.is_lt, A.mult)
+    cts("i74", "j", 7.0, 4.0, A.is_equal, A.mult)
+    cts("is3", "j", 3.0, None, A.is_equal)
+    cts("mid", "a2", 3.0, None, A.is_equal)
+    cts("bh", "a2", 2.5, "hb", A.is_lt, A.mult)
+    cts("wNG", "j", 0.0, -4096.0, A.is_equal, A.mult)
+    for n_, c in enumerate(("lo2", "k2", "q")):
+        ts(T.EQ[:, 4 * n_:4 * n_ + 4], T.IF[:, 0:4], col(c), None, A.is_equal, None, "IF c" + c, "EQ")
+    for c in range(1, 4):
+        ms(T.IDT[32:33, 128 * c:128 * c + 128], float(c), "IDT")
+    ts(T.BB[:], T.IF[:, 0:16], col("i74"), col("bh"), A.mult, A.add, "IF ci74 cbh", "BB")
+    for u in range(4):
+        onehot(T.KP[:, 136 * u:136 * u + 129], T.IF[:, 0:129], "IF", "tKP", T.EQ[:, u:u + 1], "KP")
+
+    def b_number(banks):
+        for bank in banks:
+            mm([(P[bank][:], [(T.IDL[0:64, :], T.IDT[0:64, :])])], "IDL IDT IDT0", "P%d" % bank, True, False)
+
+    def b_cells(o, base):
+        for u in range(4):
+            bank, b = base + u, 4 * o + u
+            mm([(P[bank][:], [(blk(T.EU, u, 128), blk(T.LC, o, 512))])], "EU LC%d" % o, "P%d" % bank, False, True)
+            if u % 2:
+                ts(blk(T.B, b, 512), P[bank][:], T.BB[:, b:b + 1], 0.0, A.add, A.max, "P%d BB" % bank, "B%d" % b)
+            else:
+                act(blk(T.B, b, 512), P[bank][:], F.Relu, "P%d BB" % bank, "B%d" % b, bias=T.BB[:, b:b + 1])
+    b_number(range(4))
+
+    ts(T.KI[:, 0:512], T.KT[:], 7, None, A.logical_shift_right, None, "KT", "KI")
+    ts(T.KI[:, 512:1024], T.KT[:], 127, None, A.bitwise_and, None, "KT", "KI")
+    for u in range(4):
+        ts(blk(T.EU, u, 128), T.RE[:], float(-u), None, A.is_equal, None, "RE0", "EU")
+    cp(T.KB[:], T.KI[:], "KI", "KB")
+    onehot(T.RY[:], T.IF[:, 0:128], "IF", "tRY", "w16", "RY")
+    onehot(T.NG[:], T.IF[:, 0:128], "IF", "p", "wNG", "NG")
+    b_cells(srcs[0], 0)
+    act(T.NN[:, 0:1024], T.YC[:, 0:1024], F.Relu, "YC", "NN0", scale=-1.0)
+    ts(T.NN[:, 1024:2048], T.YC[:, 1024:2048], -1.0, 0.0, A.mult, A.max, "YC", "NN1")
+    for u in range(4):
+        mm([(P[4 + u][:], [(T.KP[:, 136 * u + 1:136 * u + 129], T.KB[:, 0:512]), (T.KP[:, 136 * u:136 * u + 128], T.KB[:, 512:1024])])],
+           "KP KB", "P%d" % (4 + u), True, False)
+    for u in (2, 0, 3, 1):
+        mm([(P[4 + u][:], [(T.RY[:], blk(T.YC, u, 512)), (T.NG[:], blk(T.NN, u, 512))])], "RY NG YC NN%d" % (u // 2), "P%d" % (4 + u), False, True)
+        act(blk(T.DS, u, 512), P[4 + u][:], F.Copy, "P%d" % (4 + u), "DS")
+    dma("y", [(T.DSD[:], T.DS[:])], "DS", "DSD")
+    send(lambda o: T.DSD[o], lambda o: T.DLD[o], "ad%d" % rank, "DSD")
+    for o in peers:
+        arrival("DLD%d" % o, "ad%d" % o, [o])
+    window = lambda o, src: [(T.D[32 * y:32 * y + 32, 512 + S * o:512 + S * o + S], src) for y in range(4)]
+    dma("y", window(rank, T.DS[32 * rank:32 * rank + 32, :]), "DS DSD", "Dw%d" % rank)
+    b_number(range(4))
+    cts("i37", "lo2", 3.0, "nb3", A.is_equal, A.mult)
+    cts("wh", "bh", -1.0, 2.0 ** -13, A.is_lt, A.mult)
+    ms(T.HZ[:, 0:64], 0.5, "HZ")
+    ms(T.HZ[:, 64:128], 0.0, "HZ")
+    ts(T.D16[:], T.IF[:, 0:16], col("j"), None, A.is_equal, None, "IF cj", "D16")
+    ms(T.AU[:], 0.0, "AU")
+    op("v", lambda: V.tensor_tensor_scan(T.PW[:, 0:64], T.HZ[:, 0:64], T.HZ[:, 64:128], 2.0, A.mult, A.add), "HZ", "PW")
+    ms(T.LW[:], 0.0, "LW")
+    cts("xR", "dR", "mid", "nR", A.mult, A.add)
+    cts("xC", "dC", "mid", "nC", A.mult, A.add)
+    cts("wm", "mid", "wh", None, A.subtract)
+    tt(T.DM[:, 0:16], T.PW[:, 0:16], T.D16[:], A.mult, "PW D16", "DM")
+    tt(T.DM[:, 16:24], T.PW[:, 0:64:9], T.D16[:, 0:8], A.mult, "PW D16", "DM")
+    ts(T.TM[:, 0:16], T.RC[:, 0:16], col("xR"), None, A.add, None, "RC cxR", "TM0")
+    ts(T.TM[:, 16:32], T.RC[:, 16:32], col("xC"), None, A.add, None, "RC cxC", "TM0")
+    for x in range(4):
+        onehot(T.NI[:, 144 * x:144 * x + 140], T.IF[:, 0:140], "IF", "tNI", T.EQ[:, 4 + x:5 + x], "NI")
+    tt(T.TM[:, 32:64], T.TM[:, 0:32], T.TM[:, 0:32], A.mult, "TM0", "TM1")
+    ts(T.WJ[:, 0:1], T.WI[:, 0:1], 6, None, A.logical_shift_right, None, "WI", "WJ")
+    ts(T.WJ[:, 1:2], T.WI[:, 0:1], 63, None, A.bitwise_and, None, "WI", "WJ")
+    tt(T.TM[:, 0:16], T.TM[:, 32:48], T.TM[:, 48:64], A.add, "TM1", "TM0")
+    b_cells(srcs[1], 0)
+    b_number((4, 5, 6, 7))
+    b_cells(srcs[2], 4)
+    b_number(range(4))
+    b_cells(srcs[3], 0)
+    for o in srcs[1:]:
+        dma("y", window(o, T.DLD[o]), "DLD%d" % o, "Dw%d" % o)
+
+    for o in range(N):
+        cp(T.KL[:, o::4], T.LK[:, 160 * o:160 * o + 128], "LK LKo", "KL")
+    allb = " ".join("B%d" % b for b in range(16))
+    act(T.CC[:, 0:4096], T.B[:, 0:8192].indirect(T.KL[:, 0:256]), F.Copy, allb + " KL", "CC0")
+    act(T.CC[:, 4096:16 * CUT], T.B[:, 0:8192].indirect(T.KL[:, 256:CUT]), F.Copy, allb + " KL", "CC1")
+    for o in range(N):
+        ts(T.NA[:, 32 * o:32 * o + 32], T.LK[:, 160 * o + 128:160 * o + 160], 7, None, A.logical_shift_right, None, "LK LKo", "NA")
+        ts(T.NA[:, 128 + 32 * o:160 + 32 * o], T.LK[:, 160 * o + 128:160 * o + 160], 127, None, A.bitwise_and, None, "LK LKo", "NA")
+    ts(T.TM[:, 32:48], T.TM[:, 0:16], 2.5, col("wh"), A.is_lt, A.mult, "TM0 cwh", "TM1")
+    ts(T.NF[:, 0:128], T.NA[:, 128:256], 64.0, None, A.mult, None, "NA", "NF0")
+    ts(T.TM[:, 48:64], T.TM[:, 0:16], 0.0, col("wm"), A.is_equal, A.mult, "TM0 cwm", "TM1")
+    tt(T.NF[:, 128:256], T.NF[:, 0:128], T.NA[:, 0:128], A.add, "NA NF0", "NF")
+    mm([(P[4][:, 32 * x:32 * x + 32], [(T.NI[:, 144 * x + 12 - 4 * r:144 * x + 140 - 4 * r], T.NF[:, 128 + 32 * r:160 + 32 * r]) for r in range(N)])
+        for x in range(4)], "NI NF", "P4")
+    for s in range(2):
+        h = slice(64 * s, 64 * s + 64)
+        tt(T.AU[h, 96 + 16 * s:112 + 16 * s], T.TM[h, 32:48], T.TM[h, 48:64], A.add, "TM1 AU", "AU1")
+    ts(col("whi"), T.WJ[:, 0:1], 64.0, None, A.mult, None, "WJ", "cwhi")
+    cp(col("wlo"), T.WJ[:, 1:2], "WJ", "cwlo")
+    cp(T.CC[:, 16 * CUT:8192], T.B[:, 0:8192].indirect(T.KL[:, CUT:512]), allb + " KL", "CC2")
+    for x in range(4):
+        cp(T.PL[:, x::4], P[4][:, 32 * x:32 * x + 32], "P4", "PL")
+    allc = "CC0 CC1 CC2"
+    chain = lambda n_, i: T.LW[:, 144 * n_ + 15 - i:144 * n_ + 143 - i]
+
+    def chains(names):
+        for n_, c in names:
+            ts(T.LW[:, 144 * n_ + 15:144 * n_ + 143:16], T.OB[:, 0::16], col(c), None, A.mult, None, "OB LW c" + c, "LW%d" % n_)
+
+    iota(T.WX[:], [[0, 128]], 0, 0, "WX0")
+    iota(T.TM[:, 64:80], [[0, 16]], 1, 0, "ONF")
+    iota(T.O1[:, 0:8], [[0, 8]], 16, 0, "O1")
+    sel(T.WX[:, 8::16], T.O1[:, 0:8], [[-16, 8]], A.is_equal, 0.0, -7, 1, "WX0 O1", "WX")
+    sel(T.WX[:, 9::16], T.O1[:, 0:8], [[-16, 8]], A.is_equal, 0.0, -3, 1, "WX0 O1", "WX")
+    iota(T.NO[:], [[0, 704]], 0, 0, "NO0")
+    for r in range(4):
+        for s in range(2):
+            c0 = 176 * r + 48 + 64 * s
+            sel(T.NO[:, c0:c0 + 16], T.TM[:, 64:80], [[-1, 4], [16, 4]], A.is_equal, 0.0, -(64 * s + 48 + 4 * r), 1, "NO0 ONF", "NO")
+
+    def constants_1():
+        chains([(0, "whi"), (1, "wlo")])
+        lins([("tGW", [("b6", 16), ("k2", -2), ("is3", 1)], 110)])
+        op("v", lambda: V.tensor_reduce(col("ci"), T.DM[:, 0:16], X.X, A.add), "DM", "cci")
+        op("v", lambda: V.tensor_reduce(col("wS"), T.DM[:, 16:24], X.X, A.add), "DM", "cwS")
+        cts("is8", "j", 8.0, None, A.is_equal)
+        cts("w9", "j", 9.0, 16.0, A.is_equal, A.mult)
+        cts("is0", "j", 0.0, None, A.is_equal)
+        onehot(T.GW[:], T.IF[:, 0:224], "IF", "tGW", "i37", "GW")
+        act(T.DM[:, 32:64], T.IF[:, 0:32], F.Identity, "IF cj512", "DM", scale=-16.0, bias=col("j512"))
+
+    def constants_2():
+        lins([("c4r", [("q", -1)], 4), ("w8", [("is8", 16)], 0), ("c8", [("q", 64)], 1024), ("j4", [("j", 1)], 4),
+              ("wkey", [("is8", 128), ("w9", 0.0625)], 0), ("wRX", [("b3", 16)], 0), ("jD", [("j", 4)], 8192)])
+        chains([(2, "wS")])
+        cts("wpi", "wp0", "b3", None, A.mult)
+        ts(T.CT[:, 576:768], T.CT[:, 192:384], col("w9"), None, A.mult, None, "CT0 cw9", "CT1")
+        ms(T.RT[:], 1.0, "RT")
+        ts(T.DI[:, 0:4], T.IF[:, 0:4], col("c4r"), None, A.add, None, "IF cc4r", "DI0")
+        cts("c88", "c8", "is8", None, A.mult)
+        ts(T.DI[:, 8:12], T.DI[:, 0:4], 3, None, A.bitwise_and, None, "DI0", "DI1")
+        ts(T.CT[:, 384:576], T.CT[:, 0:192], col("w8"), col("c88"), A.mult, A.add, "CT0 cw8 cc88", "CT1")
+        ts(T.DF[:, 0:4], T.DI[:, 8:12], -1.0, col("j4"), A.mult, A.add, "DI1 cj4", "DF")
+        tt(T.CW[:, 576:768], T.CT[:, 384:576], T.CT[:, 576:768], A.add, "CT1", "CW0")
+        dma("y", [(T.CW[:, 192 * x:192 * x + 192], T.CW[:, 576:768]) for x in range(3)], "CW0", "CW")
+        ms(T.RT[:, 0::32], 0.0, "RT", "RT")
+        onehot(T.KR[:, 0:131], T.IF[:, 0:131], "IF", "tKR", "wpi", "KR")
+        chains([(3, "wkey"), (4, "is0")])
+
+    def constants_3():
+        scaled(T.RX[:], T.SH[:, 8:136], "SH", "wRX", "RX")
+        for o in range(4):
+            act(T.CA[:, 128 + 32 * o:160 + 32 * o], T.HZ[:, 64:96], F.Identity, "HZ DF", "CA1", bias=T.DF[:, o:o + 1])
+        act(T.DM[:, 0:32], T.IF[:, 0:32], F.Identity, "IF cj", "DM", scale=16.0, bias=col("j"))
+        act(T.DM[:, 64:96], T.IF[:, 0:32], F.Identity, "IF cjD", "DM", scale=64.0, bias=col("jD"))
+        scaled(T.BC[:], T.OB[:], "OB", "wkey", "BC")
+        lins([("tAY", [("b4", 16), ("h3", 1)], 0), ("tAX", [("p31", 1)], 8), ("cDL", [("q", 192), ("j", 1)], 10240),
+              ("n2", [("p", 0)], -2), ("c15", [("p", 0)], 15)])
+        act(T.PW[:, 64:112], T.PW[:, 0:48], F.Identity, "PW", "PW2", scale=2.5)
+        act(T.DL[:, 0:12], T.IF[:, 0:12], F.Identity, "IF ccDL", "DL", scale=16.0, bias=col("cDL"))
+        for d in range(4):
+            act(T.TH[:, 48 * d:48 * d + 48], T.PW[:, 64:112], F.Identity, "PW2 FQ7", "TH", scale=FQ(d))
+
+    def constants_4():
+        for d in range(4):
+            ts(T.WC[:, 3 * d:3 * d + 3], T.PW[:, 0:48:16], FQ(d), col("ci"), A.mult, A.mult, "PW FQ7 cci", "WC")
+        onehot(T.RA[:, 0:128], T.R5[:], "R5", "tAY", "w16", "RA")
+        onehot(T.RA[:, 128:256], T.R5[:], "R5", "tAX", "nb3", "RA")
+        cts("wna", "wn0", "b3", None, A.mult)
+        cts("wkn", "wn0", "nb3", None, A.mult)
+
+    def constants_5():
+        for o in range(N):
+            onehot(blk(T.RP, o, 128), T.R5[:], "R5", "p31", T.EQ[:, 8 + o:9 + o], "RP")
+
+    def constants_6():
+        onehot(T.SK[:], T.RM[:], "RM", "tRY", "wkn", "SK")
+        cp(T.KF[:], T.KT[:], "KT", "KF")
+        dma("y", [(T.KD[:], T.KF[:])], "KF", "KD")
+        dma("y", [(T.YK[t::16, 0:S], T.KD[t::4, :]) for t in range(4)], "KD", "YK")
+        onehot(T.KR[:, 136:267], T.IF[:, 0:131], "IF", "tKR", "wna", "KR")
+
+    def gather(rd):
+        if rd == 0:
+            cp(T.G[:, 0:1024], T.CC[:, 0:8192].indirect(T.PL[:, 0:64]), allc + " PL", "G")
+            act(T.G[:, 1024:2048], T.CC[:, 0:8192].indirect(T.PL[:, 64:128]), F.Copy, allc + " PL", "G1")
+        else:
+            act(T.G[:], T.CC[:, 0:8192].indirect(T.PL[:]), F.Copy, allc + " PL", "G G1")
+
+    def near():
+        for k in range(2):
+            mm([(P[k][:, 128 * i:128 * i + 128], [(T.AU[:, 96 - 32 * r:224 - 32 * r], T.G[:, 4 * r + 2 * k + i::16]) for r in range(N)])
+                for i in range(2)], "AU1 G G1", "P%d" % k)
+
+    def life(rd):
+        for k in (0, 1):
+            if rd:
+                act(blk(T.UA, k, 256), P[k][:, 0:256], F.Abs, "P%d cn2" % k, "UA", scale=8192.0, bias=col("n2"))
+            else:
+                for i in range(2):
+                    ts(T.AB[:, 512 + 2 * k + i::4], P[k][:, 128 * i:128 * i + 128], 2.0 ** -12, 15.0, A.is_equal, A.mult, "P%d" % k, "Ab")
+            for i in range(2):
+                act(T.AB[:, 2 * k + i:512:4], P[k][:, 128 * i:128 * i + 128], F.Relu, "P%d cna" % k, "Aa", bias=col("na"))
+        if rd:
+            for i in range(4):
+                act(T.AB[:, 512 + i::4], blk(T.UA, i, 128), F.Relu, "UA cc15", "Ab", scale=-15.0, bias=col("c15"))
+
+    def hash_mm():
+        mm([(P[2][:, 0:64], [(chain(n_, i), T.AB[:, i::16]) for i in range(16) for n_ in range(2)])], "LW0 LW1 Aa Ab", "P2")
+
+    def rec_mm():
+        mm([(P[3][:, 128 * i:128 * i + 128], [(T.GW[:, 96 - 32 * r:224 - 32 * r], T.G[:, 4 * r + i::16]) for r in range(N)]
+             + [(T.RY[:], T.AB[:, i:512:4]), (T.RY[:], T.AB[:, 512 + i::4])]) for i in range(4)], "GW RY G G1 Aa Ab", "P3")
+
+    def rec_out():
+        for i in range(4):
+            act(T.D[:, i:512:4], P[3][:, 128 * i:128 * i + 128], F.Copy, "P3", "REC")
+
+    H, H1, OO, TI, B0 = (T.HI[:, 32 * x:32 * x + 32] for x in range(5))
+    DH, O1, HM, TF = (T.HF[:, 32 * x:32 * x + 32] for x in range(4))
+
+    def hash_ops():
+        act(TF, P[2][:, 0:32], F.Copy, "P2", "TF")
+        tt(TI, TF, P[2][:, 32:64], A.add, "TF P2", "TI")
+        ts(B0, TI, 1, None, A.bitwise_and, None, "TI", "B0")
+        ts(H, TI, 8191, None, A.bitwise_and, None, "TI", "H")
+        ts(OO, TI, 11, 3, A.logical_shift_right, A.bitwise_and, "TI", "OO")
+        ts(DH, B0, 2.0, -1.0, A.mult, A.add, "B0", "DH")
+        ts(O1, OO, 1.0, None, A.add, None, "OO", "O1")
+        tt(H1, H, DH, A.subtract, "H DH", "H1")
+        cp(T.HL[:], T.HI[:, 0:64], "H H1", "HL")
+        tt(HM, H1, T.DM[:, 32:64], A.add, "H1 DM", "HM")
+
+    def look():
+        for x in range(2):
+            tt(blk(T.DD, x, 512), T.D[:, 512:8704].indirect(blk(T.HL, x, 32)), REC, A.subtract, "D Dw0 Dw1 Dw2 Dw3 REC HL", "DD%d" % x)
+        mm([(P[3][:], [(ID, T.AB[:, 0:512]), (ID, T.AB[:, 512:1024]), (T.RX[:], REC)])], "SH RX Aa Ab REC", "P3", True, False)
+        mm([(P[5][:, 0:64], [(chain(2, i), T.DD[:, i::16]) for i in range(16)])], "LW2 DD0 DD1", "P5")
+
+    c32 = lambda x, n_=1: T.CL[:, 32 * x:32 * (x + n_)]
+
+    def flags(rd):
+        ts(c32(0, 2), P[5][:, 0:64], -1000.0, None, A.is_lt, None, "P5", "FR")
+        ts(c32(2, 2), P[5][:, 0:64], 0.0, None, A.is_equal, None, "P5", "HT")
+        tt(c32(4), c32(0), DH, A.mult, "FR DH", "C4")
+        tt(c32(5), c32(0), c32(1), A.max, "FR", "C5")
+        tt(c32(6), c32(2), c32(3), A.max, "HT", "C6")
+        tt(c32(7), c32(4), H1, A.add, "C4 H1", "C7")
+        tt(c32(8), c32(5), c32(6), A.is_gt, "C5 C6", "C8")
+        cp(T.WL[:], c32(7), "C7", "WL")
+        tt(c32(9), c32(8), O1, A.mult, "C8 O1", "C9")
+        act(T.WG[:], T.B[:, 0:8192].indirect(T.WL[:]), F.Copy, allb + " WL", "WG")
+        tt(c32(10), c32(2), DH, A.mult, "HT DH", "C10")
+        for o in range(N):
+            ts(T.FB[:, 32 * o:32 * o + 32], c32(9), float(o + 1), 4.0, A.is_equal, A.mult, "C9", "FB")
+        mm([(P[5][:, 128:256], [(T.OB[:], T.FB[:])]), (P[5][:, 256:384], [(ID, T.CA[:, 0:128]), (ID, T.CA[:, 128:256]), (T.TR[:], T.FB[:])])],
+           "OB TR SH CA CA1 FB", "P5")
+        mm([(P[3][:], [(T.WX[:], T.WG[:])])], "WX WG", "P3", False, True)
+        tt(c32(11), c32(6), HM, A.mult, "C6 HM", "C11")
+        tt(c32(12), c32(10), T.DM[:, 0:32], A.add, "C10 DM", "C12")
+        op("v", lambda: V.tensor_tensor_scan(T.SC[:, 0:128], T.RT[:], P[5][:, 128:256], 0.0, A.mult, A.add), "RT P5", "SC0")
+        tt(c32(13), c32(11), c32(12), A.add, "C11 C12", "C13")
+        tt(T.SC[:, 128:256], T.SC[:, 0:128], P[5][:, 256:384], A.subtract, "SC0 P5", "SC1")
+        cp(T.AT[:], c32(13), "C13", "AT")
+        act(T.RQ[:], P[3][:], F.Copy, "P3", "RQ")
+        act(T.PG[:], T.D[:, 0:8704].indirect(T.AT[:]), F.Copy, "D REC AT", "PG")
+        kr = 136 if rd == RO - 1 else 0
+        mm([(P[2][:, 128:256], [(T.KR[:, kr + 3 - i:kr + 131 - i], T.PG[:, i::4]) for i in range(4)])], "KR PG", "P2")
+        tt(T.SC[:, 256:384], T.SC[:, 128:256], T.FB[:], A.mult, "SC1 FB", "SC2")
+        tt(T.SC[:, 0:64], T.SC[:, 256:320], T.SC[:, 320:384], A.add, "SC2", "SC0")
+        tt(c32(14), T.SC[:, 0:32], T.DM[:, 64:96], A.add, "SC0 DM", "C14")
+        tt(c32(15), c32(14), T.SC[:, 32:64], A.add, "C14 SC0", "C15")
+        ts(T.OL[:], c32(15), 0.25, None, A.mult, None, "C15", "OL")
+
+    def nodes_out():
+        act(T.PN[:], P[2][:, 128:256], F.Copy, "P2", "PN")
+        mm([(P[1][:, 32 * r:32 * r + 32], [(T.NO[:, 176 * r + 48 - 16 * x:176 * r + 176 - 16 * x], T.PN[:, x::4]) for x in range(4)])
+            for r in range(N)], "NO PN", "P1")
+        act(T.NS[:], P[1][:, 0:128], F.Copy, "P1", "NS")
+        send(lambda o: blk(T.NS, o, 32), lambda o: blk(T.NL, o, 32), "an", "NS")
+        arrival("NL", "an", peers)
+        dma("y", [(T.ynodes[32 * rank:32 * rank + 32, :], blk(T.NS, rank, 32))], "NS", "yn0")
+        dma("y", [(T.ynodes[32 * o:32 * o + 32, :], blk(T.NL, o, 32)) for o in peers], "NL", "yn")
+
+    def compact(rd):
+        w0 = 192 * (RO - 1 - rd)
+        cp(T.CW[:, w0:w0 + 2560].indirect(T.OL[:]), T.RQ[:], "OL RQ CW0", "CW")
+        ts(T.CI[:, 192:384], T.CW[:, w0:w0 + 192], 4, None, A.logical_shift_right, None, "CW", "CI2")
+        ts(T.CI[:, 0:192], T.CW[:, w0:w0 + 192], 15, None, A.bitwise_and, None, "CW", "CI")
+        cp(T.YX[:, 192:384], T.CI[:, 192:384], "CI2", "YX1")
+        cp(T.YX[:, 0:192], T.CI[:, 0:192], "CI", "YX0")
+        mm([(P[6][:, 192 + 48 * d:240 + 48 * d], [(shift(T.SH, d), T.YX[:, 192 + d:384:4])]) for d in range(4)], "SH YX1", "P6")
+        mm([(P[4][:, 48 * d:48 * d + 48], [(shift(T.SH, d), T.YX[:, d:192:4])]) for d in range(4)], "SH YX0", "P4")
+
+    def owners():
+        act(T.OY[:, 192:384], P[6][:, 192:384], F.Copy, "P6", "OX")
+        mm([(P[7][:, 0:192], [(T.BC[:], T.OY[:, 192:384])]),
+            (P[7][:, 192:204], [(chain(3, i), T.OY[:, 192 + i:384:16]) for i in range(16)])], "BC LW3 OX", "P7")
+        act(T.OY[:, 0:192], P[4][:, 0:192], F.Copy, "P4", "OY")
+
+    def all_mm():
+        for x in range(2):
+            for k in range(2):
+                o = 2 * k + x
+                quarters([[(P[4 + k][:, 192 * x:192 * x + 192], [(T.RA[32 * o:32 * o + 32, 0:128], T.OY[32 * o:32 * o + 32, 0:192]),
+                                                                (T.RA[32 * o:32 * o + 32, 128:256], T.OY[32 * o:32 * o + 32, 192:384])])]],
+                         "RA OY OX", "P%d" % (4 + k))
+
+    def equal():
+        cp(T.KU[:], P[7][:, 0:192], "P7", "KU")
+        cp(T.KC[:, 0:12], P[7][:, 192:204], "P7", "KC")
+        for j in range(12):
+            ts(blk(T.E, j, 192), T.KU[:], T.KC[:, j:j + 1], T.WC[:, j:j + 1], A.is_equal, A.mult, "KU KC WC", "E%d" % (j // 4))
+        tt(T.KC[:, 16:28], T.KC[:, 0:12], T.DL[:, 0:12], A.subtract, "KC DL", "K1")
+        for k in range(3):
+            mm([(P[6][:, 0:192], [(T.OB[:], blk(T.E, j, 192)) for j in range(4 * k, 4 * k + 4)])], "OB E%d" % k, "P6", k == 0, k == 2)
+
+    def winners():
+        tt(T.WN[:], P[6][:, 0:192], T.TH[:], A.is_lt, "P6 TH", "WN")
+        mm([(P[7][:, 256:268], [(chain(4, i), T.WN[:, i::16]) for i in range(16)])], "LW4 WN", "P7")
+
+    def offsets(rd):
+        tt(T.KC[:, 32:44], P[7][:, 256:268], T.KC[:, 16:28], A.mult, "P7 K1", "K2")
+        tt(T.KC[:, 48:60], T.KC[:, 32:44], T.DL[:, 0:12], A.add, "K2 DL", "K3")
+        if rd < RO - 1:
+            mm([(P[6][:, 256 + 12 * o:268 + 12 * o], [(blk(T.RP, o, 128), T.KC[:, 48:60])]) for o in range(N)], "RP K3", "P6")
+        cp(T.OH[:, 0:24:2], T.KC[:, 48:60], "K3", "OH0")
+        tt(T.OH[:, 1:24:2], T.KC[:, 48:60], T.OH[:, 0:24:2], A.subtract, "K3 OH0", "OH1")
+
+    records = lambda o: [(P[0][:, TW * o + 48 * x:TW * o + 48 * x + 48],
+                          [(qshift(T.SH, o, d - o), T.OY[32 * o:32 * o + 32, 192 * x + 48 * d:192 * x + 48 * d + 48]) for d in range(4)]) for x in range(2)]
+    places = lambda o: [(P[0][:, TW * o + 96:TW * o + 102], [(qshift(T.SH, o, d - o), T.OH[32 * o:32 * o + 32, 6 * d:6 * d + 6]) for d in range(4)])]
+
+    def parcel(rd):
+        quarters([places(o) + (records(o) if rd < RO - 1 else []) for o in range(N)], "SH OY OX OH0 OH1", "P0")
+        act(blk(T.TS, rd, N * TW), P[0][:, 0:N * TW], F.Copy, "P0", "TS%d" % rd)
+        send(lambda o: blk(T.TS, N * rd + o, TW), lambda o: blk(T.TL, N * rd + o, TW), "ar%d" % rd, "TS%d" % rd)
+        arrival("TL%d" % rd, "ar%d" % rd, peers)
+
+    def all_out():
+        for k in range(2):
+            act(T.RL[:, 384 * k:384 * k + 384], P[4 + k][:, 0:384], F.Copy, "P%d" % (4 + k), "RL")
+
+    def update():
+        cp(T.AL[:], P[6][:, 256:304], "P6", "AL")
+        cp(T.D[:, 512:512 + DW].indirect(T.AL[:]), T.RL[:], "AL RL", "D")
+
+    def unpack(rd):
+        def got(o, d, a, b, st=1):
+            c0 = TW * (N * rd + o)
+            return (T.TS if o == rank else T.TL)[32 * d:32 * d + 32, c0 + a:c0 + b:st]
+        k = "SH SK TS%d TL%d" % (rd, rd)
+        for d in range(4):
+            quarters([[(P[3][:, 300 + 48 * d:348 + 48 * d], [(qshift(T.SH, d, o - d), got(o, d, 0, 48)) for o in srcs]),
+                       (P[3][:, 492 + 3 * d:495 + 3 * d], [(qshift(T.SH, d, o - d), got(o, d, 96 + x, 102, 2)) for o in srcs for x in range(2)])]], k, "P3")
+            quarters([[(P[5][:, 48 * d:48 + 48 * d], [(qshift(T.SK, d, o - d), got(o, d, 48, 96)) for o in srcs])]], k, "P5")
+
+    def unpack_out():
+        cp(T.RBY[:], P[3][:, 300:492], "P3", "RBY")
+        ts(T.XL[:, 0:12], P[3][:, 492:504], float(-S * rank), None, A.add, None, "P3", "XL")
+        act(T.RBK[:], P[5][:, 0:192], F.Copy, "P5", "RBK")
+
+    def place(rd, x):
+        if x == 0:
+            cp(T.YC[:, 0:DW].indirect(T.XL[:, 0:12]), T.RBY[:], "XL RBY", "YC")
+            if rd == RO - 1:
+                dma("y", [(T.ycells[:], T.YC[:, 0:S])], "YC", "yc")
+        else:
+            cp(T.YK[:, 0:DW].indirect(T.XL[:, 0:12]), T.RBK[:], "XL RBK", "YK")
+            if rd == RO - 1:
+                dma("s", [(T.ykids[t::4, :], T.YK[t::16, 0:S]) for t in range(4)], "YK", "yk")
+
+    gather(0)
+    near()
+    constants_1()
+    life(0)
+    hash_mm()
+    rec_mm()
+    constants_2()
+    hash_ops()
+    rec_out()
+    constants_3()
+    for rd in range(RO):
+        more = rd < RO - 1
+        look()
+        flags(rd)
+        if more:
+            cp(T.PL[:], P[2][:, 128:256], "P2", "PL")
+            gather(rd + 1)
+        if rd:
+            unpack(rd - 1)
+        compact(rd)
+        owners()
+        if rd:
+            unpack_out()
+            place(rd - 1, 0)
+        else:
+            constants_4()
+        if more:
+            near()
+            all_mm()
+            life(rd + 1)
+        else:
+            quarters([records(o) for o in range(N)], "SH OY OX", "P0")
+        equal()
+        if more:
+            all_out()
+        winners()
+        if rd:
+            place(rd - 1, 1)
+        else:
+            constants_5()
+        offsets(rd)
+        if not rd:
+            constants_6()
+        if more:
+            hash_mm()
+            rec_mm()
+            update()
+            hash_ops()
+            rec_out()
+        parcel(rd)
+    nodes_out()
+    unpack(RO - 1)
+    unpack_out()
+    place(RO - 1, 0)
+    place(RO - 1, 1)
+    for sem, n_ in total.items():
+        need("g", (sem, n_))

@@ -2,28 +2,29 @@ from concourse.bass import DstId, RemoteDMATransfer
 from concourse.mybir import AluOpType as A, ActivationFunctionType as F, AxisListType as X
 
 N, S, RO = 4, 2048, 4
-DW = 11008
-TW = 102
+DW = 8704
+YW = 2112
+TW = 56
 CUT = 316
 f32, bf, i32, u16 = "float32", "bfloat16", "int32", "uint16"
 SB = {
-    "CS": (2048, bf), "LC": (2048, bf), "KS": (640, i32), "LK": (640, i32), "YC": (DW, bf), "YK": (DW, f32),
+    "CS": (2048, bf), "LC": (2048, bf), "KS": (640, i32), "LK": (640, i32), "YC": (YW, bf), "YK": (YW, f32),
     "KT": (512, i32), "KI": (1024, i32), "KB": (1024, bf), "KF": (512, f32), "NN": (2048, bf), "DS": (2048, bf),
-    "B": (8192, bf), "CC": (8192, bf), "D": (512 + DW, bf), "KL": (512, u16), "WI": (8, i32), "WJ": (8, i32),
-    "PI": (8, i32), "BI": (16, i32), "COL": (128, f32), "IF": (256, f32), "RM": (256, f32),
+    "B": (512 + 8192, bf), "CC": (8192, bf), "D": (512 + DW, bf), "KL": (512, u16), "WI": (8, i32), "WJ": (8, i32),
+    "PI": (8, i32), "BI": (24, i32), "COL": (128, f32), "IF": (256, f32),
     "R5": (128, f32), "RE": (128, f32), "RC": (32, f32), "EU": (512, bf), "IDT": (512, bf), "IDL": (128, bf), "BB": (16, f32),
-    "AU": (224, bf), "TM": (80, f32), "RY": (128, bf), "NG": (128, bf), "GW": (224, bf), "KP": (544, bf),
-    "KR": (272, bf), "OB": (128, bf), "O1": (128, bf), "TR": (128, bf), "RX": (128, bf), "WX": (128, bf), "SH": (256, bf), "ONE": (256, bf),
-    "BC": (128, bf), "SK": (256, bf), "RA": (256, bf), "RP": (512, f32), "NI": (576, f32), "NO": (704, f32), "LW": (720, bf),
-    "EQ": (16, f32), "PW": (128, f32), "HZ": (128, f32), "D16": (16, f32), "FQ": (32, f32), "TH": (192, f32), "WC": (16, f32),
-    "CW": (576 + 2560, i32), "CI": (384, i32), "CT": (768, f32), "DL": (16, f32), "DM": (96, f32), "RT": (128, f32), "CA": (256, bf),
-    "DI": (16, i32), "DF": (8, f32),
-    "NA": (256, i32), "NF": (256, f32), "PL": (128, u16), "G": (2048, bf), "AB": (1024, bf), "UA": (512, bf), "DD": (1024, bf),
-    "HI": (256, i32), "HF": (192, f32), "HL": (64, u16), "PN": (128, f32), "CL": (512, f32), "PG": (512, bf),
-    "FB": (128, bf), "SC": (384, f32), "WL": (32, u16), "AT": (32, u16), "OL": (32, u16), "WG": (512, bf), "RQ": (512, f32), "YX": (384, bf),
-    "OY": (384, bf), "KU": (192, u16), "KC": (64, f32), "E": (12 * 192, bf), "WN": (192, bf), "AL": (48, u16), "RL": (768, bf),
-    "OH": (32, bf), "TS": (RO * N * TW, bf), "TL": (RO * N * TW, bf), "RBY": (192, bf), "RBK": (192, f32), "XL": (16, u16),
-    "NS": (128, f32), "NL": (128, f32),
+    "AU": (224, bf), "TM": (64, f32), "RY": (128, bf), "NG": (128, bf), "GW": (224, bf), "KP": (544, bf),
+    "KR": (272, bf), "OB": (128, bf), "O1": (128, bf), "TR": (128, bf), "M2": (128, bf), "WX": (128, bf), "WE": (128, bf), "SH": (256, bf),
+    "ONE": (256, bf), "BC": (128, bf), "SK": (128, bf), "UY": (128, bf), "UZ": (256, bf), "RP": (640, f32), "RB": (512, bf), "RZ": (640, bf),
+    "NI": (576, f32), "NO": (704, f32), "LW": (576, bf), "EQ": (16, f32), "ZR": (128, bf),
+    "CW": (576 + 2560, f32), "CT": (576, f32), "OWN": (32, f32), "RT": (128, bf), "CA": (128, bf), "DP": (128, f32),
+    "MR": (384, f32), "MK": (384, bf), "RS": (576, bf), "UC": (64, f32), "XD": (16, f32),
+    "NA": (256, i32), "NF": (256, f32), "PL": (128, u16), "G": (2048, bf), "AB": (1024, bf), "UA": (512, bf), "DD": (1024, bf), "RX": (512, bf),
+    "HI": (256, i32), "HF": (128, f32), "HL": (64, u16), "PN": (128, f32), "CL": (384, f32), "PG": (512, bf),
+    "FB": (128, bf), "RR": (128, bf), "SQ": (128, f32), "AT": (32, u16), "OL": (32, u16), "WG": (512, bf), "RQ": (512, f32),
+    "HX": (192, bf), "KC": (16, f32), "E": (576, bf), "ZS": (576, bf), "AF": (64, f32), "AL": (48, u16), "RL": (768, bf),
+    "OH": (32, bf), "TS": (RO * N * TW, bf), "TL": (RO * N * TW, bf), "VT": (N * TW, bf), "VA": (N * TW, bf),
+    "RBY": (RO * N * TW, bf), "RBK": (RO * N * TW, f32), "XF": (16, f32), "XL": (RO * 16, u16), "NS": (128, f32), "NL": (128, f32),
 }
 SCRATCH = {n: ("sbuf", [128, w], d) for n, (w, d) in SB.items()}
 SCRATCH.update({"P%d" % k: ("psum", [128, 512], f32) for k in range(8)})
@@ -58,7 +59,8 @@ def rank_program(g, core, T, topo):
                         need(e, tok)
         for k in w:
             for tok in read.get(k, []):
-                need(e, tok)
+                if tok[2] != who or who != "t":
+                    need(e, tok)
             if k in wrote and (wrote[k][2] != who or who == "dma"):
                 need(e, wrote[k])
 
@@ -137,6 +139,9 @@ def rank_program(g, core, T, topo):
     def ms(o, c, w, r=""):
         op("v", lambda: V.memset(o, c), r, w)
 
+    def scan(o, a, b, init, o0, o1, r, w):
+        op("v", lambda: V.tensor_tensor_scan(o, a, b, init, o0, o1), r, w)
+
     def act(o, a, fn, r, w, **kw):
         op("s", lambda: SE.activation(o, a, fn, **kw), r, w)
 
@@ -146,6 +151,14 @@ def rank_program(g, core, T, topo):
             for o, prs in items:
                 for n_, (l, x) in enumerate(prs):
                     ins = PE.matmul(o, l, x, first and n_ == 0, last and n_ == len(prs) - 1)
+            return ins
+        op("t", run, r, w)
+
+    def more_mm(items, r, w, last=False):
+        def run():
+            ins = None
+            for n_, (o, l, x) in enumerate(items):
+                ins = PE.matmul(o, l, x, False, last and n_ == len(items) - 1)
             return ins
         op("t", run, r, w)
 
@@ -197,7 +210,6 @@ def rank_program(g, core, T, topo):
     blk = lambda t, o, w: t[:, o * w:(o + 1) * w]
     srcs = [rank] + sorted(peers, key=lambda o: -len(eng[o][rank]))
     ID, REC = T.SH[:, 0:128], T.D[:, 0:512]
-    shift = lambda m, d: m[:, 128 - 32 * (d % 4):256 - 32 * (d % 4)]
     qshift = lambda m, q, d: m[32 * q:32 * q + 32, 128 - 32 * (d % 4):256 - 32 * (d % 4)]
 
     dma("y", [(blk(T.CS, o, 512), T.cells[32 * o:32 * o + 32, :]) for o in peers], "", "CS")
@@ -232,39 +244,37 @@ def rank_program(g, core, T, topo):
     sel(T.OB[:], T.O1[:], [[16, 8], [0, 16]], A.is_ge, 0.0, 15, -1, "O1", "OB")
     send(lambda o: blk(T.KS, o, 160), lambda o: blk(T.LK, o, 160), "ak", "KS")
     arrival("LK", "ak", peers)
-    iota(T.CT[:, 0:192], [[0, 48], [1, 4]], 0, 0, "CT0")
-    iota(T.CT[:, 192:384], [[1, 48], [0, 4]], 0, 0, "CT0")
     iota(T.R5[:], [[0, 4], [1, 32]], 0, 0, "R5")
-    iota(T.RM[:], [[0, 2], [1, 128]], 0, 0, "RM")
     sel(T.TR[:], T.OB[:], [[-1, 128]], A.is_gt, 0.0, 0, 1, "OB", "TR")
-    iota(T.CA[:, 0:128], [[0, 4], [16, 32]], 2048, 0, "CA")
-    iota(T.FQ[:, 0:4], [[0, 4]], 1, 0, "FQ0")
-    for n_, thr in enumerate((-96, -64, -32, 0, 32, 64, 96)):
-        sel(T.FQ[:, 4 * n_ + 4:4 * n_ + 8], T.FQ[:, 4 * n_:4 * n_ + 4], [[32, 4]], A.is_gt, 2.0 ** (96 - 48 * ((n_ + 1) % 4)), thr, -1,
-            "FQ%d" % n_, "FQ%d" % (n_ + 1))
-    FQ = lambda d: T.FQ[:, 28 + d:29 + d]
+    iota(T.CA[:], [[0, 32], [1, 4]], -4, 0, "CA")
+    iota(T.CT[:, 0:192], [[0, 48], [512, 4]], 64 * 512, 0, "CT0")
+    iota(T.CT[:, 192:384], [[512, 48], [0, 4]], 0, 0, "CT0")
+    for jj, c0 in enumerate((0, 64, 192)):
+        iota(T.MR[:, c0:c0 + 64 * (jj + 1)], [[0, 4], [1, 16 * (jj + 1)]], -16 * jj, 0, "MR")
+    iota(T.UC[:, 0:60], [[0, 5], [128, 4], [16, 3]], 8192, 0, "UC0")
 
     fields = [("p", 0, 127), ("j", 0, 15), ("lo2", 0, 3), ("a2", 2, 3), ("b0", 0, 1), ("b1", 1, 1), ("b3", 3, 1), ("b4", 4, 1), ("b5", 5, 1),
-              ("b6", 6, 1), ("grp", 4, 7), ("q", 5, 3), ("k2", 4, 3), ("m2", 1, 3), ("h3", 1, 7), ("p31", 0, 31)]
+              ("b6", 6, 1), ("grp", 4, 7), ("q", 5, 3), ("k2", 4, 3), ("m2", 1, 3), ("h3", 1, 7), ("p31", 0, 31), ("b2", 2, 1), ("i3", 3, 3)]
     for n_, (name, sh, mk) in enumerate(fields):
         col(name)
         ts(T.BI[:, n_:n_ + 1], T.PI[:, 0:1], sh, mk, A.logical_shift_right, A.bitwise_and, "PI", "BI")
     ms(T.IDL[0:1, 3::16], 1.0, "IDL", "IDL")
     ms(T.IDL[32:33, 7::16], 1.0, "IDL")
-    cp(T.COL[:, 0:16], T.BI[:, 0:16], "BI", " ".join("c" + x[0] for x in fields))
-    lins([("tRY", [("grp", 16), ("h3", 1)], 0), ("w16", [("b0", 15)], 1), ("tKP", [("grp", 16), ("a2", 2)], 9), ("nb3", [("b3", -1)], 1)])
+    cp(T.COL[:, 0:len(fields)], T.BI[:, 0:len(fields)], "BI", " ".join("c" + x[0] for x in fields))
+    lins([("tRY", [("grp", 16), ("h3", 1)], 0), ("w16", [("b0", 15)], 1), ("tKP", [("grp", 16), ("a2", 2)], 9), ("nb3", [("b3", -1)], 1),
+          ("p8", [("p", 1)], 8)])
     lins([("nR", [("a2", -1), ("b5", 3)], -2), ("dR", [("b1", -1), ("a2", 1), ("b5", -1)], 0), ("nC", [("lo2", -1), ("b4", 3)], -2),
-          ("dC", [("b0", -1), ("lo2", 1), ("b4", -1)], 0), ("tNI", [("b6", 64), ("lo2", -16), ("a2", 1)], 60),
+          ("dC", [("b0", -1), ("lo2", 1), ("b4", -1)], 0), ("tNI", [("b6", 64), ("lo2", -16), ("i3", 1)], 60), ("xk", [("b5", 2), ("b2", 1)], 0),
           ("tKR", [("b4", 64), ("q", 4), ("m2", -16)], 51), ("wp0", [("b0", 63)], 1), ("wn0", [("b0", -127)], 128),
-          ("na", [("p", 0)], -(1.0 + 2.0 ** -10)), ("j512", [("j", -1)], 512)])
+          ("na", [("p", 0)], -(1.0 + 2.0 ** -10))])
     cts("hb", "lo2", 2.5, -14.0, A.is_lt, A.mult)
     cts("i74", "j", 7.0, 4.0, A.is_equal, A.mult)
+    cts("n0", "j", 0.0, -1.0, A.is_equal, A.mult)
+    cts("n1", "j", 1.0, -1.0, A.is_equal, A.mult)
     cts("is3", "j", 3.0, None, A.is_equal)
     cts("mid", "a2", 3.0, None, A.is_equal)
     cts("bh", "a2", 2.5, "hb", A.is_lt, A.mult)
-    cts("wNG", "j", 0.0, -4096.0, A.is_equal, A.mult)
-    for n_, c in enumerate(("lo2", "k2", "q")):
-        ts(T.EQ[:, 4 * n_:4 * n_ + 4], T.IF[:, 0:4], col(c), None, A.is_equal, None, "IF c" + c, "EQ")
+    ts(T.EQ[:, 0:4], T.IF[:, 0:4], col("lo2"), None, A.is_equal, None, "IF clo2", "EQ")
     for c in range(1, 4):
         ms(T.IDT[32:33, 128 * c:128 * c + 128], float(c), "IDT")
     ts(T.BB[:], T.IF[:, 0:16], col("i74"), col("bh"), A.mult, A.add, "IF ci74 cbh", "BB")
@@ -280,9 +290,9 @@ def rank_program(g, core, T, topo):
             bank, b = base + u, 4 * o + u
             mm([(P[bank][:], [(blk(T.EU, u, 128), blk(T.LC, o, 512))])], "EU LC%d" % o, "P%d" % bank, False, True)
             if u % 2:
-                ts(blk(T.B, b, 512), P[bank][:], T.BB[:, b:b + 1], 0.0, A.add, A.max, "P%d BB" % bank, "B%d" % b)
+                ts(blk(T.B, b + 1, 512), P[bank][:], T.BB[:, b:b + 1], 0.0, A.add, A.max, "P%d BB" % bank, "B%d" % b)
             else:
-                act(blk(T.B, b, 512), P[bank][:], F.Relu, "P%d BB" % bank, "B%d" % b, bias=T.BB[:, b:b + 1])
+                act(blk(T.B, b + 1, 512), P[bank][:], F.Relu, "P%d BB" % bank, "B%d" % b, bias=T.BB[:, b:b + 1])
     b_number(range(4))
 
     ts(T.KI[:, 0:512], T.KT[:], 7, None, A.logical_shift_right, None, "KT", "KI")
@@ -291,15 +301,15 @@ def rank_program(g, core, T, topo):
         ts(blk(T.EU, u, 128), T.RE[:], float(-u), None, A.is_equal, None, "RE0", "EU")
     cp(T.KB[:], T.KI[:], "KI", "KB")
     onehot(T.RY[:], T.IF[:, 0:128], "IF", "tRY", "w16", "RY")
-    onehot(T.NG[:], T.IF[:, 0:128], "IF", "p", "wNG", "NG")
+    onehot(T.NG[:], T.IF[:, 0:128], "IF", "p8", -1.0, "NG")
     b_cells(srcs[0], 0)
-    act(T.NN[:, 0:1024], T.YC[:, 0:1024], F.Relu, "YC", "NN0", scale=-1.0)
-    ts(T.NN[:, 1024:2048], T.YC[:, 1024:2048], -1.0, 0.0, A.mult, A.max, "YC", "NN1")
+    act(T.NN[:, 0:S:2], T.YC[:, 0:S:2], F.Relu, "YC cn0", "NN0", scale=col("n0"))
+    ts(T.NN[:, 1:S:2], T.YC[:, 1:S:2], col("n1"), 0.0, A.mult, A.max, "YC cn1", "NN1")
     for u in range(4):
         mm([(P[4 + u][:], [(T.KP[:, 136 * u + 1:136 * u + 129], T.KB[:, 0:512]), (T.KP[:, 136 * u:136 * u + 128], T.KB[:, 512:1024])])],
            "KP KB", "P%d" % (4 + u), True, False)
-    for u in (2, 0, 3, 1):
-        mm([(P[4 + u][:], [(T.RY[:], blk(T.YC, u, 512)), (T.NG[:], blk(T.NN, u, 512))])], "RY NG YC NN%d" % (u // 2), "P%d" % (4 + u), False, True)
+    for u in range(4):
+        mm([(P[4 + u][:], [(T.RY[:], blk(T.YC, u, 512)), (T.NG[:], blk(T.NN, u, 512))])], "RY YC NG NN0 NN1", "P%d" % (4 + u), False, True)
         act(blk(T.DS, u, 512), P[4 + u][:], F.Copy, "P%d" % (4 + u), "DS")
     dma("y", [(T.DSD[:], T.DS[:])], "DS", "DSD")
     send(lambda o: T.DSD[o], lambda o: T.DLD[o], "ad%d" % rank, "DSD")
@@ -310,17 +320,13 @@ def rank_program(g, core, T, topo):
     b_number(range(4))
     cts("i37", "lo2", 3.0, "nb3", A.is_equal, A.mult)
     cts("wh", "bh", -1.0, 2.0 ** -13, A.is_lt, A.mult)
-    ms(T.HZ[:, 0:64], 0.5, "HZ")
-    ms(T.HZ[:, 64:128], 0.0, "HZ")
-    ts(T.D16[:], T.IF[:, 0:16], col("j"), None, A.is_equal, None, "IF cj", "D16")
     ms(T.AU[:], 0.0, "AU")
-    op("v", lambda: V.tensor_tensor_scan(T.PW[:, 0:64], T.HZ[:, 0:64], T.HZ[:, 64:128], 2.0, A.mult, A.add), "HZ", "PW")
     ms(T.LW[:], 0.0, "LW")
     cts("xR", "dR", "mid", "nR", A.mult, A.add)
     cts("xC", "dC", "mid", "nC", A.mult, A.add)
     cts("wm", "mid", "wh", None, A.subtract)
-    tt(T.DM[:, 0:16], T.PW[:, 0:16], T.D16[:], A.mult, "PW D16", "DM")
-    tt(T.DM[:, 16:24], T.PW[:, 0:64:9], T.D16[:, 0:8], A.mult, "PW D16", "DM")
+    for n_, c in enumerate(("xk", "q", "a2")):
+        ts(T.EQ[:, 4 * n_ + 4:4 * n_ + 8], T.IF[:, 0:4], col(c), None, A.is_equal, None, "IF c" + c, "EQ")
     ts(T.TM[:, 0:16], T.RC[:, 0:16], col("xR"), None, A.add, None, "RC cxR", "TM0")
     ts(T.TM[:, 16:32], T.RC[:, 16:32], col("xC"), None, A.add, None, "RC cxC", "TM0")
     for x in range(4):
@@ -329,19 +335,96 @@ def rank_program(g, core, T, topo):
     ts(T.WJ[:, 0:1], T.WI[:, 0:1], 6, None, A.logical_shift_right, None, "WI", "WJ")
     ts(T.WJ[:, 1:2], T.WI[:, 0:1], 63, None, A.bitwise_and, None, "WI", "WJ")
     tt(T.TM[:, 0:16], T.TM[:, 32:48], T.TM[:, 48:64], A.add, "TM1", "TM0")
+    ms(T.B[:, 0:512], 0.0, "B~")
+    ms(T.TS[:], 0.0, "TS~")
+    for rd in range(RO):
+        ms(blk(T.TL, N * rd + rank, TW), 0.0, "TS~")
+    ms(T.E[:], 1.0, "E")
+    ms(T.RS[:], 0.0, "RS")
+    ms(T.RT[:], 1.0, "RT")
+    ms(T.DP[:], -1e6, "DP")
+    ms(T.ZR[:], 0.0, "ZR")
+    ms(T.RS[:, 0::48], 1.0, "RS", "RS")
+    ms(T.RT[:, 0::32], 0.0, "RT", "RT")
+    chain = lambda n_, i: T.LW[:, 144 * n_ + 15 - i:144 * n_ + 143 - i]
+
+    def chains(names):
+        for n_, c in names:
+            ts(T.LW[:, 144 * n_ + 15:144 * n_ + 143:16], T.OB[:, 0::16], col(c), None, A.mult, None, "OB LW c" + c, "LW%d" % n_)
+
+    def constants_1():
+        lins([("tGW", [("b6", 16), ("k2", -2), ("is3", 1)], 110), ("tWX", [("grp", 16), ("is3", 1)], 0), ("tWE", [("grp", 16)], 1),
+              ("mb3", [("b3", -1)], 0), ("n2", [("p", 0)], -2), ("c15", [("p", 0)], 15), ("jd", [("j", 1)], -2048),
+              ("tNO", [("b6", 64), ("lo2", 8), ("k2", -1)], 39), ("tUY", [("grp", 16), ("j", 2)], 0), ("tSK", [("grp", 16), ("m2", 1)], 0),
+              ("bY", [("b0", -2448)], 2304), ("jx", [("j", 1)], S * (rank + 1)), ("big", [("p", 0)], 65536), ("rnd", [("p", 0)], 143.53)])
+        cts("e8", "j", 8.0, -512.0, A.is_equal, A.mult)
+        cts("e9", "j", 9.0, 512.0, A.is_equal, A.mult)
+        cts("s8", "j", 7.5, -8.0, A.is_lt, A.mult)
+        cts("w37", "i37", 512.0, None, A.mult)
+        cts("k0", "n0", -0.25, None, A.mult)
+        cts("wpi", "wp0", "b3", None, A.mult)
+        cts("wna", "wn0", "b3", None, A.mult)
+        cts("wWE", "e8", "e9", None, A.add)
+        cts("wkey", "n1", -1.0 / 512, "k0", A.mult, A.add)
+        cts("wS", "wWE", 0.0, 128.0, A.not_equal, A.mult)
+        onehot(T.GW[:], T.IF[:, 0:224], "IF", "tGW", "i37", "GW")
+        cts("wS1", "wS", "s8", None, A.add)
+        onehot(T.WX[:], T.IF[:, 0:128], "IF", "tWX", "w37", "WX")
+        onehot(T.WE[:], T.IF[:, 0:128], "IF", "tWE", "wWE", "WE")
+        chains([(2, "wS1"), (3, "wkey")])
+        onehot(T.KR[:, 0:131], T.IF[:, 0:131], "IF", "tKR", "wpi", "KR")
+        onehot(T.KR[:, 136:267], T.IF[:, 0:131], "IF", "tKR", "wna", "KR")
+        ts(T.CT[:, 384:576], T.CT[:, 0:192], col("n0"), col("big"), A.mult, A.subtract, "CT0 cn0 cbig", "CT1")
+        ts(T.CT[:, 0:192], T.CT[:, 192:384], col("n1"), None, A.mult, None, "CT0 cn1", "CT0")
+        ts(T.O1[:], ID, -1024.0, None, A.mult, None, "SH O1", "O1")
+        tt(T.CT[:, 192:384], T.CT[:, 0:192], T.CT[:, 384:576], A.add, "CT0 CT1", "CT0")
+        tt(T.M2[:], T.O1[:], T.TR[:], A.subtract, "O1 TR", "M2")
+        for x in range(RO):
+            act(T.CW[:, 192 * x:192 * x + 192], T.CT[:, 192:384], F.Identity, "CT0", "CW", scale=-1.0)
+        act(T.OWN[:], T.IF[:, 0:32], F.Identity, "IF cj", "OWN", scale=16.0, bias=col("j"))
+        act(T.DP[:, 0::4], T.IF[:, 0:32], F.Identity, "IF cjd", "DP", scale=16.0, bias=col("jd"))
+        scaled(T.BC[:], T.OB[:], "OB", "wkey", "BC")
+        ts(T.MK[:], T.MR[:], col("j"), 16384.0, A.is_ge, A.mult, "MR cj", "MK")
+        act(T.UC[:, 0:60], T.UC[:, 0:60], F.Identity, "UC0 cj", "UC", bias=col("j"))
+        for o in range(N):
+            onehot(blk(T.RP, o, 128), T.R5[:], "R5", "p31", T.EQ[:, 8 + o:9 + o], "RP")
+        act(blk(T.RP, 4, 128), ID, F.Copy, "SH", "RP4")
+        act(T.RB[:], T.RP[:, 0:512], F.Copy, "RP", "RB")
+        act(T.RZ[:], T.RP[:], F.Identity, "RP RP4", "RZ", scale=-16512.0)
+
+    def constants_2():
+        onehot(T.SK[:], T.IF[:, 0:128], "IF", "tSK", "wna", "SK")
+        onehot(T.UY[:], T.IF[:, 0:128], "IF", "tUY", "nb3", "UY")
+        cts("tUZ", "tUY", 1.0, None, A.add)
+        ts(T.UZ[:, 128:256], T.UY[:], -16.0, None, A.mult, None, "UY", "UZ1")
+        onehot(T.UZ[:, 0:128], T.IF[:, 0:128], "IF", "tUZ", "nb3", "UZ0")
+        for r in range(N):
+            act(T.XD[:, 4 * r:4 * r + 4], T.IF[:, 0:4], F.Identity, "IF cjx", "XD", scale=16.0, bias=col("jx"))
+        tt(T.UZ[:, 0:128], T.UZ[:, 0:128], T.UZ[:, 128:256], A.add, "UZ0 UZ1", "UZ")
+        for r in range(N):
+            onehot(T.NO[:, 176 * r:176 * r + 164], T.IF[:, 0:164], "IF", "tNO", T.EQ[:, 12 + r:13 + r], "NO")
+        act(T.KF[:], T.KB[:, 0:512], F.Identity, "KB", "KF0", scale=128.0)
+        tt(T.KF[:], T.KF[:], T.KB[:, 512:1024], A.add, "KF0 KB", "KF")
+
+    constants_1()
     b_cells(srcs[1], 0)
+    constants_2()
     b_number((4, 5, 6, 7))
     b_cells(srcs[2], 4)
     b_number(range(4))
     b_cells(srcs[3], 0)
     for o in srcs[1:]:
         dma("y", window(o, T.DLD[o]), "DLD%d" % o, "Dw%d" % o)
+    dma("y", [(T.KD[:], T.KF[:])], "KF Dw0 Dw1 Dw2 Dw3", "KD")
+    dma("y", [(T.YK[t::16, 0:S], T.KD[t::4, :]) for t in range(4)], "KD", "WK")
+    wrote["WY"] = wrote["YC"]
+    read["WY"] = read["YC"]
 
     for o in range(N):
         cp(T.KL[:, o::4], T.LK[:, 160 * o:160 * o + 128], "LK LKo", "KL")
     allb = " ".join("B%d" % b for b in range(16))
-    act(T.CC[:, 0:4096], T.B[:, 0:8192].indirect(T.KL[:, 0:256]), F.Copy, allb + " KL", "CC0")
-    act(T.CC[:, 4096:16 * CUT], T.B[:, 0:8192].indirect(T.KL[:, 256:CUT]), F.Copy, allb + " KL", "CC1")
+    act(T.CC[:, 0:4096], T.B[:, 512:8704].indirect(T.KL[:, 0:256]), F.Copy, allb + " KL", "CC0")
+    act(T.CC[:, 4096:16 * CUT], T.B[:, 512:8704].indirect(T.KL[:, 256:CUT]), F.Copy, allb + " KL", "CC1")
     for o in range(N):
         ts(T.NA[:, 32 * o:32 * o + 32], T.LK[:, 160 * o + 128:160 * o + 160], 7, None, A.logical_shift_right, None, "LK LKo", "NA")
         ts(T.NA[:, 128 + 32 * o:160 + 32 * o], T.LK[:, 160 * o + 128:160 * o + 160], 127, None, A.bitwise_and, None, "LK LKo", "NA")
@@ -356,333 +439,258 @@ def rank_program(g, core, T, topo):
         tt(T.AU[h, 96 + 16 * s:112 + 16 * s], T.TM[h, 32:48], T.TM[h, 48:64], A.add, "TM1 AU", "AU1")
     ts(col("whi"), T.WJ[:, 0:1], 64.0, None, A.mult, None, "WJ", "cwhi")
     cp(col("wlo"), T.WJ[:, 1:2], "WJ", "cwlo")
-    cp(T.CC[:, 16 * CUT:8192], T.B[:, 0:8192].indirect(T.KL[:, CUT:512]), allb + " KL", "CC2")
+    chains([(0, "whi"), (1, "wlo")])
     for x in range(4):
-        cp(T.PL[:, x::4], P[4][:, 32 * x:32 * x + 32], "P4", "PL")
+        cp(T.PL[:, 64 * (x % 2) + x // 2:64 * (x % 2) + 64:2], P[4][:, 32 * x:32 * x + 32], "P4", "PL")
+    cp(T.CC[:, 16 * CUT:8192], T.B[:, 512:8704].indirect(T.KL[:, CUT:512]), allb + " KL", "CC2")
     allc = "CC0 CC1 CC2"
-    chain = lambda n_, i: T.LW[:, 144 * n_ + 15 - i:144 * n_ + 143 - i]
 
-    def chains(names):
-        for n_, c in names:
-            ts(T.LW[:, 144 * n_ + 15:144 * n_ + 143:16], T.OB[:, 0::16], col(c), None, A.mult, None, "OB LW c" + c, "LW%d" % n_)
+    half = lambda k, a: T.G[:, 1024 * k + a:1024 * k + 1024:16]
 
-    iota(T.WX[:], [[0, 128]], 0, 0, "WX0")
-    iota(T.TM[:, 64:80], [[0, 16]], 1, 0, "ONF")
-    iota(T.O1[:, 0:8], [[0, 8]], 16, 0, "O1")
-    sel(T.WX[:, 8::16], T.O1[:, 0:8], [[-16, 8]], A.is_equal, 0.0, -7, 1, "WX0 O1", "WX")
-    sel(T.WX[:, 9::16], T.O1[:, 0:8], [[-16, 8]], A.is_equal, 0.0, -3, 1, "WX0 O1", "WX")
-    iota(T.NO[:], [[0, 704]], 0, 0, "NO0")
-    for r in range(4):
-        for s in range(2):
-            c0 = 176 * r + 48 + 64 * s
-            sel(T.NO[:, c0:c0 + 16], T.TM[:, 64:80], [[-1, 4], [16, 4]], A.is_equal, 0.0, -(64 * s + 48 + 4 * r), 1, "NO0 ONF", "NO")
-
-    def constants_1():
-        chains([(0, "whi"), (1, "wlo")])
-        lins([("tGW", [("b6", 16), ("k2", -2), ("is3", 1)], 110)])
-        op("v", lambda: V.tensor_reduce(col("ci"), T.DM[:, 0:16], X.X, A.add), "DM", "cci")
-        op("v", lambda: V.tensor_reduce(col("wS"), T.DM[:, 16:24], X.X, A.add), "DM", "cwS")
-        cts("is8", "j", 8.0, None, A.is_equal)
-        cts("w9", "j", 9.0, 16.0, A.is_equal, A.mult)
-        cts("is0", "j", 0.0, None, A.is_equal)
-        onehot(T.GW[:], T.IF[:, 0:224], "IF", "tGW", "i37", "GW")
-        act(T.DM[:, 32:64], T.IF[:, 0:32], F.Identity, "IF cj512", "DM", scale=-16.0, bias=col("j512"))
-
-    def constants_2():
-        lins([("c4r", [("q", -1)], 4), ("w8", [("is8", 16)], 0), ("c8", [("q", 64)], 1024), ("j4", [("j", 1)], 4),
-              ("wkey", [("is8", 128), ("w9", 0.0625)], 0), ("wRX", [("b3", 16)], 0), ("jD", [("j", 4)], 8192)])
-        chains([(2, "wS")])
-        cts("wpi", "wp0", "b3", None, A.mult)
-        ts(T.CT[:, 576:768], T.CT[:, 192:384], col("w9"), None, A.mult, None, "CT0 cw9", "CT1")
-        ms(T.RT[:], 1.0, "RT")
-        ts(T.DI[:, 0:4], T.IF[:, 0:4], col("c4r"), None, A.add, None, "IF cc4r", "DI0")
-        cts("c88", "c8", "is8", None, A.mult)
-        ts(T.DI[:, 8:12], T.DI[:, 0:4], 3, None, A.bitwise_and, None, "DI0", "DI1")
-        ts(T.CT[:, 384:576], T.CT[:, 0:192], col("w8"), col("c88"), A.mult, A.add, "CT0 cw8 cc88", "CT1")
-        ts(T.DF[:, 0:4], T.DI[:, 8:12], -1.0, col("j4"), A.mult, A.add, "DI1 cj4", "DF")
-        tt(T.CW[:, 576:768], T.CT[:, 384:576], T.CT[:, 576:768], A.add, "CT1", "CW0")
-        dma("y", [(T.CW[:, 192 * x:192 * x + 192], T.CW[:, 576:768]) for x in range(3)], "CW0", "CW")
-        ms(T.RT[:, 0::32], 0.0, "RT", "RT")
-        onehot(T.KR[:, 0:131], T.IF[:, 0:131], "IF", "tKR", "wpi", "KR")
-        chains([(3, "wkey"), (4, "is0")])
-
-    def constants_3():
-        scaled(T.RX[:], T.SH[:, 8:136], "SH", "wRX", "RX")
-        for o in range(4):
-            act(T.CA[:, 128 + 32 * o:160 + 32 * o], T.HZ[:, 64:96], F.Identity, "HZ DF", "CA1", bias=T.DF[:, o:o + 1])
-        act(T.DM[:, 0:32], T.IF[:, 0:32], F.Identity, "IF cj", "DM", scale=16.0, bias=col("j"))
-        act(T.DM[:, 64:96], T.IF[:, 0:32], F.Identity, "IF cjD", "DM", scale=64.0, bias=col("jD"))
-        scaled(T.BC[:], T.OB[:], "OB", "wkey", "BC")
-        lins([("tAY", [("b4", 16), ("h3", 1)], 0), ("tAX", [("p31", 1)], 8), ("cDL", [("q", 192), ("j", 1)], 10240),
-              ("n2", [("p", 0)], -2), ("c15", [("p", 0)], 15)])
-        act(T.PW[:, 64:112], T.PW[:, 0:48], F.Identity, "PW", "PW2", scale=2.5)
-        act(T.DL[:, 0:12], T.IF[:, 0:12], F.Identity, "IF ccDL", "DL", scale=16.0, bias=col("cDL"))
-        for d in range(4):
-            act(T.TH[:, 48 * d:48 * d + 48], T.PW[:, 64:112], F.Identity, "PW2 FQ7", "TH", scale=FQ(d))
-
-    def constants_4():
-        for d in range(4):
-            ts(T.WC[:, 3 * d:3 * d + 3], T.PW[:, 0:48:16], FQ(d), col("ci"), A.mult, A.mult, "PW FQ7 cci", "WC")
-        onehot(T.RA[:, 0:128], T.R5[:], "R5", "tAY", "w16", "RA")
-        onehot(T.RA[:, 128:256], T.R5[:], "R5", "tAX", "nb3", "RA")
-        cts("wna", "wn0", "b3", None, A.mult)
-        cts("wkn", "wn0", "nb3", None, A.mult)
-
-    def constants_5():
-        for o in range(N):
-            onehot(blk(T.RP, o, 128), T.R5[:], "R5", "p31", T.EQ[:, 8 + o:9 + o], "RP")
-
-    def constants_6():
-        onehot(T.SK[:], T.RM[:], "RM", "tRY", "wkn", "SK")
-        cp(T.KF[:], T.KT[:], "KT", "KF")
-        dma("y", [(T.KD[:], T.KF[:])], "KF", "KD")
-        dma("y", [(T.YK[t::16, 0:S], T.KD[t::4, :]) for t in range(4)], "KD", "YK")
-        onehot(T.KR[:, 136:267], T.IF[:, 0:131], "IF", "tKR", "wna", "KR")
-
-    def gather(rd):
-        if rd == 0:
-            cp(T.G[:, 0:1024], T.CC[:, 0:8192].indirect(T.PL[:, 0:64]), allc + " PL", "G")
-            act(T.G[:, 1024:2048], T.CC[:, 0:8192].indirect(T.PL[:, 64:128]), F.Copy, allc + " PL", "G1")
+    def gather(k, e="s"):
+        if e == "v":
+            cp(blk(T.G, k, 1024), T.CC[:, 0:8192].indirect(blk(T.PL, k, 64)), allc + " PL", "G%d" % k)
         else:
-            act(T.G[:], T.CC[:, 0:8192].indirect(T.PL[:]), F.Copy, allc + " PL", "G G1")
+            act(blk(T.G, k, 1024), T.CC[:, 0:8192].indirect(blk(T.PL, k, 64)), F.Copy, allc + " PL", "G%d" % k)
 
-    def near():
-        for k in range(2):
-            mm([(P[k][:, 128 * i:128 * i + 128], [(T.AU[:, 96 - 32 * r:224 - 32 * r], T.G[:, 4 * r + 2 * k + i::16]) for r in range(N)])
-                for i in range(2)], "AU1 G G1", "P%d" % k)
+    def near(k):
+        mm([(P[k][:, i:256:4], [(T.AU[:, 96 - 32 * r:224 - 32 * r], half(k, 4 * r + i)) for r in range(N)]) for i in range(4)],
+           "AU1 G%d" % k, "P%d" % k)
 
-    def life(rd):
-        for k in (0, 1):
-            if rd:
-                act(blk(T.UA, k, 256), P[k][:, 0:256], F.Abs, "P%d cn2" % k, "UA", scale=8192.0, bias=col("n2"))
-            else:
-                for i in range(2):
-                    ts(T.AB[:, 512 + 2 * k + i::4], P[k][:, 128 * i:128 * i + 128], 2.0 ** -12, 15.0, A.is_equal, A.mult, "P%d" % k, "Ab")
-            for i in range(2):
-                act(T.AB[:, 2 * k + i:512:4], P[k][:, 128 * i:128 * i + 128], F.Relu, "P%d cna" % k, "Aa", bias=col("na"))
-        if rd:
-            for i in range(4):
-                act(T.AB[:, 512 + i::4], blk(T.UA, i, 128), F.Relu, "UA cc15", "Ab", scale=-15.0, bias=col("c15"))
+    def life(k, e="s"):
+        if e == "v":
+            ts(T.AB[:, 512 + k::2], P[k][:, 0:256], 2.0 ** -12, 15.0, A.is_equal, A.mult, "P%d" % k, "Ab%d" % k)
+        else:
+            act(blk(T.UA, k, 256), P[k][:, 0:256], F.Abs, "P%d cn2" % k, "UA%d" % k, scale=8192.0, bias=col("n2"))
+        act(T.AB[:, k:512:2], P[k][:, 0:256], F.Relu, "P%d cna" % k, "Aa%d" % k, bias=col("na"))
+        if e != "v":
+            act(T.AB[:, 512 + k::2], blk(T.UA, k, 256), F.Relu, "UA%d cc15" % k, "Ab%d" % k, scale=-15.0, bias=col("c15"))
 
-    def hash_mm():
-        mm([(P[2][:, 0:64], [(chain(n_, i), T.AB[:, i::16]) for i in range(16) for n_ in range(2)])], "LW0 LW1 Aa Ab", "P2")
+    def hash_mm(k):
+        mm([(P[2][:, 0:64], [(chain(n_, i), T.AB[:, i::16]) for i in range(k, 16, 2) for n_ in range(2)])],
+           "LW0 LW1 Aa0 Ab0" + (" Aa1 Ab1" if k else ""), "P2", k == 0, k == 1)
+
+    def rec_kids(k):
+        if k == 0:
+            mm([(P[3][:], [(T.ZR[:], T.B[:, 0:512])])], "ZR B~", "P3", True, False)
+        more_mm([(P[3][:, 2 * i + k::8], T.GW[:, 96 - 32 * r:224 - 32 * r], half(k, 4 * r + i)) for i in range(4) for r in range(N)],
+                "GW G%d" % k, "P3")
 
     def rec_mm():
-        mm([(P[3][:, 128 * i:128 * i + 128], [(T.GW[:, 96 - 32 * r:224 - 32 * r], T.G[:, 4 * r + i::16]) for r in range(N)]
-             + [(T.RY[:], T.AB[:, i:512:4]), (T.RY[:], T.AB[:, 512 + i::4])]) for i in range(4)], "GW RY G G1 Aa Ab", "P3")
+        mm([(P[3][:], [(T.RY[:], T.AB[:, 0:512]), (T.RY[:], T.AB[:, 512:1024])])], "RY Aa0 Aa1 Ab0 Ab1", "P3", False, True)
 
     def rec_out():
-        for i in range(4):
-            act(T.D[:, i:512:4], P[3][:, 128 * i:128 * i + 128], F.Copy, "P3", "REC")
+        act(T.RX[:], P[3][:], F.Identity, "P3 cnb3 cmb3", "RX", scale=col("nb3"), bias=col("mb3"))
+        act(REC, P[3][:], F.Copy, "P3", "REC")
 
-    H, H1, OO, TI, B0 = (T.HI[:, 32 * x:32 * x + 32] for x in range(5))
-    DH, O1, HM, TF = (T.HF[:, 32 * x:32 * x + 32] for x in range(4))
+    H, H5, H15, OO, TI, B0 = (T.HI[:, 32 * x:32 * x + 32] for x in range(6))
+    DH, O1, TF = (T.HF[:, 32 * x:32 * x + 32] for x in range(3))
+
+    def hash_out():
+        act(TF, P[2][:, 0:32], F.Copy, "P2", "TF")
 
     def hash_ops():
-        act(TF, P[2][:, 0:32], F.Copy, "P2", "TF")
         tt(TI, TF, P[2][:, 32:64], A.add, "TF P2", "TI")
-        ts(B0, TI, 1, None, A.bitwise_and, None, "TI", "B0")
         ts(H, TI, 8191, None, A.bitwise_and, None, "TI", "H")
-        ts(OO, TI, 11, 3, A.logical_shift_right, A.bitwise_and, "TI", "OO")
+        ts(B0, TI, 1, None, A.bitwise_and, None, "TI", "B0")
+        ts(H5, H, 512.0, None, A.add, None, "H", "H5")
         ts(DH, B0, 2.0, -1.0, A.mult, A.add, "B0", "DH")
+        cp(T.HL[:, 0:32], H5, "H5", "HL0")
+        tt(H15, H5, DH, A.subtract, "H5 DH", "H15")
+        ts(OO, TI, 11, 3, A.logical_shift_right, A.bitwise_and, "TI", "OO")
+        cp(T.HL[:, 32:64], H15, "H15", "HL1")
         ts(O1, OO, 1.0, None, A.add, None, "OO", "O1")
-        tt(H1, H, DH, A.subtract, "H DH", "H1")
-        cp(T.HL[:], T.HI[:, 0:64], "H H1", "HL")
-        tt(HM, H1, T.DM[:, 32:64], A.add, "H1 DM", "HM")
+        act(T.WG[:], T.B[:, 0:8704].indirect(T.HL[:, 32:64]), F.Copy, allb + " B~ HL1", "WG")
+
+    c32 = lambda x: T.CL[:, 32 * x:32 * x + 32]
+    S0, S1 = P[6][:, 0:32], P[7][:, 0:32]
 
     def look():
         for x in range(2):
-            tt(blk(T.DD, x, 512), T.D[:, 512:8704].indirect(blk(T.HL, x, 32)), REC, A.subtract, "D Dw0 Dw1 Dw2 Dw3 REC HL", "DD%d" % x)
-        mm([(P[3][:], [(ID, T.AB[:, 0:512]), (ID, T.AB[:, 512:1024]), (T.RX[:], REC)])], "SH RX Aa Ab REC", "P3", True, False)
-        mm([(P[5][:, 0:64], [(chain(2, i), T.DD[:, i::16]) for i in range(16)])], "LW2 DD0 DD1", "P5")
-
-    c32 = lambda x, n_=1: T.CL[:, 32 * x:32 * (x + n_)]
+            tt(blk(T.DD, x, 512), T.D[:, 0:8704].indirect(blk(T.HL, x, 32)), T.RX[:], A.is_equal, "D Dw0 Dw1 Dw2 Dw3 REC RX HL%d" % x, "DD%d" % x)
+            if x == 0:
+                mm([(P[3][:], [(ID, REC)])], "SH REC", "P3", True, False)
+            mm([((S0, S1)[x], [(chain(2, i), T.DD[:, 512 * x + i:512 * x + 512:16]) for i in range(16)])], "LW2 DD%d" % x, "P%d" % (6 + x))
+            if x == 0:
+                mm([(P[3][:], [(T.WE[:], T.DD[:, 0:512])])], "WE DD0", "P3", False, False)
+        mm([(P[3][:], [(T.WX[:], T.WG[:])])], "WX WG", "P3", False, True)
+        act(T.RQ[:], P[3][:], F.Identity, "P3 cbig", "RQ", bias=col("big"))
 
     def flags(rd):
-        ts(c32(0, 2), P[5][:, 0:64], -1000.0, None, A.is_lt, None, "P5", "FR")
-        ts(c32(2, 2), P[5][:, 0:64], 0.0, None, A.is_equal, None, "P5", "HT")
-        tt(c32(4), c32(0), DH, A.mult, "FR DH", "C4")
-        tt(c32(5), c32(0), c32(1), A.max, "FR", "C5")
-        tt(c32(6), c32(2), c32(3), A.max, "HT", "C6")
-        tt(c32(7), c32(4), H1, A.add, "C4 H1", "C7")
-        tt(c32(8), c32(5), c32(6), A.is_gt, "C5 C6", "C8")
-        cp(T.WL[:], c32(7), "C7", "WL")
-        tt(c32(9), c32(8), O1, A.mult, "C8 O1", "C9")
-        act(T.WG[:], T.B[:, 0:8192].indirect(T.WL[:]), F.Copy, allb + " WL", "WG")
-        tt(c32(10), c32(2), DH, A.mult, "HT DH", "C10")
+        ts(c32(0), S0, -1.0, 68.0, A.mult, A.add, "P6", "C0")
+        ts(c32(1), S0, -64.0, None, A.is_equal, None, "P6", "C1")
+        ts(c32(2), S0, -64.0, -64.0, A.is_equal, A.add, "P6", "C2")
+        mm([(P[6][:, 128:256], [(ID, T.CA[:])])], "SH CA", "P6", True, False)
+        tt(c32(3), c32(1), H5, A.mult, "C1 H5", "C3")
+        tt(c32(4), c32(3), T.OWN[:], A.max, "C3 OWN", "C4")
+        tt(c32(5), S1, c32(0), A.subtract, "P7 C0", "C5")
+        tt(c32(7), S1, c32(2), A.is_equal, "P7 C2", "C7")
+        tt(c32(6), c32(5), O1, A.min, "C5 O1", "C6")
+        tt(c32(8), c32(7), H15, A.mult, "C7 H15", "C8")
         for o in range(N):
-            ts(T.FB[:, 32 * o:32 * o + 32], c32(9), float(o + 1), 4.0, A.is_equal, A.mult, "C9", "FB")
-        mm([(P[5][:, 128:256], [(T.OB[:], T.FB[:])]), (P[5][:, 256:384], [(ID, T.CA[:, 0:128]), (ID, T.CA[:, 128:256]), (T.TR[:], T.FB[:])])],
-           "OB TR SH CA CA1 FB", "P5")
-        mm([(P[3][:], [(T.WX[:], T.WG[:])])], "WX WG", "P3", False, True)
-        tt(c32(11), c32(6), HM, A.mult, "C6 HM", "C11")
-        tt(c32(12), c32(10), T.DM[:, 0:32], A.add, "C10 DM", "C12")
-        op("v", lambda: V.tensor_tensor_scan(T.SC[:, 0:128], T.RT[:], P[5][:, 128:256], 0.0, A.mult, A.add), "RT P5", "SC0")
-        tt(c32(13), c32(11), c32(12), A.add, "C11 C12", "C13")
-        tt(T.SC[:, 128:256], T.SC[:, 0:128], P[5][:, 256:384], A.subtract, "SC0 P5", "SC1")
-        cp(T.AT[:], c32(13), "C13", "AT")
-        act(T.RQ[:], P[3][:], F.Copy, "P3", "RQ")
+            ts(blk(T.FB, o, 32), c32(6), float(o + 1), 4.0, A.is_equal, A.mult, "C6", "FB")
+        more_mm([(P[6][:, 128 + o:256:4], T.M2[:], blk(T.FB, o, 32)) for o in range(N)], "M2 FB", "P6")
+        scan(T.RR[:], T.RT[:], T.FB[:], 0.0, A.mult, A.add, "RT FB", "RR")
+        more_mm([(P[6][:, 128 + o:256:4], T.OB[:], blk(T.RR, o, 32)) for o in range(N)], "OB RR", "P6", True)
+        tt(c32(9), c32(8), c32(4), A.max, "C8 C4", "C9")
+        cp(T.AT[:], c32(9), "C9", "AT")
         act(T.PG[:], T.D[:, 0:8704].indirect(T.AT[:]), F.Copy, "D REC AT", "PG")
         kr = 136 if rd == RO - 1 else 0
-        mm([(P[2][:, 128:256], [(T.KR[:, kr + 3 - i:kr + 131 - i], T.PG[:, i::4]) for i in range(4)])], "KR PG", "P2")
-        tt(T.SC[:, 256:384], T.SC[:, 128:256], T.FB[:], A.mult, "SC1 FB", "SC2")
-        tt(T.SC[:, 0:64], T.SC[:, 256:320], T.SC[:, 320:384], A.add, "SC2", "SC0")
-        tt(c32(14), T.SC[:, 0:32], T.DM[:, 64:96], A.add, "SC0 DM", "C14")
-        tt(c32(15), c32(14), T.SC[:, 32:64], A.add, "C14 SC0", "C15")
-        ts(T.OL[:], c32(15), 0.25, None, A.mult, None, "C15", "OL")
+        mm([(P[2][:, 128 + 64 * k:192 + 64 * k], [(T.KR[:, kr + 3 - i:kr + 131 - i], T.PG[:, 2 * i + k::8]) for i in range(4)]) for k in range(2)],
+           "KR PG", "P2")
+        scan(T.SQ[:], T.DP[:], P[6][:, 128:256], -1e6, A.max, A.min, "DP P6", "SQ")
+        ts(T.OL[:], T.SQ[:, 3::4], 4096.0, None, A.add, None, "SQ", "OL")
 
     def nodes_out():
         act(T.PN[:], P[2][:, 128:256], F.Copy, "P2", "PN")
-        mm([(P[1][:, 32 * r:32 * r + 32], [(T.NO[:, 176 * r + 48 - 16 * x:176 * r + 176 - 16 * x], T.PN[:, x::4]) for x in range(4)])
-            for r in range(N)], "NO PN", "P1")
+        mm([(P[1][:, 32 * r:32 * r + 32], [(T.NO[:, 176 * r + 36 - 32 * x - 4 * k:176 * r + 164 - 32 * x - 4 * k], T.PN[:, 64 * k + x:64 * k + 64:2])
+                                           for x in range(2) for k in range(2)]) for r in range(N)], "NO PN", "P1")
         act(T.NS[:], P[1][:, 0:128], F.Copy, "P1", "NS")
         send(lambda o: blk(T.NS, o, 32), lambda o: blk(T.NL, o, 32), "an", "NS")
         arrival("NL", "an", peers)
         dma("y", [(T.ynodes[32 * rank:32 * rank + 32, :], blk(T.NS, rank, 32))], "NS", "yn0")
         dma("y", [(T.ynodes[32 * o:32 * o + 32, :], blk(T.NL, o, 32)) for o in peers], "NL", "yn")
 
+    def mine(rd, o, a, b):
+        c0 = TW * (N * rd + o)
+        return (T.TL if o == rank else T.TS)[:, c0 + a:c0 + b]
+
+    tri = lambda o, jj: P[7][:, 64 + (0, 64, 192)[jj] + 16 * (jj + 1) * o:64 + (0, 64, 192)[jj] + 16 * (jj + 1) * (o + 1)]
+
     def compact(rd):
         w0 = 192 * (RO - 1 - rd)
-        cp(T.CW[:, w0:w0 + 2560].indirect(T.OL[:]), T.RQ[:], "OL RQ CW0", "CW")
-        ts(T.CI[:, 192:384], T.CW[:, w0:w0 + 192], 4, None, A.logical_shift_right, None, "CW", "CI2")
-        ts(T.CI[:, 0:192], T.CW[:, w0:w0 + 192], 15, None, A.bitwise_and, None, "CW", "CI")
-        cp(T.YX[:, 192:384], T.CI[:, 192:384], "CI2", "YX1")
-        cp(T.YX[:, 0:192], T.CI[:, 0:192], "CI", "YX0")
-        mm([(P[6][:, 192 + 48 * d:240 + 48 * d], [(shift(T.SH, d), T.YX[:, 192 + d:384:4])]) for d in range(4)], "SH YX1", "P6")
-        mm([(P[4][:, 48 * d:48 * d + 48], [(shift(T.SH, d), T.YX[:, d:192:4])]) for d in range(4)], "SH YX0", "P4")
-
-    def owners():
-        act(T.OY[:, 192:384], P[6][:, 192:384], F.Copy, "P6", "OX")
-        mm([(P[7][:, 0:192], [(T.BC[:], T.OY[:, 192:384])]),
-            (P[7][:, 192:204], [(chain(3, i), T.OY[:, 192 + i:384:16]) for i in range(16)])], "BC LW3 OX", "P7")
-        act(T.OY[:, 0:192], P[4][:, 0:192], F.Copy, "P4", "OY")
-
-    def all_mm():
-        for x in range(2):
-            for k in range(2):
-                o = 2 * k + x
-                quarters([[(P[4 + k][:, 192 * x:192 * x + 192], [(T.RA[32 * o:32 * o + 32, 0:128], T.OY[32 * o:32 * o + 32, 0:192]),
-                                                                (T.RA[32 * o:32 * o + 32, 128:256], T.OY[32 * o:32 * o + 32, 192:384])])]],
-                         "RA OY OX", "P%d" % (4 + k))
-
-    def equal():
-        cp(T.KU[:], P[7][:, 0:192], "P7", "KU")
-        cp(T.KC[:, 0:12], P[7][:, 192:204], "P7", "KC")
-        for j in range(12):
-            ts(blk(T.E, j, 192), T.KU[:], T.KC[:, j:j + 1], T.WC[:, j:j + 1], A.is_equal, A.mult, "KU KC WC", "E%d" % (j // 4))
-        tt(T.KC[:, 16:28], T.KC[:, 0:12], T.DL[:, 0:12], A.subtract, "KC DL", "K1")
-        for k in range(3):
-            mm([(P[6][:, 0:192], [(T.OB[:], blk(T.E, j, 192)) for j in range(4 * k, 4 * k + 4)])], "OB E%d" % k, "P6", k == 0, k == 2)
-
-    def winners():
-        tt(T.WN[:], P[6][:, 0:192], T.TH[:], A.is_lt, "P6 TH", "WN")
-        mm([(P[7][:, 256:268], [(chain(4, i), T.WN[:, i::16]) for i in range(16)])], "LW4 WN", "P7")
-
-    def offsets(rd):
-        tt(T.KC[:, 32:44], P[7][:, 256:268], T.KC[:, 16:28], A.mult, "P7 K1", "K2")
-        tt(T.KC[:, 48:60], T.KC[:, 32:44], T.DL[:, 0:12], A.add, "K2 DL", "K3")
+        mm([(P[7][:, 64:448], [(ID, T.MK[:])])], "SH MK", "P7", True, False)
+        mm([(P[6][:, 256:316], [(ID, T.ZR[:, 0:60])])], "SH ZR", "P6", True, False)
         if rd < RO - 1:
-            mm([(P[6][:, 256 + 12 * o:268 + 12 * o], [(blk(T.RP, o, 128), T.KC[:, 48:60])]) for o in range(N)], "RP K3", "P6")
-        cp(T.OH[:, 0:24:2], T.KC[:, 48:60], "K3", "OH0")
-        tt(T.OH[:, 1:24:2], T.KC[:, 48:60], T.OH[:, 0:24:2], A.subtract, "K3 OH0", "OH1")
+            cp(T.CW[:, w0:w0 + 2560].indirect(T.OL[:, 0:16]), T.RQ[:, 0:256], "OL RQ", "CW")
+            cp(T.PL[:], P[2][:, 128:256], "P2", "PL")
+            cp(T.CW[:, w0:w0 + 2560].indirect(T.OL[:, 16:32]), T.RQ[:, 256:512], "OL RQ CW", "CW")
+        else:
+            cp(T.CW[:, w0:w0 + 2560].indirect(T.OL[:]), T.RQ[:], "OL RQ", "CW")
+        for o in range(N):
+            cp(blk(T.HX, o, 48), T.CW[:, w0 + o:w0 + 192:4], "CW", "HX%d" % o)
+            more_mm([(tri(o, jj), T.BC[:], T.HX[:, 48 * o:48 * o + 16 * (jj + 1)]) for jj in range(3)], "BC HX%d" % o, "P7", o == N - 1)
+        mm([(P[7][:, 480:492], [(chain(3, i), T.HX[:, i::16]) for i in range(16)])], "LW3 HX0 HX1 HX2 HX3", "P7")
+        for o in range(N):
+            tt(mine(rd, o, 0, 48), T.CW[:, w0 + o:w0 + 192:4], blk(T.HX, o, 48), A.subtract, "CW HX%d TS~" % o, "LO")
 
-    records = lambda o: [(P[0][:, TW * o + 48 * x:TW * o + 48 * x + 48],
-                          [(qshift(T.SH, o, d - o), T.OY[32 * o:32 * o + 32, 192 * x + 48 * d:192 * x + 48 * d + 48]) for d in range(4)]) for x in range(2)]
-    places = lambda o: [(P[0][:, TW * o + 96:TW * o + 102], [(qshift(T.SH, o, d - o), T.OH[32 * o:32 * o + 32, 6 * d:6 * d + 6]) for d in range(4)])]
-
-    def parcel(rd):
-        quarters([places(o) + (records(o) if rd < RO - 1 else []) for o in range(N)], "SH OY OX OH0 OH1", "P0")
-        act(blk(T.TS, rd, N * TW), P[0][:, 0:N * TW], F.Copy, "P0", "TS%d" % rd)
-        send(lambda o: blk(T.TS, N * rd + o, TW), lambda o: blk(T.TL, N * rd + o, TW), "ar%d" % rd, "TS%d" % rd)
-        arrival("TL%d" % rd, "ar%d" % rd, peers)
+    def all_mm(rd):
+        for k in range(2):
+            mm([(P[4 + k][:, 192 * x + 48 * o:192 * x + 48 * o + 48], [(blk(T.RB, 2 * k + x, 128), mine(rd, o, 0, 48))])
+                for x in range(2) for o in range(N)], "RB LO", "P%d" % (4 + k))
 
     def all_out():
-        for k in range(2):
-            act(T.RL[:, 384 * k:384 * k + 384], P[4 + k][:, 0:384], F.Copy, "P%d" % (4 + k), "RL")
+        for k in (1, 0):
+            act(blk(T.RL, k, 384), P[4 + k][:, 0:384], F.Copy, "P%d" % (4 + k), "RL%d" % k)
+
+    def equal(rd):
+        last = rd == RO - 1
+        cp(T.KC[:, 0:12], P[7][:, 480:492], "P7", "KC")
+        more_mm([(P[6][:, 256 + 12 * r:268 + 12 * r], blk(T.RP, r, 128), T.KC[:, 0:12]) for r in range(N if last else 0, N + 1)], "RP RP4 KC", "P6")
+        for o in range(N):
+            for jj in range(3):
+                n_ = 3 * o + jj
+                ts(T.E[:, 48 * n_:48 * n_ + 16 * (jj + 1)], tri(o, jj), T.KC[:, n_:n_ + 1], None, A.not_equal, None, "P7 KC", "E")
+        scan(T.ZS[:], T.RS[:], T.E[:], 1.0, A.max, A.min, "RS E", "ZS")
+        more_mm([(P[6][:, 256 + 12 * r:268 + 12 * r], blk(T.RZ, r, 128), T.ZS[:, 47::48]) for r in range(N if last else 0, N + 1)], "RZ ZS", "P6", True)
+        tt(T.AF[:, 0:60], P[6][:, 256:316], T.UC[:, 0:60], A.min, "P6 UC", "AF")
 
     def update():
-        cp(T.AL[:], P[6][:, 256:304], "P6", "AL")
-        cp(T.D[:, 512:512 + DW].indirect(T.AL[:]), T.RL[:], "AL RL", "D")
+        cp(T.AL[:], T.AF[:, 0:48], "AF", "AL")
+        for r in reversed(range(N)):
+            cp(T.D[:, 512:512 + DW].indirect(blk(T.AL, r, 12)), blk(T.RL, r, 192), "AL D RL%d" % (r // 2), "D")
+
+    def parcel(rd):
+        cp(T.OH[:, 0:24:2], T.AF[:, 48:60], "AF", "OH0")
+        tt(T.OH[:, 1:24:2], T.AF[:, 48:60], T.OH[:, 0:24:2], A.subtract, "AF OH0", "OH1")
+        for o in range(N):
+            act(mine(rd, o, 48, 54), T.OH[:, 6 * o:6 * o + 6], F.Copy, "OH0 OH1 TS~", "OF")
+        send(lambda o: blk(T.TS, N * rd + o, TW), lambda o: blk(T.TL, N * rd + o, TW), "ar%d" % rd, "LO OF")
+        arrival("TL%d" % rd, "ar%d" % rd, peers)
+        wrote["LO%d" % rd], wrote["OF%d" % rd] = wrote["LO"], wrote["OF"]
+
+    def regroup(rd):
+        got = lambda d, r: T.TL[32 * r:32 * r + 32, TW * (N * rd + d):TW * (N * rd + d + 1)]
+        quarters([[(blk(P[4], r, TW), [(qshift(T.SH, r, d - r), got(d, r)) for d in srcs])] for r in range(N)],
+                 "SH LO%d OF%d TL%d" % (rd, rd, rd), "P4")
+        act(T.VT[:], P[4][:, 0:N * TW], F.Copy, "P4", "VT")
+        act(T.VA[:], P[4][:, 0:N * TW], F.Identity, "P4 crnd", "VA", scale=1.0 / 16, bias=col("rnd"))
 
     def unpack(rd):
-        def got(o, d, a, b, st=1):
-            c0 = TW * (N * rd + o)
-            return (T.TS if o == rank else T.TL)[32 * d:32 * d + 32, c0 + a:c0 + b:st]
-        k = "SH SK TS%d TL%d" % (rd, rd)
-        for d in range(4):
-            quarters([[(P[3][:, 300 + 48 * d:348 + 48 * d], [(qshift(T.SH, d, o - d), got(o, d, 0, 48)) for o in srcs]),
-                       (P[3][:, 492 + 3 * d:495 + 3 * d], [(qshift(T.SH, d, o - d), got(o, d, 96 + x, 102, 2)) for o in srcs for x in range(2)])]], k, "P3")
-            quarters([[(P[5][:, 48 * d:48 + 48 * d], [(qshift(T.SK, d, o - d), got(o, d, 48, 96)) for o in srcs])]], k, "P5")
+        mm([(P[4][:, 480 + 4 * r:484 + 4 * r], [(ID, T.VT[:, TW * r + 48 + x:TW * r + TW:2]) for x in range(2)]) for r in range(N)], "SH VT", "P4")
+        mm([(P[5][:, 0:N * TW], [(T.UY[:], T.VT[:]), (T.UZ[:, 0:128], T.VA[:])]), (P[5][:, 256:256 + N * TW], [(T.SK[:], T.VT[:])])],
+           "UY UZ SK VT VA", "P5")
+        act(blk(T.RBY, rd, N * TW), P[5][:, 0:N * TW], F.Identity, "P5 cbY", "RBY%d" % rd, bias=col("bY"))
+        act(blk(T.RBK, rd, N * TW), P[5][:, 256:256 + N * TW], F.Copy, "P5", "RBK%d" % rd)
 
-    def unpack_out():
-        cp(T.RBY[:], P[3][:, 300:492], "P3", "RBY")
-        ts(T.XL[:, 0:12], P[3][:, 492:504], float(-S * rank), None, A.add, None, "P3", "XL")
-        act(T.RBK[:], P[5][:, 0:192], F.Copy, "P5", "RBK")
+    def slots(rd):
+        tt(T.XF[:], P[4][:, 480:496], T.XD[:], A.min, "P4 XD", "XF")
+        ts(blk(T.XL, rd, 16), T.XF[:], float(-S * rank), None, A.add, None, "XF", "XL%d" % rd)
 
-    def place(rd, x):
-        if x == 0:
-            cp(T.YC[:, 0:DW].indirect(T.XL[:, 0:12]), T.RBY[:], "XL RBY", "YC")
-            if rd == RO - 1:
-                dma("y", [(T.ycells[:], T.YC[:, 0:S])], "YC", "yc")
-        else:
-            cp(T.YK[:, 0:DW].indirect(T.XL[:, 0:12]), T.RBK[:], "XL RBK", "YK")
-            if rd == RO - 1:
-                dma("s", [(T.ykids[t::4, :], T.YK[t::16, 0:S]) for t in range(4)], "YK", "yk")
+    def place(rd):
+        for r in reversed(range(N)):
+            c0 = TW * (N * rd + r)
+            for win, src, key in ((T.YC, T.RBY, "Y"), (T.YK, T.RBK, "K")):
+                cp(win[:, 0:YW].indirect(T.XL[:, 16 * rd + 4 * r:16 * rd + 4 * r + 3]), src[:, c0:c0 + 48],
+                   "XL%d RB%s%d W%s" % (rd, key, rd, key), "W" + key)
 
-    gather(0)
-    near()
-    constants_1()
-    life(0)
-    hash_mm()
+    gather(0, "v")
+    gather(1)
+    for k in range(2):
+        near(k)
+    for k in range(2):
+        life(k, "v")
+        rec_kids(k)
+    for k in range(2):
+        hash_mm(k)
     rec_mm()
-    constants_2()
-    hash_ops()
+    hash_out()
     rec_out()
-    constants_3()
+    hash_ops()
     for rd in range(RO):
         more = rd < RO - 1
         look()
         flags(rd)
-        if more:
-            cp(T.PL[:], P[2][:, 128:256], "P2", "PL")
-            gather(rd + 1)
-        if rd:
-            unpack(rd - 1)
+        if rd > 1:
+            unpack(rd - 2)
         compact(rd)
-        owners()
-        if rd:
-            unpack_out()
-            place(rd - 1, 0)
-        else:
-            constants_4()
+        if rd > 1:
+            slots(rd - 2)
         if more:
-            near()
-            all_mm()
-            life(rd + 1)
+            gather(0)
+            gather(1)
+            all_mm(rd)
+            near(0)
         else:
-            quarters([records(o) for o in range(N)], "SH OY OX", "P0")
-        equal()
+            nodes_out()
+            regroup(rd - 1)
+            unpack(rd - 1)
+        equal(rd)
         if more:
             all_out()
-        winners()
-        if rd:
-            place(rd - 1, 1)
-        else:
-            constants_5()
-        offsets(rd)
-        if not rd:
-            constants_6()
-        if more:
-            hash_mm()
-            rec_mm()
+            near(1)
+            life(0)
+            rec_kids(0)
             update()
-            hash_ops()
+            rec_kids(1)
+            life(1)
+            hash_mm(0)
+            hash_mm(1)
+            rec_mm()
+            hash_out()
             rec_out()
+            hash_ops()
         parcel(rd)
-    nodes_out()
+        if more and rd:
+            regroup(rd - 1)
+    slots(RO - 2)
+    for rd in range(RO - 1):
+        place(rd)
+    regroup(RO - 1)
     unpack(RO - 1)
-    unpack_out()
-    place(RO - 1, 0)
-    place(RO - 1, 1)
+    slots(RO - 1)
+    place(RO - 1)
+    dma("y", [(T.ycells[:], T.YC[:, 0:S])], "WY", "yc")
+    dma("s", [(T.ykids[t::4, :], T.YK[t::16, 0:S]) for t in range(4)], "WK", "yk")
     for sem, n_ in total.items():
         need("g", (sem, n_))

@@ -5,18 +5,18 @@ N, S, RO = 4, 2048, 4
 DW = 8704
 YW = 2112
 TW = 56
-CUT = 316
+CUT = 272
 f32, bf, i32, u16 = "float32", "bfloat16", "int32", "uint16"
 SB = {
-    "CS": (2048, bf), "LC": (2048, bf), "KS": (640, i32), "LK": (640, i32), "YC": (YW, bf), "YK": (YW, f32),
-    "KT": (512, i32), "KI": (1024, i32), "KB": (1024, bf), "KF": (512, f32), "NN": (2048, bf), "DS": (2048, bf),
+    "CS": (2048, bf), "LC": (2048, bf), "KS": (640, i32), "KU": (640, u16), "LK": (640, u16), "YC": (YW, bf), "YK": (YW, f32),
+    "KI": (640, i32), "KB": (1152, bf), "KF": (512, f32), "NN": (2048, bf), "DS": (2048, bf), "RF": (128, bf),
     "B": (512 + 8192, bf), "CC": (8192, bf), "D": (512 + DW, bf), "KL": (512, u16), "WI": (8, i32), "WJ": (8, i32),
     "PI": (8, i32), "BI": (24, i32), "COL": (128, f32), "IF": (256, f32),
     "R5": (128, f32), "RE": (128, f32), "RC": (32, f32), "EU": (512, bf), "IDT": (512, bf), "IDL": (128, bf), "BB": (16, f32),
     "AU": (224, bf), "TM": (64, f32), "RY": (128, bf), "NG": (128, bf), "GW": (224, bf), "KP": (544, bf),
-    "KR": (272, bf), "OB": (128, bf), "O1": (128, bf), "TR": (128, bf), "M2": (128, bf), "WX": (128, bf), "WE": (128, bf), "SH": (256, bf),
-    "ONE": (256, bf), "BC": (128, bf), "SK": (128, bf), "UY": (128, bf), "UZ": (256, bf), "RP": (640, f32), "RB": (512, bf), "RZ": (640, bf),
-    "NI": (576, f32), "NO": (704, f32), "LW": (576, bf), "EQ": (16, f32), "ZR": (128, bf),
+    "KR": (272, bf), "OB": (128, bf), "O1": (128, bf), "TR": (128, bf), "M2": (128, bf), "WX": (128, bf), "WE": (128, bf), "SH": (128, bf),
+    "BC": (128, bf), "SK": (128, bf), "UY": (128, bf), "UZ": (128, bf), "RP": (640, f32), "RB": (512, bf), "RZ": (640, bf),
+    "NI": (576, f32), "NO": (704, f32), "LW": (576, bf), "EQ": (16, f32), "ZR": (128, bf), "WR": (896, bf),
     "CW": (576 + 2560, f32), "CT": (576, f32), "OWN": (32, f32), "RT": (128, bf), "CA": (128, bf), "DP": (128, f32),
     "MR": (384, f32), "MK": (384, bf), "RS": (576, bf), "UC": (64, f32), "XD": (16, f32),
     "NA": (256, i32), "NF": (256, f32), "PL": (128, u16), "G": (2048, bf), "AB": (1024, bf), "UA": (512, bf), "DD": (1024, bf), "RX": (512, bf),
@@ -28,9 +28,9 @@ SB = {
 }
 SCRATCH = {n: ("sbuf", [128, w], d) for n, (w, d) in SB.items()}
 SCRATCH.update({"P%d" % k: ("psum", [128, 512], f32) for k in range(8)})
-SCRATCH.update({"DSD": ("dram", [4, 128, 512], bf), "DLD": ("dram", [4, 128, 512], bf), "KD": ("dram", [32, 2048], f32)})
+SCRATCH.update({"DLD": ("dram", [4, 128, 512], bf)})
 SEMAPHORES = (["eg", "ev", "es", "et", "sent", "ak", "an"] + ["ac%d" % k for k in range(N)] + ["ad%d" % k for k in range(N)]
-              + ["ar%d" % k for k in range(RO)] + ["d%d" % k for k in range(24)])
+              + ["ar%d" % k for k in range(RO - 1)] + ["al%d" % k for k in range(N)] + ["d%d" % k for k in range(24)])
 
 
 def rank_program(g, core, T, topo):
@@ -213,60 +213,56 @@ def rank_program(g, core, T, topo):
     qshift = lambda m, q, d: m[32 * q:32 * q + 32, 128 - 32 * (d % 4):256 - 32 * (d % 4)]
 
     dma("y", [(blk(T.CS, o, 512), T.cells[32 * o:32 * o + 32, :]) for o in peers], "", "CS")
-    dma("y", [(T.KT[:], T.kids[:])], "", "KT")
+    dma("y", [(blk(T.KS, o, 128), T.kids[8 * o:8 * o + 8, :]) for o in range(N)]
+        + [(blk(T.KS, 16 + o, 32), T.nodes[32 * o:32 * o + 32, :]) for o in range(N)], "", "KS")
     dma("y", [(blk(T.LC, rank, 512), T.cells[32 * rank:32 * rank + 32, :])], "", "LC%d" % rank)
-    dma("y", [(T.YC[:, 0:S], T.cells[:])], "", "YC")
-    dma("y", [(T.KS[:, 160 * o:160 * o + 128], T.kids[8 * o:8 * o + 8, :]) for o in peers]
-        + [(T.KS[:, 160 * o + 128:160 * o + 160], T.nodes[32 * o:32 * o + 32, :]) for o in peers], "", "KS")
-    dma("y", [(T.LK[:, 160 * rank:160 * rank + 128], T.kids[8 * rank:8 * rank + 8, :]),
-              (T.LK[:, 160 * rank + 128:160 * rank + 160], T.nodes[32 * rank:32 * rank + 32, :])]
-        + [(T.WI[32 * q:32 * q + 32, 0:1], T.wt[32 * rank:32 * rank + 32, :]) for q in range(4)], "", "LKo WI")
+    dma("y", [(T.WI[32 * q:32 * q + 32, 0:1], T.wt[32 * rank:32 * rank + 32, :]) for q in range(4)], "", "WI")
     iota(T.PI[:, 0:1], [[0, 1]], 0, 1, "PI")
     iota(T.IF[:], [[1, 256]], 0, 0, "IF")
     ms(T.RE[:], 1000.0, "RE")
     ms(T.IDT[0:64, :], 0.0, "IDT")
     ms(T.IDL[0:64, :], 0.0, "IDL")
-    ms(T.ONE[:], 1.0, "ONE")
     for a in range(3):
         for b in range(3):
             iota(T.RE[:, 4 * a + b::16], [[64, 2], [16, 2], [4, 2]], 4 * (4 * a + b), -1, "RE0", "RE")
     for a in range(2):
         for b in range(2):
             iota(T.RE[:, 12 + 2 * a + b::16], [[64, 2], [32, 2], [8, 2]], 4 * (4 * a + b), -1, "RE0")
-    iota(T.IDT[0:1, :], [[0, 4], [1, 128]], 0, 0, "IDT0", "IDT")
+    iota(T.RC[:, 0:16], [[1, 4], [0, 4]], 0, 0, "RC")
+    iota(T.RC[:, 16:32], [[0, 4], [1, 4]], 0, 0, "RC")
+    iota(T.UC[:, 0:60], [[0, 5], [128, 4], [16, 3]], 8192, 0, "UC0")
+    iota(T.CA[:], [[0, 32], [1, 4]], -4, 0, "CA")
     send(lambda o: blk(T.CS, o, 512), lambda o: blk(T.LC, o, 512), "ac%d" % rank, "CS")
     for o in peers:
         arrival("LC%d" % o, "ac%d" % o, [o])
-    sel(T.SH[:], T.ONE[:], [[0, 2], [-1, 128]], A.is_equal, 0.0, 0, 1, "ONE", "SH")
-    iota(T.RC[:, 0:16], [[1, 4], [0, 4]], 0, 0, "RC")
-    iota(T.RC[:, 16:32], [[0, 4], [1, 4]], 0, 0, "RC")
-    sel(T.O1[:], T.ONE[:, 0:128], [[-16, 8], [0, 16]], A.is_ge, 0.0, 0, 1, "ONE", "O1")
-    sel(T.OB[:], T.O1[:], [[16, 8], [0, 16]], A.is_ge, 0.0, 15, -1, "O1", "OB")
-    send(lambda o: blk(T.KS, o, 160), lambda o: blk(T.LK, o, 160), "ak", "KS")
-    arrival("LK", "ak", peers)
-    iota(T.R5[:], [[0, 4], [1, 32]], 0, 0, "R5")
-    sel(T.TR[:], T.OB[:], [[-1, 128]], A.is_gt, 0.0, 0, 1, "OB", "TR")
-    iota(T.CA[:], [[0, 32], [1, 4]], -4, 0, "CA")
-    iota(T.CT[:, 0:192], [[0, 48], [512, 4]], 64 * 512, 0, "CT0")
-    iota(T.CT[:, 192:384], [[512, 48], [0, 4]], 0, 0, "CT0")
-    for jj, c0 in enumerate((0, 64, 192)):
-        iota(T.MR[:, c0:c0 + 64 * (jj + 1)], [[0, 4], [1, 16 * (jj + 1)]], -16 * jj, 0, "MR")
-    iota(T.UC[:, 0:60], [[0, 5], [128, 4], [16, 3]], 8192, 0, "UC0")
 
     fields = [("p", 0, 127), ("j", 0, 15), ("lo2", 0, 3), ("a2", 2, 3), ("b0", 0, 1), ("b1", 1, 1), ("b3", 3, 1), ("b4", 4, 1), ("b5", 5, 1),
-              ("b6", 6, 1), ("grp", 4, 7), ("q", 5, 3), ("k2", 4, 3), ("m2", 1, 3), ("h3", 1, 7), ("p31", 0, 31), ("b2", 2, 1), ("i3", 3, 3)]
+              ("b6", 6, 1), ("grp", 4, 7), ("q", 5, 3), ("k2", 4, 3), ("m2", 1, 3), ("h3", 1, 7), ("p31", 0, 31), ("b2", 2, 1), ("i3", 3, 3),
+              ("i8", 3, 7), ("i16", 2, 15)]
     for n_, (name, sh, mk) in enumerate(fields):
         col(name)
         ts(T.BI[:, n_:n_ + 1], T.PI[:, 0:1], sh, mk, A.logical_shift_right, A.bitwise_and, "PI", "BI")
     ms(T.IDL[0:1, 3::16], 1.0, "IDL", "IDL")
     ms(T.IDL[32:33, 7::16], 1.0, "IDL")
     cp(T.COL[:, 0:len(fields)], T.BI[:, 0:len(fields)], "BI", " ".join("c" + x[0] for x in fields))
-    lins([("tRY", [("grp", 16), ("h3", 1)], 0), ("w16", [("b0", 15)], 1), ("tKP", [("grp", 16), ("a2", 2)], 9), ("nb3", [("b3", -1)], 1),
-          ("p8", [("p", 1)], 8)])
-    lins([("nR", [("a2", -1), ("b5", 3)], -2), ("dR", [("b1", -1), ("a2", 1), ("b5", -1)], 0), ("nC", [("lo2", -1), ("b4", 3)], -2),
+    lins([("tRF", [("b6", 64), ("i8", 4), ("lo2", 1)], 0), ("wRF", [("b2", 15)], 1), ("tKP", [("b6", 64), ("k2", 8), ("a2", 1)], 36),
+          ("p32", [("p", 1)], 32), ("nb2", [("b2", 144)], -144)])
+    cts("f0", "i16", 0.0, -1.0, A.is_equal, A.mult)
+    cts("f1", "i16", 1.0, -1.0, A.is_equal, A.mult)
+    ts(T.EQ[:, 0:4], T.IF[:, 0:4], col("lo2"), None, A.is_equal, None, "IF clo2", "EQ")
+    cts("bD", "nb2", "b5", None, A.mult)
+    onehot(T.RF[:], T.IF[:, 0:128], "IF", "tRF", "wRF", "RF")
+    onehot(T.NG[:], T.IF[:, 0:128], "IF", "p32", -1.0, "NG")
+    for u in range(4):
+        onehot(T.KP[:, 136 * u:136 * u + 132], T.IF[:, 0:132], "IF", "tKP", T.EQ[:, u:u + 1], "KP")
+    lins([("tRY", [("grp", 16), ("h3", 1)], 0), ("w16", [("b0", 15)], 1), ("nb3", [("b3", -1)], 1), ("mOB", [("grp", -16)], -7.5),
+          ("mTR", [("grp", -16), ("j", -0.5)], 0.5), ("rTR", [("j", 0.5)], 0),
+          ("nR", [("a2", -1), ("b5", 3)], -2), ("dR", [("b1", -1), ("a2", 1), ("b5", -1)], 0), ("nC", [("lo2", -1), ("b4", 3)], -2),
           ("dC", [("b0", -1), ("lo2", 1), ("b4", -1)], 0), ("tNI", [("b6", 64), ("lo2", -16), ("i3", 1)], 60), ("xk", [("b5", 2), ("b2", 1)], 0),
           ("tKR", [("b4", 64), ("q", 4), ("m2", -16)], 51), ("wp0", [("b0", 63)], 1), ("wn0", [("b0", -127)], 128),
           ("na", [("p", 0)], -(1.0 + 2.0 ** -10))])
+    act(T.MR[:, 0:128], T.IF[:, 0:128], F.Abs, "IF cmOB", "MR0", bias=col("mOB"))
+    act(T.MR[:, 128:256], T.IF[:, 0:128], F.Abs, "IF cmTR", "MR1", bias=col("mTR"))
     cts("hb", "lo2", 2.5, -14.0, A.is_lt, A.mult)
     cts("i74", "j", 7.0, 4.0, A.is_equal, A.mult)
     cts("n0", "j", 0.0, -1.0, A.is_equal, A.mult)
@@ -274,78 +270,116 @@ def rank_program(g, core, T, topo):
     cts("is3", "j", 3.0, None, A.is_equal)
     cts("mid", "a2", 3.0, None, A.is_equal)
     cts("bh", "a2", 2.5, "hb", A.is_lt, A.mult)
-    ts(T.EQ[:, 0:4], T.IF[:, 0:4], col("lo2"), None, A.is_equal, None, "IF clo2", "EQ")
     for c in range(1, 4):
-        ms(T.IDT[32:33, 128 * c:128 * c + 128], float(c), "IDT")
+        ms(T.IDT[32:33, 128 * c:128 * c + 128], float(c), "IDT1", "IDT")
+    for c in range(4):
+        cp(T.IDT[0:1, 128 * c:128 * c + 128], T.IF[0:1, 0:128], "IF IDT", "IDT0")
     ts(T.BB[:], T.IF[:, 0:16], col("i74"), col("bh"), A.mult, A.add, "IF ci74 cbh", "BB")
     for u in range(4):
-        onehot(T.KP[:, 136 * u:136 * u + 129], T.IF[:, 0:129], "IF", "tKP", T.EQ[:, u:u + 1], "KP")
+        ts(blk(T.EU, u, 128), T.RE[:], float(-u), None, A.is_equal, None, "RE0", "EU")
+    onehot(T.SH[:], T.IF[:, 0:128], "IF", "p", 1.0, "SH")
+    ms(T.AU[:], 0.0, "AU")
+    ms(T.LW[:], 0.0, "LW")
+
+    lists = lambda o, a, b: (T.LK if o == rank else T.KU)[:, 160 * o + a:160 * o + b]
+    ts(T.KB[:, 0:640], T.KS[:], 2.0 ** -7, 143.504, A.mult, A.add, "KS", "KB0")
+    ts(T.KI[:], T.KS[:], 127, None, A.bitwise_and, None, "KS", "KI")
+    for o in peers + [rank]:
+        cp(lists(o, 0, 128), blk(T.KS, o, 128), "KS", "KU")
+    ts(T.NF[:, 0:128], T.KI[:, 512:640], 64.0, -144.0, A.mult, A.add, "KI", "NF0")
+    cp(T.KB[:, 640:1152], T.KI[:, 0:512], "KI", "KB1")
+    tt(T.NF[:, 128:256], T.NF[:, 0:128], T.KB[:, 512:640], A.add, "NF0 KB0", "NF1")
+    for o in peers + [rank]:
+        cp(lists(o, 128, 160), blk(T.NF, 4 + o, 32), "NF1", "KU")
+    send(lambda o: blk(T.KU, o, 160), lambda o: blk(T.LK, o, 160), "ak", "KU")
+    arrival("LK", "ak", peers)
+
+    cs = lambda o, a=0, st=1: (T.LC if o == rank else T.CS)[:, 512 * o + a:512 * o + 512:st]
+    for o in peers + [rank]:
+        ck = "LC%d" % o if o == rank else "CS"
+        act(T.NN[:, 512 * o:512 * o + 512:2], cs(o, 0, 2), F.Relu, ck + " cf0", "NN%d" % o, scale=col("f0"))
+        act(T.NN[:, 512 * o + 1:512 * o + 512:2], cs(o, 1, 2), F.Relu, ck + " cf1", "NN%d" % o, scale=col("f1"))
+        mm([(P[4 + o][:], [(T.RF[:], cs(o)), (T.NG[:], blk(T.NN, o, 512))])], "RF NG NN%d %s" % (o, ck), "P%d" % (4 + o), True, False)
+    for n_, o in enumerate(peers + [rank]):
+        more_mm([(blk(P[4 + o], u, 128), T.KP[:, 136 * u + 4 - 4 * x:136 * u + 132 - 4 * x], T.KB[:, 640 * x + 128 * o:640 * x + 128 * o + 128])
+                 for x in range(2) for u in range(4)], "KP KB0 KB1", "P%d" % (4 + o), True)
+        if n_ == 1:
+            ts(blk(T.DS, o, 512), P[4 + o][:], col("bD"), None, A.add, None, "P%d cbD" % (4 + o), "DS%d" % o)
+        else:
+            act(blk(T.DS, o, 512), P[4 + o][:], F.Identity, "P%d cbD" % (4 + o), "DS%d" % o, bias=col("bD"))
+    send(lambda o: blk(T.DS, o, 512), lambda o: T.DLD[o], "ad%d" % rank, " ".join("DS%d" % o for o in peers))
+    for o in peers:
+        arrival("DLD%d" % o, "ad%d" % o, [o])
+    window = lambda o: [(T.D[32 * y:32 * y + 32, 512 + S * o:512 + S * o + S], T.DLD[o]) for y in range(4)]
+    dma("y", [(T.DLD[rank], blk(T.DS, rank, 512))], "DS%d" % rank, "DLD%d" % rank)
+    dma("y", window(rank), "DLD%d" % rank, "Dw%d" % rank)
+
+    def fill_g(t, c, key):
+        iota(t, [[0, t.shape[1]]], c, 0, key)
+
+    def paint(t, pat, base, w, key):
+        sel(t, t, pat, A.not_equal, w, base, 1, key, key)
+    fill_g(T.B[:, 0:512], 0, "B~")
+    fill_g(T.ZR[:], 0, "ZR")
+    fill_g(T.DP[:], -1000000, "DP0")
+    fill_g(T.RT[:], 1, "RT0")
+    sel(T.RT[:], T.RT[:], [[0, 4], [1, 32]], A.not_equal, 0.0, 0, 0, "RT0", "RT")
+    fill_g(T.RP[:], 0, "RP")
+    paint(T.RP[:, 0:512], [[-32, 4], [0, 4], [-1, 32]], 0, 1.0, "RP")
+    paint(T.RP[:, 512:640], [[-1, 128]], 0, 1.0, "RP")
+    fill_g(T.E[:], 1, "E")
+    sel(T.RS[:], T.E[:], [[0, 12], [1, 48]], A.is_equal, 0.0, 0, 0, "E", "RS")
+    fill_g(T.TS[:], 0, "TS~")
+    for rd in range(RO):
+        fill_g(blk(T.TL, N * rd + rank, TW), 0, "TS~")
+    fill_g(T.WR[:], 0, "WR")
+    for r in range(N):
+        paint(T.WR[:, 224 * r + 96:224 * r + 128], [[-1, 32]], -32 * r, 1.0, "WR")
+    for t, key in ((T.SK, "SK"), (T.UY, "UY"), (T.UZ, "UZ")):
+        fill_g(t[:], 0, key)
+    for x in range(2):
+        paint(T.SK[:], [[-16, 8], [1000, 4], [-2, 4]], -8 - x, (128.0, 1.0)[x], "SK")
+        paint(T.UZ[:, x::2], [[-16, 8], [-1, 8]], 0, (-16.0, 1.0)[x], "UZ")
+    paint(T.UY[:, 0::2], [[-16, 8], [-1, 8]], 0, 1.0, "UY")
+    fill_g(T.NO[:], 0, "NO")
+    for r in range(N):
+        for s in range(2):
+            c0 = 176 * r + 36 + 64 * s
+            paint(T.NO[:, c0:c0 + 32], [[-1, 4], [1000, 2], [16, 4]], -(64 * s + 48 + 4 * r), 1.0, "NO")
 
     def b_number(banks):
         for bank in banks:
-            mm([(P[bank][:], [(T.IDL[0:64, :], T.IDT[0:64, :])])], "IDL IDT IDT0", "P%d" % bank, True, False)
+            mm([(P[bank][:], [(T.IDL[0:64, :], T.IDT[0:64, :])])], "IDL IDT0 IDT1", "P%d" % bank, True, False)
 
-    def b_cells(o, base):
+    def b_cells(o, base, both=True):
         for u in range(4):
             bank, b = base + u, 4 * o + u
             mm([(P[bank][:], [(blk(T.EU, u, 128), blk(T.LC, o, 512))])], "EU LC%d" % o, "P%d" % bank, False, True)
-            if u % 2:
+            if u % 2 and both:
                 ts(blk(T.B, b + 1, 512), P[bank][:], T.BB[:, b:b + 1], 0.0, A.add, A.max, "P%d BB" % bank, "B%d" % b)
             else:
                 act(blk(T.B, b + 1, 512), P[bank][:], F.Relu, "P%d BB" % bank, "B%d" % b, bias=T.BB[:, b:b + 1])
     b_number(range(4))
-
-    ts(T.KI[:, 0:512], T.KT[:], 7, None, A.logical_shift_right, None, "KT", "KI")
-    ts(T.KI[:, 512:1024], T.KT[:], 127, None, A.bitwise_and, None, "KT", "KI")
-    for u in range(4):
-        ts(blk(T.EU, u, 128), T.RE[:], float(-u), None, A.is_equal, None, "RE0", "EU")
-    cp(T.KB[:], T.KI[:], "KI", "KB")
-    onehot(T.RY[:], T.IF[:, 0:128], "IF", "tRY", "w16", "RY")
-    onehot(T.NG[:], T.IF[:, 0:128], "IF", "p8", -1.0, "NG")
     b_cells(srcs[0], 0)
-    act(T.NN[:, 0:S:2], T.YC[:, 0:S:2], F.Relu, "YC cn0", "NN0", scale=col("n0"))
-    ts(T.NN[:, 1:S:2], T.YC[:, 1:S:2], col("n1"), 0.0, A.mult, A.max, "YC cn1", "NN1")
-    for u in range(4):
-        mm([(P[4 + u][:], [(T.KP[:, 136 * u + 1:136 * u + 129], T.KB[:, 0:512]), (T.KP[:, 136 * u:136 * u + 128], T.KB[:, 512:1024])])],
-           "KP KB", "P%d" % (4 + u), True, False)
-    for u in range(4):
-        mm([(P[4 + u][:], [(T.RY[:], blk(T.YC, u, 512)), (T.NG[:], blk(T.NN, u, 512))])], "RY YC NG NN0 NN1", "P%d" % (4 + u), False, True)
-        act(blk(T.DS, u, 512), P[4 + u][:], F.Copy, "P%d" % (4 + u), "DS")
-    dma("y", [(T.DSD[:], T.DS[:])], "DS", "DSD")
-    send(lambda o: T.DSD[o], lambda o: T.DLD[o], "ad%d" % rank, "DSD")
-    for o in peers:
-        arrival("DLD%d" % o, "ad%d" % o, [o])
-    window = lambda o, src: [(T.D[32 * y:32 * y + 32, 512 + S * o:512 + S * o + S], src) for y in range(4)]
-    dma("y", window(rank, T.DS[32 * rank:32 * rank + 32, :]), "DS DSD", "Dw%d" % rank)
     b_number(range(4))
+    b_number((4, 5, 6, 7))
+    onehot(T.RY[:], T.IF[:, 0:128], "IF", "tRY", "w16", "RY")
+    ts(T.OB[:], T.MR[:, 0:128], 8.0, None, A.is_lt, None, "MR0", "OB")
+    ts(T.TR[:], T.MR[:, 128:256], col("rTR"), None, A.is_lt, None, "MR1 crTR", "TR")
     cts("i37", "lo2", 3.0, "nb3", A.is_equal, A.mult)
     cts("wh", "bh", -1.0, 2.0 ** -13, A.is_lt, A.mult)
-    ms(T.AU[:], 0.0, "AU")
-    ms(T.LW[:], 0.0, "LW")
     cts("xR", "dR", "mid", "nR", A.mult, A.add)
     cts("xC", "dC", "mid", "nC", A.mult, A.add)
     cts("wm", "mid", "wh", None, A.subtract)
-    for n_, c in enumerate(("xk", "q", "a2")):
-        ts(T.EQ[:, 4 * n_ + 4:4 * n_ + 8], T.IF[:, 0:4], col(c), None, A.is_equal, None, "IF c" + c, "EQ")
+    ts(T.EQ[:, 4:8], T.IF[:, 0:4], col("xk"), None, A.is_equal, None, "IF cxk", "EQ")
     ts(T.TM[:, 0:16], T.RC[:, 0:16], col("xR"), None, A.add, None, "RC cxR", "TM0")
     ts(T.TM[:, 16:32], T.RC[:, 16:32], col("xC"), None, A.add, None, "RC cxC", "TM0")
     for x in range(4):
         onehot(T.NI[:, 144 * x:144 * x + 140], T.IF[:, 0:140], "IF", "tNI", T.EQ[:, 4 + x:5 + x], "NI")
     tt(T.TM[:, 32:64], T.TM[:, 0:32], T.TM[:, 0:32], A.mult, "TM0", "TM1")
+    tt(T.TM[:, 0:16], T.TM[:, 32:48], T.TM[:, 48:64], A.add, "TM1", "TM0")
     ts(T.WJ[:, 0:1], T.WI[:, 0:1], 6, None, A.logical_shift_right, None, "WI", "WJ")
     ts(T.WJ[:, 1:2], T.WI[:, 0:1], 63, None, A.bitwise_and, None, "WI", "WJ")
-    tt(T.TM[:, 0:16], T.TM[:, 32:48], T.TM[:, 48:64], A.add, "TM1", "TM0")
-    ms(T.B[:, 0:512], 0.0, "B~")
-    ms(T.TS[:], 0.0, "TS~")
-    for rd in range(RO):
-        ms(blk(T.TL, N * rd + rank, TW), 0.0, "TS~")
-    ms(T.E[:], 1.0, "E")
-    ms(T.RS[:], 0.0, "RS")
-    ms(T.RT[:], 1.0, "RT")
-    ms(T.DP[:], -1e6, "DP")
-    ms(T.ZR[:], 0.0, "ZR")
-    ms(T.RS[:, 0::48], 1.0, "RS", "RS")
-    ms(T.RT[:, 0::32], 0.0, "RT", "RT")
     chain = lambda n_, i: T.LW[:, 144 * n_ + 15 - i:144 * n_ + 143 - i]
 
     def chains(names):
@@ -355,7 +389,6 @@ def rank_program(g, core, T, topo):
     def constants_1():
         lins([("tGW", [("b6", 16), ("k2", -2), ("is3", 1)], 110), ("tWX", [("grp", 16), ("is3", 1)], 0), ("tWE", [("grp", 16)], 1),
               ("mb3", [("b3", -1)], 0), ("n2", [("p", 0)], -2), ("c15", [("p", 0)], 15), ("jd", [("j", 1)], -2048),
-              ("tNO", [("b6", 64), ("lo2", 8), ("k2", -1)], 39), ("tUY", [("grp", 16), ("j", 2)], 0), ("tSK", [("grp", 16), ("m2", 1)], 0),
               ("bY", [("b0", -2448)], 2304), ("jx", [("j", 1)], S * (rank + 1)), ("big", [("p", 0)], 65536), ("rnd", [("p", 0)], 143.53)])
         cts("e8", "j", 8.0, -512.0, A.is_equal, A.mult)
         cts("e9", "j", 9.0, 512.0, A.is_equal, A.mult)
@@ -374,75 +407,63 @@ def rank_program(g, core, T, topo):
         chains([(2, "wS1"), (3, "wkey")])
         onehot(T.KR[:, 0:131], T.IF[:, 0:131], "IF", "tKR", "wpi", "KR")
         onehot(T.KR[:, 136:267], T.IF[:, 0:131], "IF", "tKR", "wna", "KR")
-        ts(T.CT[:, 384:576], T.CT[:, 0:192], col("n0"), col("big"), A.mult, A.subtract, "CT0 cn0 cbig", "CT1")
-        ts(T.CT[:, 0:192], T.CT[:, 192:384], col("n1"), None, A.mult, None, "CT0 cn1", "CT0")
-        ts(T.O1[:], ID, -1024.0, None, A.mult, None, "SH O1", "O1")
-        tt(T.CT[:, 192:384], T.CT[:, 0:192], T.CT[:, 384:576], A.add, "CT0 CT1", "CT0")
-        tt(T.M2[:], T.O1[:], T.TR[:], A.subtract, "O1 TR", "M2")
-        for x in range(RO):
-            act(T.CW[:, 192 * x:192 * x + 192], T.CT[:, 192:384], F.Identity, "CT0", "CW", scale=-1.0)
-        act(T.OWN[:], T.IF[:, 0:32], F.Identity, "IF cj", "OWN", scale=16.0, bias=col("j"))
-        act(T.DP[:, 0::4], T.IF[:, 0:32], F.Identity, "IF cjd", "DP", scale=16.0, bias=col("jd"))
-        scaled(T.BC[:], T.OB[:], "OB", "wkey", "BC")
-        ts(T.MK[:], T.MR[:], col("j"), 16384.0, A.is_ge, A.mult, "MR cj", "MK")
-        act(T.UC[:, 0:60], T.UC[:, 0:60], F.Identity, "UC0 cj", "UC", bias=col("j"))
+        b_cells(srcs[1], 0, False)
+        b_number(range(4))
+        cts("s1", "n1", -512.0, None, A.mult)
         for o in range(N):
-            onehot(blk(T.RP, o, 128), T.R5[:], "R5", "p31", T.EQ[:, 8 + o:9 + o], "RP")
-        act(blk(T.RP, 4, 128), ID, F.Copy, "SH", "RP4")
-        act(T.RB[:], T.RP[:, 0:512], F.Copy, "RP", "RB")
-        act(T.RZ[:], T.RP[:], F.Identity, "RP RP4", "RZ", scale=-16512.0)
-
-    def constants_2():
-        onehot(T.SK[:], T.IF[:, 0:128], "IF", "tSK", "wna", "SK")
-        onehot(T.UY[:], T.IF[:, 0:128], "IF", "tUY", "nb3", "UY")
-        cts("tUZ", "tUY", 1.0, None, A.add)
-        ts(T.UZ[:, 128:256], T.UY[:], -16.0, None, A.mult, None, "UY", "UZ1")
-        onehot(T.UZ[:, 0:128], T.IF[:, 0:128], "IF", "tUZ", "nb3", "UZ0")
+            cts("u%d" % o, "n0", -512.0 * (64 + o), 65536.0, A.mult, A.add)
+        ts(T.O1[:], ID, -1024.0, None, A.mult, None, "SH", "O1")
+        ms(T.MK[:], 0.0, "MK0")
+        tt(T.M2[:], T.O1[:], T.TR[:], A.subtract, "O1 TR", "M2")
+        for o in range(N):
+            act(T.CW[:, o:192:4], T.IF[:, 0:48], F.Identity, "IF cs1 cu%d" % o, "CW0", scale=col("s1"), bias=col("u%d" % o))
+        for x in range(1, RO):
+            act(blk(T.CW, x, 192), T.CW[:, 0:192], F.Copy, "CW0", "CW")
+        for jj, c0 in enumerate((0, 80, 224)):
+            for o in range(N):
+                c1 = c0 + 16 * (jj + 1) * o
+                ts(T.MK[:, c1:c1 + 16], T.IF[:, 0:16], col("j"), 16384.0, A.is_ge, A.mult, "IF cj MK0", "MK")
+        act(T.OWN[:], T.IF[:, 0:32], F.Identity, "IF cj", "OWN", scale=16.0, bias=col("j"))
+        scaled(T.BC[:], T.OB[:], "OB", "wkey", "BC")
+        act(T.UC[:, 0:60], T.UC[:, 0:60], F.Identity, "UC0 cj", "UC", bias=col("j"))
         for r in range(N):
             act(T.XD[:, 4 * r:4 * r + 4], T.IF[:, 0:4], F.Identity, "IF cjx", "XD", scale=16.0, bias=col("jx"))
-        tt(T.UZ[:, 0:128], T.UZ[:, 0:128], T.UZ[:, 128:256], A.add, "UZ0 UZ1", "UZ")
-        for r in range(N):
-            onehot(T.NO[:, 176 * r:176 * r + 164], T.IF[:, 0:164], "IF", "tNO", T.EQ[:, 12 + r:13 + r], "NO")
-        act(T.KF[:], T.KB[:, 0:512], F.Identity, "KB", "KF0", scale=128.0)
-        tt(T.KF[:], T.KF[:], T.KB[:, 512:1024], A.add, "KF0 KB", "KF")
+        cp(T.KF[:], T.KS[:, 0:512], "KS", "KF")
 
+    def constants_2():
+        act(T.DP[:, 0::4], T.IF[:, 0:32], F.Identity, "IF cjd DP0", "DP", scale=16.0, bias=col("jd"))
+        act(T.RB[:], T.RP[:, 0:512], F.Copy, "RP", "RB")
+        act(T.RZ[:], T.RP[:], F.Identity, "RP", "RZ", scale=-16512.0)
+
+    ts(T.TM[:, 32:48], T.TM[:, 0:16], 2.5, col("wh"), A.is_lt, A.mult, "TM0 cwh", "TM1")
+    ts(T.TM[:, 48:64], T.TM[:, 0:16], 0.0, col("wm"), A.is_equal, A.mult, "TM0 cwm", "TM1")
+    ts(col("whi"), T.WJ[:, 0:1], 64.0, None, A.mult, None, "WJ", "cwhi")
+    cp(col("wlo"), T.WJ[:, 1:2], "WJ", "cwlo")
+    for s in range(2):
+        h = slice(64 * s, 64 * s + 64)
+        tt(T.AU[h, 96 + 16 * s:112 + 16 * s], T.TM[h, 32:48], T.TM[h, 48:64], A.add, "TM1 AU", "AU1")
+    chains([(0, "whi"), (1, "wlo")])
     constants_1()
-    b_cells(srcs[1], 0)
-    constants_2()
-    b_number((4, 5, 6, 7))
     b_cells(srcs[2], 4)
-    b_number(range(4))
     b_cells(srcs[3], 0)
     for o in srcs[1:]:
-        dma("y", window(o, T.DLD[o]), "DLD%d" % o, "Dw%d" % o)
-    dma("y", [(T.KD[:], T.KF[:])], "KF Dw0 Dw1 Dw2 Dw3", "KD")
-    dma("y", [(T.YK[t::16, 0:S], T.KD[t::4, :]) for t in range(4)], "KD", "WK")
-    wrote["WY"] = wrote["YC"]
-    read["WY"] = read["YC"]
+        dma("y", window(o), "DLD%d" % o, "Dw%d" % o)
+    dma("y", [(T.YC[:, 0:S], T.cells[:])], "Dw0 Dw1 Dw2 Dw3", "WY")
+    dma("y", [(T.YK[16 * q:16 * q + 4, 0:S], T.KF[64 * (q % 2):64 * (q % 2) + 64, 128 * (q // 2):128 * (q // 2) + 128]) for q in range(8)],
+        "KF", "WK")
 
     for o in range(N):
-        cp(T.KL[:, o::4], T.LK[:, 160 * o:160 * o + 128], "LK LKo", "KL")
+        cp(T.KL[:, o::4], T.LK[:, 160 * o:160 * o + 128], "LK KU", "KL")
     allb = " ".join("B%d" % b for b in range(16))
     act(T.CC[:, 0:4096], T.B[:, 512:8704].indirect(T.KL[:, 0:256]), F.Copy, allb + " KL", "CC0")
     act(T.CC[:, 4096:16 * CUT], T.B[:, 512:8704].indirect(T.KL[:, 256:CUT]), F.Copy, allb + " KL", "CC1")
     for o in range(N):
-        ts(T.NA[:, 32 * o:32 * o + 32], T.LK[:, 160 * o + 128:160 * o + 160], 7, None, A.logical_shift_right, None, "LK LKo", "NA")
-        ts(T.NA[:, 128 + 32 * o:160 + 32 * o], T.LK[:, 160 * o + 128:160 * o + 160], 127, None, A.bitwise_and, None, "LK LKo", "NA")
-    ts(T.TM[:, 32:48], T.TM[:, 0:16], 2.5, col("wh"), A.is_lt, A.mult, "TM0 cwh", "TM1")
-    ts(T.NF[:, 0:128], T.NA[:, 128:256], 64.0, None, A.mult, None, "NA", "NF0")
-    ts(T.TM[:, 48:64], T.TM[:, 0:16], 0.0, col("wm"), A.is_equal, A.mult, "TM0 cwm", "TM1")
-    tt(T.NF[:, 128:256], T.NF[:, 0:128], T.NA[:, 0:128], A.add, "NA NF0", "NF")
-    mm([(P[4][:, 32 * x:32 * x + 32], [(T.NI[:, 144 * x + 12 - 4 * r:144 * x + 140 - 4 * r], T.NF[:, 128 + 32 * r:160 + 32 * r]) for r in range(N)])
-        for x in range(4)], "NI NF", "P4")
-    for s in range(2):
-        h = slice(64 * s, 64 * s + 64)
-        tt(T.AU[h, 96 + 16 * s:112 + 16 * s], T.TM[h, 32:48], T.TM[h, 48:64], A.add, "TM1 AU", "AU1")
-    ts(col("whi"), T.WJ[:, 0:1], 64.0, None, A.mult, None, "WJ", "cwhi")
-    cp(col("wlo"), T.WJ[:, 1:2], "WJ", "cwlo")
-    chains([(0, "whi"), (1, "wlo")])
+        cp(blk(T.NF, o, 32), T.LK[:, 160 * o + 128:160 * o + 160], "LK KU", "NF0")
+    mm([(P[4][:, 32 * x:32 * x + 32], [(T.NI[:, 144 * x + 12 - 4 * r:144 * x + 140 - 4 * r], blk(T.NF, r, 32)) for r in range(N)])
+        for x in range(4)], "NI NF0", "P4")
+    cp(T.CC[:, 16 * CUT:8192], T.B[:, 512:8704].indirect(T.KL[:, CUT:512]), allb + " KL", "CC2")
     for x in range(4):
         cp(T.PL[:, 64 * (x % 2) + x // 2:64 * (x % 2) + 64:2], P[4][:, 32 * x:32 * x + 32], "P4", "PL")
-    cp(T.CC[:, 16 * CUT:8192], T.B[:, 512:8704].indirect(T.KL[:, CUT:512]), allb + " KL", "CC2")
     allc = "CC0 CC1 CC2"
 
     half = lambda k, a: T.G[:, 1024 * k + a:1024 * k + 1024:16]
@@ -470,9 +491,10 @@ def rank_program(g, core, T, topo):
         mm([(P[2][:, 0:64], [(chain(n_, i), T.AB[:, i::16]) for i in range(k, 16, 2) for n_ in range(2)])],
            "LW0 LW1 Aa0 Ab0" + (" Aa1 Ab1" if k else ""), "P2", k == 0, k == 1)
 
+    def rec_start():
+        mm([(P[3][:], [(T.ZR[:], T.B[:, 0:512])])], "ZR B~", "P3", True, False)
+
     def rec_kids(k):
-        if k == 0:
-            mm([(P[3][:], [(T.ZR[:], T.B[:, 0:512])])], "ZR B~", "P3", True, False)
         more_mm([(P[3][:, 2 * i + k::8], T.GW[:, 96 - 32 * r:224 - 32 * r], half(k, 4 * r + i)) for i in range(4) for r in range(N)],
                 "GW G%d" % k, "P3")
 
@@ -484,7 +506,7 @@ def rank_program(g, core, T, topo):
         act(REC, P[3][:], F.Copy, "P3", "REC")
 
     H, H5, H15, OO, TI, B0 = (T.HI[:, 32 * x:32 * x + 32] for x in range(6))
-    DH, O1, TF = (T.HF[:, 32 * x:32 * x + 32] for x in range(3))
+    DH, TF = (T.HF[:, 32 * x:32 * x + 32] for x in range(2))
 
     def hash_out():
         act(TF, P[2][:, 0:32], F.Copy, "P2", "TF")
@@ -493,21 +515,20 @@ def rank_program(g, core, T, topo):
         tt(TI, TF, P[2][:, 32:64], A.add, "TF P2", "TI")
         ts(H, TI, 8191, None, A.bitwise_and, None, "TI", "H")
         ts(B0, TI, 1, None, A.bitwise_and, None, "TI", "B0")
+        ts(OO, TI, 11, 3, A.logical_shift_right, A.bitwise_and, "TI", "OO")
         ts(H5, H, 512.0, None, A.add, None, "H", "H5")
         ts(DH, B0, 2.0, -1.0, A.mult, A.add, "B0", "DH")
-        cp(T.HL[:, 0:32], H5, "H5", "HL0")
+        cp(T.HL[:, 0:32], H, "H", "HL0")
         tt(H15, H5, DH, A.subtract, "H5 DH", "H15")
-        ts(OO, TI, 11, 3, A.logical_shift_right, A.bitwise_and, "TI", "OO")
-        cp(T.HL[:, 32:64], H15, "H15", "HL1")
-        ts(O1, OO, 1.0, None, A.add, None, "OO", "O1")
-        act(T.WG[:], T.B[:, 0:8704].indirect(T.HL[:, 32:64]), F.Copy, allb + " B~ HL1", "WG")
+        ts(T.HL[:, 32:64], H15, -512.0, None, A.add, None, "H15", "HL1")
+        act(T.WG[:], T.B[:, 512:8704].indirect(T.HL[:, 32:64]), F.Copy, allb + " HL1", "WG")
 
     c32 = lambda x: T.CL[:, 32 * x:32 * x + 32]
     S0, S1 = P[6][:, 0:32], P[7][:, 0:32]
 
     def look():
         for x in range(2):
-            tt(blk(T.DD, x, 512), T.D[:, 0:8704].indirect(blk(T.HL, x, 32)), T.RX[:], A.is_equal, "D Dw0 Dw1 Dw2 Dw3 REC RX HL%d" % x, "DD%d" % x)
+            tt(blk(T.DD, x, 512), T.D[:, 512:8704].indirect(blk(T.HL, x, 32)), T.RX[:], A.is_equal, "D Dw0 Dw1 Dw2 Dw3 RX HL%d" % x, "DD%d" % x)
             if x == 0:
                 mm([(P[3][:], [(ID, REC)])], "SH REC", "P3", True, False)
             mm([((S0, S1)[x], [(chain(2, i), T.DD[:, 512 * x + i:512 * x + 512:16]) for i in range(16)])], "LW2 DD%d" % x, "P%d" % (6 + x))
@@ -522,34 +543,42 @@ def rank_program(g, core, T, topo):
         ts(c32(2), S0, -64.0, -64.0, A.is_equal, A.add, "P6", "C2")
         mm([(P[6][:, 128:256], [(ID, T.CA[:])])], "SH CA", "P6", True, False)
         tt(c32(3), c32(1), H5, A.mult, "C1 H5", "C3")
+        fill(1)
         tt(c32(4), c32(3), T.OWN[:], A.max, "C3 OWN", "C4")
         tt(c32(5), S1, c32(0), A.subtract, "P7 C0", "C5")
         tt(c32(7), S1, c32(2), A.is_equal, "P7 C2", "C7")
-        tt(c32(6), c32(5), O1, A.min, "C5 O1", "C6")
+        tt(c32(6), c32(5), OO, A.min, "C5 OO", "C6")
         tt(c32(8), c32(7), H15, A.mult, "C7 H15", "C8")
         for o in range(N):
-            ts(blk(T.FB, o, 32), c32(6), float(o + 1), 4.0, A.is_equal, A.mult, "C6", "FB")
+            ts(blk(T.FB, o, 32), c32(6), float(o), 4.0, A.is_equal, A.mult, "C6", "FB")
         more_mm([(P[6][:, 128 + o:256:4], T.M2[:], blk(T.FB, o, 32)) for o in range(N)], "M2 FB", "P6")
         scan(T.RR[:], T.RT[:], T.FB[:], 0.0, A.mult, A.add, "RT FB", "RR")
         more_mm([(P[6][:, 128 + o:256:4], T.OB[:], blk(T.RR, o, 32)) for o in range(N)], "OB RR", "P6", True)
         tt(c32(9), c32(8), c32(4), A.max, "C8 C4", "C9")
         cp(T.AT[:], c32(9), "C9", "AT")
         act(T.PG[:], T.D[:, 0:8704].indirect(T.AT[:]), F.Copy, "D REC AT", "PG")
+        scan(T.SQ[:], T.DP[:], P[6][:, 128:256], -1e6, A.max, A.min, "DP P6", "SQ")
+        ts(T.OL[:], T.SQ[:, 3::4], 4096.0, None, A.add, None, "SQ", "OL")
+        mm([(P[7][:, 64:448], [(ID, T.MK[:])])], "SH MK", "P7", True, False)
+        mm([(P[6][:, 256:316], [(ID, T.ZR[:, 0:60])])], "SH ZR", "P6", True, False)
+
+    def pointers(rd):
         kr = 136 if rd == RO - 1 else 0
         mm([(P[2][:, 128 + 64 * k:192 + 64 * k], [(T.KR[:, kr + 3 - i:kr + 131 - i], T.PG[:, 2 * i + k::8]) for i in range(4)]) for k in range(2)],
            "KR PG", "P2")
-        scan(T.SQ[:], T.DP[:], P[6][:, 128:256], -1e6, A.max, A.min, "DP P6", "SQ")
-        ts(T.OL[:], T.SQ[:, 3::4], 4096.0, None, A.add, None, "SQ", "OL")
+
+    def nodes_mm(h):
+        if h == 0:
+            act(T.PN[:], P[2][:, 128:256], F.Copy, "P2", "PN")
+        mm([(P[1][:, 32 * r:32 * r + 32], [(T.NO[:, 176 * r + 36 - 32 * x - 4 * k:176 * r + 164 - 32 * x - 4 * k], T.PN[:, 64 * k + x:64 * k + 64:2])
+                                           for x in range(2) for k in range(2)]) for r in (2 * h, 2 * h + 1)], "NO PN", "P1")
 
     def nodes_out():
-        act(T.PN[:], P[2][:, 128:256], F.Copy, "P2", "PN")
-        mm([(P[1][:, 32 * r:32 * r + 32], [(T.NO[:, 176 * r + 36 - 32 * x - 4 * k:176 * r + 164 - 32 * x - 4 * k], T.PN[:, 64 * k + x:64 * k + 64:2])
-                                           for x in range(2) for k in range(2)]) for r in range(N)], "NO PN", "P1")
         act(T.NS[:], P[1][:, 0:128], F.Copy, "P1", "NS")
         send(lambda o: blk(T.NS, o, 32), lambda o: blk(T.NL, o, 32), "an", "NS")
         arrival("NL", "an", peers)
         dma("y", [(T.ynodes[32 * rank:32 * rank + 32, :], blk(T.NS, rank, 32))], "NS", "yn0")
-        dma("y", [(T.ynodes[32 * o:32 * o + 32, :], blk(T.NL, o, 32)) for o in peers], "NL", "yn")
+
 
     def mine(rd, o, a, b):
         c0 = TW * (N * rd + o)
@@ -559,8 +588,6 @@ def rank_program(g, core, T, topo):
 
     def compact(rd):
         w0 = 192 * (RO - 1 - rd)
-        mm([(P[7][:, 64:448], [(ID, T.MK[:])])], "SH MK", "P7", True, False)
-        mm([(P[6][:, 256:316], [(ID, T.ZR[:, 0:60])])], "SH ZR", "P6", True, False)
         if rd < RO - 1:
             cp(T.CW[:, w0:w0 + 2560].indirect(T.OL[:, 0:16]), T.RQ[:, 0:256], "OL RQ", "CW")
             cp(T.PL[:], P[2][:, 128:256], "P2", "PL")
@@ -574,68 +601,89 @@ def rank_program(g, core, T, topo):
         for o in range(N):
             tt(mine(rd, o, 0, 48), T.CW[:, w0 + o:w0 + 192:4], blk(T.HX, o, 48), A.subtract, "CW HX%d TS~" % o, "LO")
 
-    def all_mm(rd):
-        for k in range(2):
-            mm([(P[4 + k][:, 192 * x + 48 * o:192 * x + 48 * o + 48], [(blk(T.RB, 2 * k + x, 128), mine(rd, o, 0, 48))])
-                for x in range(2) for o in range(N)], "RB LO", "P%d" % (4 + k))
+    def all_mm(rd, k):
+        mm([(P[4 + k][:, 192 * x + 48 * o:192 * x + 48 * o + 48], [(blk(T.RB, 2 * k + x, 128), mine(rd, o, 0, 48))])
+            for x in range(2) for o in range(N)], "RB LO", "P%d" % (4 + k))
 
-    def all_out():
-        for k in (1, 0):
-            act(blk(T.RL, k, 384), P[4 + k][:, 0:384], F.Copy, "P%d" % (4 + k), "RL%d" % k)
+    def all_out(k):
+        act(blk(T.RL, k, 384), P[4 + k][:, 0:384], F.Copy, "P%d" % (4 + k), "RL%d" % k)
+
+    def keys(rd):
+        cp(T.KC[:, 0:12], P[7][:, 480:492], "P7", "KC")
+        more_mm([(P[6][:, 256 + 12 * r:268 + 12 * r], blk(T.RP, r, 128), T.KC[:, 0:12]) for r in range(N if rd == RO - 1 else 0, N + 1)],
+                "RP KC", "P6")
 
     def equal(rd):
         last = rd == RO - 1
-        cp(T.KC[:, 0:12], P[7][:, 480:492], "P7", "KC")
-        more_mm([(P[6][:, 256 + 12 * r:268 + 12 * r], blk(T.RP, r, 128), T.KC[:, 0:12]) for r in range(N if last else 0, N + 1)], "RP RP4 KC", "P6")
         for o in range(N):
             for jj in range(3):
                 n_ = 3 * o + jj
                 ts(T.E[:, 48 * n_:48 * n_ + 16 * (jj + 1)], tri(o, jj), T.KC[:, n_:n_ + 1], None, A.not_equal, None, "P7 KC", "E")
         scan(T.ZS[:], T.RS[:], T.E[:], 1.0, A.max, A.min, "RS E", "ZS")
         more_mm([(P[6][:, 256 + 12 * r:268 + 12 * r], blk(T.RZ, r, 128), T.ZS[:, 47::48]) for r in range(N if last else 0, N + 1)], "RZ ZS", "P6", True)
+        fill(1)
         tt(T.AF[:, 0:60], P[6][:, 256:316], T.UC[:, 0:60], A.min, "P6 UC", "AF")
+        if not last:
+            cp(T.AL[:], T.AF[:, 0:48], "AF", "AL")
 
-    def update():
-        cp(T.AL[:], T.AF[:, 0:48], "AF", "AL")
-        for r in reversed(range(N)):
-            cp(T.D[:, 512:512 + DW].indirect(blk(T.AL, r, 12)), blk(T.RL, r, 192), "AL D RL%d" % (r // 2), "D")
+    def update(r):
+        cp(T.D[:, 512:512 + DW].indirect(blk(T.AL, r, 12)), blk(T.RL, r, 192), "AL D RL%d" % (r // 2), "D")
+
+    def halves(x):
+        if x == 0:
+            cp(T.OH[:, 0:24:2], T.AF[:, 48:60], "AF", "OH0")
+        else:
+            tt(T.OH[:, 1:24:2], T.AF[:, 48:60], T.OH[:, 0:24:2], A.subtract, "AF OH0", "OH1")
 
     def parcel(rd):
-        cp(T.OH[:, 0:24:2], T.AF[:, 48:60], "AF", "OH0")
-        tt(T.OH[:, 1:24:2], T.AF[:, 48:60], T.OH[:, 0:24:2], A.subtract, "AF OH0", "OH1")
-        for o in range(N):
-            act(mine(rd, o, 48, 54), T.OH[:, 6 * o:6 * o + 6], F.Copy, "OH0 OH1 TS~", "OF")
-        send(lambda o: blk(T.TS, N * rd + o, TW), lambda o: blk(T.TL, N * rd + o, TW), "ar%d" % rd, "LO OF")
-        arrival("TL%d" % rd, "ar%d" % rd, peers)
-        wrote["LO%d" % rd], wrote["OF%d" % rd] = wrote["LO"], wrote["OF"]
+        last = rd == RO - 1
+        for o in peers + [rank]:
+            if last:
+                cp(mine(rd, o, 48, 54), T.OH[:, 6 * o:6 * o + 6], "OH0 OH1 TS~", "OF" if o != rank else "OFo")
+            else:
+                act(mine(rd, o, 48, 54), T.OH[:, 6 * o:6 * o + 6], F.Copy, "OH0 OH1 TS~", "OF" if o != rank else "OFo")
+        send(lambda o: blk(T.TS, N * rd + o, TW), lambda o: blk(T.TL, N * rd + o, TW), "al%d" % rank if last else "ar%d" % rd, "LO OF")
+        for o in peers:
+            arrival("TL%d%d" % (rd, o), "al%d" % o if last else "ar%d" % rd, [o] if last else peers)
+        wrote["TL%d%d" % (rd, rank)], wrote["LO%d" % rd] = wrote["OFo"], wrote["LO"]
 
     def regroup(rd):
-        got = lambda d, r: T.TL[32 * r:32 * r + 32, TW * (N * rd + d):TW * (N * rd + d + 1)]
-        quarters([[(blk(P[4], r, TW), [(qshift(T.SH, r, d - r), got(d, r)) for d in srcs])] for r in range(N)],
-                 "SH LO%d OF%d TL%d" % (rd, rd, rd), "P4")
+        mm([(P[4][:, 0:N * TW], [(T.ZR[:], T.B[:, 0:N * TW])])], "ZR B~", "P4", True, False)
+        for d in srcs:
+            more_mm([(blk(P[4], r, TW), T.WR[:, 224 * r + 96 - 32 * d:224 * r + 224 - 32 * d], blk(T.TL, N * rd + d, TW)) for r in range(N)],
+                    "WR LO%d TL%d%d" % (rd, rd, d), "P4", d == srcs[-1])
         act(T.VT[:], P[4][:, 0:N * TW], F.Copy, "P4", "VT")
         act(T.VA[:], P[4][:, 0:N * TW], F.Identity, "P4 crnd", "VA", scale=1.0 / 16, bias=col("rnd"))
 
     def unpack(rd):
-        mm([(P[4][:, 480 + 4 * r:484 + 4 * r], [(ID, T.VT[:, TW * r + 48 + x:TW * r + TW:2]) for x in range(2)]) for r in range(N)], "SH VT", "P4")
-        mm([(P[5][:, 0:N * TW], [(T.UY[:], T.VT[:]), (T.UZ[:, 0:128], T.VA[:])]), (P[5][:, 256:256 + N * TW], [(T.SK[:], T.VT[:])])],
-           "UY UZ SK VT VA", "P5")
+        mm([(P[5][:, 0:N * TW], [(T.UY[:], T.VT[:]), (T.UZ[:, 0:128], T.VA[:])])], "UY UZ VT VA", "P5")
         act(blk(T.RBY, rd, N * TW), P[5][:, 0:N * TW], F.Identity, "P5 cbY", "RBY%d" % rd, bias=col("bY"))
-        act(blk(T.RBK, rd, N * TW), P[5][:, 256:256 + N * TW], F.Copy, "P5", "RBK%d" % rd)
+        mm([(P[4][:, 480 + 4 * r:484 + 4 * r], [(ID, T.VT[:, TW * r + 48 + x:TW * r + TW:2]) for x in range(2)]) for r in range(N)]
+           + [(P[4][:, 256:256 + N * TW], [(T.SK[:], T.VT[:])])], "SH SK VT", "P4")
+        if rd == RO - 1:
+            slots(rd)
+        act(blk(T.RBK, rd, N * TW), P[4][:, 256:256 + N * TW], F.Copy, "P4", "RBK%d" % rd)
 
     def slots(rd):
         tt(T.XF[:], P[4][:, 480:496], T.XD[:], A.min, "P4 XD", "XF")
         ts(blk(T.XL, rd, 16), T.XF[:], float(-S * rank), None, A.add, None, "XF", "XL%d" % rd)
+        if rd < RO - 1:
+            todo.extend((rd, r, key) for r in reversed(range(N)) for key in "YK")
 
-    def place(rd):
-        for r in reversed(range(N)):
-            c0 = TW * (N * rd + r)
-            for win, src, key in ((T.YC, T.RBY, "Y"), (T.YK, T.RBK, "K")):
-                cp(win[:, 0:YW].indirect(T.XL[:, 16 * rd + 4 * r:16 * rd + 4 * r + 3]), src[:, c0:c0 + 48],
-                   "XL%d RB%s%d W%s" % (rd, key, rd, key), "W" + key)
+    todo = []
+
+    def fill(n_):
+        for _ in range(min(n_, len(todo))):
+            place(*todo.pop(0))
+
+    def place(rd, r, key):
+        win, src = (T.YC, T.RBY) if key == "Y" else (T.YK, T.RBK)
+        c0 = TW * (N * rd + r)
+        cp(win[:, 0:YW].indirect(T.XL[:, 16 * rd + 4 * r:16 * rd + 4 * r + 3]), src[:, c0:c0 + 48], "XL%d RB%s%d W%s" % (rd, key, rd, key), "W" + key)
 
     gather(0, "v")
     gather(1)
+    rec_start()
     for k in range(2):
         near(k)
     for k in range(2):
@@ -647,50 +695,73 @@ def rank_program(g, core, T, topo):
     hash_out()
     rec_out()
     hash_ops()
+    constants_2()
     for rd in range(RO):
         more = rd < RO - 1
         look()
         flags(rd)
         if rd > 1:
             unpack(rd - 2)
+        pointers(rd)
+        if more:
+            rec_start()
+        else:
+            nodes_mm(0)
         compact(rd)
         if rd > 1:
             slots(rd - 2)
+        fill(1)
         if more:
             gather(0)
             gather(1)
-            all_mm(rd)
             near(0)
+        keys(rd)
+        if more:
+            all_mm(rd, 1)
         else:
-            nodes_out()
-            regroup(rd - 1)
-            unpack(rd - 1)
+            nodes_mm(1)
         equal(rd)
         if more:
-            all_out()
+            all_mm(rd, 0)
             near(1)
+            all_out(1)
             life(0)
+            update(3)
+            halves(0)
             rec_kids(0)
-            update()
-            rec_kids(1)
+            all_out(0)
             life(1)
+            update(2)
+            halves(1)
+            rec_kids(1)
             hash_mm(0)
             hash_mm(1)
             rec_mm()
             hash_out()
+            update(1)
+            update(0)
+            parcel(rd)
             rec_out()
             hash_ops()
-        parcel(rd)
-        if more and rd:
+            if rd:
+                regroup(rd - 1)
+        else:
+            halves(0)
+            halves(1)
+            parcel(rd)
+            nodes_out()
             regroup(rd - 1)
-    slots(RO - 2)
-    for rd in range(RO - 1):
-        place(rd)
+            unpack(rd - 1)
+            fill(4)
+            slots(rd - 1)
+    fill(len(todo))
     regroup(RO - 1)
     unpack(RO - 1)
-    slots(RO - 1)
-    place(RO - 1)
+    for key in "YK":
+        for r in reversed(range(N)):
+            place(RO - 1, r, key)
     dma("y", [(T.ycells[:], T.YC[:, 0:S])], "WY", "yc")
+    dma("y", [(T.ynodes[32 * o:32 * o + 32, :], blk(T.NL, o, 32)) for o in peers], "NL", "yn")
     dma("s", [(T.ykids[t::4, :], T.YK[t::16, 0:S]) for t in range(4)], "WK", "yk")
     for sem, n_ in total.items():
         need("g", (sem, n_))

@@ -1,36 +1,37 @@
 from concourse.bass import DstId, RemoteDMATransfer
-from concourse.mybir import AluOpType as A, ActivationFunctionType as F, AxisListType as X
+from concourse.mybir import AluOpType as A, ActivationFunctionType as F
 
 N, S, RO = 4, 2048, 4
 DW = 8704
 YW = 2112
-TW = 56
-CUT = 272
+TW = 64
+EQW = 16384.0
+WON = -16512.0
 f32, bf, i32, u16 = "float32", "bfloat16", "int32", "uint16"
 SB = {
     "CS": (2048, bf), "LC": (2048, bf), "KS": (640, i32), "KU": (640, u16), "LK": (640, u16), "YC": (YW, bf), "YK": (YW, f32),
-    "KI": (640, i32), "KB": (1152, bf), "KF": (512, f32), "NN": (2048, bf), "DS": (2048, bf), "RF": (128, bf),
+    "KI": (640, i32), "KB": (1152, bf), "KF": (512, f32), "NN": (2048, bf), "DS": (1024, bf), "PT": (1024, bf), "RF": (129, bf),
     "B": (512 + 8192, bf), "CC": (8192, bf), "D": (512 + DW, bf), "KL": (512, u16), "WI": (8, i32), "WJ": (8, i32),
-    "PI": (8, i32), "BI": (24, i32), "COL": (128, f32), "IF": (256, f32),
-    "R5": (128, f32), "RE": (128, f32), "RC": (32, f32), "EU": (512, bf), "IDT": (512, bf), "IDL": (128, bf), "BB": (16, f32),
-    "AU": (224, bf), "TM": (64, f32), "RY": (128, bf), "NG": (128, bf), "GW": (224, bf), "KP": (544, bf),
-    "KR": (272, bf), "OB": (128, bf), "O1": (128, bf), "TR": (128, bf), "M2": (128, bf), "WX": (128, bf), "WE": (128, bf), "SH": (128, bf),
-    "BC": (128, bf), "SK": (128, bf), "UY": (128, bf), "UZ": (128, bf), "RP": (640, f32), "RB": (512, bf), "RZ": (640, bf),
-    "NI": (576, f32), "NO": (704, f32), "LW": (576, bf), "EQ": (16, f32), "ZR": (128, bf), "WR": (896, bf),
-    "CW": (576 + 2560, f32), "CT": (576, f32), "OWN": (32, f32), "RT": (128, bf), "CA": (128, bf), "DP": (128, f32),
-    "MR": (384, f32), "MK": (384, bf), "RS": (576, bf), "UC": (64, f32), "XD": (16, f32),
-    "NA": (256, i32), "NF": (256, f32), "PL": (128, u16), "G": (2048, bf), "AB": (1024, bf), "UA": (512, bf), "DD": (1024, bf), "RX": (512, bf),
-    "HI": (256, i32), "HF": (128, f32), "HL": (64, u16), "PN": (128, f32), "CL": (384, f32), "PG": (512, bf),
+    "PI": (8, i32), "BI": (16, i32), "COL": (64, f32), "IF": (192, f32), "RG": (128, f32),
+    "RE": (128, f32), "RC": (32, f32), "EU": (512, bf), "IDT": (512, bf), "IDL": (128, bf), "BB": (16, f32),
+    "AU": (224, bf), "TM": (64, f32), "RY": (128, bf), "NG": (137, bf), "GW": (224, bf), "KP": (272, bf),
+    "KR": (272, bf), "OB": (128, bf), "M2": (128, bf), "WX": (256, bf), "SH": (128, bf),
+    "BC": (128, bf), "SK": (128, bf), "UY": (128, bf), "UZ": (128, bf), "RB": (512, bf),
+    "NI": (576, f32), "NO": (704, f32), "LW": (576, bf), "EQ": (8, f32), "ZR": (128, bf), "WR": (896, bf),
+    "CW": (576 + 2560, f32), "CT": (192, f32), "OWN": (32, f32), "RT": (128, bf), "CA": (128, bf), "DP": (128, f32),
+    "MR": (384, bf), "MK": (384, bf), "RS": (576, bf), "UC": (48, f32), "XD": (16, f32),
+    "NF": (256, f32), "PL": (128, u16), "G": (2048, bf), "AB": (1024, bf), "UA": (256, bf), "DD": (1024, bf), "RX": (512, bf),
+    "HI": (160, i32), "HF": (64, f32), "HL": (64, u16), "PN": (128, f32), "CL": (320, f32), "PG": (512, bf),
     "FB": (128, bf), "RR": (128, bf), "SQ": (128, f32), "AT": (32, u16), "OL": (32, u16), "WG": (512, bf), "RQ": (512, f32),
-    "HX": (192, bf), "KC": (16, f32), "E": (576, bf), "ZS": (576, bf), "AF": (64, f32), "AL": (48, u16), "RL": (768, bf),
-    "OH": (32, bf), "TS": (RO * N * TW, bf), "TL": (RO * N * TW, bf), "VT": (N * TW, bf), "VA": (N * TW, bf),
+    "HX": (192, bf), "KC": (32, bf), "E": (576, bf), "ZS": (576, bf), "AF": (48, f32), "AL": (48, u16), "RL": (768, bf),
+    "TS": (RO * N * TW, bf), "TL": (RO * N * TW, bf), "VT": (N * TW, bf), "VA": (N * TW, bf), "ZT": (32, bf), "ZL": (32, bf),
     "RBY": (RO * N * TW, bf), "RBK": (RO * N * TW, f32), "XF": (16, f32), "XL": (RO * 16, u16), "NS": (128, f32), "NL": (128, f32),
 }
 SCRATCH = {n: ("sbuf", [128, w], d) for n, (w, d) in SB.items()}
 SCRATCH.update({"P%d" % k: ("psum", [128, 512], f32) for k in range(8)})
-SCRATCH.update({"DLD": ("dram", [4, 128, 512], bf)})
-SEMAPHORES = (["eg", "ev", "es", "et", "sent", "ak", "an"] + ["ac%d" % k for k in range(N)] + ["ad%d" % k for k in range(N)]
-              + ["ar%d" % k for k in range(RO - 1)] + ["al%d" % k for k in range(N)] + ["d%d" % k for k in range(24)])
+SCRATCH.update({"DLD": ("dram", [4, 128, 256], bf)})
+SEMAPHORES = (["eg", "ev", "es", "et", "sent", "ak", "am", "an"] + ["ac%d" % k for k in range(N)] + ["ad%d" % k for k in range(N)]
+              + ["ar%d" % k for k in range(RO)] + ["al%d" % k for k in range(N)] + ["d%d" % k for k in range(32)])
 
 
 def rank_program(g, core, T, topo):
@@ -107,20 +108,23 @@ def rank_program(g, core, T, topo):
     eng = {o: masks(o) for o in range(N)}
     peers = [o for o in range(N) if o != rank]
     sent = [0]
+    off_chip = lambda a, b: T.cores[b] not in topo.cores_of(T.cores[a])
+    alone = lambda a, b: topo.engines(T.cores[a], T.cores[b]) if off_chip(a, b) else eng[a][b]
 
-    def send(src, dst, sem, r):
+    def send(src, dst, sem, r, to=None):
         order("g", r.split(), [], "dma")
         trs = []
-        for o in peers:
+        for o in to or peers:
             rid, pid = topo.addr(T.cores[o], core)
-            trs.append(RemoteDMATransfer(dst_ids=[DstId(rid=rid, pnc=pid)], dma_engine_mask=sum(1 << x for x in eng[rank][o]),
+            en = alone(rank, o) if to else eng[rank][o]
+            trs.append(RemoteDMATransfer(dst_ids=[DstId(rid=rid, pnc=pid)], dma_engine_mask=sum(1 << x for x in en),
                                          remote_sem=T.sem[sem], src=src(o), dst=dst(rank)))
-            sent[0] += len(eng[rank][o])
+            sent[0] += len(en)
         g.remote_dma_fused(trs, local_sem=T.sem.sent)
         total["sent"] = sent[0]
 
-    def arrival(key, sem, from_):
-        n_ = sum(len(eng[o][rank]) for o in from_)
+    def arrival(key, sem, from_, one=False):
+        n_ = sum(len(alone(o, rank) if one else eng[o][rank]) for o in from_)
         wrote[key] = (sem, n_, "dma")
         total[sem] = n_
 
@@ -162,15 +166,19 @@ def rank_program(g, core, T, topo):
             return ins
         op("t", run, r, w)
 
-    def quarters(parts, r, w):
-        for items in parts:
-            mm(items, r + " " + w, w)
-
     def iota(o, pat, base, cm, w, r=""):
         op("g", lambda: g.iota(o, pat, base, cm, allow_small_or_imprecise_dtypes=True), r, w)
 
     def sel(o, a, pat, cmp, fill, base, cm, r, w):
         op("g", lambda: g.affine_select(o, a, pat, cmp, fill, base, cm), r, w)
+
+    def move(e, o, a, r, w):
+        if e == "v":
+            cp(o, a, r, w)
+        elif e == "s":
+            act(o, a, F.Copy, r, w)
+        else:
+            sel(o, a, [[0, a.shape[1]]], A.is_equal, 0.0, 0, 0, r, w)
 
     cols = {}
 
@@ -178,20 +186,6 @@ def rank_program(g, core, T, topo):
         if name not in cols:
             cols[name] = len(cols)
         return T.COL[:, cols[name]:cols[name] + 1]
-
-    def lins(specs):
-        for n_ in range(3):
-            for name, terms, const in specs:
-                if n_ < len(terms):
-                    c, k = terms[n_]
-                    dst = name if n_ == len(terms) - 1 else name + "~%d" % n_
-                    if n_ == 0 and not const:
-                        act(col(dst), col(c), F.Identity, "c" + c, "c" + dst, scale=float(k))
-                    elif n_ == 0:
-                        act(col(dst), col(c), F.Identity, "c" + c, "c" + dst, scale=float(k), bias=float(const))
-                    else:
-                        prev = name + "~%d" % (n_ - 1)
-                        act(col(dst), col(c), F.Identity, "c%s c%s" % (c, prev), "c" + dst, scale=float(k), bias=col(prev))
 
     def cts(name, c, s1, s2, o0, o1=None):
         r = " ".join("c" + x for x in (c, s1, s2) if isinstance(x, str))
@@ -203,149 +197,69 @@ def rank_program(g, core, T, topo):
         else:
             ts(out, row, col(tc), wc, A.is_equal, A.mult, "%s c%s EQ" % (rk, tc), key)
 
-    def scaled(out, a, ak, c, key):
-        act(out, a, F.Identity, "%s c%s" % (ak, c), key, scale=col(c))
-
     P = [T["P%d" % k] for k in range(8)]
     blk = lambda t, o, w: t[:, o * w:(o + 1) * w]
-    srcs = [rank] + sorted(peers, key=lambda o: -len(eng[o][rank]))
-    ID, REC = T.SH[:, 0:128], T.D[:, 0:512]
-    qshift = lambda m, q, d: m[32 * q:32 * q + 32, 128 - 32 * (d % 4):256 - 32 * (d % 4)]
+    srcs = [rank] + sorted(peers, key=lambda o: (off_chip(rank, o), topo.die(T.cores[o]) != topo.die(core)))
+    near_, far = srcs[1:2], srcs[2:]
+    ID, REC = T.SH[:], T.D[:, 0:512]
 
-    dma("y", [(blk(T.CS, o, 512), T.cells[32 * o:32 * o + 32, :]) for o in peers], "", "CS")
-    dma("y", [(blk(T.KS, o, 128), T.kids[8 * o:8 * o + 8, :]) for o in range(N)]
-        + [(blk(T.KS, 16 + o, 32), T.nodes[32 * o:32 * o + 32, :]) for o in range(N)], "", "KS")
+    for o in far:
+        dma("y", [(blk(T.CS, o, 512), T.cells[32 * o:32 * o + 32, :])], "", "CS%d" % o)
+    dma("y", [(blk(T.KS, o, 128), T.kids[8 * o:8 * o + 8, :]) for o in range(N)], "", "KS")
+    dma("y", [(blk(T.CS, o, 512), T.cells[32 * o:32 * o + 32, :]) for o in near_], "", "CS%d" % near_[0])
+    dma("y", [(blk(T.KS, 16 + o, 32), T.nodes[32 * o:32 * o + 32, :]) for o in range(N)], "", "KN")
     dma("y", [(blk(T.LC, rank, 512), T.cells[32 * rank:32 * rank + 32, :])], "", "LC%d" % rank)
     dma("y", [(T.WI[32 * q:32 * q + 32, 0:1], T.wt[32 * rank:32 * rank + 32, :]) for q in range(4)], "", "WI")
     iota(T.PI[:, 0:1], [[0, 1]], 0, 1, "PI")
-    iota(T.IF[:], [[1, 256]], 0, 0, "IF")
+    iota(T.IF[:], [[1, 192]], -64, 0, "IF")
+    IF = lambda a, b: T.IF[:, 64 + a:64 + b]
     ms(T.RE[:], 1000.0, "RE")
     ms(T.IDT[0:64, :], 0.0, "IDT")
     ms(T.IDL[0:64, :], 0.0, "IDL")
     for a in range(3):
         for b in range(3):
             iota(T.RE[:, 4 * a + b::16], [[64, 2], [16, 2], [4, 2]], 4 * (4 * a + b), -1, "RE0", "RE")
+    send(lambda o: blk(T.CS, o, 512), lambda o: blk(T.LC, o, 512), "ac%d" % rank, "CS%d" % far[0], far[:1])
     for a in range(2):
         for b in range(2):
             iota(T.RE[:, 12 + 2 * a + b::16], [[64, 2], [32, 2], [8, 2]], 4 * (4 * a + b), -1, "RE0")
+    send(lambda o: blk(T.CS, o, 512), lambda o: blk(T.LC, o, 512), "ac%d" % rank, "CS%d CS%d" % (far[1], near_[0]), far[1:] + near_)
+    for o in peers:
+        arrival("LC%d" % o, "ac%d" % o, [o], True)
     iota(T.RC[:, 0:16], [[1, 4], [0, 4]], 0, 0, "RC")
     iota(T.RC[:, 16:32], [[0, 4], [1, 4]], 0, 0, "RC")
-    iota(T.UC[:, 0:60], [[0, 5], [128, 4], [16, 3]], 8192, 0, "UC0")
-    iota(T.CA[:], [[0, 32], [1, 4]], -4, 0, "CA")
-    send(lambda o: blk(T.CS, o, 512), lambda o: blk(T.LC, o, 512), "ac%d" % rank, "CS")
-    for o in peers:
-        arrival("LC%d" % o, "ac%d" % o, [o])
+    iota(T.RG[:], [[16, 8], [0, 16]], 0, 0, "RG")
 
-    fields = [("p", 0, 127), ("j", 0, 15), ("lo2", 0, 3), ("a2", 2, 3), ("b0", 0, 1), ("b1", 1, 1), ("b3", 3, 1), ("b4", 4, 1), ("b5", 5, 1),
-              ("b6", 6, 1), ("grp", 4, 7), ("q", 5, 3), ("k2", 4, 3), ("m2", 1, 3), ("h3", 1, 7), ("p31", 0, 31), ("b2", 2, 1), ("i3", 3, 3),
-              ("i8", 3, 7), ("i16", 2, 15)]
+    fields = [("p", 0, 127), ("j", 0, 15), ("lo2", 0, 3), ("a2", 2, 3), ("b0", 0, 1), ("b1", 1, 1), ("b2", 2, 1), ("b3", 3, 1), ("b4", 4, 1),
+              ("b5", 5, 1), ("x64", 0, 64), ("x60", 0, 60), ("x112", 0, 112), ("x120", 0, 120), ("h3", 1, 7)]
     for n_, (name, sh, mk) in enumerate(fields):
         col(name)
         ts(T.BI[:, n_:n_ + 1], T.PI[:, 0:1], sh, mk, A.logical_shift_right, A.bitwise_and, "PI", "BI")
     ms(T.IDL[0:1, 3::16], 1.0, "IDL", "IDL")
     ms(T.IDL[32:33, 7::16], 1.0, "IDL")
     cp(T.COL[:, 0:len(fields)], T.BI[:, 0:len(fields)], "BI", " ".join("c" + x[0] for x in fields))
-    lins([("tRF", [("b6", 64), ("i8", 4), ("lo2", 1)], 0), ("wRF", [("b2", 15)], 1), ("tKP", [("b6", 64), ("k2", 8), ("a2", 1)], 36),
-          ("p32", [("p", 1)], 32), ("nb2", [("b2", 144)], -144)])
-    cts("f0", "i16", 0.0, -1.0, A.is_equal, A.mult)
-    cts("f1", "i16", 1.0, -1.0, A.is_equal, A.mult)
-    ts(T.EQ[:, 0:4], T.IF[:, 0:4], col("lo2"), None, A.is_equal, None, "IF clo2", "EQ")
-    cts("bD", "nb2", "b5", None, A.mult)
-    onehot(T.RF[:], T.IF[:, 0:128], "IF", "tRF", "wRF", "RF")
-    onehot(T.NG[:], T.IF[:, 0:128], "IF", "p32", -1.0, "NG")
-    for u in range(4):
-        onehot(T.KP[:, 136 * u:136 * u + 132], T.IF[:, 0:132], "IF", "tKP", T.EQ[:, u:u + 1], "KP")
-    lins([("tRY", [("grp", 16), ("h3", 1)], 0), ("w16", [("b0", 15)], 1), ("nb3", [("b3", -1)], 1), ("mOB", [("grp", -16)], -7.5),
-          ("mTR", [("grp", -16), ("j", -0.5)], 0.5), ("rTR", [("j", 0.5)], 0),
-          ("nR", [("a2", -1), ("b5", 3)], -2), ("dR", [("b1", -1), ("a2", 1), ("b5", -1)], 0), ("nC", [("lo2", -1), ("b4", 3)], -2),
-          ("dC", [("b0", -1), ("lo2", 1), ("b4", -1)], 0), ("tNI", [("b6", 64), ("lo2", -16), ("i3", 1)], 60), ("xk", [("b5", 2), ("b2", 1)], 0),
-          ("tKR", [("b4", 64), ("q", 4), ("m2", -16)], 51), ("wp0", [("b0", 63)], 1), ("wn0", [("b0", -127)], 128),
-          ("na", [("p", 0)], -(1.0 + 2.0 ** -10))])
-    act(T.MR[:, 0:128], T.IF[:, 0:128], F.Abs, "IF cmOB", "MR0", bias=col("mOB"))
-    act(T.MR[:, 128:256], T.IF[:, 0:128], F.Abs, "IF cmTR", "MR1", bias=col("mTR"))
-    cts("hb", "lo2", 2.5, -14.0, A.is_lt, A.mult)
-    cts("i74", "j", 7.0, 4.0, A.is_equal, A.mult)
-    cts("n0", "j", 0.0, -1.0, A.is_equal, A.mult)
-    cts("n1", "j", 1.0, -1.0, A.is_equal, A.mult)
-    cts("is3", "j", 3.0, None, A.is_equal)
-    cts("mid", "a2", 3.0, None, A.is_equal)
-    cts("bh", "a2", 2.5, "hb", A.is_lt, A.mult)
     for c in range(1, 4):
         ms(T.IDT[32:33, 128 * c:128 * c + 128], float(c), "IDT1", "IDT")
+    ms(T.ZR[:], 0.0, "ZR")
+    cts("tRF", "lo2", 2.0, "x120", A.mult, A.add)
+    cts("wRF", "b2", 15.0, 1.0, A.mult, A.add)
+    cts("tKP", "x112", "h3", None, A.add)
+    cts("tNG", "lo2", 2.0, "x64", A.mult, A.add)
+    cts("f0", "x60", 0.0, -1.0, A.is_equal, A.mult)
+    cts("bD", "b3", 144.0, -144.0, A.mult, A.add)
+    ts(T.EQ[:, 0:2], IF(0, 2), col("b0"), None, A.is_equal, None, "IF cb0", "EQ")
+    onehot(T.NG[:], IF(-9, 128), "IF", "tNG", "f0", "NG")
+    for e in range(2):
+        onehot(blk(T.KP, e, 136), IF(-8, 128), "IF", "tKP", T.EQ[:, e:e + 1], "KP")
+    onehot(T.RF[:], IF(-1, 128), "IF", "tRF", "wRF", "RF")
     for c in range(4):
-        cp(T.IDT[0:1, 128 * c:128 * c + 128], T.IF[0:1, 0:128], "IF IDT", "IDT0")
-    ts(T.BB[:], T.IF[:, 0:16], col("i74"), col("bh"), A.mult, A.add, "IF ci74 cbh", "BB")
-    for u in range(4):
-        ts(blk(T.EU, u, 128), T.RE[:], float(-u), None, A.is_equal, None, "RE0", "EU")
-    onehot(T.SH[:], T.IF[:, 0:128], "IF", "p", 1.0, "SH")
-    ms(T.AU[:], 0.0, "AU")
-    ms(T.LW[:], 0.0, "LW")
-
-    lists = lambda o, a, b: (T.LK if o == rank else T.KU)[:, 160 * o + a:160 * o + b]
-    ts(T.KB[:, 0:640], T.KS[:], 2.0 ** -7, 143.504, A.mult, A.add, "KS", "KB0")
-    ts(T.KI[:], T.KS[:], 127, None, A.bitwise_and, None, "KS", "KI")
-    for o in peers + [rank]:
-        cp(lists(o, 0, 128), blk(T.KS, o, 128), "KS", "KU")
-    ts(T.NF[:, 0:128], T.KI[:, 512:640], 64.0, -144.0, A.mult, A.add, "KI", "NF0")
-    cp(T.KB[:, 640:1152], T.KI[:, 0:512], "KI", "KB1")
-    tt(T.NF[:, 128:256], T.NF[:, 0:128], T.KB[:, 512:640], A.add, "NF0 KB0", "NF1")
-    for o in peers + [rank]:
-        cp(lists(o, 128, 160), blk(T.NF, 4 + o, 32), "NF1", "KU")
-    send(lambda o: blk(T.KU, o, 160), lambda o: blk(T.LK, o, 160), "ak", "KU")
-    arrival("LK", "ak", peers)
-
-    cs = lambda o, a=0, st=1: (T.LC if o == rank else T.CS)[:, 512 * o + a:512 * o + 512:st]
-    for o in peers + [rank]:
-        ck = "LC%d" % o if o == rank else "CS"
-        act(T.NN[:, 512 * o:512 * o + 512:2], cs(o, 0, 2), F.Relu, ck + " cf0", "NN%d" % o, scale=col("f0"))
-        act(T.NN[:, 512 * o + 1:512 * o + 512:2], cs(o, 1, 2), F.Relu, ck + " cf1", "NN%d" % o, scale=col("f1"))
-        mm([(P[4 + o][:], [(T.RF[:], cs(o)), (T.NG[:], blk(T.NN, o, 512))])], "RF NG NN%d %s" % (o, ck), "P%d" % (4 + o), True, False)
-    for n_, o in enumerate(peers + [rank]):
-        more_mm([(blk(P[4 + o], u, 128), T.KP[:, 136 * u + 4 - 4 * x:136 * u + 132 - 4 * x], T.KB[:, 640 * x + 128 * o:640 * x + 128 * o + 128])
-                 for x in range(2) for u in range(4)], "KP KB0 KB1", "P%d" % (4 + o), True)
-        if n_ == 1:
-            ts(blk(T.DS, o, 512), P[4 + o][:], col("bD"), None, A.add, None, "P%d cbD" % (4 + o), "DS%d" % o)
-        else:
-            act(blk(T.DS, o, 512), P[4 + o][:], F.Identity, "P%d cbD" % (4 + o), "DS%d" % o, bias=col("bD"))
-    send(lambda o: blk(T.DS, o, 512), lambda o: T.DLD[o], "ad%d" % rank, " ".join("DS%d" % o for o in peers))
-    for o in peers:
-        arrival("DLD%d" % o, "ad%d" % o, [o])
-    window = lambda o: [(T.D[32 * y:32 * y + 32, 512 + S * o:512 + S * o + S], T.DLD[o]) for y in range(4)]
-    dma("y", [(T.DLD[rank], blk(T.DS, rank, 512))], "DS%d" % rank, "DLD%d" % rank)
-    dma("y", window(rank), "DLD%d" % rank, "Dw%d" % rank)
-
-    def fill_g(t, c, key):
-        iota(t, [[0, t.shape[1]]], c, 0, key)
-
-    def paint(t, pat, base, w, key):
-        sel(t, t, pat, A.not_equal, w, base, 1, key, key)
-    fill_g(T.B[:, 0:512], 0, "B~")
-    fill_g(T.ZR[:], 0, "ZR")
-    fill_g(T.DP[:], -1000000, "DP0")
-    fill_g(T.RT[:], 1, "RT0")
-    sel(T.RT[:], T.RT[:], [[0, 4], [1, 32]], A.not_equal, 0.0, 0, 0, "RT0", "RT")
-    fill_g(T.RP[:], 0, "RP")
-    paint(T.RP[:, 0:512], [[-32, 4], [0, 4], [-1, 32]], 0, 1.0, "RP")
-    paint(T.RP[:, 512:640], [[-1, 128]], 0, 1.0, "RP")
-    fill_g(T.E[:], 1, "E")
-    sel(T.RS[:], T.E[:], [[0, 12], [1, 48]], A.is_equal, 0.0, 0, 0, "E", "RS")
-    fill_g(T.TS[:], 0, "TS~")
-    for rd in range(RO):
-        fill_g(blk(T.TL, N * rd + rank, TW), 0, "TS~")
-    fill_g(T.WR[:], 0, "WR")
-    for r in range(N):
-        paint(T.WR[:, 224 * r + 96:224 * r + 128], [[-1, 32]], -32 * r, 1.0, "WR")
-    for t, key in ((T.SK, "SK"), (T.UY, "UY"), (T.UZ, "UZ")):
-        fill_g(t[:], 0, key)
-    for x in range(2):
-        paint(T.SK[:], [[-16, 8], [1000, 4], [-2, 4]], -8 - x, (128.0, 1.0)[x], "SK")
-        paint(T.UZ[:, x::2], [[-16, 8], [-1, 8]], 0, (-16.0, 1.0)[x], "UZ")
-    paint(T.UY[:, 0::2], [[-16, 8], [-1, 8]], 0, 1.0, "UY")
-    fill_g(T.NO[:], 0, "NO")
-    for r in range(N):
-        for s in range(2):
-            c0 = 176 * r + 36 + 64 * s
-            paint(T.NO[:, c0:c0 + 32], [[-1, 4], [1000, 2], [16, 4]], -(64 * s + 48 + 4 * r), 1.0, "NO")
+        cp(T.IDT[0:1, 128 * c:128 * c + 128], T.IF[0:1, 64:192], "IF IDT", "IDT0")
+    cts("hb", "lo2", 2.5, -14.0, A.is_lt, A.mult)
+    cts("i74", "j", 7.0, 4.0, A.is_equal, A.mult)
+    cts("mid", "a2", 3.0, None, A.is_equal)
+    cts("bh", "a2", 2.5, "hb", A.is_lt, A.mult)
+    ms(col("rnd"), 143.53, "crnd")
+    ts(T.BB[:], IF(0, 16), col("i74"), col("bh"), A.mult, A.add, "IF ci74 cbh", "BB")
 
     def b_number(banks):
         for bank in banks:
@@ -359,133 +273,229 @@ def rank_program(g, core, T, topo):
                 ts(blk(T.B, b + 1, 512), P[bank][:], T.BB[:, b:b + 1], 0.0, A.add, A.max, "P%d BB" % bank, "B%d" % b)
             else:
                 act(blk(T.B, b + 1, 512), P[bank][:], F.Relu, "P%d BB" % bank, "B%d" % b, bias=T.BB[:, b:b + 1])
+
+    ts(T.KI[:, 0:512], T.KS[:, 0:512], 127, None, A.bitwise_and, None, "KS", "KI")
+    ts(T.KB[:, 0:512], T.KS[:, 0:512], 2.0 ** -7, 143.504, A.mult, A.add, "KS", "KB0")
+    cp(T.KB[:, 640:1152], T.KI[:, 0:512], "KI", "KB1")
+    cp(T.KU[:, 0:512], T.KS[:, 0:512], "KS", "KU")
+    ts(T.KI[:, 512:640], T.KS[:, 512:640], 127, None, A.bitwise_and, None, "KN", "KJ")
+    ts(T.KB[:, 512:640], T.KS[:, 512:640], 2.0 ** -7, 143.504, A.mult, A.add, "KN", "KB2")
+    ts(T.NF[:, 0:128], T.KI[:, 512:640], 64.0, -144.0, A.mult, A.add, "KJ", "NF0")
+    cp(T.KL[:, rank::4], blk(T.KU, rank, 128), "KU", "KL")
+    tt(T.NF[:, 128:256], T.NF[:, 0:128], T.KB[:, 512:640], A.add, "NF0 KB2", "NF1")
+    cp(T.KU[:, 512:640], T.NF[:, 128:256], "NF1", "NU")
+    cp(blk(T.LK, 16 + rank, 32), blk(T.NF, 4 + rank, 32), "NF1", "LNo")
+    send(lambda o: blk(T.KU, o, 128), lambda o: blk(T.LK, o, 128), "ak", "KU")
+    arrival("LK", "ak", peers)
+    send(lambda o: blk(T.KU, 16 + o, 32), lambda o: blk(T.LK, 16 + o, 32), "am", "NU")
+    arrival("LN", "am", peers)
+
+    def d_marks(o):
+        src, key = (T.LC, "LC%d" % o) if o == rank else (T.CS, "CS%d" % o)
+        act(blk(T.NN, o, 512), blk(src, o, 512), F.Relu, key, "NN%d" % o, scale=-1.0)
+        mm([(P[4 + o][:, 0:256], [(T.ZR[:], blk(T.NN, 2 * o, 256))])], "ZR NN%d" % o, "P%d" % (4 + o), True, False)
+        more_mm([(P[4 + o][:, x:256:2], T.NG[:, 9 - h - 8 * x:137 - h - 8 * x], T.NN[:, 512 * o + 256 * h + x:512 * o + 256 * h + 256:2])
+                 for x in range(2) for h in range(2)], "NG NN%d" % o, "P%d" % (4 + o))
+
+    def d_kids(o):
+        more_mm([(blk(P[4 + o], e, 128), T.KP[:, 136 * e + 8 - 8 * x:136 * e + 136 - 8 * x], T.KB[:, 640 * x + 128 * o:640 * x + 128 * o + 128])
+                 for x in range(2) for e in range(2)], "KP KB0 KB1", "P%d" % (4 + o), True)
+        act(blk(T.DS, o, 256), P[4 + o][:, 0:256], F.Identity, "P%d cbD" % (4 + o), "DS%d" % o, bias=col("bD"))
+
+    def window(o, x, src):
+        return [(T.D[32 * y + 16 * s + 8 * x:32 * y + 16 * s + 8 * x + 8, 512 + S * o:512 + S * o + S], src(slice(64 * s, 64 * s + 64)))
+                for y in range(4) for s in range(2)]
+
+    def d_pairs(o, bank):
+        mm([(P[bank][:, 0:256], [(T.RF[:, 1 - h:129 - h], blk(T.LC, 2 * o + h, 256)) for h in range(2)])], "RF LC%d" % o, "P%d" % bank)
+        act(blk(T.PT, o, 256), P[bank][:, 0:256], F.Copy, "P%d" % bank, "PT%d" % o)
+        dma("y", window(o, 0, lambda q: T.PT[q, 256 * o:256 * o + 256]), "PT%d" % o, "Dp%d" % o)
     b_number(range(4))
-    b_cells(srcs[0], 0)
-    b_number(range(4))
-    b_number((4, 5, 6, 7))
-    onehot(T.RY[:], T.IF[:, 0:128], "IF", "tRY", "w16", "RY")
-    ts(T.OB[:], T.MR[:, 0:128], 8.0, None, A.is_lt, None, "MR0", "OB")
-    ts(T.TR[:], T.MR[:, 128:256], col("rTR"), None, A.is_lt, None, "MR1 crTR", "TR")
-    cts("i37", "lo2", 3.0, "nb3", A.is_equal, A.mult)
-    cts("wh", "bh", -1.0, 2.0 ** -13, A.is_lt, A.mult)
-    cts("xR", "dR", "mid", "nR", A.mult, A.add)
-    cts("xC", "dC", "mid", "nC", A.mult, A.add)
-    cts("wm", "mid", "wh", None, A.subtract)
-    ts(T.EQ[:, 4:8], T.IF[:, 0:4], col("xk"), None, A.is_equal, None, "IF cxk", "EQ")
-    ts(T.TM[:, 0:16], T.RC[:, 0:16], col("xR"), None, A.add, None, "RC cxR", "TM0")
-    ts(T.TM[:, 16:32], T.RC[:, 16:32], col("xC"), None, A.add, None, "RC cxC", "TM0")
+    for grp in (far + near_, [rank]):
+        for o in grp:
+            d_marks(o)
+        for o in grp:
+            d_kids(o)
+    send(lambda o: blk(T.DS, o, 256), lambda o: T.DLD[o], "ad%d" % rank, " ".join("DS%d" % o for o in peers))
+    for o in peers:
+        arrival("DLD%d" % o, "ad%d" % o, [o])
+    dma("y", window(rank, 1, lambda q: T.DS[q, 256 * rank:256 * rank + 256]), "DS%d" % rank, "Dw%d" % rank)
+    for u in range(4):
+        ts(blk(T.EU, u, 128), T.RE[:], float(-u), None, A.is_equal, None, "RE0", "EU")
+    d_pairs(rank, 4)
+    b_cells(srcs[0], 0, False)
+    b_number((4, 5, 6, 7, 0, 1, 2, 3))
+    b_cells(srcs[2], 4, False)
+    d_pairs(srcs[2], 4)
+    b_number((5, 6, 7, 4))
+
+    def fill_g(t, c, key):
+        iota(t, [[0, t.shape[1]]], c, 0, key)
+
+    def paint(t, pat, base, w, key):
+        sel(t, t, pat, A.not_equal, w, base, 1, key, key)
+
+    def keep(t, pat, base, key, cmp=A.is_equal, cm=1):
+        sel(t, t, pat, cmp, 0.0, base, cm, key, key)
+    fill_g(T.NI[:], 0, "NI")
     for x in range(4):
-        onehot(T.NI[:, 144 * x:144 * x + 140], T.IF[:, 0:140], "IF", "tNI", T.EQ[:, 4 + x:5 + x], "NI")
-    tt(T.TM[:, 32:64], T.TM[:, 0:32], T.TM[:, 0:32], A.mult, "TM0", "TM1")
-    tt(T.TM[:, 0:16], T.TM[:, 32:48], T.TM[:, 48:64], A.add, "TM1", "TM0")
+        for s in range(2):
+            c0 = 144 * x + 12 + 64 * s
+            paint(T.NI[:, c0:c0 + 64], [[1, 4], [1000, 4], [-8, 4]], -(64 * s + 32 * (x // 2) + 4 * (x % 2) + 3), 1.0, "NI")
+    fill_g(T.GW[:], 0, "GW")
+    for s in range(2):
+        for x in range(2):
+            paint(T.GW[:, 104 + 16 * s + x:112 + 16 * s:2], [[16, 4]], -(64 * s + 55 - 4 * x), 1.0, "GW")
+    fill_g(T.RY[:], 0, "RY")
+    for x in range(2):
+        paint(T.RY[:], [[-16, 8], [1000, 2], [-2, 8]], -x, (1.0, 16.0)[x], "RY")
+    fill_g(T.WX[:], 0, "WX")
+    for c0, row, w in ((0, 7, 512.0), (1, 3, 512.0), (129, 8, -512.0), (129, 9, 512.0)):
+        paint(T.WX[:, c0:c0 + 127:16], [[-16, 8]], -row, w, "WX")
+    iota(T.CA[:], [[0, 32], [-1, 4]], 4, 0, "CA")
+    fill_g(T.M2[:], 1, "M2")
+    keep(T.M2[:], [[16, 8], [0, 16]], 15, "M2", A.is_ge, -1)
+    keep(T.M2[:], [[-1, 128]], 0, "M2", A.is_gt)
+    paint(T.M2[:], [[-1, 128]], 0, 1024.0, "M2")
+    fill_g(T.RT[:], 1, "RT")
+    keep(T.RT[:], [[0, 4], [1, 32]], 0, "RT", A.not_equal, 0)
+    fill_g(T.KR[:], 0, "KR")
+    for c0, ws in ((0, (1.0, 64.0)), (136, (128.0, 1.0))):
+        for x in range(2):
+            paint(T.KR[:, c0 + 3:c0 + 131:4], [[-16, 2], [2, 4], [-32, 4]], -14 - x, ws[x], "KR")
+    for jj, c0 in enumerate((0, 64, 192)):
+        iota(T.MR[:, c0:c0 + 64 * (jj + 1)], [[0, 4], [1, 16 * (jj + 1)]], -16 * jj, 0, "MR")
+    fill_g(T.RB[:], 1, "RB")
+    keep(T.RB[:], [[-32, 4], [0, 4], [-1, 32]], 0, "RB")
+    iota(T.UC[:], [[0, 4], [128, 4], [16, 3]], 8192, 0, "UC0")
+    for rd in range(RO):
+        fill_g(T.TL[:, TW * (N * rd + rank) + 48:TW * (N * rd + rank + 1)], 0, "TL~")
+    iota(T.XD[:], [[0, 4], [16, 4]], S * (rank + 1), 0, "XD0")
+    fill_g(T.WR[:], 0, "WR")
+    for r in range(N):
+        paint(T.WR[:, 224 * r + 96:224 * r + 128], [[-1, 32]], -32 * r, 1.0, "WR")
+    for t, key in ((T.SK, "SK"), (T.UY, "UY"), (T.UZ, "UZ")):
+        fill_g(t[:], 0, key)
+    for x in range(2):
+        paint(T.SK[:, 0::4], [[-16, 8], [-2, 4]], -8 - x, (128.0, 1.0)[x], "SK")
+        paint(T.UZ[:, x::2], [[-16, 8], [-1, 8]], 0, (-16.0, 1.0)[x], "UZ")
+    paint(T.UY[:, 0::2], [[-16, 8], [-1, 8]], 0, 1.0, "UY")
+    fill_g(T.ZT[:], 0, "ZT~")
+    fill_g(T.NO[:], 0, "NO")
+    for r in range(N):
+        for s in range(2):
+            c0 = 176 * r + 36 + 64 * s
+            paint(T.NO[:, c0:c0 + 32], [[-1, 4], [1000, 2], [16, 4]], -(64 * s + 48 + 4 * r), 1.0, "NO")
+
+    ms(T.AU[:], 0.0, "AU")
+    ms(T.LW[:], 0.0, "LW")
+    ms(T.B[:, 0:512], 0.0, "B~")
+    for x, (lo, hi, bit) in enumerate((("a2", "b5", "b1"), ("lo2", "b4", "b0"))):
+        cts("n%d" % x, hi, 3.0, lo, A.mult, A.subtract)
+        cts("d%d" % x, lo, bit, hi, A.subtract, A.subtract)
+    cts("wh", "bh", -1.0, 2.0 ** -13, A.is_lt, A.mult)
+    for x in range(2):
+        cts("x%d" % x, "d%d" % x, "mid", "n%d" % x, A.mult, A.add)
+    cts("wm", "mid", "wh", None, A.subtract)
     ts(T.WJ[:, 0:1], T.WI[:, 0:1], 6, None, A.logical_shift_right, None, "WI", "WJ")
     ts(T.WJ[:, 1:2], T.WI[:, 0:1], 63, None, A.bitwise_and, None, "WI", "WJ")
-    chain = lambda n_, i: T.LW[:, 144 * n_ + 15 - i:144 * n_ + 143 - i]
-
-    def chains(names):
-        for n_, c in names:
-            ts(T.LW[:, 144 * n_ + 15:144 * n_ + 143:16], T.OB[:, 0::16], col(c), None, A.mult, None, "OB LW c" + c, "LW%d" % n_)
-
-    def constants_1():
-        lins([("tGW", [("b6", 16), ("k2", -2), ("is3", 1)], 110), ("tWX", [("grp", 16), ("is3", 1)], 0), ("tWE", [("grp", 16)], 1),
-              ("mb3", [("b3", -1)], 0), ("n2", [("p", 0)], -2), ("c15", [("p", 0)], 15), ("jd", [("j", 1)], -2048),
-              ("bY", [("b0", -2448)], 2304), ("jx", [("j", 1)], S * (rank + 1)), ("big", [("p", 0)], 65536), ("rnd", [("p", 0)], 143.53)])
-        cts("e8", "j", 8.0, -512.0, A.is_equal, A.mult)
-        cts("e9", "j", 9.0, 512.0, A.is_equal, A.mult)
-        cts("s8", "j", 7.5, -8.0, A.is_lt, A.mult)
-        cts("w37", "i37", 512.0, None, A.mult)
-        cts("k0", "n0", -0.25, None, A.mult)
-        cts("wpi", "wp0", "b3", None, A.mult)
-        cts("wna", "wn0", "b3", None, A.mult)
-        cts("wWE", "e8", "e9", None, A.add)
-        cts("wkey", "n1", -1.0 / 512, "k0", A.mult, A.add)
-        cts("wS", "wWE", 0.0, 128.0, A.not_equal, A.mult)
-        onehot(T.GW[:], T.IF[:, 0:224], "IF", "tGW", "i37", "GW")
-        cts("wS1", "wS", "s8", None, A.add)
-        onehot(T.WX[:], T.IF[:, 0:128], "IF", "tWX", "w37", "WX")
-        onehot(T.WE[:], T.IF[:, 0:128], "IF", "tWE", "wWE", "WE")
-        chains([(2, "wS1"), (3, "wkey")])
-        onehot(T.KR[:, 0:131], T.IF[:, 0:131], "IF", "tKR", "wpi", "KR")
-        onehot(T.KR[:, 136:267], T.IF[:, 0:131], "IF", "tKR", "wna", "KR")
-        b_cells(srcs[1], 0, False)
-        b_number(range(4))
-        cts("s1", "n1", -512.0, None, A.mult)
-        for o in range(N):
-            cts("u%d" % o, "n0", -512.0 * (64 + o), 65536.0, A.mult, A.add)
-        ts(T.O1[:], ID, -1024.0, None, A.mult, None, "SH", "O1")
-        ms(T.MK[:], 0.0, "MK0")
-        tt(T.M2[:], T.O1[:], T.TR[:], A.subtract, "O1 TR", "M2")
-        for o in range(N):
-            act(T.CW[:, o:192:4], T.IF[:, 0:48], F.Identity, "IF cs1 cu%d" % o, "CW0", scale=col("s1"), bias=col("u%d" % o))
-        for x in range(1, RO):
-            act(blk(T.CW, x, 192), T.CW[:, 0:192], F.Copy, "CW0", "CW")
-        for jj, c0 in enumerate((0, 80, 224)):
-            for o in range(N):
-                c1 = c0 + 16 * (jj + 1) * o
-                ts(T.MK[:, c1:c1 + 16], T.IF[:, 0:16], col("j"), 16384.0, A.is_ge, A.mult, "IF cj MK0", "MK")
-        act(T.OWN[:], T.IF[:, 0:32], F.Identity, "IF cj", "OWN", scale=16.0, bias=col("j"))
-        scaled(T.BC[:], T.OB[:], "OB", "wkey", "BC")
-        act(T.UC[:, 0:60], T.UC[:, 0:60], F.Identity, "UC0 cj", "UC", bias=col("j"))
-        for r in range(N):
-            act(T.XD[:, 4 * r:4 * r + 4], T.IF[:, 0:4], F.Identity, "IF cjx", "XD", scale=16.0, bias=col("jx"))
-        cp(T.KF[:], T.KS[:, 0:512], "KS", "KF")
-
-    def constants_2():
-        act(T.DP[:, 0::4], T.IF[:, 0:32], F.Identity, "IF cjd DP0", "DP", scale=16.0, bias=col("jd"))
-        act(T.RB[:], T.RP[:, 0:512], F.Copy, "RP", "RB")
-        act(T.RZ[:], T.RP[:], F.Identity, "RP", "RZ", scale=-16512.0)
-
-    ts(T.TM[:, 32:48], T.TM[:, 0:16], 2.5, col("wh"), A.is_lt, A.mult, "TM0 cwh", "TM1")
-    ts(T.TM[:, 48:64], T.TM[:, 0:16], 0.0, col("wm"), A.is_equal, A.mult, "TM0 cwm", "TM1")
+    for x in range(2):
+        ts(blk(T.TM, x, 16), blk(T.RC, x, 16), col("x%d" % x), -2.0, A.add, A.add, "RC cx%d" % x, "TM0")
     ts(col("whi"), T.WJ[:, 0:1], 64.0, None, A.mult, None, "WJ", "cwhi")
     cp(col("wlo"), T.WJ[:, 1:2], "WJ", "cwlo")
+    tt(T.TM[:, 32:64], T.TM[:, 0:32], T.TM[:, 0:32], A.mult, "TM0", "TM1")
+    cts("mb3", "b3", -1.0, None, A.mult)
+    tt(T.TM[:, 0:16], T.TM[:, 32:48], T.TM[:, 48:64], A.add, "TM1", "TM0")
+    ms(col("na"), -(1.0 + 2.0 ** -10), "cna")
+    ms(col("big"), 65536.0, "cbig")
+    ts(T.TM[:, 32:48], T.TM[:, 0:16], 2.5, col("wh"), A.is_lt, A.mult, "TM0 cwh", "TM1")
+    ts(T.TM[:, 48:64], T.TM[:, 0:16], 0.0, col("wm"), A.is_equal, A.mult, "TM0 cwm", "TM1")
     for s in range(2):
         h = slice(64 * s, 64 * s + 64)
         tt(T.AU[h, 96 + 16 * s:112 + 16 * s], T.TM[h, 32:48], T.TM[h, 48:64], A.add, "TM1 AU", "AU1")
-    chains([(0, "whi"), (1, "wlo")])
-    constants_1()
-    b_cells(srcs[2], 4)
-    b_cells(srcs[3], 0)
-    for o in srcs[1:]:
-        dma("y", window(o), "DLD%d" % o, "Dw%d" % o)
-    dma("y", [(T.YC[:, 0:S], T.cells[:])], "Dw0 Dw1 Dw2 Dw3", "WY")
-    dma("y", [(T.YK[16 * q:16 * q + 4, 0:S], T.KF[64 * (q % 2):64 * (q % 2) + 64, 128 * (q // 2):128 * (q // 2) + 128]) for q in range(8)],
-        "KF", "WK")
 
+    chain = lambda n_, i: T.LW[:, 144 * n_ + 15 - i:144 * n_ + 143 - i]
+    cts("s8", "j", 7.5, -EQW, A.is_lt, A.mult)
+    cts("s9", "j", 9.5, 16 * EQW, A.is_lt, A.mult)
+    cts("r0", "j", 0.0, None, A.is_equal)
+    cts("r1", "j", 1.0, 512.0, A.is_equal, A.mult)
+    cts("jd", "j", -1.0, 2048.0, A.mult, A.add)
+    cts("wS", "s9", "b3", "s8", A.mult, A.add)
+    cts("k0", "r0", 0.25, None, A.mult)
     for o in range(N):
-        cp(T.KL[:, o::4], T.LK[:, 160 * o:160 * o + 128], "LK KU", "KL")
+        cts("u%d" % o, "r0", 512.0 * (64 + o), 65536.0, A.mult, A.add)
+    ts(T.OWN[:], IF(-32, 0), 16.0, col("j"), A.mult, A.add, "IF cj", "OWN")
+    cts("wkey", "r1", 2.0 ** -18, "k0", A.mult, A.add)
+    for o in range(N):
+        ts(T.CT[:, o::4], IF(0, 48), col("r1"), col("u%d" % o), A.mult, A.add, "IF cr1 cu%d" % o, "CT")
+    ms(col("m2"), -2.0, "cm2")
+    ms(col("c15"), 15.0, "cc15")
+    ms(T.DP[:], 1e6, "DP0")
+    onehot(T.SH[:], IF(0, 128), "IF", "p", 1.0, "SH")
+    onehot(T.OB[:], T.RG[:], "RG", "x112", 1.0, "OB")
+    ts(T.DP[:, 0::4], IF(0, 32), -16.0, col("jd"), A.mult, A.add, "IF cjd DP0", "DP")
+    for n_, c in enumerate(("whi", "wlo", "wS", "wkey")):
+        ts(T.LW[:, 144 * n_ + 15:144 * n_ + 143:16], T.OB[:, 0::16], col(c), None, A.mult, None, "OB LW c" + c, "LW%d" % n_)
+    ts(T.BC[:], T.OB[:], col("wkey"), None, A.mult, None, "OB cwkey", "BC")
+    ms(T.RS[:], 0.0, "RS")
+    ms(T.E[:], WON, "E")
+    ms(T.RS[:, 0::48], WON, "RS", "RS")
+    ms(T.TS[:], 0.0, "TS~")
+
+    def constants(n_):
+        if n_ == 0:
+            ts(T.MK[:], T.MR[:], col("j"), 16384.0, A.is_ge, A.mult, "MR cj", "MK")
+        if n_ == 1:
+            ts(T.UC[:], T.UC[:], col("j"), None, A.add, None, "UC0 cj", "UC")
+            ts(T.XD[:], T.XD[:], col("j"), None, A.add, None, "XD0 cj", "XD")
+            cts("bY", "b0", -2448.0, 2304.0, A.mult, A.add)
+
+    cp(T.KF[:], T.KS[:, 0:512], "KS", "KF")
+    b_cells(srcs[1], 0)
+    b_cells(srcs[3], 4)
+    d_pairs(srcs[1], 0)
+    d_pairs(srcs[3], 1)
+    for o in srcs[1:]:
+        dma("y", window(o, 1, lambda q: T.DLD[o, q, :]), "DLD%d" % o, "Dw%d" % o)
+    dma("y", [(blk(T.CW, x, 192), T.CT[:]) for x in range(RO)], "CT", "CW")
+    dma("y", [(T.YC[:, 0:S], T.cells[:])], "Dw0 Dw1 Dw2 Dw3", "WY")
+    dma("y", [(T.YK[16 * q:16 * q + 16:4, 0:S], T.KF[64 * (q % 2):64 * (q % 2) + 64, 128 * (q // 2):128 * (q // 2) + 128]) for q in range(8)], "KF", "WK")
+
+    for o in peers:
+        cp(T.KL[:, o::4], blk(T.LK, o, 128), "LK", "KL")
     allb = " ".join("B%d" % b for b in range(16))
     act(T.CC[:, 0:4096], T.B[:, 512:8704].indirect(T.KL[:, 0:256]), F.Copy, allb + " KL", "CC0")
-    act(T.CC[:, 4096:16 * CUT], T.B[:, 512:8704].indirect(T.KL[:, 256:CUT]), F.Copy, allb + " KL", "CC1")
-    for o in range(N):
-        cp(blk(T.NF, o, 32), T.LK[:, 160 * o + 128:160 * o + 160], "LK KU", "NF0")
-    mm([(P[4][:, 32 * x:32 * x + 32], [(T.NI[:, 144 * x + 12 - 4 * r:144 * x + 140 - 4 * r], blk(T.NF, r, 32)) for r in range(N)])
+    cp(T.CC[:, 4096:6144], T.B[:, 512:8704].indirect(T.KL[:, 256:384]), allb + " KL", "CC1")
+    cp(T.NF[:, 0:128], T.LK[:, 512:640], "LN LNo", "NF0")
+    mm([(P[4][:, 64 * (x % 2) + x // 2:64 * (x % 2) + 64:2], [(T.NI[:, 144 * x + 12 - 4 * r:144 * x + 140 - 4 * r], blk(T.NF, r, 32)) for r in range(N)])
         for x in range(4)], "NI NF0", "P4")
-    cp(T.CC[:, 16 * CUT:8192], T.B[:, 512:8704].indirect(T.KL[:, CUT:512]), allb + " KL", "CC2")
-    for x in range(4):
-        cp(T.PL[:, 64 * (x % 2) + x // 2:64 * (x % 2) + 64:2], P[4][:, 32 * x:32 * x + 32], "P4", "PL")
+    cp(T.CC[:, 6144:8192], T.B[:, 512:8704].indirect(T.KL[:, 384:512]), allb + " KL", "CC2")
+    cp(T.PL[:], P[4][:, 0:128], "P4", "PL")
     allc = "CC0 CC1 CC2"
 
     half = lambda k, a: T.G[:, 1024 * k + a:1024 * k + 1024:16]
 
-    def gather(k, e="s"):
-        if e == "v":
-            cp(blk(T.G, k, 1024), T.CC[:, 0:8192].indirect(blk(T.PL, k, 64)), allc + " PL", "G%d" % k)
+    def gather(k, both=False):
+        if both:
+            cp(blk(T.G, 2 * k, 512), T.CC[:, 0:8192].indirect(blk(T.PL, 2 * k, 32)), allc + " PL", "Gv%d" % k)
+            act(blk(T.G, 2 * k + 1, 512), T.CC[:, 0:8192].indirect(blk(T.PL, 2 * k + 1, 32)), F.Copy, allc + " PL", "G%d" % k)
         else:
-            act(blk(T.G, k, 1024), T.CC[:, 0:8192].indirect(blk(T.PL, k, 64)), F.Copy, allc + " PL", "G%d" % k)
+            act(blk(T.G, k, 1024), T.CC[:, 0:8192].indirect(blk(T.PL, k, 64)), F.Copy, allc + " PL", "G%d Gv%d" % (k, k))
 
     def near(k):
         mm([(P[k][:, i:256:4], [(T.AU[:, 96 - 32 * r:224 - 32 * r], half(k, 4 * r + i)) for r in range(N)]) for i in range(4)],
-           "AU1 G%d" % k, "P%d" % k)
+           "AU1 G%d Gv%d" % (k, k), "P%d" % k)
 
-    def life(k, e="s"):
-        if e == "v":
-            ts(T.AB[:, 512 + k::2], P[k][:, 0:256], 2.0 ** -12, 15.0, A.is_equal, A.mult, "P%d" % k, "Ab%d" % k)
-        else:
-            act(blk(T.UA, k, 256), P[k][:, 0:256], F.Abs, "P%d cn2" % k, "UA%d" % k, scale=8192.0, bias=col("n2"))
+    def life_a(k):
         act(T.AB[:, k:512:2], P[k][:, 0:256], F.Relu, "P%d cna" % k, "Aa%d" % k, bias=col("na"))
-        if e != "v":
-            act(T.AB[:, 512 + k::2], blk(T.UA, k, 256), F.Relu, "UA%d cc15" % k, "Ab%d" % k, scale=-15.0, bias=col("c15"))
+
+    def life_b(k):
+        ts(T.AB[:, 512 + k::2], P[k][:, 0:256], 2.0 ** -12, 15.0, A.is_equal, A.mult, "P%d" % k, "Ab%d" % k)
+
+    def life_s(k):
+        act(T.UA[:], P[k][:, 0:256], F.Abs, "P%d cm2" % k, "UA", scale=8192.0, bias=col("m2"))
+        life_a(k)
+        act(T.AB[:, 512 + k::2], T.UA[:], F.Relu, "UA cc15", "Ab%d" % k, scale=-15.0, bias=col("c15"))
 
     def hash_mm(k):
         mm([(P[2][:, 0:64], [(chain(n_, i), T.AB[:, i::16]) for i in range(k, 16, 2) for n_ in range(2)])],
@@ -496,71 +506,76 @@ def rank_program(g, core, T, topo):
 
     def rec_kids(k):
         more_mm([(P[3][:, 2 * i + k::8], T.GW[:, 96 - 32 * r:224 - 32 * r], half(k, 4 * r + i)) for i in range(4) for r in range(N)],
-                "GW G%d" % k, "P3")
+                "GW G%d Gv%d" % (k, k), "P3")
 
     def rec_mm():
         mm([(P[3][:], [(T.RY[:], T.AB[:, 0:512]), (T.RY[:], T.AB[:, 512:1024])])], "RY Aa0 Aa1 Ab0 Ab1", "P3", False, True)
 
-    def rec_out():
-        act(T.RX[:], P[3][:], F.Identity, "P3 cnb3 cmb3", "RX", scale=col("nb3"), bias=col("mb3"))
-        act(REC, P[3][:], F.Copy, "P3", "REC")
+    def rec_pairs():
+        mm([(P[5][:], [(T.RY[:], T.AB[:, 0:512]), (T.RY[:], T.AB[:, 512:1024])])], "RY Aa0 Aa1 Ab0 Ab1", "P5")
 
-    H, H5, H15, OO, TI, B0 = (T.HI[:, 32 * x:32 * x + 32] for x in range(6))
-    DH, TF = (T.HF[:, 32 * x:32 * x + 32] for x in range(2))
+    def rec_out():
+        act(T.RX[:], P[5][:], F.Identity, "P5 cmb3", "RX", bias=col("mb3"))
+
+    H, H1, OO, TI, B0 = (blk(T.HI, x, 32) for x in range(5))
+    DH, TF = blk(T.HF, 0, 32), blk(T.HF, 1, 32)
+    HIT = -8.0 * EQW
+    LOW = HIT - EQW
 
     def hash_out():
         act(TF, P[2][:, 0:32], F.Copy, "P2", "TF")
 
-    def hash_ops():
+    def hash_sum():
         tt(TI, TF, P[2][:, 32:64], A.add, "TF P2", "TI")
-        ts(H, TI, 8191, None, A.bitwise_and, None, "TI", "H")
-        ts(B0, TI, 1, None, A.bitwise_and, None, "TI", "B0")
-        ts(OO, TI, 11, 3, A.logical_shift_right, A.bitwise_and, "TI", "OO")
-        ts(H5, H, 512.0, None, A.add, None, "H", "H5")
-        ts(DH, B0, 2.0, -1.0, A.mult, A.add, "B0", "DH")
-        cp(T.HL[:, 0:32], H, "H", "HL0")
-        tt(H15, H5, DH, A.subtract, "H5 DH", "H15")
-        ts(T.HL[:, 32:64], H15, -512.0, None, A.add, None, "H15", "HL1")
-        act(T.WG[:], T.B[:, 512:8704].indirect(T.HL[:, 32:64]), F.Copy, allb + " HL1", "WG")
 
-    c32 = lambda x: T.CL[:, 32 * x:32 * x + 32]
+    def hash_ops():
+        ts(B0, TI, 1, None, A.bitwise_and, None, "TI", "B0")
+        ts(H, TI, 8191, None, A.bitwise_and, None, "TI", "H")
+        ts(DH, B0, 2.0, -1.0 - LOW, A.mult, A.add, "B0", "DH")
+        cp(T.HL[:, 0:32], H, "H", "HL0")
+        tt(H1, H, DH, A.subtract, "H DH", "H1")
+        ts(T.HL[:, 32:64], H1, -LOW, None, A.add, None, "H1", "HL1")
+
+    c32 = lambda x: blk(T.CL, x, 32)
     S0, S1 = P[6][:, 0:32], P[7][:, 0:32]
 
     def look():
+        act(REC, P[3][:], F.Copy, "P3", "REC")
+        act(T.WG[:], T.B[:, 512:8704].indirect(T.HL[:, 32:64]), F.Copy, allb + " HL1", "WG")
         for x in range(2):
-            tt(blk(T.DD, x, 512), T.D[:, 512:8704].indirect(blk(T.HL, x, 32)), T.RX[:], A.is_equal, "D Dw0 Dw1 Dw2 Dw3 RX HL%d" % x, "DD%d" % x)
-            if x == 0:
-                mm([(P[3][:], [(ID, REC)])], "SH REC", "P3", True, False)
+            tt(blk(T.DD, x, 512), T.D[:, 512:8704].indirect(blk(T.HL, x, 32)), T.RX[:], A.is_equal,
+               "D Dw0 Dw1 Dw2 Dw3 Dp0 Dp1 Dp2 Dp3 RX HL%d" % x, "DD%d" % x)
             mm([((S0, S1)[x], [(chain(2, i), T.DD[:, 512 * x + i:512 * x + 512:16]) for i in range(16)])], "LW2 DD%d" % x, "P%d" % (6 + x))
             if x == 0:
-                mm([(P[3][:], [(T.WE[:], T.DD[:, 0:512])])], "WE DD0", "P3", False, False)
-        mm([(P[3][:], [(T.WX[:], T.WG[:])])], "WX WG", "P3", False, True)
+                mm([(P[3][:], [(ID, REC)])], "SH REC", "P3", True, False)
+        mm([(P[3][:], [(blk(T.WX, 1, 128), T.DD[:, 0:512]), (blk(T.WX, 0, 128), T.WG[:])])], "WX DD0 WG", "P3", False, True)
         act(T.RQ[:], P[3][:], F.Identity, "P3 cbig", "RQ", bias=col("big"))
 
     def flags(rd):
-        ts(c32(0), S0, -1.0, 68.0, A.mult, A.add, "P6", "C0")
-        ts(c32(1), S0, -64.0, None, A.is_equal, None, "P6", "C1")
-        ts(c32(2), S0, -64.0, -64.0, A.is_equal, A.add, "P6", "C2")
+        ts(c32(0), S0, -1.0, 8.5 * EQW, A.mult, A.add, "P6", "C0")
+        ts(c32(2), S0, HIT, EQW, A.not_equal, A.mult, "P6", "C2")
         mm([(P[6][:, 128:256], [(ID, T.CA[:])])], "SH CA", "P6", True, False)
-        tt(c32(3), c32(1), H5, A.mult, "C1 H5", "C3")
         fill(1)
+        tt(c32(3), H, c32(2), A.subtract, "C2 H", "C3")
+        ts(OO, TI, 11, 3, A.logical_shift_right, A.bitwise_and, "TI", "OO")
         tt(c32(4), c32(3), T.OWN[:], A.max, "C3 OWN", "C4")
         tt(c32(5), S1, c32(0), A.subtract, "P7 C0", "C5")
-        tt(c32(7), S1, c32(2), A.is_equal, "P7 C2", "C7")
+        tt(c32(7), S1, c32(2), A.subtract, "P7 C2", "C7")
         tt(c32(6), c32(5), OO, A.min, "C5 OO", "C6")
-        tt(c32(8), c32(7), H15, A.mult, "C7 H15", "C8")
+        tt(c32(8), H1, c32(7), A.subtract, "C7 H1", "C8")
         for o in range(N):
             ts(blk(T.FB, o, 32), c32(6), float(o), 4.0, A.is_equal, A.mult, "C6", "FB")
         more_mm([(P[6][:, 128 + o:256:4], T.M2[:], blk(T.FB, o, 32)) for o in range(N)], "M2 FB", "P6")
-        scan(T.RR[:], T.RT[:], T.FB[:], 0.0, A.mult, A.add, "RT FB", "RR")
+        scan(T.RR[:], T.RT[:], T.FB[:], 0.0, A.mult, A.subtract, "RT FB", "RR")
         more_mm([(P[6][:, 128 + o:256:4], T.OB[:], blk(T.RR, o, 32)) for o in range(N)], "OB RR", "P6", True)
         tt(c32(9), c32(8), c32(4), A.max, "C8 C4", "C9")
-        cp(T.AT[:], c32(9), "C9", "AT")
+        ts(T.AT[:], c32(9), 512.0, None, A.add, None, "C9", "AT")
         act(T.PG[:], T.D[:, 0:8704].indirect(T.AT[:]), F.Copy, "D REC AT", "PG")
-        scan(T.SQ[:], T.DP[:], P[6][:, 128:256], -1e6, A.max, A.min, "DP P6", "SQ")
-        ts(T.OL[:], T.SQ[:, 3::4], 4096.0, None, A.add, None, "SQ", "OL")
+        scan(T.SQ[:], T.DP[:], P[6][:, 128:256], 1e6, A.min, A.max, "DP P6", "SQ")
+        ts(T.OL[:], T.SQ[:, 3::4], -1.0, 4096.0, A.mult, A.add, "SQ", "OL")
         mm([(P[7][:, 64:448], [(ID, T.MK[:])])], "SH MK", "P7", True, False)
-        mm([(P[6][:, 256:316], [(ID, T.ZR[:, 0:60])])], "SH ZR", "P6", True, False)
+        if rd < RO - 1:
+            mm([(P[6][:, 256:304], [(ID, T.ZR[:, 0:48])])], "SH ZR", "P6", True, False)
 
     def pointers(rd):
         kr = 136 if rd == RO - 1 else 0
@@ -570,15 +585,14 @@ def rank_program(g, core, T, topo):
     def nodes_mm(h):
         if h == 0:
             act(T.PN[:], P[2][:, 128:256], F.Copy, "P2", "PN")
-        mm([(P[1][:, 32 * r:32 * r + 32], [(T.NO[:, 176 * r + 36 - 32 * x - 4 * k:176 * r + 164 - 32 * x - 4 * k], T.PN[:, 64 * k + x:64 * k + 64:2])
-                                           for x in range(2) for k in range(2)]) for r in (2 * h, 2 * h + 1)], "NO PN", "P1")
+        mm([(P[3][:, 32 * r:32 * r + 32], [(T.NO[:, 176 * r + 36 - 32 * x - 4 * k:176 * r + 164 - 32 * x - 4 * k], T.PN[:, 64 * k + x:64 * k + 64:2])
+                                           for x in range(2) for k in range(2)]) for r in (2 * h, 2 * h + 1)], "NO PN", "P3")
 
     def nodes_out():
-        act(T.NS[:], P[1][:, 0:128], F.Copy, "P1", "NS")
+        act(T.NS[:], P[3][:, 0:128], F.Copy, "P3", "NS")
         send(lambda o: blk(T.NS, o, 32), lambda o: blk(T.NL, o, 32), "an", "NS")
         arrival("NL", "an", peers)
         dma("y", [(T.ynodes[32 * rank:32 * rank + 32, :], blk(T.NS, rank, 32))], "NS", "yn0")
-
 
     def mine(rd, o, a, b):
         c0 = TW * (N * rd + o)
@@ -608,160 +622,200 @@ def rank_program(g, core, T, topo):
     def all_out(k):
         act(blk(T.RL, k, 384), P[4 + k][:, 0:384], F.Copy, "P%d" % (4 + k), "RL%d" % k)
 
-    def keys(rd):
-        cp(T.KC[:, 0:12], P[7][:, 480:492], "P7", "KC")
-        more_mm([(P[6][:, 256 + 12 * r:268 + 12 * r], blk(T.RP, r, 128), T.KC[:, 0:12]) for r in range(N if rd == RO - 1 else 0, N + 1)],
-                "RP KC", "P6")
+    def keys():
+        cp(T.KC[:, 0:24:2], P[7][:, 480:492], "P7", "KC0")
+
+    spread = lambda x: [(P[6][:, 256 + 12 * r:268 + 12 * r], blk(T.RB, r, 128), x) for r in range(N)]
 
     def equal(rd):
         last = rd == RO - 1
         for o in range(N):
             for jj in range(3):
                 n_ = 3 * o + jj
-                ts(T.E[:, 48 * n_:48 * n_ + 16 * (jj + 1)], tri(o, jj), T.KC[:, n_:n_ + 1], None, A.not_equal, None, "P7 KC", "E")
-        scan(T.ZS[:], T.RS[:], T.E[:], 1.0, A.max, A.min, "RS E", "ZS")
-        more_mm([(P[6][:, 256 + 12 * r:268 + 12 * r], blk(T.RZ, r, 128), T.ZS[:, 47::48]) for r in range(N if last else 0, N + 1)], "RZ ZS", "P6", True)
-        fill(1)
-        tt(T.AF[:, 0:60], P[6][:, 256:316], T.UC[:, 0:60], A.min, "P6 UC", "AF")
+                ts(T.E[:, 48 * n_:48 * n_ + 16 * (jj + 1)], tri(o, jj), P[7][:, 480 + n_:481 + n_], WON, A.not_equal, A.mult, "P7", "E")
+            if o == 0:
+                tt(T.KC[:, 1:24:2], P[7][:, 480:492], T.KC[:, 0:24:2], A.subtract, "P7 KC0", "KC1")
+                if not last:
+                    more_mm(spread(T.KC[:, 0:24:2]) + spread(T.KC[:, 1:24:2]), "RB KC0 KC1", "P6")
+                for d in peers + [rank]:
+                    if last:
+                        move("s", mark(d, 4), T.KC[:, 6 * d + 1:6 * d + 6:2], "KC1 ZT~", "OK%d" % (d == rank))
+                    else:
+                        move("g", mine(rd, d, 48, 54), T.KC[:, 6 * d:6 * d + 6], "KC0 KC1 TS~ TL~", "OK%d" % (d == rank))
+        scan(T.ZS[:], T.RS[:], T.E[:], WON, A.min, A.max, "RS E", "ZS")
         if not last:
-            cp(T.AL[:], T.AF[:, 0:48], "AF", "AL")
+            more_mm(spread(T.ZS[:, 47::48]), "RB ZS", "P6", True)
+            life_b(0)
+            tt(T.AF[:], P[6][:, 256:304], T.UC[:], A.min, "P6 UC", "AF")
+            cp(T.AL[:], T.AF[:], "AF", "AL")
 
     def update(r):
         cp(T.D[:, 512:512 + DW].indirect(blk(T.AL, r, 12)), blk(T.RL, r, 192), "AL D RL%d" % (r // 2), "D")
 
-    def halves(x):
-        if x == 0:
-            cp(T.OH[:, 0:24:2], T.AF[:, 48:60], "AF", "OH0")
-        else:
-            tt(T.OH[:, 1:24:2], T.AF[:, 48:60], T.OH[:, 0:24:2], A.subtract, "AF OH0", "OH1")
-
     def parcel(rd):
         last = rd == RO - 1
-        for o in peers + [rank]:
-            if last:
-                cp(mine(rd, o, 48, 54), T.OH[:, 6 * o:6 * o + 6], "OH0 OH1 TS~", "OF" if o != rank else "OFo")
-            else:
-                act(mine(rd, o, 48, 54), T.OH[:, 6 * o:6 * o + 6], F.Copy, "OH0 OH1 TS~", "OF" if o != rank else "OFo")
-        send(lambda o: blk(T.TS, N * rd + o, TW), lambda o: blk(T.TL, N * rd + o, TW), "al%d" % rank if last else "ar%d" % rd, "LO OF")
+        for o in [] if last else peers + [rank]:
+            move("g", mine(rd, o, 54, 57), T.ZS[:, 144 * o + 47:144 * o + 144:48], "ZS TS~ TL~", "OF%d" % (o == rank))
+        send(lambda o: blk(T.TS, N * rd + o, TW), lambda o: blk(T.TL, N * rd + o, TW), "ar%d" % rd, "LO" if last else "LO OK0 OF0")
         for o in peers:
-            arrival("TL%d%d" % (rd, o), "al%d" % o if last else "ar%d" % rd, [o] if last else peers)
-        wrote["TL%d%d" % (rd, rank)], wrote["LO%d" % rd] = wrote["OFo"], wrote["LO"]
+            arrival("TL%d%d" % (rd, o), "ar%d" % rd, peers)
+        wrote["TL%d%d" % (rd, rank)], wrote["LO%d" % rd], wrote["OK1%d" % rd] = wrote["TL~" if last else "OF1"], wrote["LO"], wrote["OK1"]
+
+    mark = lambda o, a: (T.ZL if o == rank else T.ZT)[:, 8 * o + a:8 * o + a + 3]
+
+    def marks():
+        for o in peers + [rank]:
+            tt(mark(o, 0), T.KC[:, 6 * o:6 * o + 6:2], T.ZS[:, 144 * o + 47:144 * o + 144:48], A.add, "KC0 ZS ZT~", "ZT%d" % (o == rank))
+        send(lambda o: blk(T.ZT, o, 8), lambda o: blk(T.ZL, o, 8), "al%d" % rank, "ZT0 OK0")
+        for o in peers:
+            arrival("ZL%d" % o, "al%d" % o, [o])
+        wrote["ZL%d" % rank] = wrote["ZT1"]
+
+    def marks_in():
+        mm([(P[5][:, 480:496], [(ID, T.ZR[:, 0:16])])], "SH ZR", "P5", True, False)
+        for d in srcs:
+            more_mm([(P[5][:, 480 + 4 * r:483 + 4 * r], T.WR[:, 224 * r + 96 - 32 * d:224 * r + 224 - 32 * d], T.ZL[:, 8 * d + a:8 * d + a + 3])
+                     for r in range(N) for a in (0, 4)], "WR OK1 ZL%d" % d, "P5", d == srcs[-1])
 
     def regroup(rd):
         mm([(P[4][:, 0:N * TW], [(T.ZR[:], T.B[:, 0:N * TW])])], "ZR B~", "P4", True, False)
         for d in srcs:
             more_mm([(blk(P[4], r, TW), T.WR[:, 224 * r + 96 - 32 * d:224 * r + 224 - 32 * d], blk(T.TL, N * rd + d, TW)) for r in range(N)],
-                    "WR LO%d TL%d%d" % (rd, rd, d), "P4", d == srcs[-1])
+                    "WR LO%d OK1%d TL%d%d" % (rd, rd, rd, d), "P4", d == srcs[-1])
+
+    def unpack_in():
         act(T.VT[:], P[4][:, 0:N * TW], F.Copy, "P4", "VT")
         act(T.VA[:], P[4][:, 0:N * TW], F.Identity, "P4 crnd", "VA", scale=1.0 / 16, bias=col("rnd"))
 
-    def unpack(rd):
-        mm([(P[5][:, 0:N * TW], [(T.UY[:], T.VT[:]), (T.UZ[:, 0:128], T.VA[:])])], "UY UZ VT VA", "P5")
-        act(blk(T.RBY, rd, N * TW), P[5][:, 0:N * TW], F.Identity, "P5 cbY", "RBY%d" % rd, bias=col("bY"))
-        mm([(P[4][:, 480 + 4 * r:484 + 4 * r], [(ID, T.VT[:, TW * r + 48 + x:TW * r + TW:2]) for x in range(2)]) for r in range(N)]
-           + [(P[4][:, 256:256 + N * TW], [(T.SK[:], T.VT[:])])], "SH SK VT", "P4")
-        if rd == RO - 1:
-            slots(rd)
-        act(blk(T.RBK, rd, N * TW), P[4][:, 256:256 + N * TW], F.Copy, "P4", "RBK%d" % rd)
+    def unpack(last=False):
+        if not last:
+            mm([(P[5][:, 480 + 4 * r:484 + 4 * r], [(ID, T.VT[:, TW * r + a:TW * r + b:st]) for a, b, st in ((48, 56, 2), (49, 57, 2), (54, 58, 1))])
+                for r in range(N)], "SH VT", "P5")
+        mm([(P[0][:, 256:512], [(T.UY[:], T.VT[:]), (T.UZ[:], T.VA[:])])], "UY UZ VT VA", "P0")
+        mm([(P[1][:, 256:512], [(T.SK[:], T.VT[:])])], "SK VT", "P1")
+
+    def unpack_out(rd):
+        act(blk(T.RBY, rd, N * TW), P[0][:, 256:512], F.Identity, "P0 cbY", "RBY%d" % rd, bias=col("bY"))
+        act(blk(T.RBK, rd, N * TW), P[1][:, 256:512], F.Copy, "P1", "RBK%d" % rd)
+        if rd < RO - 1:
+            todo.extend((place, rd, r, key) for r in reversed(range(N)) for key in "YK")
+
+    def slots_in():
+        tt(T.XF[:], P[5][:, 480:496], T.XD[:], A.min, "P5 XD", "XF")
 
     def slots(rd):
-        tt(T.XF[:], P[4][:, 480:496], T.XD[:], A.min, "P4 XD", "XF")
         ts(blk(T.XL, rd, 16), T.XF[:], float(-S * rank), None, A.add, None, "XF", "XL%d" % rd)
-        if rd < RO - 1:
-            todo.extend((rd, r, key) for r in reversed(range(N)) for key in "YK")
-
-    todo = []
-
-    def fill(n_):
-        for _ in range(min(n_, len(todo))):
-            place(*todo.pop(0))
 
     def place(rd, r, key):
         win, src = (T.YC, T.RBY) if key == "Y" else (T.YK, T.RBK)
         c0 = TW * (N * rd + r)
         cp(win[:, 0:YW].indirect(T.XL[:, 16 * rd + 4 * r:16 * rd + 4 * r + 3]), src[:, c0:c0 + 48], "XL%d RB%s%d W%s" % (rd, key, rd, key), "W" + key)
 
-    gather(0, "v")
-    gather(1)
+    todo = [(constants, n_) for n_ in range(2)]
+
+    def fill(n_):
+        for _ in range(min(n_, len(todo))):
+            job = todo.pop(0)
+            job[0](*job[1:])
+
+    gather(0, True)
+    gather(1, True)
     rec_start()
+    near(0)
+    near(1)
     for k in range(2):
-        near(k)
-    for k in range(2):
-        life(k, "v")
-        rec_kids(k)
-    for k in range(2):
-        hash_mm(k)
+        life_b(k)
+        life_a(k)
+    hash_mm(0)
+    hash_mm(1)
+    rec_pairs()
+    rec_kids(0)
+    rec_kids(1)
     rec_mm()
     hash_out()
+    hash_sum()
     rec_out()
     hash_ops()
-    constants_2()
-    for rd in range(RO):
-        more = rd < RO - 1
+    for rd in range(RO - 1):
         look()
         flags(rd)
-        if rd > 1:
-            unpack(rd - 2)
-        pointers(rd)
-        if more:
-            rec_start()
-        else:
-            nodes_mm(0)
-        compact(rd)
-        if rd > 1:
-            slots(rd - 2)
-        fill(1)
-        if more:
-            gather(0)
-            gather(1)
-            near(0)
-        keys(rd)
-        if more:
-            all_mm(rd, 1)
-        else:
-            nodes_mm(1)
-        equal(rd)
-        if more:
-            all_mm(rd, 0)
-            near(1)
-            all_out(1)
-            life(0)
-            update(3)
-            halves(0)
-            rec_kids(0)
-            all_out(0)
-            life(1)
-            update(2)
-            halves(1)
-            rec_kids(1)
-            hash_mm(0)
-            hash_mm(1)
-            rec_mm()
-            hash_out()
-            update(1)
-            update(0)
-            parcel(rd)
-            rec_out()
-            hash_ops()
-            if rd:
-                regroup(rd - 1)
-        else:
-            halves(0)
-            halves(1)
-            parcel(rd)
-            nodes_out()
+        if rd:
             regroup(rd - 1)
-            unpack(rd - 1)
-            fill(4)
+        pointers(rd)
+        rec_start()
+        if rd:
+            unpack_in()
+            unpack()
+        compact(rd)
+        fill(1)
+        gather(0)
+        gather(1)
+        near(0)
+        keys()
+        all_mm(rd, 1)
+        equal(rd)
+        all_mm(rd, 0)
+        near(1)
+        all_out(1)
+        life_a(0)
+        parcel(rd)
+        update(3)
+        if rd:
+            slots_in()
+        rec_kids(0)
+        all_out(0)
+        hash_mm(0)
+        life_s(1)
+        update(2)
+        if rd:
             slots(rd - 1)
+        hash_mm(1)
+        rec_pairs()
+        rec_kids(1)
+        rec_mm()
+        hash_out()
+        if rd:
+            unpack_out(rd - 1)
+        update(1)
+        hash_sum()
+        update(0)
+        rec_out()
+        hash_ops()
+
+    rd = RO - 1
+    look()
+    flags(rd)
+    regroup(rd - 1)
+    pointers(rd)
+    nodes_mm(0)
+    unpack_in()
+    compact(rd)
+    parcel(rd)
+    fill(1)
+    keys()
+    unpack()
+    nodes_mm(1)
+    equal(rd)
+    marks()
+    unpack_out(rd - 1)
+    nodes_out()
+    slots_in()
+    fill(1)
+    slots(rd - 1)
+    regroup(rd)
+    unpack_in()
+    unpack(True)
+    unpack_out(rd)
     fill(len(todo))
-    regroup(RO - 1)
-    unpack(RO - 1)
-    for key in "YK":
-        for r in reversed(range(N)):
-            place(RO - 1, r, key)
-    dma("y", [(T.ycells[:], T.YC[:, 0:S])], "WY", "yc")
+    marks_in()
+    slots_in()
+    slots(rd)
     dma("y", [(T.ynodes[32 * o:32 * o + 32, :], blk(T.NL, o, 32)) for o in peers], "NL", "yn")
-    dma("s", [(T.ykids[t::4, :], T.YK[t::16, 0:S]) for t in range(4)], "WK", "yk")
+    for r in reversed(range(N)):
+        place(rd, r, "Y")
+    dma("y", [(T.ycells[:], T.YC[:, 0:S])], "WY", "yc")
+    for r in reversed(range(N)):
+        place(rd, r, "K")
+    dma("s", [(T.ykids[:], T.YK[0::4, 0:S])], "WK", "yk")
     for sem, n_ in total.items():
         need("g", (sem, n_))

@@ -2,22 +2,31 @@ from concourse.bass import DstId, RemoteDMATransfer
 from concourse.mybir import AluOpType as A, ActivationFunctionType as F
 
 N, S, RO = 4, 2048, 4
-DW = 8704
-YW = 2112
+DW = 9472
+YW = 2304
 TW = 64
 EQW = 16384.0
 WON = -16512.0
+CYCLE, PE_CYCLE, FIXED, GATHER, SCATTER, HOP = 0.83, 0.42, 55.0, 1.25, 2.5, 120.0
+DMA_ISSUE, DMA_LATE, DMA_RATE, CALL, FIRST, FLIGHT, PORT_RATE = 60.0, 2000.0, 250.0, 400.0, 4200.0, 2000.0, 55.0
+ROUND = """DD0 DD1 OO C3 C0 put.0 C4 C5 C8 C6 C7 FB C9 RR AT SQ OL CW.0 PL CW.1 HX0 HX1 HX2 HX3 LO.0 LO.1 XF LO.2 xl LO E.0 KC0 E KC1 ZS Ab0 AF put.1 AL
+    D.0 D.1 D.2 TI D.3 B0 H DH HL0 H1 HL1
+    WG RQ PG VT VA G0 G1 RL1 RL0 Aa0 UA Aa1 Ab1 TF ry RX REC rk
+    P2b.0 P4a.0 P5.0 P6a P7a P5.1 P5.2 P2b P7b.0 P4a P6b P1b P3b P0b P7b P7c P5.3 P0a P6c.0 P4 P6c P1a P3.0 P2a P5.4 P3.1"""
+LAST = """DD0 DD1 put.0 OO C0 C5 C6 FB C8 RR C3 C7 C4 SQ C9 OL AT CW HX0 HX1 HX2 HX3 LO XF.0 put.1 E.0 KC0 E KC1 ZS ZT0 xl.0 ZT1 put XF.1 xl.1 end
+    WG RQ VT.0 PG PN ZK0 ZK1 VA.0 NS rk.0 ry.0 VA.1 VT.1 ry.1 rk.1 yk
+    P2b.0 P5.0 P6a P7a P5.1 P5.2 P4a.0 P2b P7b.0 P4a.1 P4a.2 P4a.3 P3b.0 P7b P7c P6b P3 P4a.4 P0b.0 P1b.0 P4a P3b.1 P0b.1 P3b P1b.1"""
 f32, bf, i32, u16 = "float32", "bfloat16", "int32", "uint16"
 SB = {
     "CS": (2048, bf), "LC": (2048, bf), "KS": (640, i32), "KU": (640, u16), "LK": (640, u16), "YC": (YW, bf), "YK": (YW, f32),
-    "KI": (640, i32), "KB": (1152, bf), "KF": (512, f32), "NN": (2048, bf), "DS": (1024, bf), "PT": (1024, bf), "RF": (129, bf),
+    "KI": (640, i32), "KB": (1152, bf), "KF": (512, f32), "NN": (256, bf), "DS": (1024, bf), "PT": (1024, bf), "RF": (129, bf),
     "B": (512 + 8192, bf), "CC": (8192, bf), "D": (512 + DW, bf), "KL": (512, u16), "WI": (8, i32), "WJ": (8, i32),
-    "PI": (8, i32), "BI": (16, i32), "COL": (64, f32), "IF": (192, f32), "RG": (128, f32),
-    "RE": (128, f32), "RC": (32, f32), "EU": (512, bf), "IDT": (512, bf), "IDL": (128, bf), "BB": (16, f32),
-    "AU": (224, bf), "TM": (64, f32), "RY": (128, bf), "NG": (137, bf), "GW": (224, bf), "KP": (272, bf),
+    "PI": (8, i32), "BI": (16, i32), "COL": (64, f32), "IF": (192, bf), "RG": (128, bf),
+    "RE": (128, bf), "RC": (32, bf), "EU": (512, bf), "IDT": (512, bf), "IDL": (128, bf), "BB": (16, f32),
+    "AU": (224, bf), "TM": (64, f32), "RY": (128, bf), "NG": (272, bf), "GW": (224, bf), "KP": (272, bf),
     "KR": (272, bf), "OB": (128, bf), "M2": (128, bf), "WX": (256, bf), "SH": (128, bf),
     "BC": (128, bf), "SK": (128, bf), "UY": (128, bf), "UZ": (128, bf), "RB": (512, bf),
-    "NI": (576, f32), "NO": (704, f32), "LW": (576, bf), "EQ": (8, f32), "ZR": (128, bf), "WR": (896, bf),
+    "NI": (576, f32), "NO": (704, f32), "LW": (576, bf), "EQ": (8, f32), "WR": (896, bf),
     "CW": (576 + 2560, f32), "CT": (192, f32), "OWN": (32, f32), "RT": (128, bf), "CA": (128, bf), "DP": (128, f32),
     "MR": (384, bf), "MK": (384, bf), "RS": (576, bf), "UC": (48, f32), "XD": (16, f32),
     "NF": (256, f32), "PL": (128, u16), "G": (2048, bf), "AB": (1024, bf), "UA": (256, bf), "DD": (1024, bf), "RX": (512, bf),
@@ -30,8 +39,8 @@ SB = {
 SCRATCH = {n: ("sbuf", [128, w], d) for n, (w, d) in SB.items()}
 SCRATCH.update({"P%d" % k: ("psum", [128, 512], f32) for k in range(8)})
 SCRATCH.update({"DLD": ("dram", [4, 128, 256], bf)})
-SEMAPHORES = (["eg", "ev", "es", "et", "sent", "ak", "am", "an"] + ["ac%d" % k for k in range(N)] + ["ad%d" % k for k in range(N)]
-              + ["ar%d" % k for k in range(RO)] + ["al%d" % k for k in range(N)] + ["d%d" % k for k in range(32)])
+SEMAPHORES = (["eg", "ev", "es", "et", "sent", "gi", "ak", "an"] + ["ac%d" % k for k in range(N)] + ["ad%d" % k for k in range(N)]
+              + ["ar%d" % k for k in range(RO)] + ["al%d" % k for k in range(N)] + ["d%d" % k for k in range(40)])
 
 
 def rank_program(g, core, T, topo):
@@ -40,54 +49,53 @@ def rank_program(g, core, T, topo):
         return
     Q = {"g": g, "v": g.vector, "s": g.scalar, "t": g.tensor, "y": g.sync}
     V, SE, PE = g.vector, g.scalar, g.tensor
-    count = {"g": 0, "v": 0, "s": 0, "t": 0}
-    seen = {e: {} for e in Q}
-    total, wrote, read = {}, {}, {}
-    ndma = [0]
+    P = [T["P%d" % k] for k in range(8)]
+    jobs, wrote, read, group = [], {}, {}, {}
+    ndma, pinned = [0], []
+    size_of = lambda a: 2 if "16" in str(a.dtype) else 4
+    in_psum = lambda a: a.name in [x.name for x in P]
 
-    def need(e, tok):
-        if seen[e].get(tok[0], 0) < tok[1]:
-            Q[e].wait_ge(T.sem[tok[0]], tok[1])
-            seen[e][tok[0]] = tok[1]
-
-    def order(e, r, w, who):
+    def job(e, fn, r, w, ns, late=0.0, kind="c", busy=0.0, tok=None):
+        keys = lambda x: [k + z for k in x.split() for z in ("abc" if k[0] == "P" and len(k) == 2 and k[1].isdigit() else ("",))]
+        name = (w.split() + [""])[0]
+        r, w, me, pre = keys(r), keys(w), len(jobs), {}
         for k in r:
             if k in wrote:
-                need(e, wrote[k])
-            if k[0] == "P" and k[1].isdigit():
-                for tok in read.get(k, []):
-                    if tok[2] != who:
-                        need(e, tok)
+                pre[wrote[k]] = True
         for k in w:
-            for tok in read.get(k, []):
-                if tok[2] != who or who != "t":
-                    need(e, tok)
-            if k in wrote and (wrote[k][2] != who or who == "dma"):
-                need(e, wrote[k])
-
-    def note(tok, r, w):
-        total[tok[0]] = tok[1]
+            for i in read.get(k, []):
+                pre[i] = pre.get(i, False) or jobs[i]["e"] != e or e != "t"
+            if k in wrote:
+                i = wrote[k]
+                pre[i] = pre.get(i, False) or jobs[i]["e"] != e or kind != "c" or jobs[i]["kind"] != "c"
         for k in r:
-            read.setdefault(k, []).append(tok)
+            read.setdefault(k, []).append(me)
         for k in w:
-            wrote[k] = tok
-            read[k] = []
+            wrote[k], read[k] = me, []
+        banks = {k[:2] for k in r + w if k[0] == "P" and k[1].isdigit()}
+        jobs.append(dict(e=e, fn=fn, pre=pre, ns=ns, late=late, kind=kind, busy=busy, tok=tok, banks=banks, name=name))
+        return me
 
-    def op(e, fn, r, w):
-        r, w = r.split(), w.split()
-        order(e, r, w, e)
-        count[e] += 1
-        fn().then_inc(T.sem["e" + e], 1)
-        note(("e" + e, count[e], e), r, w)
+    def pin(order, *steps):
+        first, met = len(jobs), {}
+        for step in steps:
+            step[0](*step[1:])
+        place = {n_: x for x, n_ in enumerate(order.split())}
+        for me in range(first, len(jobs)):
+            j = jobs[me]
+            met[j["name"]] = met.get(j["name"], -1) + 1
+            j["name"] += ".%d" % met[j["name"]]
+            pinned.append((first, place.get(j["name"], place.get(j["name"].split(".")[0], 0)), me))
 
     def dma(e, pairs, r, w):
-        r, w = r.split(), w.split()
-        order(e, r, w, "dma")
         sem = "d%d" % ndma[0]
         ndma[0] += 1
-        for o, i in pairs:
-            Q[e].dma_start(o, i).then_inc(T.sem[sem], 16)
-        note((sem, 16 * len(pairs), "dma"), r, w)
+
+        def run():
+            for o, i in pairs:
+                Q[e].dma_start(o, i).then_inc(T.sem[sem], 16)
+        busy = sum(size_of(o) * o.shape[0] * o.shape[-1] / DMA_RATE for o, i in pairs)
+        job(e, run, r, w, DMA_ISSUE * len(pairs), DMA_LATE, "dma", busy, (sem, 16 * len(pairs)))
 
     def masks(src):
         others = [o for o in range(N) if o != src]
@@ -107,78 +115,97 @@ def rank_program(g, core, T, topo):
         return out
     eng = {o: masks(o) for o in range(N)}
     peers = [o for o in range(N) if o != rank]
-    sent = [0]
+    sent, marks_ = [0], [0]
     off_chip = lambda a, b: T.cores[b] not in topo.cores_of(T.cores[a])
     alone = lambda a, b: topo.engines(T.cores[a], T.cores[b]) if off_chip(a, b) else eng[a][b]
 
-    def send(src, dst, sem, r, to=None):
-        order("g", r.split(), [], "dma")
-        trs = []
+    def send(src, dst, sem, r, to=None, first=0.0):
+        trs, n_far = [], 0
         for o in to or peers:
             rid, pid = topo.addr(T.cores[o], core)
             en = alone(rank, o) if to else eng[rank][o]
             trs.append(RemoteDMATransfer(dst_ids=[DstId(rid=rid, pnc=pid)], dma_engine_mask=sum(1 << x for x in en),
                                          remote_sem=T.sem[sem], src=src(o), dst=dst(rank)))
             sent[0] += len(en)
-        g.remote_dma_fused(trs, local_sem=T.sem.sent)
-        total["sent"] = sent[0]
+            n_far += off_chip(rank, o)
+        a = src(peers[0])
+        sent[1:] = [job("g", lambda: g.remote_dma_fused(trs, local_sem=T.sem.sent), r, "", first + CALL, FLIGHT, "rem",
+                        n_far * 128 * a.shape[1] * size_of(a) / PORT_RATE, ("sent", sent[0]))]
 
     def arrival(key, sem, from_, one=False):
         n_ = sum(len(alone(o, rank) if one else eng[o][rank]) for o in from_)
-        wrote[key] = (sem, n_, "dma")
-        total[sem] = n_
+        jobs[job("a", None, "", key, 1.0, 0.0, "arr", 0.0, (sem, n_))]["pre"][sent[1]] = True
+
+    def issued(key):
+        marks_[0] += 1
+        job("g", lambda: g.sem_inc(T.sem.gi, 1), "", key, 20.0, 0.0, "inc", 0.0, ("gi", marks_[0]))
+
+    def cycles(n, sides, two=False):
+        if two:
+            return FIXED + CYCLE * n * (1 if any(in_psum(a) for a in sides[1:]) else 2)
+        return FIXED + CYCLE * n * (0.5 if all(size_of(a) == 2 for a in sides) else 1)
 
     def ts(o, a, s1, s2, o0, o1, r, w):
         if o1 is None:
-            op("v", lambda: V.tensor_scalar(o, a, s1, None, o0), r, w)
+            job("v", lambda: V.tensor_scalar(o, a, s1, None, o0), r, w, cycles(o.shape[1], (o, a)))
         else:
-            op("v", lambda: V.tensor_scalar(o, a, s1, s2, o0, o1), r, w)
+            job("v", lambda: V.tensor_scalar(o, a, s1, s2, o0, o1), r, w, cycles(o.shape[1], (o, a)))
 
-    def tt(o, a, b, o0, r, w):
-        op("v", lambda: V.tensor_tensor(o, a, b, o0), r, w)
+    def tt(o, a, b, o0, r, w, gathers=False):
+        job("v", lambda: V.tensor_tensor(o, a, b, o0), r, w, FIXED + GATHER * o.shape[1] if gathers else cycles(o.shape[1], (o, a, b), True))
 
-    def cp(o, a, r, w):
-        op("v", lambda: V.tensor_copy(o, a), r, w)
+    def cp(o, a, r, w, gathers=False, scatters=False):
+        ns = FIXED + GATHER * o.shape[1] if gathers else FIXED + SCATTER * a.shape[1] if scatters else cycles(o.shape[1], (o, a))
+        job("v", lambda: V.tensor_copy(o, a), r, w, ns)
 
     def ms(o, c, w, r=""):
-        op("v", lambda: V.memset(o, c), r, w)
+        job("v", lambda: V.memset(o, c), r, w, cycles(o.shape[1], (o,)))
 
     def scan(o, a, b, init, o0, o1, r, w):
-        op("v", lambda: V.tensor_tensor_scan(o, a, b, init, o0, o1), r, w)
+        job("v", lambda: V.tensor_tensor_scan(o, a, b, init, o0, o1), r, w, cycles(o.shape[1], (o, a, b)))
 
-    def act(o, a, fn, r, w, **kw):
-        op("s", lambda: SE.activation(o, a, fn, **kw), r, w)
+    def act(o, a, fn, r, w, gathers=False, **kw):
+        job("s", lambda: SE.activation(o, a, fn, **kw), r, w, FIXED + 15 + (GATHER if gathers else CYCLE) * o.shape[1])
+
+    def matmuls(calls, r, w):
+        def run():
+            for c in calls:
+                ins = PE.matmul(*c)
+            return ins
+        me = job("t", run, r, w, sum(max(64, x.shape[1]) * PE_CYCLE * (size_of(x) // 2) ** 2 for o, l, x, a, b in calls))
+        for b in {c[0].name for c in calls}:
+            if b in group:
+                jobs[me]["pre"].setdefault(group[b], False)
+            group[b] = me
 
     def mm(items, r, w, first=True, last=True):
-        def run():
-            ins = None
-            for o, prs in items:
-                for n_, (l, x) in enumerate(prs):
-                    ins = PE.matmul(o, l, x, first and n_ == 0, last and n_ == len(prs) - 1)
-            return ins
-        op("t", run, r, w)
+        matmuls([(o, l, x, first and n_ == 0, last and n_ == len(prs) - 1) for o, prs in items for n_, (l, x) in enumerate(prs)], r, w)
 
-    def more_mm(items, r, w, last=False):
-        def run():
-            ins = None
-            for n_, (o, l, x) in enumerate(items):
-                ins = PE.matmul(o, l, x, False, last and n_ == len(items) - 1)
-            return ins
-        op("t", run, r, w)
+    def more_mm(items, r, w, last=False, first=False):
+        matmuls([(o, l, x, first and n_ == 0, last and n_ == len(items) - 1) for n_, (o, l, x) in enumerate(items)], r, w)
 
     def iota(o, pat, base, cm, w, r=""):
-        op("g", lambda: g.iota(o, pat, base, cm, allow_small_or_imprecise_dtypes=True), r, w)
+        job("g", lambda: g.iota(o, pat, base, cm, allow_small_or_imprecise_dtypes=True), r, w, 130 + 2 * CYCLE * o.shape[1])
 
     def sel(o, a, pat, cmp, fill, base, cm, r, w):
-        op("g", lambda: g.affine_select(o, a, pat, cmp, fill, base, cm), r, w)
+        job("g", lambda: g.affine_select(o, a, pat, cmp, fill, base, cm), r, w, 170 + 2 * CYCLE * o.shape[1])
 
     def move(e, o, a, r, w):
-        if e == "v":
-            cp(o, a, r, w)
-        elif e == "s":
+        if e == "s":
             act(o, a, F.Copy, r, w)
         else:
             sel(o, a, [[0, a.shape[1]]], A.is_equal, 0.0, 0, 0, r, w)
+
+    def fill_g(t, c, key):
+        iota(t, [[0, t.shape[1]]], c, 0, key)
+
+    def paint(t, pat, base, w, key, new=False, cmp=A.not_equal, cm=1):
+        sel(t, T.B[:, 0:t.shape[1]] if new else t, pat, cmp, w, base, cm, "B~" if new else key, key)
+
+    def zero(t, key):
+        for c in range(0, t.shape[1], 512):
+            n_ = min(512, t.shape[1] - c)
+            act(t[:, c:c + n_], T.B[:, 0:n_], F.Copy, "B~", key)
 
     cols = {}
 
@@ -191,325 +218,314 @@ def rank_program(g, core, T, topo):
         r = " ".join("c" + x for x in (c, s1, s2) if isinstance(x, str))
         ts(col(name), col(c), col(s1) if isinstance(s1, str) else s1, col(s2) if isinstance(s2, str) else s2, o0, o1, r, "c" + name)
 
+    def line(o, a, scale, bias, r, w):
+        r += "".join(" c" + x for x in (scale, bias) if isinstance(x, str))
+        ts(o, a, col(scale) if isinstance(scale, str) else scale, col(bias) if isinstance(bias, str) else bias, A.mult, A.add, r, w)
+
     def onehot(out, row, rk, tc, wc, key):
         if isinstance(wc, str):
             ts(out, row, col(tc), col(wc), A.is_equal, A.mult, "%s c%s c%s" % (rk, tc, wc), key)
         else:
             ts(out, row, col(tc), wc, A.is_equal, A.mult, "%s c%s EQ" % (rk, tc), key)
 
-    P = [T["P%d" % k] for k in range(8)]
+    rows = lambda r: slice(32 * r, 32 * r + 32)
     blk = lambda t, o, w: t[:, o * w:(o + 1) * w]
     srcs = [rank] + sorted(peers, key=lambda o: (off_chip(rank, o), topo.die(T.cores[o]) != topo.die(core)))
     near_, far = srcs[1:2], srcs[2:]
     ID, REC = T.SH[:], T.D[:, 0:512]
-
-    for o in far:
-        dma("y", [(blk(T.CS, o, 512), T.cells[32 * o:32 * o + 32, :])], "", "CS%d" % o)
-    dma("y", [(blk(T.KS, o, 128), T.kids[8 * o:8 * o + 8, :]) for o in range(N)], "", "KS")
-    dma("y", [(blk(T.CS, o, 512), T.cells[32 * o:32 * o + 32, :]) for o in near_], "", "CS%d" % near_[0])
-    dma("y", [(blk(T.KS, 16 + o, 32), T.nodes[32 * o:32 * o + 32, :]) for o in range(N)], "", "KN")
-    dma("y", [(blk(T.LC, rank, 512), T.cells[32 * rank:32 * rank + 32, :])], "", "LC%d" % rank)
-    dma("y", [(T.WI[32 * q:32 * q + 32, 0:1], T.wt[32 * rank:32 * rank + 32, :]) for q in range(4)], "", "WI")
-    iota(T.PI[:, 0:1], [[0, 1]], 0, 1, "PI")
-    iota(T.IF[:], [[1, 192]], -64, 0, "IF")
     IF = lambda a, b: T.IF[:, 64 + a:64 + b]
-    ms(T.RE[:], 1000.0, "RE")
-    ms(T.IDT[0:64, :], 0.0, "IDT")
-    ms(T.IDL[0:64, :], 0.0, "IDL")
-    for a in range(3):
-        for b in range(3):
-            iota(T.RE[:, 4 * a + b::16], [[64, 2], [16, 2], [4, 2]], 4 * (4 * a + b), -1, "RE0", "RE")
-    send(lambda o: blk(T.CS, o, 512), lambda o: blk(T.LC, o, 512), "ac%d" % rank, "CS%d" % far[0], far[:1])
-    for a in range(2):
-        for b in range(2):
-            iota(T.RE[:, 12 + 2 * a + b::16], [[64, 2], [32, 2], [8, 2]], 4 * (4 * a + b), -1, "RE0")
-    send(lambda o: blk(T.CS, o, 512), lambda o: blk(T.LC, o, 512), "ac%d" % rank, "CS%d CS%d" % (far[1], near_[0]), far[1:] + near_)
-    for o in peers:
-        arrival("LC%d" % o, "ac%d" % o, [o], True)
-    iota(T.RC[:, 0:16], [[1, 4], [0, 4]], 0, 0, "RC")
-    iota(T.RC[:, 16:32], [[0, 4], [1, 4]], 0, 0, "RC")
-    iota(T.RG[:], [[16, 8], [0, 16]], 0, 0, "RG")
+    chain = lambda n_, i: T.LW[:, 144 * n_ + 15 - i:144 * n_ + 143 - i]
+    shift = lambda r, d: T.WR[:, 224 * r + 96 - 32 * d:224 * r + 224 - 32 * d]
+    allb, allc, alld = " ".join("B%d" % b for b in range(16)), "CC0 CC1 CC2", "Dw0 Dw1 Dw2 Dw3 Dp0 Dp1 Dp2 Dp3"
 
-    fields = [("p", 0, 127), ("j", 0, 15), ("lo2", 0, 3), ("a2", 2, 3), ("b0", 0, 1), ("b1", 1, 1), ("b2", 2, 1), ("b3", 3, 1), ("b4", 4, 1),
-              ("b5", 5, 1), ("x64", 0, 64), ("x60", 0, 60), ("x112", 0, 112), ("x120", 0, 120), ("h3", 1, 7)]
-    for n_, (name, sh, mk) in enumerate(fields):
-        col(name)
-        ts(T.BI[:, n_:n_ + 1], T.PI[:, 0:1], sh, mk, A.logical_shift_right, A.bitwise_and, "PI", "BI")
-    ms(T.IDL[0:1, 3::16], 1.0, "IDL", "IDL")
-    ms(T.IDL[32:33, 7::16], 1.0, "IDL")
-    cp(T.COL[:, 0:len(fields)], T.BI[:, 0:len(fields)], "BI", " ".join("c" + x[0] for x in fields))
-    for c in range(1, 4):
-        ms(T.IDT[32:33, 128 * c:128 * c + 128], float(c), "IDT1", "IDT")
-    ms(T.ZR[:], 0.0, "ZR")
-    cts("tRF", "lo2", 2.0, "x120", A.mult, A.add)
-    cts("wRF", "b2", 15.0, 1.0, A.mult, A.add)
-    cts("tKP", "x112", "h3", None, A.add)
-    cts("tNG", "lo2", 2.0, "x64", A.mult, A.add)
-    cts("f0", "x60", 0.0, -1.0, A.is_equal, A.mult)
-    cts("bD", "b3", 144.0, -144.0, A.mult, A.add)
-    ts(T.EQ[:, 0:2], IF(0, 2), col("b0"), None, A.is_equal, None, "IF cb0", "EQ")
-    onehot(T.NG[:], IF(-9, 128), "IF", "tNG", "f0", "NG")
-    for e in range(2):
-        onehot(blk(T.KP, e, 136), IF(-8, 128), "IF", "tKP", T.EQ[:, e:e + 1], "KP")
-    onehot(T.RF[:], IF(-1, 128), "IF", "tRF", "wRF", "RF")
-    for c in range(4):
-        cp(T.IDT[0:1, 128 * c:128 * c + 128], T.IF[0:1, 64:192], "IF IDT", "IDT0")
-    cts("hb", "lo2", 2.5, -14.0, A.is_lt, A.mult)
-    cts("i74", "j", 7.0, 4.0, A.is_equal, A.mult)
-    cts("mid", "a2", 3.0, None, A.is_equal)
-    cts("bh", "a2", 2.5, "hb", A.is_lt, A.mult)
-    ms(col("rnd"), 143.53, "crnd")
-    ts(T.BB[:], IF(0, 16), col("i74"), col("bh"), A.mult, A.add, "IF ci74 cbh", "BB")
+    def loads():
+        for o in far:
+            dma("y", [(blk(T.CS, o, 512), T.cells[rows(o), :])], "", "CS%d" % o)
+        dma("y", [(blk(T.KS, o, 128), T.kids[8 * o:8 * o + 8, :]) for o in range(N)], "", "KS")
+        dma("y", [(T.NN[:, 0:128], T.cells[0::16, :])], "", "N0")
+        dma("y", [(blk(T.CS, o, 512), T.cells[rows(o), :]) for o in near_], "", "CS%d" % near_[0])
+        dma("y", [(blk(T.KS, 16 + o, 32), T.nodes[rows(o), :]) for o in range(N)], "", "KN")
+        dma("y", [(blk(T.LC, rank, 512), T.cells[rows(rank), :])], "", "LC%d" % rank)
+        dma("y", [(T.WI[rows(q), 0:1], T.wt[rows(rank), :]) for q in range(4)], "", "WI")
+
+    def cells_out():
+        iota(T.PI[:, 0:1], [[0, 1]], 0, 1, "PI")
+        iota(T.IF[:], [[1, 192]], -64, 0, "IF")
+        for s in range(2):
+            iota(blk(T.RE, s, 64), [[16, 2], [4, 2], [4, 16]], 64 * s, -1, "RE")
+        iota(T.RE[:, 3::4], [[0, 32]], 1000, 0, "RE1", "RE")
+        for a in range(2):
+            for b in range(2):
+                iota(T.RE[:, 12 + 2 * a + b::16], [[64, 2], [32, 2], [8, 2]], 4 * (4 * a + b), -1, "RE0", "RE1" if a + b == 2 else "RE")
+        send(lambda o: blk(T.CS, o, 512), lambda o: blk(T.LC, o, 512), "ac%d" % rank, "CS%d" % far[0], far[:1], FIRST)
+        arrival("LC%d" % far[0], "ac%d" % far[0], far[:1], True)
+        send(lambda o: blk(T.CS, o, 512), lambda o: blk(T.LC, o, 512), "ac%d" % rank, "CS%d CS%d" % (far[1], near_[0]), far[1:] + near_, FIRST / 4)
+        for o in far[1:] + near_:
+            arrival("LC%d" % o, "ac%d" % o, [o], True)
+
+    def first_constants():
+        ms(T.B[:, 0:512], 0.0, "B~")
+        for t in "IDL NI GW AU LW WX KR".split():
+            zero(T[t], t)
+        fields = [("p", 0, 127), ("j", 0, 15), ("lo2", 0, 3), ("a2", 2, 3), ("b0", 0, 1), ("b1", 1, 1), ("b2", 2, 1), ("b3", 3, 1), ("b4", 4, 1),
+                  ("b5", 5, 1), ("x112", 0, 112), ("x120", 0, 120), ("h3", 1, 7)]
+        for n_, (name, sh, mk) in enumerate(fields):
+            col(name)
+            ts(T.BI[:, n_:n_ + 1], T.PI[:, 0:1], sh, mk, A.logical_shift_right, A.bitwise_and, "PI", "BI")
+        for row, c0 in ((0, 3), (32, 7), (64, 11)):
+            ms(T.IDL[row:row + 1, c0::16], 1.0, "IDL0", "IDL")
+        for x in range(2):
+            ms(T.IDT[64:96, x::2], float(x), "IDT1")
+        cp(T.COL[:, 0:len(fields)], T.BI[:, 0:len(fields)], "BI", " ".join("c" + x[0] for x in fields))
+        for c in range(4):
+            ms(T.IDT[32:64, 128 * c:128 * c + 128], float(c), "IDT1")
+            cp(T.IDT[0:32, 128 * c:128 * c + 128], T.IF[0:32, 64:192], "IF", "IDT0")
+        cts("tRF", "lo2", 2.0, "x120", A.mult, A.add)
+        cts("wRF", "b2", 15.0, 1.0, A.mult, A.add)
+        cts("tKP", "x112", "h3", None, A.add)
+        cts("tNG", "b4", 64.0, "h3", A.mult, A.add)
+        cts("bD", "b3", 144.0, -144.0, A.mult, A.add)
+        ts(T.EQ[:, 0:2], IF(0, 2), col("b0"), None, A.is_equal, None, "IF cb0", "EQ")
+        cts("hb", "lo2", 2.5, -14.0, A.is_lt, A.mult)
+        cts("i74", "j", 7.0, 4.0, A.is_equal, A.mult)
+        cts("mid", "a2", 3.0, None, A.is_equal)
+        cts("bh", "a2", 2.5, "hb", A.is_lt, A.mult)
+        for e in range(2):
+            onehot(blk(T.NG, e, 136), IF(-8, 128), "IF", "tNG", T.EQ[:, e:e + 1], "NG")
+            onehot(blk(T.KP, e, 136), IF(-8, 128), "IF", "tKP", T.EQ[:, e:e + 1], "KP")
+        onehot(T.RF[:], IF(-1, 128), "IF", "tRF", "wRF", "RF")
+        line(T.BB[:], IF(0, 16), "i74", "bh", "IF", "BB")
+        for u in range(4):
+            ts(blk(T.EU, u, 128), T.RE[:], float(-u), None, A.is_equal, None, "RE0 RE1", "EU")
 
     def b_number(banks):
         for bank in banks:
-            mm([(P[bank][:], [(T.IDL[0:64, :], T.IDT[0:64, :])])], "IDL IDT0 IDT1", "P%d" % bank, True, False)
+            mm([(P[bank][:], [(T.IDL[0:96, :], T.IDT[0:96, :])])], "IDL0 IDT0 IDT1", "P%d" % bank, True, False)
 
-    def b_cells(o, base, both=True):
-        for u in range(4):
-            bank, b = base + u, 4 * o + u
+    def b_cells(o, banks):
+        for u, bank in enumerate(banks):
+            b = 4 * o + u
             mm([(P[bank][:], [(blk(T.EU, u, 128), blk(T.LC, o, 512))])], "EU LC%d" % o, "P%d" % bank, False, True)
-            if u % 2 and both:
+            if u % 2:
                 ts(blk(T.B, b + 1, 512), P[bank][:], T.BB[:, b:b + 1], 0.0, A.add, A.max, "P%d BB" % bank, "B%d" % b)
             else:
                 act(blk(T.B, b + 1, 512), P[bank][:], F.Relu, "P%d BB" % bank, "B%d" % b, bias=T.BB[:, b:b + 1])
 
-    ts(T.KI[:, 0:512], T.KS[:, 0:512], 127, None, A.bitwise_and, None, "KS", "KI")
-    ts(T.KB[:, 0:512], T.KS[:, 0:512], 2.0 ** -7, 143.504, A.mult, A.add, "KS", "KB0")
-    cp(T.KB[:, 640:1152], T.KI[:, 0:512], "KI", "KB1")
-    cp(T.KU[:, 0:512], T.KS[:, 0:512], "KS", "KU")
-    ts(T.KI[:, 512:640], T.KS[:, 512:640], 127, None, A.bitwise_and, None, "KN", "KJ")
-    ts(T.KB[:, 512:640], T.KS[:, 512:640], 2.0 ** -7, 143.504, A.mult, A.add, "KN", "KB2")
-    ts(T.NF[:, 0:128], T.KI[:, 512:640], 64.0, -144.0, A.mult, A.add, "KJ", "NF0")
-    cp(T.KL[:, rank::4], blk(T.KU, rank, 128), "KU", "KL")
-    tt(T.NF[:, 128:256], T.NF[:, 0:128], T.KB[:, 512:640], A.add, "NF0 KB2", "NF1")
-    cp(T.KU[:, 512:640], T.NF[:, 128:256], "NF1", "NU")
-    cp(blk(T.LK, 16 + rank, 32), blk(T.NF, 4 + rank, 32), "NF1", "LNo")
-    send(lambda o: blk(T.KU, o, 128), lambda o: blk(T.LK, o, 128), "ak", "KU")
-    arrival("LK", "ak", peers)
-    send(lambda o: blk(T.KU, 16 + o, 32), lambda o: blk(T.LK, 16 + o, 32), "am", "NU")
-    arrival("LN", "am", peers)
+    def halves():
+        ts(T.KI[:, 0:512], T.KS[:, 0:512], 127, None, A.bitwise_and, None, "KS", "KI")
+        ts(T.KB[:, 0:512], T.KS[:, 0:512], 2.0 ** -7, 143.504, A.mult, A.add, "KS", "KB0")
+        cp(T.KB[:, 640:1152], T.KI[:, 0:512], "KI", "KB1")
+        ts(T.NN[:, 128:256], T.NN[:, 0:128], 0.0, None, A.min, None, "N0", "NN")
 
-    def d_marks(o):
-        src, key = (T.LC, "LC%d" % o) if o == rank else (T.CS, "CS%d" % o)
-        act(blk(T.NN, o, 512), blk(src, o, 512), F.Relu, key, "NN%d" % o, scale=-1.0)
-        mm([(P[4 + o][:, 0:256], [(T.ZR[:], blk(T.NN, 2 * o, 256))])], "ZR NN%d" % o, "P%d" % (4 + o), True, False)
-        more_mm([(P[4 + o][:, x:256:2], T.NG[:, 9 - h - 8 * x:137 - h - 8 * x], T.NN[:, 512 * o + 256 * h + x:512 * o + 256 * h + 256:2])
-                 for x in range(2) for h in range(2)], "NG NN%d" % o, "P%d" % (4 + o))
+    def lists_out():
+        for o in peers:
+            cp(T.KU[:, 160 * o:160 * o + 128], blk(T.KS, o, 128), "KS", "KU")
+        ts(T.KI[:, 512:640], T.KS[:, 512:640], 127, None, A.bitwise_and, None, "KN", "KJ")
+        ts(T.KB[:, 512:640], T.KS[:, 512:640], 2.0 ** -7, 143.504, A.mult, A.add, "KN", "KB2")
+        ts(T.NF[:, 0:128], T.KI[:, 512:640], 64.0, -144.0, A.mult, A.add, "KJ", "NF0")
+        cp(T.KL[:, rank::4], blk(T.KS, rank, 128), "KS", "KL")
+        tt(T.NF[:, 128:256], T.NF[:, 0:128], T.KB[:, 512:640], A.add, "NF0 KB2", "NF1")
+        for o in peers:
+            cp(T.KU[:, 160 * o + 128:160 * o + 160], blk(T.NF, 4 + o, 32), "NF1", "KU")
+        send(lambda o: blk(T.KU, o, 160), lambda o: blk(T.LK, o, 160), "ak", "KU")
+        arrival("LK", "ak", peers)
 
     def d_kids(o):
+        more_mm([(P[4 + o][:, 128 * e + x:128 * e + 128:2], T.NG[rows(o), 136 * e + 8 - 8 * x:136 * e + 136 - 8 * x], T.NN[rows(o), 128 + x:256:2])
+                 for x in range(2) for e in range(2)], "NG NN", "P%d" % (4 + o), False, True)
         more_mm([(blk(P[4 + o], e, 128), T.KP[:, 136 * e + 8 - 8 * x:136 * e + 136 - 8 * x], T.KB[:, 640 * x + 128 * o:640 * x + 128 * o + 128])
                  for x in range(2) for e in range(2)], "KP KB0 KB1", "P%d" % (4 + o), True)
         act(blk(T.DS, o, 256), P[4 + o][:, 0:256], F.Identity, "P%d cbD" % (4 + o), "DS%d" % o, bias=col("bD"))
 
-    def window(o, x, src):
-        return [(T.D[32 * y + 16 * s + 8 * x:32 * y + 16 * s + 8 * x + 8, 512 + S * o:512 + S * o + S], src(slice(64 * s, 64 * s + 64)))
-                for y in range(4) for s in range(2)]
+    at = lambda o, a, n_: T.D[a:a + n_, 512 + S * o:512 + S * o + S]
+
+    def window(o, x, src, r, w, groups):
+        dma("y", [(at(o, 16 * a + 8 * x, 8), src(slice(64 * (a % 2), 64 * (a % 2) + 64))) for a in groups], r, w)
 
     def d_pairs(o, bank):
         mm([(P[bank][:, 0:256], [(T.RF[:, 1 - h:129 - h], blk(T.LC, 2 * o + h, 256)) for h in range(2)])], "RF LC%d" % o, "P%d" % bank)
         act(blk(T.PT, o, 256), P[bank][:, 0:256], F.Copy, "P%d" % bank, "PT%d" % o)
-        dma("y", window(o, 0, lambda q: T.PT[q, 256 * o:256 * o + 256]), "PT%d" % o, "Dp%d" % o)
-    b_number(range(4))
-    for grp in (far + near_, [rank]):
-        for o in grp:
-            d_marks(o)
-        for o in grp:
-            d_kids(o)
-    send(lambda o: blk(T.DS, o, 256), lambda o: T.DLD[o], "ad%d" % rank, " ".join("DS%d" % o for o in peers))
-    for o in peers:
-        arrival("DLD%d" % o, "ad%d" % o, [o])
-    dma("y", window(rank, 1, lambda q: T.DS[q, 256 * rank:256 * rank + 256]), "DS%d" % rank, "Dw%d" % rank)
-    for u in range(4):
-        ts(blk(T.EU, u, 128), T.RE[:], float(-u), None, A.is_equal, None, "RE0", "EU")
-    d_pairs(rank, 4)
-    b_cells(srcs[0], 0, False)
-    b_number((4, 5, 6, 7, 0, 1, 2, 3))
-    b_cells(srcs[2], 4, False)
-    d_pairs(srcs[2], 4)
-    b_number((5, 6, 7, 4))
+        window(o, 0, lambda q: T.PT[q, 256 * o:256 * o + 256], "GO PT%d" % o, "Dp%d" % o, range(2))
 
-    def fill_g(t, c, key):
-        iota(t, [[0, t.shape[1]]], c, 0, key)
+    def kids_out():
+        send(lambda o: blk(T.DS, o, 256), lambda o: T.DLD[o], "ad%d" % rank, " ".join("DS%d" % o for o in peers))
+        for o in peers:
+            arrival("DLD%d" % o, "ad%d" % o, [o])
+        issued("GO")
+        window(rank, 1, lambda q: T.DS[q, 256 * rank:256 * rank + 256], "GO DS%d" % rank, "Dw%d" % rank, range(2))
 
-    def paint(t, pat, base, w, key):
-        sel(t, t, pat, A.not_equal, w, base, 1, key, key)
+    def d_copies():
+        dma("y", [(at(rank, 32 * y, 32), at(rank, 0, 32)) for y in range(1, 4)], "Dw%d Dp%d" % (rank, rank), "Dw%d Dp%d" % (rank, rank))
+        for o in (far[0], near_[0], far[1]):
+            dma("y", [(at(o, 16 * a, 8), at(o, 16 * (a % 2), 8)) for a in range(2, 8)], "Dp%d" % o, "Dp%d" % o)
+        for o in srcs[1:]:
+            window(o, 1, lambda q: T.DLD[o, q, :], "DLD%d" % o, "Dw%d" % o, range(8))
 
-    def keep(t, pat, base, key, cmp=A.is_equal, cm=1):
-        sel(t, t, pat, cmp, 0.0, base, cm, key, key)
-    fill_g(T.NI[:], 0, "NI")
-    for x in range(4):
+    def painted():
+        for x in range(4):
+            for s in range(2):
+                c0 = 144 * x + 12 + 64 * s
+                paint(T.NI[:, c0:c0 + 64], [[1, 4], [1000, 4], [-8, 4]], -(64 * s + 32 * (x // 2) + 4 * (x % 2) + 3), 1.0, "NI")
         for s in range(2):
-            c0 = 144 * x + 12 + 64 * s
-            paint(T.NI[:, c0:c0 + 64], [[1, 4], [1000, 4], [-8, 4]], -(64 * s + 32 * (x // 2) + 4 * (x % 2) + 3), 1.0, "NI")
-    fill_g(T.GW[:], 0, "GW")
-    for s in range(2):
+            for x in range(2):
+                paint(T.GW[:, 104 + 16 * s + x:112 + 16 * s:2], [[16, 4]], -(64 * s + 55 - 4 * x), 1.0, "GW")
         for x in range(2):
-            paint(T.GW[:, 104 + 16 * s + x:112 + 16 * s:2], [[16, 4]], -(64 * s + 55 - 4 * x), 1.0, "GW")
-    fill_g(T.RY[:], 0, "RY")
-    for x in range(2):
-        paint(T.RY[:], [[-16, 8], [1000, 2], [-2, 8]], -x, (1.0, 16.0)[x], "RY")
-    fill_g(T.WX[:], 0, "WX")
-    for c0, row, w in ((0, 7, 512.0), (1, 3, 512.0), (129, 8, -512.0), (129, 9, 512.0)):
-        paint(T.WX[:, c0:c0 + 127:16], [[-16, 8]], -row, w, "WX")
-    iota(T.CA[:], [[0, 32], [-1, 4]], 4, 0, "CA")
-    fill_g(T.M2[:], 1, "M2")
-    keep(T.M2[:], [[16, 8], [0, 16]], 15, "M2", A.is_ge, -1)
-    keep(T.M2[:], [[-1, 128]], 0, "M2", A.is_gt)
-    paint(T.M2[:], [[-1, 128]], 0, 1024.0, "M2")
-    fill_g(T.RT[:], 1, "RT")
-    keep(T.RT[:], [[0, 4], [1, 32]], 0, "RT", A.not_equal, 0)
-    fill_g(T.KR[:], 0, "KR")
-    for c0, ws in ((0, (1.0, 64.0)), (136, (128.0, 1.0))):
+            paint(T.RY[:], [[-16, 8], [1000, 2], [-2, 8]], -x, (1.0, 16.0)[x], "RY", x == 0)
+        iota(T.CA[:], [[0, 32], [-1, 4]], 4, 0, "CA")
+        for c0, row, w in ((0, 7, 512.0), (1, 3, 512.0), (1, 11, -1024.0), (129, 8, 512.0), (129, 9, -512.0)):
+            paint(T.WX[:, c0:c0 + 127:16], [[-16, 8]], -row, w, "WX")
+        for jj, c0 in enumerate((0, 64, 192)):
+            iota(T.MR[:, c0:c0 + 64 * (jj + 1)], [[0, 4], [1, 16 * (jj + 1)]], -16 * jj, 0, "MR")
+        paint(T.M2[:], [[-16, 8], [0, 16]], -15, 1.0, "M2", True, A.is_gt)
+        paint(T.RT[:], [[0, 4], [1, 32]], 0, 1.0, "RT", True, A.is_equal, 0)
+        paint(T.M2[:], [[-1, 128]], 0, 0.0, "M2", False, A.is_gt)
+        paint(T.M2[:], [[-1, 128]], 0, 1024.0, "M2")
+        for c0, ws in ((0, (1.0, 64.0)), (136, (128.0, 1.0))):
+            for x in range(2):
+                paint(T.KR[:, c0 + 3:c0 + 131:4], [[-16, 2], [2, 4], [-32, 4]], -14 - x, ws[x], "KR")
+        paint(T.RB[:], [[-32, 4], [0, 4], [-1, 32]], 0, 1.0, "RB", True)
+        for rd in range(RO):
+            fill_g(T.TL[:, TW * (N * rd + rank) + 48:TW * (N * rd + rank + 1)], 0, "TL~")
+        fill_g(T.WR[:], 0, "WR")
+        for t, key in ((T.SK, "SK"), (T.UY, "UY"), (T.UZ, "UZ")):
+            fill_g(t[:], 0, key)
+        for r in range(N):
+            paint(T.WR[:, 224 * r + 96:224 * r + 128], [[-1, 32]], -32 * r, 1.0, "WR")
         for x in range(2):
-            paint(T.KR[:, c0 + 3:c0 + 131:4], [[-16, 2], [2, 4], [-32, 4]], -14 - x, ws[x], "KR")
-    for jj, c0 in enumerate((0, 64, 192)):
-        iota(T.MR[:, c0:c0 + 64 * (jj + 1)], [[0, 4], [1, 16 * (jj + 1)]], -16 * jj, 0, "MR")
-    fill_g(T.RB[:], 1, "RB")
-    keep(T.RB[:], [[-32, 4], [0, 4], [-1, 32]], 0, "RB")
-    iota(T.UC[:], [[0, 4], [128, 4], [16, 3]], 8192, 0, "UC0")
-    for rd in range(RO):
-        fill_g(T.TL[:, TW * (N * rd + rank) + 48:TW * (N * rd + rank + 1)], 0, "TL~")
-    iota(T.XD[:], [[0, 4], [16, 4]], S * (rank + 1), 0, "XD0")
-    fill_g(T.WR[:], 0, "WR")
-    for r in range(N):
-        paint(T.WR[:, 224 * r + 96:224 * r + 128], [[-1, 32]], -32 * r, 1.0, "WR")
-    for t, key in ((T.SK, "SK"), (T.UY, "UY"), (T.UZ, "UZ")):
-        fill_g(t[:], 0, key)
-    for x in range(2):
-        paint(T.SK[:, 0::4], [[-16, 8], [-2, 4]], -8 - x, (128.0, 1.0)[x], "SK")
-        paint(T.UZ[:, x::2], [[-16, 8], [-1, 8]], 0, (-16.0, 1.0)[x], "UZ")
-    paint(T.UY[:, 0::2], [[-16, 8], [-1, 8]], 0, 1.0, "UY")
-    fill_g(T.ZT[:], 0, "ZT~")
-    fill_g(T.NO[:], 0, "NO")
-    for r in range(N):
+            paint(T.SK[:, 0::4], [[-16, 8], [-2, 4]], -8 - x, (128.0, 1.0)[x], "SK")
+            paint(T.UZ[:, x::2], [[-16, 8], [-1, 8]], 0, (-16.0, 1.0)[x], "UZ")
+        paint(T.UY[:, 0::2], [[-16, 8], [-1, 8]], 0, 1.0, "UY")
+
+    def painted_last():
+        fill_g(T.NO[:], 0, "NO")
+        fill_g(T.ZT[:], 0, "ZT~")
+        fill_g(blk(T.ZL, rank, 8), 0, "ZL~")
+        for r in range(N):
+            for s in range(2):
+                c0 = 176 * r + 36 + 64 * s
+                paint(T.NO[:, c0:c0 + 32], [[-1, 4], [1000, 2], [16, 4]], -(64 * s + 48 + 4 * r), 1.0, "NO")
+
+    def weights():
+        ts(T.RG[:], IF(0, 128), 1.0 / 16, 143.53, A.mult, A.add, "IF", "RG")
+        ts(T.RC[:, 0:16], IF(0, 16), 0.25, 143.6, A.mult, A.add, "IF", "RC0")
+        cts("g144", "x112", 1.0 / 16, 144.0, A.mult, A.add)
+        for x, (lo, hi, bit) in enumerate((("a2", "b5", "b1"), ("lo2", "b4", "b0"))):
+            cts("n%d" % x, hi, 3.0, lo, A.mult, A.subtract)
+            cts("d%d" % x, lo, bit, hi, A.subtract, A.subtract)
+        ts(T.TM[:, 48:64], T.RC[:, 0:16], -4.0, 720.0, A.mult, A.add, "RC0", "TM1")
+        onehot(T.OB[:], T.RG[:], "RG", "g144", 1.0, "OB")
+        cts("wh", "bh", -1.0, 2.0 ** -13, A.is_lt, A.mult)
+        tt(T.RC[:, 16:32], T.TM[:, 48:64], IF(0, 16), A.add, "TM1 IF", "RC")
+        for x in range(2):
+            cts("x%d" % x, "d%d" % x, "mid", "n%d" % x, A.mult, A.add)
+        cts("wm", "mid", "wh", None, A.subtract)
+        ts(T.WJ[:, 0:1], T.WI[:, 0:1], 6, None, A.logical_shift_right, None, "WI", "WJ")
+        ts(T.WJ[:, 1:2], T.WI[:, 0:1], 63, None, A.bitwise_and, None, "WI", "WJ")
+        for x in range(2):
+            ts(blk(T.TM, x, 16), blk(T.RC, x, 16), col("x%d" % x), -146.0, A.add, A.add, "RC0 RC cx%d" % x, "TM0")
+        ts(col("whi"), T.WJ[:, 0:1], 64.0, None, A.mult, None, "WJ", "cwhi")
+        cp(col("wlo"), T.WJ[:, 1:2], "WJ", "cwlo")
+        tt(T.TM[:, 32:64], T.TM[:, 0:32], T.TM[:, 0:32], A.mult, "TM0", "TM1")
+        cts("s8", "j", 7.5, EQW, A.is_lt, A.mult)
+        cts("s10", "j", 10.0, 48 * EQW, A.is_equal, A.mult)
+        tt(T.TM[:, 0:16], T.TM[:, 32:48], T.TM[:, 48:64], A.add, "TM1", "TM0")
+        cts("s11", "j", 10.5, -16 * EQW, A.is_lt, A.mult)
+        cts("r0", "j", 0.0, None, A.is_equal)
+        ts(T.TM[:, 32:48], T.TM[:, 0:16], 2.5, col("wh"), A.is_lt, A.mult, "TM0 cwh", "TM1")
+        ts(T.TM[:, 48:64], T.TM[:, 0:16], 0.0, col("wm"), A.is_equal, A.mult, "TM0 cwm", "TM1")
+        cts("r1", "j", 1.0, 512.0, A.is_equal, A.mult)
+        cts("s9", "s10", "s11", None, A.add)
         for s in range(2):
-            c0 = 176 * r + 36 + 64 * s
-            paint(T.NO[:, c0:c0 + 32], [[-1, 4], [1000, 2], [16, 4]], -(64 * s + 48 + 4 * r), 1.0, "NO")
+            h = slice(64 * s, 64 * s + 64)
+            tt(T.AU[h, 96 + 16 * s:112 + 16 * s], T.TM[h, 32:48], T.TM[h, 48:64], A.add, "TM1 AU", "AU1")
+        cts("k0", "r0", 0.25, None, A.mult)
+        cts("wS", "s9", "b3", "s8", A.mult, A.add)
+        for o in range(N):
+            cts("u%d" % o, "r0", 512.0 * (64 + o), 65536.0, A.mult, A.add)
+        cts("wkey", "r1", 2.0 ** -18, "k0", A.mult, A.add)
+        for o in range(N):
+            line(T.CT[:, o::4], IF(0, 48), "r1", "u%d" % o, "IF", "CT")
+        dma("y", [(blk(T.CW, x, 192), T.CT[:]) for x in range(RO)], "CT", "CW")
+        for n_, c in enumerate(("whi", "wlo", "wS", "wkey")):
+            line(T.LW[:, 144 * n_ + 15:144 * n_ + 143:16], T.OB[:, 0::16], c, 0.0, "OB LW", "LW%d" % n_)
+        cts("mb3", "b3", -1.0, None, A.mult)
+        onehot(T.SH[:], IF(0, 128), "IF", "p", 1.0, "SH")
 
-    ms(T.AU[:], 0.0, "AU")
-    ms(T.LW[:], 0.0, "LW")
-    ms(T.B[:, 0:512], 0.0, "B~")
-    for x, (lo, hi, bit) in enumerate((("a2", "b5", "b1"), ("lo2", "b4", "b0"))):
-        cts("n%d" % x, hi, 3.0, lo, A.mult, A.subtract)
-        cts("d%d" % x, lo, bit, hi, A.subtract, A.subtract)
-    cts("wh", "bh", -1.0, 2.0 ** -13, A.is_lt, A.mult)
-    for x in range(2):
-        cts("x%d" % x, "d%d" % x, "mid", "n%d" % x, A.mult, A.add)
-    cts("wm", "mid", "wh", None, A.subtract)
-    ts(T.WJ[:, 0:1], T.WI[:, 0:1], 6, None, A.logical_shift_right, None, "WI", "WJ")
-    ts(T.WJ[:, 1:2], T.WI[:, 0:1], 63, None, A.bitwise_and, None, "WI", "WJ")
-    for x in range(2):
-        ts(blk(T.TM, x, 16), blk(T.RC, x, 16), col("x%d" % x), -2.0, A.add, A.add, "RC cx%d" % x, "TM0")
-    ts(col("whi"), T.WJ[:, 0:1], 64.0, None, A.mult, None, "WJ", "cwhi")
-    cp(col("wlo"), T.WJ[:, 1:2], "WJ", "cwlo")
-    tt(T.TM[:, 32:64], T.TM[:, 0:32], T.TM[:, 0:32], A.mult, "TM0", "TM1")
-    cts("mb3", "b3", -1.0, None, A.mult)
-    tt(T.TM[:, 0:16], T.TM[:, 32:48], T.TM[:, 48:64], A.add, "TM1", "TM0")
-    ms(col("na"), -(1.0 + 2.0 ** -10), "cna")
-    ms(col("big"), 65536.0, "cbig")
-    ts(T.TM[:, 32:48], T.TM[:, 0:16], 2.5, col("wh"), A.is_lt, A.mult, "TM0 cwh", "TM1")
-    ts(T.TM[:, 48:64], T.TM[:, 0:16], 0.0, col("wm"), A.is_equal, A.mult, "TM0 cwm", "TM1")
-    for s in range(2):
-        h = slice(64 * s, 64 * s + 64)
-        tt(T.AU[h, 96 + 16 * s:112 + 16 * s], T.TM[h, 32:48], T.TM[h, 48:64], A.add, "TM1 AU", "AU1")
-
-    chain = lambda n_, i: T.LW[:, 144 * n_ + 15 - i:144 * n_ + 143 - i]
-    cts("s8", "j", 7.5, -EQW, A.is_lt, A.mult)
-    cts("s9", "j", 9.5, 16 * EQW, A.is_lt, A.mult)
-    cts("r0", "j", 0.0, None, A.is_equal)
-    cts("r1", "j", 1.0, 512.0, A.is_equal, A.mult)
-    cts("jd", "j", -1.0, 2048.0, A.mult, A.add)
-    cts("wS", "s9", "b3", "s8", A.mult, A.add)
-    cts("k0", "r0", 0.25, None, A.mult)
-    for o in range(N):
-        cts("u%d" % o, "r0", 512.0 * (64 + o), 65536.0, A.mult, A.add)
-    ts(T.OWN[:], IF(-32, 0), 16.0, col("j"), A.mult, A.add, "IF cj", "OWN")
-    cts("wkey", "r1", 2.0 ** -18, "k0", A.mult, A.add)
-    for o in range(N):
-        ts(T.CT[:, o::4], IF(0, 48), col("r1"), col("u%d" % o), A.mult, A.add, "IF cr1 cu%d" % o, "CT")
-    ms(col("m2"), -2.0, "cm2")
-    ms(col("c15"), 15.0, "cc15")
-    ms(T.DP[:], 1e6, "DP0")
-    onehot(T.SH[:], IF(0, 128), "IF", "p", 1.0, "SH")
-    onehot(T.OB[:], T.RG[:], "RG", "x112", 1.0, "OB")
-    ts(T.DP[:, 0::4], IF(0, 32), -16.0, col("jd"), A.mult, A.add, "IF cjd DP0", "DP")
-    for n_, c in enumerate(("whi", "wlo", "wS", "wkey")):
-        ts(T.LW[:, 144 * n_ + 15:144 * n_ + 143:16], T.OB[:, 0::16], col(c), None, A.mult, None, "OB LW c" + c, "LW%d" % n_)
-    ts(T.BC[:], T.OB[:], col("wkey"), None, A.mult, None, "OB cwkey", "BC")
-    ms(T.RS[:], 0.0, "RS")
-    ms(T.E[:], WON, "E")
-    ms(T.RS[:, 0::48], WON, "RS", "RS")
-    ms(T.TS[:], 0.0, "TS~")
-
-    def constants(n_):
+    def late_constants(n_):
         if n_ == 0:
-            ts(T.MK[:], T.MR[:], col("j"), 16384.0, A.is_ge, A.mult, "MR cj", "MK")
+            ms(T.RS[:], 0.0, "RS0")
+            ms(T.E[:], WON, "E")
+            ms(T.DP[:], 1e6, "DP0")
         if n_ == 1:
-            ts(T.UC[:], T.UC[:], col("j"), None, A.add, None, "UC0 cj", "UC")
-            ts(T.XD[:], T.XD[:], col("j"), None, A.add, None, "XD0 cj", "XD")
+            cts("jd", "j", -1.0, 2048.0, A.mult, A.add)
+            cts("big", "r1", 65536.0, "b3", A.add, A.add)
+            ms(T.RS[:, 0::48], WON, "RS", "RS0")
+            cts("ju", "j", 8704.0, None, A.add)
+            cts("jx", "j", float(S * (rank + 1)), None, A.add)
+        if n_ == 2:
+            ms(T.TS[:], 0.0, "TS~")
+            line(T.OWN[:], IF(-32, 0), 16.0, "j", "IF", "OWN")
+            line(T.DP[:, 0::4], IF(0, 32), -16.0, "jd", "IF DP0", "DP")
+            line(T.BC[:], T.OB[:], "wkey", 0.0, "OB", "BC")
+            line(T.UC[:], IF(0, 48), 16.0, "ju", "IF", "UC")
+            line(T.XD[:], IF(0, 16), 16.0, "jx", "IF", "XD")
             cts("bY", "b0", -2448.0, 2304.0, A.mult, A.add)
+        if n_ == 3:
+            ts(T.MK[:], T.MR[:], col("j"), 16384.0, A.is_ge, A.mult, "MR cj", "MK")
 
-    cp(T.KF[:], T.KS[:, 0:512], "KS", "KF")
-    b_cells(srcs[1], 0)
-    b_cells(srcs[3], 4)
-    d_pairs(srcs[1], 0)
-    d_pairs(srcs[3], 1)
-    for o in srcs[1:]:
-        dma("y", window(o, 1, lambda q: T.DLD[o, q, :]), "DLD%d" % o, "Dw%d" % o)
-    dma("y", [(blk(T.CW, x, 192), T.CT[:]) for x in range(RO)], "CT", "CW")
-    dma("y", [(T.YC[:, 0:S], T.cells[:])], "Dw0 Dw1 Dw2 Dw3", "WY")
-    dma("y", [(T.YK[16 * q:16 * q + 16:4, 0:S], T.KF[64 * (q % 2):64 * (q % 2) + 64, 128 * (q // 2):128 * (q // 2) + 128]) for q in range(8)], "KF", "WK")
+    def first_outputs():
+        cp(T.KF[:], T.KS[:, 0:512], "KS", "put KF")
+        dma("y", [(T.YC[:, 0:S], T.cells[:])], alld, "WY")
+        dma("y", [(T.YK[16 * q:16 * q + 16:4, 0:S], T.KF[64 * (q % 2):64 * (q % 2) + 64, 128 * (q // 2):128 * (q // 2) + 128]) for q in range(8)], "KF", "WK")
 
-    for o in peers:
-        cp(T.KL[:, o::4], blk(T.LK, o, 128), "LK", "KL")
-    allb = " ".join("B%d" % b for b in range(16))
-    act(T.CC[:, 0:4096], T.B[:, 512:8704].indirect(T.KL[:, 0:256]), F.Copy, allb + " KL", "CC0")
-    cp(T.CC[:, 4096:6144], T.B[:, 512:8704].indirect(T.KL[:, 256:384]), allb + " KL", "CC1")
-    cp(T.NF[:, 0:128], T.LK[:, 512:640], "LN LNo", "NF0")
-    mm([(P[4][:, 64 * (x % 2) + x // 2:64 * (x % 2) + 64:2], [(T.NI[:, 144 * x + 12 - 4 * r:144 * x + 140 - 4 * r], blk(T.NF, r, 32)) for r in range(N)])
-        for x in range(4)], "NI NF0", "P4")
-    cp(T.CC[:, 6144:8192], T.B[:, 512:8704].indirect(T.KL[:, 384:512]), allb + " KL", "CC2")
-    cp(T.PL[:], P[4][:, 0:128], "P4", "PL")
-    allc = "CC0 CC1 CC2"
+    def lists():
+        for o in peers:
+            cp(T.KL[:, o::4], T.LK[:, 160 * o:160 * o + 128], "LK", "KL")
+        for o in peers:
+            cp(blk(T.NF, 4 + o, 32), T.LK[:, 160 * o + 128:160 * o + 160], "LK", "NF1")
+
+    def table_cc():
+        act(T.CC[:, 0:4096], T.B[:, 512:8704].indirect(T.KL[:, 0:256]), F.Copy, allb + " KL", "CC0", gathers=True)
+        cp(T.CC[:, 4096:6144], T.B[:, 512:8704].indirect(T.KL[:, 256:384]), allb + " KL", "CC1", gathers=True)
+        mm([(P[7][:, 64 * (x % 2) + x // 2:64 * (x % 2) + 64:2], [(T.NI[:, 144 * x + 12 - 4 * r:144 * x + 140 - 4 * r], blk(T.NF, 4 + r, 32)) for r in range(N)])
+            for x in range(4)], "NI NF1", "P7")
+        cp(T.CC[:, 6144:8192], T.B[:, 512:8704].indirect(T.KL[:, 384:512]), allb + " KL", "CC2", gathers=True)
+        cp(T.PL[:], P[7][:, 0:128], "P7", "PL")
 
     half = lambda k, a: T.G[:, 1024 * k + a:1024 * k + 1024:16]
 
     def gather(k, both=False):
         if both:
-            cp(blk(T.G, 2 * k, 512), T.CC[:, 0:8192].indirect(blk(T.PL, 2 * k, 32)), allc + " PL", "Gv%d" % k)
-            act(blk(T.G, 2 * k + 1, 512), T.CC[:, 0:8192].indirect(blk(T.PL, 2 * k + 1, 32)), F.Copy, allc + " PL", "G%d" % k)
+            cp(blk(T.G, 2 * k, 512), T.CC[:, 0:8192].indirect(blk(T.PL, 2 * k, 32)), allc + " PL", "Gv%d" % k, gathers=True)
+            act(blk(T.G, 2 * k + 1, 512), T.CC[:, 0:8192].indirect(blk(T.PL, 2 * k + 1, 32)), F.Copy, allc + " PL", "G%d" % k, gathers=True)
         else:
-            act(blk(T.G, k, 1024), T.CC[:, 0:8192].indirect(blk(T.PL, k, 64)), F.Copy, allc + " PL", "G%d Gv%d" % (k, k))
+            act(blk(T.G, k, 1024), T.CC[:, 0:8192].indirect(blk(T.PL, k, 64)), F.Copy, allc + " PL", "G%d Gv%d" % (k, k), gathers=True)
 
     def near(k):
         mm([(P[k][:, i:256:4], [(T.AU[:, 96 - 32 * r:224 - 32 * r], half(k, 4 * r + i)) for r in range(N)]) for i in range(4)],
-           "AU1 G%d Gv%d" % (k, k), "P%d" % k)
+           "AU1 G%d Gv%d" % (k, k), "P%da" % k)
 
     def life_a(k):
-        act(T.AB[:, k:512:2], P[k][:, 0:256], F.Relu, "P%d cna" % k, "Aa%d" % k, bias=col("na"))
+        act(T.AB[:, k:512:2], P[k][:, 0:256], F.Relu, "P%da" % k, "Aa%d" % k, bias=-(1.0 + 2.0 ** -10))
 
     def life_b(k):
-        ts(T.AB[:, 512 + k::2], P[k][:, 0:256], 2.0 ** -12, 15.0, A.is_equal, A.mult, "P%d" % k, "Ab%d" % k)
+        ts(T.AB[:, 512 + k::2], P[k][:, 0:256], 2.0 ** -12, 15.0, A.is_equal, A.mult, "P%da" % k, "Ab%d" % k)
 
     def life_s(k):
-        act(T.UA[:], P[k][:, 0:256], F.Abs, "P%d cm2" % k, "UA", scale=8192.0, bias=col("m2"))
+        act(T.UA[:], P[k][:, 0:256], F.Abs, "P%da" % k, "UA", scale=8192.0, bias=-2.0)
         life_a(k)
-        act(T.AB[:, 512 + k::2], T.UA[:], F.Relu, "UA cc15", "Ab%d" % k, scale=-15.0, bias=col("c15"))
+        act(T.AB[:, 512 + k::2], T.UA[:], F.Relu, "UA", "Ab%d" % k, scale=-15.0, bias=15.0)
 
     def hash_mm(k):
         mm([(P[2][:, 0:64], [(chain(n_, i), T.AB[:, i::16]) for i in range(k, 16, 2) for n_ in range(2)])],
-           "LW0 LW1 Aa0 Ab0" + (" Aa1 Ab1" if k else ""), "P2", k == 0, k == 1)
-
-    def rec_start():
-        mm([(P[3][:], [(T.ZR[:], T.B[:, 0:512])])], "ZR B~", "P3", True, False)
+           "LW0 LW1 Aa0 Ab0" + (" Aa1 Ab1" if k else ""), "P2a", k == 0, k == 1)
 
     def rec_kids(k):
         more_mm([(P[3][:, 2 * i + k::8], T.GW[:, 96 - 32 * r:224 - 32 * r], half(k, 4 * r + i)) for i in range(4) for r in range(N)],
-                "GW G%d Gv%d" % (k, k), "P3")
+                "GW G%d Gv%d" % (k, k), "P3", k == 1, k == 0)
 
-    def rec_mm():
-        mm([(P[3][:], [(T.RY[:], T.AB[:, 0:512]), (T.RY[:], T.AB[:, 512:1024])])], "RY Aa0 Aa1 Ab0 Ab1", "P3", False, True)
+    def rec_copy():
+        act(REC, P[3][:], F.Copy, "P3", "REC")
 
     def rec_pairs():
         mm([(P[5][:], [(T.RY[:], T.AB[:, 0:512]), (T.RY[:], T.AB[:, 512:1024])])], "RY Aa0 Aa1 Ab0 Ab1", "P5")
@@ -519,80 +535,70 @@ def rank_program(g, core, T, topo):
 
     H, H1, OO, TI, B0 = (blk(T.HI, x, 32) for x in range(5))
     DH, TF = blk(T.HF, 0, 32), blk(T.HF, 1, 32)
-    HIT = -8.0 * EQW
-    LOW = HIT - EQW
 
     def hash_out():
-        act(TF, P[2][:, 0:32], F.Copy, "P2", "TF")
+        act(TF, P[2][:, 0:32], F.Copy, "P2a", "TF")
 
     def hash_sum():
-        tt(TI, TF, P[2][:, 32:64], A.add, "TF P2", "TI")
+        tt(TI, TF, P[2][:, 32:64], A.add, "TF P2a", "TI")
 
     def hash_ops():
         ts(B0, TI, 1, None, A.bitwise_and, None, "TI", "B0")
         ts(H, TI, 8191, None, A.bitwise_and, None, "TI", "H")
-        ts(DH, B0, 2.0, -1.0 - LOW, A.mult, A.add, "B0", "DH")
+        ts(DH, B0, 2.0, -1.0, A.mult, A.add, "B0", "DH")
         cp(T.HL[:, 0:32], H, "H", "HL0")
         tt(H1, H, DH, A.subtract, "H DH", "H1")
-        ts(T.HL[:, 32:64], H1, -LOW, None, A.add, None, "H1", "HL1")
+        cp(T.HL[:, 32:64], H1, "H1", "HL1")
 
     c32 = lambda x: blk(T.CL, x, 32)
     S0, S1 = P[6][:, 0:32], P[7][:, 0:32]
 
     def look():
-        act(REC, P[3][:], F.Copy, "P3", "REC")
-        act(T.WG[:], T.B[:, 512:8704].indirect(T.HL[:, 32:64]), F.Copy, allb + " HL1", "WG")
+        act(T.WG[:], T.B[:, 512:8704].indirect(T.HL[:, 0:32]), F.Copy, allb + " HL0", "WG", gathers=True)
+        mm([(P[2][:, 256:384], [(ID, T.CA[:])])], "SH CA", "P2b", True, False)
+        mm([(P[5][:], [(ID, T.RX[:]), (ID, REC)])], "SH RX REC", "P5", True, False)
+        mm([(P[5][:], [(blk(T.WX, 0, 128), T.WG[:])])], "WX WG", "P5", False, False)
         for x in range(2):
-            tt(blk(T.DD, x, 512), T.D[:, 512:8704].indirect(blk(T.HL, x, 32)), T.RX[:], A.is_equal,
-               "D Dw0 Dw1 Dw2 Dw3 Dp0 Dp1 Dp2 Dp3 RX HL%d" % x, "DD%d" % x)
-            mm([((S0, S1)[x], [(chain(2, i), T.DD[:, 512 * x + i:512 * x + 512:16]) for i in range(16)])], "LW2 DD%d" % x, "P%d" % (6 + x))
-            if x == 0:
-                mm([(P[3][:], [(ID, REC)])], "SH REC", "P3", True, False)
-        mm([(P[3][:], [(blk(T.WX, 1, 128), T.DD[:, 0:512]), (blk(T.WX, 0, 128), T.WG[:])])], "WX DD0 WG", "P3", False, True)
-        act(T.RQ[:], P[3][:], F.Identity, "P3 cbig", "RQ", bias=col("big"))
+            tt(blk(T.DD, x, 512), T.D[:, 512:8704].indirect(blk(T.HL, x, 32)), T.RX[:], A.not_equal, "D %s RX HL%d" % (alld, x), "DD%d" % x, True)
+            mm([((S0, S1)[x], [(chain(2, i), T.DD[:, 512 * x + i:512 * x + 512:16]) for i in range(16)])], "LW2 DD%d" % x, "P%da" % (6 + x))
+        mm([(P[5][:], [(blk(T.WX, 1, 128), T.DD[:, 0:512])])], "WX DD0", "P5", False, True)
+        act(T.RQ[:], P[5][:], F.Identity, "P5 cbig", "RQ", bias=col("big"))
 
-    def flags(rd):
-        ts(c32(0), S0, -1.0, 8.5 * EQW, A.mult, A.add, "P6", "C0")
-        ts(c32(2), S0, HIT, EQW, A.not_equal, A.mult, "P6", "C2")
-        mm([(P[6][:, 128:256], [(ID, T.CA[:])])], "SH CA", "P6", True, False)
-        fill(1)
-        tt(c32(3), H, c32(2), A.subtract, "C2 H", "C3")
+    def flags():
+        tt(c32(3), H, S0, A.subtract, "P6a H", "C3")
+        ts(c32(0), S0, -1.0, 24.5 * EQW, A.mult, A.add, "P6a", "C0")
         ts(OO, TI, 11, 3, A.logical_shift_right, A.bitwise_and, "TI", "OO")
         tt(c32(4), c32(3), T.OWN[:], A.max, "C3 OWN", "C4")
-        tt(c32(5), S1, c32(0), A.subtract, "P7 C0", "C5")
-        tt(c32(7), S1, c32(2), A.subtract, "P7 C2", "C7")
+        tt(c32(5), S1, c32(0), A.subtract, "P7a C0", "C5")
+        tt(c32(8), H1, S1, A.subtract, "P7a H1", "C8")
         tt(c32(6), c32(5), OO, A.min, "C5 OO", "C6")
-        tt(c32(8), H1, c32(7), A.subtract, "C7 H1", "C8")
+        tt(c32(7), S0, c32(8), A.min, "P6a C8", "C7")
         for o in range(N):
             ts(blk(T.FB, o, 32), c32(6), float(o), 4.0, A.is_equal, A.mult, "C6", "FB")
-        more_mm([(P[6][:, 128 + o:256:4], T.M2[:], blk(T.FB, o, 32)) for o in range(N)], "M2 FB", "P6")
+        tt(c32(9), c32(7), c32(4), A.max, "C7 C4", "C9")
+        more_mm([(P[2][:, 256 + o:384:4], T.M2[:], blk(T.FB, o, 32)) for o in range(N)], "M2 FB", "P2b")
         scan(T.RR[:], T.RT[:], T.FB[:], 0.0, A.mult, A.subtract, "RT FB", "RR")
-        more_mm([(P[6][:, 128 + o:256:4], T.OB[:], blk(T.RR, o, 32)) for o in range(N)], "OB RR", "P6", True)
-        tt(c32(9), c32(8), c32(4), A.max, "C8 C4", "C9")
+        more_mm([(P[2][:, 256 + o:384:4], T.OB[:], blk(T.RR, o, 32)) for o in range(N)], "OB RR", "P2b", True)
         ts(T.AT[:], c32(9), 512.0, None, A.add, None, "C9", "AT")
-        act(T.PG[:], T.D[:, 0:8704].indirect(T.AT[:]), F.Copy, "D REC AT", "PG")
-        scan(T.SQ[:], T.DP[:], P[6][:, 128:256], 1e6, A.min, A.max, "DP P6", "SQ")
+        act(T.PG[:], T.D[:, 0:8704].indirect(T.AT[:]), F.Copy, "D REC AT", "PG", gathers=True)
+        mm([(P[7][:, 64:448], [(ID, T.MK[:])])], "SH MK", "P7b", True, False)
+        scan(T.SQ[:], T.DP[:], P[2][:, 256:384], 1e6, A.min, A.max, "DP P2b", "SQ")
         ts(T.OL[:], T.SQ[:, 3::4], -1.0, 4096.0, A.mult, A.add, "SQ", "OL")
-        mm([(P[7][:, 64:448], [(ID, T.MK[:])])], "SH MK", "P7", True, False)
-        if rd < RO - 1:
-            mm([(P[6][:, 256:304], [(ID, T.ZR[:, 0:48])])], "SH ZR", "P6", True, False)
 
     def pointers(rd):
         kr = 136 if rd == RO - 1 else 0
-        mm([(P[2][:, 128 + 64 * k:192 + 64 * k], [(T.KR[:, kr + 3 - i:kr + 131 - i], T.PG[:, 2 * i + k::8]) for i in range(4)]) for k in range(2)],
-           "KR PG", "P2")
-
-    def nodes_mm(h):
-        if h == 0:
-            act(T.PN[:], P[2][:, 128:256], F.Copy, "P2", "PN")
-        mm([(P[3][:, 32 * r:32 * r + 32], [(T.NO[:, 176 * r + 36 - 32 * x - 4 * k:176 * r + 164 - 32 * x - 4 * k], T.PN[:, 64 * k + x:64 * k + 64:2])
-                                           for x in range(2) for k in range(2)]) for r in (2 * h, 2 * h + 1)], "NO PN", "P3")
+        mm([(P[6][:, 128 + 64 * k:192 + 64 * k], [(T.KR[:, kr + 3 - i:kr + 131 - i], T.PG[:, 2 * i + k::8]) for i in range(4)]) for k in range(2)],
+           "KR PG", "P6b")
 
     def nodes_out():
+        act(T.PN[:], P[6][:, 128:256], F.Copy, "P6b", "PN")
+        for r in range(N):
+            mm([(blk(P[3], r, 32), [(T.NO[:, 176 * r + 36 - 32 * x - 4 * k:176 * r + 164 - 32 * x - 4 * k], T.PN[:, 64 * k + x:64 * k + 64:2])
+                                    for x in range(2) for k in range(2)])], "NO PN", "P3")
         act(T.NS[:], P[3][:, 0:128], F.Copy, "P3", "NS")
         send(lambda o: blk(T.NS, o, 32), lambda o: blk(T.NL, o, 32), "an", "NS")
         arrival("NL", "an", peers)
-        dma("y", [(T.ynodes[32 * rank:32 * rank + 32, :], blk(T.NS, rank, 32))], "NS", "yn0")
+        dma("y", [(T.ynodes[rows(rank), :], blk(T.NS, rank, 32))], "NS", "yn0")
 
     def mine(rd, o, a, b):
         c0 = TW * (N * rd + o)
@@ -603,15 +609,15 @@ def rank_program(g, core, T, topo):
     def compact(rd):
         w0 = 192 * (RO - 1 - rd)
         if rd < RO - 1:
-            cp(T.CW[:, w0:w0 + 2560].indirect(T.OL[:, 0:16]), T.RQ[:, 0:256], "OL RQ", "CW")
-            cp(T.PL[:], P[2][:, 128:256], "P2", "PL")
-            cp(T.CW[:, w0:w0 + 2560].indirect(T.OL[:, 16:32]), T.RQ[:, 256:512], "OL RQ CW", "CW")
+            cp(T.CW[:, w0:w0 + 2560].indirect(T.OL[:, 0:16]), T.RQ[:, 0:256], "OL RQ", "CW", scatters=True)
+            cp(T.PL[:], P[6][:, 128:256], "P6b", "PL")
+            cp(T.CW[:, w0:w0 + 2560].indirect(T.OL[:, 16:32]), T.RQ[:, 256:512], "OL RQ CW", "CW", scatters=True)
         else:
-            cp(T.CW[:, w0:w0 + 2560].indirect(T.OL[:]), T.RQ[:], "OL RQ", "CW")
+            cp(T.CW[:, w0:w0 + 2560].indirect(T.OL[:]), T.RQ[:], "OL RQ", "CW", scatters=True)
         for o in range(N):
             cp(blk(T.HX, o, 48), T.CW[:, w0 + o:w0 + 192:4], "CW", "HX%d" % o)
-            more_mm([(tri(o, jj), T.BC[:], T.HX[:, 48 * o:48 * o + 16 * (jj + 1)]) for jj in range(3)], "BC HX%d" % o, "P7", o == N - 1)
-        mm([(P[7][:, 480:492], [(chain(3, i), T.HX[:, i::16]) for i in range(16)])], "LW3 HX0 HX1 HX2 HX3", "P7")
+            more_mm([(tri(o, jj), T.BC[:], T.HX[:, 48 * o:48 * o + 16 * (jj + 1)]) for jj in range(3)], "BC HX%d" % o, "P7b", o == N - 1)
+        mm([(P[7][:, 480:492], [(chain(3, i), T.HX[:, i::16]) for i in range(16)])], "LW3 HX0 HX1 HX2 HX3", "P7c")
         for o in range(N):
             tt(mine(rd, o, 0, 48), T.CW[:, w0 + o:w0 + 192:4], blk(T.HX, o, 48), A.subtract, "CW HX%d TS~" % o, "LO")
 
@@ -623,199 +629,151 @@ def rank_program(g, core, T, topo):
         act(blk(T.RL, k, 384), P[4 + k][:, 0:384], F.Copy, "P%d" % (4 + k), "RL%d" % k)
 
     def keys():
-        cp(T.KC[:, 0:24:2], P[7][:, 480:492], "P7", "KC0")
+        cp(T.KC[:, 0:24:2], P[7][:, 480:492], "P7c", "KC0")
 
-    spread = lambda x: [(P[6][:, 256 + 12 * r:268 + 12 * r], blk(T.RB, r, 128), x) for r in range(N)]
-
-    def equal(rd):
-        last = rd == RO - 1
+    def equal():
         for o in range(N):
             for jj in range(3):
                 n_ = 3 * o + jj
-                ts(T.E[:, 48 * n_:48 * n_ + 16 * (jj + 1)], tri(o, jj), P[7][:, 480 + n_:481 + n_], WON, A.not_equal, A.mult, "P7", "E")
-            if o == 0:
-                tt(T.KC[:, 1:24:2], P[7][:, 480:492], T.KC[:, 0:24:2], A.subtract, "P7 KC0", "KC1")
-                if not last:
-                    more_mm(spread(T.KC[:, 0:24:2]) + spread(T.KC[:, 1:24:2]), "RB KC0 KC1", "P6")
-                for d in peers + [rank]:
-                    if last:
-                        move("s", mark(d, 4), T.KC[:, 6 * d + 1:6 * d + 6:2], "KC1 ZT~", "OK%d" % (d == rank))
-                    else:
-                        move("g", mine(rd, d, 48, 54), T.KC[:, 6 * d:6 * d + 6], "KC0 KC1 TS~ TL~", "OK%d" % (d == rank))
+                ts(T.E[:, 48 * n_:48 * n_ + 16 * (jj + 1)], tri(o, jj), P[7][:, 480 + n_:481 + n_], WON, A.not_equal, A.mult, "P7b P7c", "E")
+        tt(T.KC[:, 1:24:2], P[7][:, 480:492], T.KC[:, 0:24:2], A.subtract, "P7c KC0", "KC1")
         scan(T.ZS[:], T.RS[:], T.E[:], WON, A.min, A.max, "RS E", "ZS")
-        if not last:
-            more_mm(spread(T.ZS[:, 47::48]), "RB ZS", "P6", True)
-            life_b(0)
-            tt(T.AF[:], P[6][:, 256:304], T.UC[:], A.min, "P6 UC", "AF")
-            cp(T.AL[:], T.AF[:], "AF", "AL")
+
+    spread = lambda t, c: [(P[6][:, 256 + 12 * r:268 + 12 * r], blk(T.RB, r, 128), t[:, c]) for r in range(N)]
+
+    def winners(x):
+        if x == 0:
+            more_mm(spread(T.KC, slice(0, 24, 2)), "RB KC0", "P6c", False, True)
+        else:
+            more_mm(spread(T.KC, slice(1, 24, 2)), "RB KC1", "P6c")
+            more_mm(spread(T.ZS, slice(47, 576, 48)), "RB ZS", "P6c", True)
+
+    def targets():
+        tt(T.AF[:], P[6][:, 256:304], T.UC[:], A.min, "P6c UC", "AF")
+        cp(T.AL[:], T.AF[:], "AF", "AL")
 
     def update(r):
-        cp(T.D[:, 512:512 + DW].indirect(blk(T.AL, r, 12)), blk(T.RL, r, 192), "AL D RL%d" % (r // 2), "D")
+        cp(T.D[:, 512:512 + DW].indirect(blk(T.AL, r, 12)), blk(T.RL, r, 192), "AL D RL%d" % (r // 2), "D", scatters=True)
 
     def parcel(rd):
         last = rd == RO - 1
         for o in [] if last else peers + [rank]:
-            move("g", mine(rd, o, 54, 57), T.ZS[:, 144 * o + 47:144 * o + 144:48], "ZS TS~ TL~", "OF%d" % (o == rank))
-        send(lambda o: blk(T.TS, N * rd + o, TW), lambda o: blk(T.TL, N * rd + o, TW), "ar%d" % rd, "LO" if last else "LO OK0 OF0")
+            move("g", mine(rd, o, 48, 54), T.KC[:, 6 * o:6 * o + 6], "KC0 KC1 TS~ TL~", "OK%d" % (o == rank))
+            move("g", mine(rd, o, 54, 57), T.ZS[:, 144 * o + 47:144 * o + 144:48], "ZS TS~ TL~", "OK%d" % (o == rank))
+        send(lambda o: blk(T.TS, N * rd + o, TW), lambda o: blk(T.TL, N * rd + o, TW), "ar%d" % rd, "LO" if last else "LO OK0")
         for o in peers:
             arrival("TL%d%d" % (rd, o), "ar%d" % rd, peers)
-        wrote["TL%d%d" % (rd, rank)], wrote["LO%d" % rd], wrote["OK1%d" % rd] = wrote["TL~" if last else "OF1"], wrote["LO"], wrote["OK1"]
+        wrote["TL%d%d" % (rd, rank)], wrote["LO%d" % rd] = wrote["TL~" if last else "OK1"], wrote["LO"]
 
     mark = lambda o, a: (T.ZL if o == rank else T.ZT)[:, 8 * o + a:8 * o + a + 3]
 
     def marks():
         for o in peers + [rank]:
-            tt(mark(o, 0), T.KC[:, 6 * o:6 * o + 6:2], T.ZS[:, 144 * o + 47:144 * o + 144:48], A.add, "KC0 ZS ZT~", "ZT%d" % (o == rank))
-        send(lambda o: blk(T.ZT, o, 8), lambda o: blk(T.ZL, o, 8), "al%d" % rank, "ZT0 OK0")
+            move("s", mark(o, 4), T.KC[:, 6 * o + 1:6 * o + 6:2], "KC1 ZT~ ZL~", "ZK%d" % (o == rank))
+            tt(mark(o, 0), T.KC[:, 6 * o:6 * o + 6:2], T.ZS[:, 144 * o + 47:144 * o + 144:48], A.add, "KC0 ZS ZT~ ZL~", "ZT%d" % (o == rank))
+        send(lambda o: blk(T.ZT, o, 8), lambda o: blk(T.ZL, o, 8), "al%d" % rank, "ZT0 ZK0")
         for o in peers:
             arrival("ZL%d" % o, "al%d" % o, [o])
         wrote["ZL%d" % rank] = wrote["ZT1"]
 
     def marks_in():
-        mm([(P[5][:, 480:496], [(ID, T.ZR[:, 0:16])])], "SH ZR", "P5", True, False)
         for d in srcs:
-            more_mm([(P[5][:, 480 + 4 * r:483 + 4 * r], T.WR[:, 224 * r + 96 - 32 * d:224 * r + 224 - 32 * d], T.ZL[:, 8 * d + a:8 * d + a + 3])
-                     for r in range(N) for a in (0, 4)], "WR OK1 ZL%d" % d, "P5", d == srcs[-1])
+            more_mm([(P[3][:, 480 + 4 * r:484 + 4 * r], shift(r, d), T.ZL[:, 8 * d + a:8 * d + a + 4])
+                     for r in range(N) for a in (0, 4)], "WR ZK1 ZL%d" % d, "P3b", d == srcs[-1], d == srcs[0])
 
     def regroup(rd):
-        mm([(P[4][:, 0:N * TW], [(T.ZR[:], T.B[:, 0:N * TW])])], "ZR B~", "P4", True, False)
         for d in srcs:
-            more_mm([(blk(P[4], r, TW), T.WR[:, 224 * r + 96 - 32 * d:224 * r + 224 - 32 * d], blk(T.TL, N * rd + d, TW)) for r in range(N)],
-                    "WR LO%d OK1%d TL%d%d" % (rd, rd, rd, d), "P4", d == srcs[-1])
+            more_mm([(blk(P[4], r, TW), shift(r, d), blk(T.TL, N * rd + d, TW)) for r in range(N)],
+                    "WR LO%d TL%d%d" % (rd, rd, d), "P4a", d == srcs[-1], d == srcs[0])
+        act(T.VT[:], P[4][:, 0:N * TW], F.Copy, "P4a", "VT")
+        act(T.VA[:], P[4][:, 0:N * TW], F.Identity, "P4a", "VA", scale=1.0 / 16, bias=143.53)
 
-    def unpack_in():
-        act(T.VT[:], P[4][:, 0:N * TW], F.Copy, "P4", "VT")
-        act(T.VA[:], P[4][:, 0:N * TW], F.Identity, "P4 crnd", "VA", scale=1.0 / 16, bias=col("rnd"))
-
-    def unpack(last=False):
-        if not last:
-            mm([(P[5][:, 480 + 4 * r:484 + 4 * r], [(ID, T.VT[:, TW * r + a:TW * r + b:st]) for a, b, st in ((48, 56, 2), (49, 57, 2), (54, 58, 1))])
-                for r in range(N)], "SH VT", "P5")
-        mm([(P[0][:, 256:512], [(T.UY[:], T.VT[:]), (T.UZ[:], T.VA[:])])], "UY UZ VT VA", "P0")
-        mm([(P[1][:, 256:512], [(T.SK[:], T.VT[:])])], "SK VT", "P1")
-
-    def unpack_out(rd):
-        act(blk(T.RBY, rd, N * TW), P[0][:, 256:512], F.Identity, "P0 cbY", "RBY%d" % rd, bias=col("bY"))
-        act(blk(T.RBK, rd, N * TW), P[1][:, 256:512], F.Copy, "P1", "RBK%d" % rd)
+    def unpack(rd):
         if rd < RO - 1:
-            todo.extend((place, rd, r, key) for r in reversed(range(N)) for key in "YK")
-
-    def slots_in():
-        tt(T.XF[:], P[5][:, 480:496], T.XD[:], A.min, "P5 XD", "XF")
+            mm([(P[3][:, 480 + 4 * r:484 + 4 * r], [(ID, T.VT[:, TW * r + a:TW * r + b:st]) for a, b, st in ((48, 56, 2), (49, 57, 2), (54, 58, 1))])
+                for r in range(N)], "SH VT", "P3b")
+        mm([(P[0][:, 256:512], [(T.UY[:], T.VT[:]), (T.UZ[:], T.VA[:])])], "UY UZ VT VA", "P0b")
+        mm([(P[1][:, 256:512], [(T.SK[:], T.VT[:])])], "SK VT", "P1b")
+        act(blk(T.RBY, rd, N * TW), P[0][:, 256:512], F.Identity, "P0b cbY", "ry RBY%d" % rd, bias=col("bY"))
+        act(blk(T.RBK, rd, N * TW), P[1][:, 256:512], F.Copy, "P1b", "rk RBK%d" % rd)
 
     def slots(rd):
-        ts(blk(T.XL, rd, 16), T.XF[:], float(-S * rank), None, A.add, None, "XF", "XL%d" % rd)
+        tt(T.XF[:], P[3][:, 480:496], T.XD[:], A.min, "P3b XD", "XF")
+        ts(blk(T.XL, rd, 16), T.XF[:], float(-S * rank), None, A.add, None, "XF", "xl XL%d" % rd)
+        todo.extend((rd, r, key) for r in reversed(range(N)) for key in "YK")
 
-    def place(rd, r, key):
-        win, src = (T.YC, T.RBY) if key == "Y" else (T.YK, T.RBK)
-        c0 = TW * (N * rd + r)
-        cp(win[:, 0:YW].indirect(T.XL[:, 16 * rd + 4 * r:16 * rd + 4 * r + 3]), src[:, c0:c0 + 48], "XL%d RB%s%d W%s" % (rd, key, rd, key), "W" + key)
+    def place(n_, name="put"):
+        for rd, r, key in todo[:n_]:
+            win, src, c0 = T.YC if key == "Y" else T.YK, T["RB" + key], TW * (N * rd + r)
+            cp(win[:, 0:YW].indirect(T.XL[:, 16 * rd + 4 * r:16 * rd + 4 * r + 3]), src[:, c0:c0 + 48],
+               "XL%d RB%s%d W%s" % (rd, key, rd, key), name + " W" + key, scatters=True)
+        del todo[:n_]
+    todo = []
 
-    todo = [(constants, n_) for n_ in range(2)]
+    def stores():
+        todo.sort(key=lambda x: x[2] == "K")
+        place(2 * N, "end")
+        dma("y", [(T.ynodes[rows(o), :], blk(T.NL, o, 32)) for o in peers], "NL", "yn")
+        dma("y", [(T.ycells[:], T.YC[:, 0:S])], "WY", "yc")
+        dma("s", [(T.ykids[:], T.YK[0::4, 0:S])], "WK", "yk")
 
-    def fill(n_):
-        for _ in range(min(n_, len(todo))):
-            job = todo.pop(0)
-            job[0](*job[1:])
+    pin("", (loads,), (cells_out,), (first_constants,), (b_number, range(4)), (halves,), (d_kids, far[0]), (d_kids, far[1]), (d_kids, near_[0]),
+        (d_kids, rank), (lists_out,), (kids_out,), (painted,), (d_pairs, rank, 4), (b_cells, rank, range(4)), (b_number, (4, 5, 6, 7, 0, 1, 2, 3)),
+        (weights,), (b_cells, far[0], range(4, 8)), (b_cells, near_[0], range(4)), (b_number, range(4, 8)), (b_cells, far[1], range(4, 8)),
+        (d_pairs, far[0], 0), (d_pairs, near_[0], 1), (d_pairs, far[1], 2), (d_copies,), (lists,), (table_cc,),
+        (gather, 0, True), (gather, 1, True), (near, 0), (near, 1), (late_constants, 0), (life_a, 0), (life_b, 0), (late_constants, 1), (life_b, 1),
+        (life_a, 1), (hash_mm, 0), (rec_kids, 0), (hash_mm, 1), (rec_pairs,), (rec_kids, 1), (late_constants, 2), (hash_out,), (rec_out,),
+        (rec_copy,), (hash_sum,), (late_constants, 3), (hash_ops,))
 
-    gather(0, True)
-    gather(1, True)
-    rec_start()
-    near(0)
-    near(1)
-    for k in range(2):
-        life_b(k)
-        life_a(k)
-    hash_mm(0)
-    hash_mm(1)
-    rec_pairs()
-    rec_kids(0)
-    rec_kids(1)
-    rec_mm()
-    hash_out()
-    hash_sum()
-    rec_out()
-    hash_ops()
     for rd in range(RO - 1):
-        look()
-        flags(rd)
-        if rd:
-            regroup(rd - 1)
-        pointers(rd)
-        rec_start()
-        if rd:
-            unpack_in()
-            unpack()
-        compact(rd)
-        fill(1)
-        gather(0)
-        gather(1)
-        near(0)
-        keys()
-        all_mm(rd, 1)
-        equal(rd)
-        all_mm(rd, 0)
-        near(1)
-        all_out(1)
-        life_a(0)
-        parcel(rd)
-        update(3)
-        if rd:
-            slots_in()
-        rec_kids(0)
-        all_out(0)
-        hash_mm(0)
-        life_s(1)
-        update(2)
-        if rd:
-            slots(rd - 1)
-        hash_mm(1)
-        rec_pairs()
-        rec_kids(1)
-        rec_mm()
-        hash_out()
-        if rd:
-            unpack_out(rd - 1)
-        update(1)
-        hash_sum()
-        update(0)
-        rec_out()
-        hash_ops()
+        owner = [(regroup, rd - 1), (unpack, rd - 1), (slots, rd - 1)] if rd else [(first_outputs,)]
+        pin(ROUND, (look,), (flags,), (place, 2), (pointers, rd), *owner, (compact, rd), (gather, 0), (gather, 1), (near, 0), (all_mm, rd, 1), (keys,),
+            (winners, 0), (equal,), (life_a, 0), (all_out, 1), (near, 1), (winners, 1), (life_b, 0), (targets,), (life_s, 1),
+            (all_mm, rd, 0), (hash_mm, 0), (update, 3), (all_out, 0), (hash_mm, 1), (hash_out,), (update, 2), (rec_pairs,), (rec_out,),
+            (hash_sum,), (rec_kids, 0), (rec_kids, 1), (rec_copy,), (update, 1), (hash_ops,), (update, 0), (parcel, rd))
+        if rd == 0:
+            pin("", (painted_last,))
 
     rd = RO - 1
-    look()
-    flags(rd)
-    regroup(rd - 1)
-    pointers(rd)
-    nodes_mm(0)
-    unpack_in()
-    compact(rd)
-    parcel(rd)
-    fill(1)
-    keys()
-    unpack()
-    nodes_mm(1)
-    equal(rd)
-    marks()
-    unpack_out(rd - 1)
-    nodes_out()
-    slots_in()
-    fill(1)
-    slots(rd - 1)
-    regroup(rd)
-    unpack_in()
-    unpack(True)
-    unpack_out(rd)
-    fill(len(todo))
-    marks_in()
-    slots_in()
-    slots(rd)
-    dma("y", [(T.ynodes[32 * o:32 * o + 32, :], blk(T.NL, o, 32)) for o in peers], "NL", "yn")
-    for r in reversed(range(N)):
-        place(rd, r, "Y")
-    dma("y", [(T.ycells[:], T.YC[:, 0:S])], "WY", "yc")
-    for r in reversed(range(N)):
-        place(rd, r, "K")
-    dma("s", [(T.ykids[:], T.YK[0::4, 0:S])], "WK", "yk")
+    pin(LAST, (look,), (flags,), (place, 2), (pointers, rd), (regroup, rd - 1), (unpack, rd - 1), (slots, rd - 1), (compact, rd), (parcel, rd), (keys,),
+        (equal,), (marks,), (nodes_out,), (place, 22), (regroup, rd), (unpack, rd), (marks_in,), (slots, rd), (stores,))
+
+    last_of = {}
+    queue = {e: [me for first, at_, me in sorted(pinned) if jobs[me]["e"] == e] for e in "vstgya"}
+    start, free, used = {}, {e: 0.0 for e in queue}, {}
+    count, seen, total, user = {}, {e: {} for e in Q}, {}, {}
+
+    def need(e, tok):
+        if seen[e].get(tok[0], 0) < tok[1]:
+            Q[e].wait_ge(T.sem[tok[0]], tok[1])
+            seen[e][tok[0]] = tok[1]
+
+    def earliest(me):
+        j = jobs[me]
+        if any(i not in start for i in j["pre"]):
+            return 1e12
+        return max([free[j["e"]]] + [start[i] + jobs[i]["ns"] + (jobs[i]["late"] + jobs[i]["busy"] + HOP) * sem for i, sem in j["pre"].items()]
+                   + [t + HOP for b in j["banks"] for x, t in used.get(b, {}).items() if x != j["e"]])
+    for _ in jobs:
+        t, e = min((earliest(q[0]), e) for e, q in queue.items() if q)
+        me = queue[e].pop(0)
+        j = jobs[me]
+        start[me], free[e] = t, t + j["ns"]
+        if e != "a":
+            for i, sem in j["pre"].items():
+                if sem and jobs[i]["kind"] != "rem":
+                    need(e, jobs[i]["tok"])
+            for b in sorted(j["banks"]):
+                for x, tok in user.setdefault(b, {}).items():
+                    if x != e:
+                        need(e, tok)
+            ins = j["fn"]()
+            if j["kind"] == "c":
+                count[e] = count.get(e, 0) + 1
+                ins.then_inc(T.sem["e" + e], 1)
+                j["tok"] = ("e" + e, count[e])
+            for b in j["banks"]:
+                user[b][e], used.setdefault(b, {})[e] = j["tok"], free[e]
+        total[j["tok"][0]] = j["tok"][1]
     for sem, n_ in total.items():
         need("g", (sem, n_))

from concourse.bass import DstId, RemoteDMATransfer
from concourse.mybir import AluOpType as A, ActivationFunctionType as F

N, S, RO = 4, 2048, 4
DW = 9472
YW = 2304
TW = 64
EQW = 16384.0
WON = -16512.0
CYCLE, PE_CYCLE, FIXED, GATHER, SCATTER, HOP = 0.83, 0.42, 55.0, 1.25, 2.5, 120.0
DMA_ISSUE, DMA_LATE, DMA_RATE, CALL, FIRST, FLIGHT, PORT_RATE = 60.0, 2000.0, 250.0, 400.0, 4200.0, 2000.0, 55.0
ROUND = """DD0 DD1 OO C3 C0 put.0 C4 C5 C8 C6 C7 FB C9 RR AT SQ OL CW.0 PL CW.1 HX0 HX1 HX2 HX3 LO.0 LO.1 XF LO.2 xl LO E.0 KC0 E KC1 ZS Ab0 AF put.1 AL
    D.0 D.1 D.2 TI D.3 B0 H DH HL0 H1 HL1
    WG RQ PG VT VA G0 G1 RL1 RL0 Aa0 UA Aa1 Ab1 TF ry RX REC rk
    P2b.0 P4a.0 P5.0 P6a P7a P5.1 P5.2 P2b P7b.0 P4a P6b P1b P3b P0b P7b P7c P5.3 P0a P6c.0 P4 P6c P1a P3.0 P2a P5.4 P3.1"""
LAST = """DD0 DD1 put.0 OO C0 C5 C6 FB C8 RR C3 C7 C4 SQ C9 OL AT CW HX0 HX1 HX2 HX3 LO XF.0 put.1 E.0 KC0 E KC1 ZS ZT0 xl.0 ZT1 put XF.1 xl.1 end
    WG RQ VT.0 PG PN ZK0 ZK1 VA.0 NS rk.0 ry.0 VA.1 VT.1 ry.1 rk.1 yk
    P2b.0 P5.0 P6a P7a P5.1 P5.2 P4a.0 P2b P7b.0 P4a.1 P4a.2 P4a.3 P3b.0 P7b P7c P6b P3 P4a.4 P0b.0 P1b.0 P4a P3b.1 P0b.1 P3b P1b.1"""
f32, bf, i32, u16 = "float32", "bfloat16", "int32", "uint16"
SB = {
    "CS": (2048, bf), "LC": (2048, bf), "KS": (640, i32), "KU": (640, u16), "LK": (640, u16), "YC": (YW, bf), "YK": (YW, f32),
    "KI": (640, i32), "KB": (1152, bf), "KF": (512, f32), "NN": (256, bf), "DS": (1024, bf), "PT": (1024, bf), "RF": (129, bf),
    "B": (512 + 8192, bf), "CC": (8192, bf), "D": (512 + DW, bf), "KL": (512, u16), "WI": (8, i32), "WJ": (8, i32),
    "PI": (8, i32), "BI": (16, i32), "COL": (64, f32), "IF": (192, bf), "RG": (128, bf),
    "RE": (128, bf), "RC": (32, bf), "EU": (512, bf), "IDT": (512, bf), "IDL": (128, bf), "BB": (16, f32),
    "AU": (224, bf), "TM": (64, f32), "RY": (128, bf), "NG": (272, bf), "GW": (224, bf), "KP": (272, bf),
    "KR": (272, bf), "OB": (128, bf), "M2": (128, bf), "WX": (256, bf), "SH": (128, bf),
    "BC": (128, bf), "SK": (128, bf), "UY": (128, bf), "UZ": (128, bf), "RB": (512, bf),
    "NI": (576, f32), "NO": (704, f32), "LW": (576, bf), "EQ": (8, f32), "WR": (896, bf),
    "CW": (576 + 2560, f32), "CT": (192, f32), "OWN": (32, f32), "RT": (128, bf), "CA": (128, bf), "DP": (128, f32),
    "MR": (384, bf), "MK": (384, bf), "RS": (576, bf), "UC": (48, f32), "XD": (16, f32),
    "NF": (256, f32), "PL": (128, u16), "G": (2048, bf), "AB": (1024, bf), "UA": (256, bf), "DD": (1024, bf), "RX": (512, bf),
    "HI": (160, i32), "HF": (64, f32), "HL": (64, u16), "PN": (128, f32), "CL": (320, f32), "PG": (512, bf),
    "FB": (128, bf), "RR": (128, bf), "SQ": (128, f32), "AT": (32, u16), "OL": (32, u16), "WG": (512, bf), "RQ": (512, f32),
    "HX": (192, bf), "KC": (32, bf), "E": (576, bf), "ZS": (576, bf), "AF": (48, f32), "AL": (48, u16), "RL": (768, bf),
    "TS": (RO * N * TW, bf), "TL": (RO * N * TW, bf), "VT": (N * TW, bf), "VA": (N * TW, bf), "ZT": (32, bf), "ZL": (32, bf),
    "RBY": (RO * N * TW, bf), "RBK": (RO * N * TW, f32), "XF": (16, f32), "XL": (RO * 16, u16), "NS": (128, f32), "NL": (128, f32),
}
SCRATCH = {n: ("sbuf", [128, w], d) for n, (w, d) in SB.items()}
SCRATCH.update({"P%d" % k: ("psum", [128, 512], f32) for k in range(8)})
SCRATCH.update({"DLD": ("dram", [4, 128, 256], bf)})
SEMAPHORES = (["eg", "ev", "es", "et", "sent", "gi", "ak", "an"] + ["ac%d" % k for k in range(N)] + ["ad%d" % k for k in range(N)]
              + ["ar%d" % k for k in range(RO)] + ["al%d" % k for k in range(N)] + ["d%d" % k for k in range(40)])


def rank_program(g, core, T, topo):
    rank = T.rank_of(core)
    if rank is None:
        return
    Q = {"g": g, "v": g.vector, "s": g.scalar, "t": g.tensor, "y": g.sync}
    V, SE, PE = g.vector, g.scalar, g.tensor
    P = [T["P%d" % k] for k in range(8)]
    jobs, wrote, read, group = [], {}, {}, {}
    ndma, pinned = [0], []
    size_of = lambda a: 2 if "16" in str(a.dtype) else 4
    in_psum = lambda a: a.name in [x.name for x in P]

    def job(e, fn, r, w, ns, late=0.0, kind="c", busy=0.0, tok=None):
        keys = lambda x: [k + z for k in x.split() for z in ("abc" if k[0] == "P" and len(k) == 2 and k[1].isdigit() else ("",))]
        name = (w.split() + [""])[0]
        r, w, me, pre = keys(r), keys(w), len(jobs), {}
        for k in r:
            if k in wrote:
                pre[wrote[k]] = True
        for k in w:
            for i in read.get(k, []):
                pre[i] = pre.get(i, False) or jobs[i]["e"] != e or e != "t"
            if k in wrote:
                i = wrote[k]
                pre[i] = pre.get(i, False) or jobs[i]["e"] != e or kind != "c" or jobs[i]["kind"] != "c"
        for k in r:
            read.setdefault(k, []).append(me)
        for k in w:
            wrote[k], read[k] = me, []
        banks = {k[:2] for k in r + w if k[0] == "P" and k[1].isdigit()}
        jobs.append(dict(e=e, fn=fn, pre=pre, ns=ns, late=late, kind=kind, busy=busy, tok=tok, banks=banks, name=name))
        return me

    def pin(order, *steps):
        first, met = len(jobs), {}
        for step in steps:
            step[0](*step[1:])
        place = {n_: x for x, n_ in enumerate(order.split())}
        for me in range(first, len(jobs)):
            j = jobs[me]
            met[j["name"]] = met.get(j["name"], -1) + 1
            j["name"] += ".%d" % met[j["name"]]
            pinned.append((first, place.get(j["name"], place.get(j["name"].split(".")[0], 0)), me))

    def dma(e, pairs, r, w):
        sem = "d%d" % ndma[0]
        ndma[0] += 1

        def run():
            for o, i in pairs:
                Q[e].dma_start(o, i).then_inc(T.sem[sem], 16)
        busy = sum(size_of(o) * o.shape[0] * o.shape[-1] / DMA_RATE for o, i in pairs)
        job(e, run, r, w, DMA_ISSUE * len(pairs), DMA_LATE, "dma", busy, (sem, 16 * len(pairs)))

    def masks(src):
        others = [o for o in range(N) if o != src]
        en = {o: topo.engines(T.cores[src], T.cores[o]) for o in others}
        least = min(len(v) for v in en.values())
        far = [o for o in others if len(en[o]) == least]
        near_ = [o for o in others if o not in far]
        out, used = {}, set()
        for grp in (far, near_):
            for n_, o in enumerate(grp):
                free = [x for x in en[o] if x not in used]
                k = 1
                while 2 * k <= len(free) // (len(grp) - n_):
                    k *= 2
                out[o] = free[:k]
                used.update(free[:k])
        return out
    eng = {o: masks(o) for o in range(N)}
    peers = [o for o in range(N) if o != rank]
    sent, marks_ = [0], [0]
    off_chip = lambda a, b: T.cores[b] not in topo.cores_of(T.cores[a])
    alone = lambda a, b: topo.engines(T.cores[a], T.cores[b]) if off_chip(a, b) else eng[a][b]

    def send(src, dst, sem, r, to=None, first=0.0):
        trs, n_far = [], 0
        for o in to or peers:
            rid, pid = topo.addr(T.cores[o], core)
            en = alone(rank, o) if to else eng[rank][o]
            trs.append(RemoteDMATransfer(dst_ids=[DstId(rid=rid, pnc=pid)], dma_engine_mask=sum(1 << x for x in en),
                                         remote_sem=T.sem[sem], src=src(o), dst=dst(rank)))
            sent[0] += len(en)
            n_far += off_chip(rank, o)
        a = src(peers[0])
        sent[1:] = [job("g", lambda: g.remote_dma_fused(trs, local_sem=T.sem.sent), r, "", first + CALL, FLIGHT, "rem",
                        n_far * 128 * a.shape[1] * size_of(a) / PORT_RATE, ("sent", sent[0]))]

    def arrival(key, sem, from_, one=False):
        n_ = sum(len(alone(o, rank) if one else eng[o][rank]) for o in from_)
        jobs[job("a", None, "", key, 1.0, 0.0, "arr", 0.0, (sem, n_))]["pre"][sent[1]] = True

    def issued(key):
        marks_[0] += 1
        job("g", lambda: g.sem_inc(T.sem.gi, 1), "", key, 20.0, 0.0, "inc", 0.0, ("gi", marks_[0]))

    def cycles(n, sides, two=False):
        if two:
            return FIXED + CYCLE * n * (1 if any(in_psum(a) for a in sides[1:]) else 2)
        return FIXED + CYCLE * n * (0.5 if all(size_of(a) == 2 for a in sides) else 1)

    def ts(o, a, s1, s2, o0, o1, r, w):
        if o1 is None:
            job("v", lambda: V.tensor_scalar(o, a, s1, None, o0), r, w, cycles(o.shape[1], (o, a)))
        else:
            job("v", lambda: V.tensor_scalar(o, a, s1, s2, o0, o1), r, w, cycles(o.shape[1], (o, a)))

    def tt(o, a, b, o0, r, w, gathers=False):
        job("v", lambda: V.tensor_tensor(o, a, b, o0), r, w, FIXED + GATHER * o.shape[1] if gathers else cycles(o.shape[1], (o, a, b), True))

    def cp(o, a, r, w, gathers=False, scatters=False):
        ns = FIXED + GATHER * o.shape[1] if gathers else FIXED + SCATTER * a.shape[1] if scatters else cycles(o.shape[1], (o, a))
        job("v", lambda: V.tensor_copy(o, a), r, w, ns)

    def ms(o, c, w, r=""):
        job("v", lambda: V.memset(o, c), r, w, cycles(o.shape[1], (o,)))

    def scan(o, a, b, init, o0, o1, r, w):
        job("v", lambda: V.tensor_tensor_scan(o, a, b, init, o0, o1), r, w, cycles(o.shape[1], (o, a, b)))

    def act(o, a, fn, r, w, gathers=False, **kw):
        job("s", lambda: SE.activation(o, a, fn, **kw), r, w, FIXED + 15 + (GATHER if gathers else CYCLE) * o.shape[1])

    def matmuls(calls, r, w):
        def run():
            for c in calls:
                ins = PE.matmul(*c)
            return ins
        me = job("t", run, r, w, sum(max(64, x.shape[1]) * PE_CYCLE * (size_of(x) // 2) ** 2 for o, l, x, a, b in calls))
        for b in {c[0].name for c in calls}:
            if b in group:
                jobs[me]["pre"].setdefault(group[b], False)
            group[b] = me

    def mm(items, r, w, first=True, last=True):
        matmuls([(o, l, x, first and n_ == 0, last and n_ == len(prs) - 1) for o, prs in items for n_, (l, x) in enumerate(prs)], r, w)

    def more_mm(items, r, w, last=False, first=False):
        matmuls([(o, l, x, first and n_ == 0, last and n_ == len(items) - 1) for n_, (o, l, x) in enumerate(items)], r, w)

    def iota(o, pat, base, cm, w, r=""):
        job("g", lambda: g.iota(o, pat, base, cm, allow_small_or_imprecise_dtypes=True), r, w, 130 + 2 * CYCLE * o.shape[1])

    def sel(o, a, pat, cmp, fill, base, cm, r, w):
        job("g", lambda: g.affine_select(o, a, pat, cmp, fill, base, cm), r, w, 170 + 2 * CYCLE * o.shape[1])

    def move(e, o, a, r, w):
        if e == "s":
            act(o, a, F.Copy, r, w)
        else:
            sel(o, a, [[0, a.shape[1]]], A.is_equal, 0.0, 0, 0, r, w)

    def fill_g(t, c, key):
        iota(t, [[0, t.shape[1]]], c, 0, key)

    def paint(t, pat, base, w, key, new=False, cmp=A.not_equal, cm=1):
        sel(t, T.B[:, 0:t.shape[1]] if new else t, pat, cmp, w, base, cm, "B~" if new else key, key)

    def zero(t, key):
        for c in range(0, t.shape[1], 512):
            n_ = min(512, t.shape[1] - c)
            act(t[:, c:c + n_], T.B[:, 0:n_], F.Copy, "B~", key)

    cols = {}

    def col(name):
        if name not in cols:
            cols[name] = len(cols)
        return T.COL[:, cols[name]:cols[name] + 1]

    def cts(name, c, s1, s2, o0, o1=None):
        r = " ".join("c" + x for x in (c, s1, s2) if isinstance(x, str))
        ts(col(name), col(c), col(s1) if isinstance(s1, str) else s1, col(s2) if isinstance(s2, str) else s2, o0, o1, r, "c" + name)

    def line(o, a, scale, bias, r, w):
        r += "".join(" c" + x for x in (scale, bias) if isinstance(x, str))
        ts(o, a, col(scale) if isinstance(scale, str) else scale, col(bias) if isinstance(bias, str) else bias, A.mult, A.add, r, w)

    def onehot(out, row, rk, tc, wc, key):
        if isinstance(wc, str):
            ts(out, row, col(tc), col(wc), A.is_equal, A.mult, "%s c%s c%s" % (rk, tc, wc), key)
        else:
            ts(out, row, col(tc), wc, A.is_equal, A.mult, "%s c%s EQ" % (rk, tc), key)

    rows = lambda r: slice(32 * r, 32 * r + 32)
    blk = lambda t, o, w: t[:, o * w:(o + 1) * w]
    srcs = [rank] + sorted(peers, key=lambda o: (off_chip(rank, o), topo.die(T.cores[o]) != topo.die(core)))
    near_, far = srcs[1:2], srcs[2:]
    ID, REC = T.SH[:], T.D[:, 0:512]
    IF = lambda a, b: T.IF[:, 64 + a:64 + b]
    chain = lambda n_, i: T.LW[:, 144 * n_ + 15 - i:144 * n_ + 143 - i]
    shift = lambda r, d: T.WR[:, 224 * r + 96 - 32 * d:224 * r + 224 - 32 * d]
    allb, allc, alld = " ".join("B%d" % b for b in range(16)), "CC0 CC1 CC2", "Dw0 Dw1 Dw2 Dw3 Dp0 Dp1 Dp2 Dp3"

    def loads():
        for o in far:
            dma("y", [(blk(T.CS, o, 512), T.cells[rows(o), :])], "", "CS%d" % o)
        dma("y", [(blk(T.KS, o, 128), T.kids[8 * o:8 * o + 8, :]) for o in range(N)], "", "KS")
        dma("y", [(T.NN[:, 0:128], T.cells[0::16, :])], "", "N0")
        dma("y", [(blk(T.CS, o, 512), T.cells[rows(o), :]) for o in near_], "", "CS%d" % near_[0])
        dma("y", [(blk(T.KS, 16 + o, 32), T.nodes[rows(o), :]) for o in range(N)], "", "KN")
        dma("y", [(blk(T.LC, rank, 512), T.cells[rows(rank), :])], "", "LC%d" % rank)
        dma("y", [(T.WI[rows(q), 0:1], T.wt[rows(rank), :]) for q in range(4)], "", "WI")

    def cells_out():
        iota(T.PI[:, 0:1], [[0, 1]], 0, 1, "PI")
        iota(T.IF[:], [[1, 192]], -64, 0, "IF")
        for s in range(2):
            iota(blk(T.RE, s, 64), [[16, 2], [4, 2], [4, 16]], 64 * s, -1, "RE")
        iota(T.RE[:, 3::4], [[0, 32]], 1000, 0, "RE1", "RE")
        for a in range(2):
            for b in range(2):
                iota(T.RE[:, 12 + 2 * a + b::16], [[64, 2], [32, 2], [8, 2]], 4 * (4 * a + b), -1, "RE0", "RE1" if a + b == 2 else "RE")
        send(lambda o: blk(T.CS, o, 512), lambda o: blk(T.LC, o, 512), "ac%d" % rank, "CS%d" % far[0], far[:1], FIRST)
        arrival("LC%d" % far[0], "ac%d" % far[0], far[:1], True)
        send(lambda o: blk(T.CS, o, 512), lambda o: blk(T.LC, o, 512), "ac%d" % rank, "CS%d CS%d" % (far[1], near_[0]), far[1:] + near_, FIRST / 4)
        for o in far[1:] + near_:
            arrival("LC%d" % o, "ac%d" % o, [o], True)

    def first_constants():
        ms(T.B[:, 0:512], 0.0, "B~")
        for t in "IDL NI GW AU LW WX KR".split():
            zero(T[t], t)
        fields = [("p", 0, 127), ("j", 0, 15), ("lo2", 0, 3), ("a2", 2, 3), ("b0", 0, 1), ("b1", 1, 1), ("b2", 2, 1), ("b3", 3, 1), ("b4", 4, 1),
                  ("b5", 5, 1), ("x112", 0, 112), ("x120", 0, 120), ("h3", 1, 7)]
        for n_, (name, sh, mk) in enumerate(fields):
            col(name)
            ts(T.BI[:, n_:n_ + 1], T.PI[:, 0:1], sh, mk, A.logical_shift_right, A.bitwise_and, "PI", "BI")
        for row, c0 in ((0, 3), (32, 7), (64, 11)):
            ms(T.IDL[row:row + 1, c0::16], 1.0, "IDL0", "IDL")
        for x in range(2):
            ms(T.IDT[64:96, x::2], float(x), "IDT1")
        cp(T.COL[:, 0:len(fields)], T.BI[:, 0:len(fields)], "BI", " ".join("c" + x[0] for x in fields))
        for c in range(4):
            ms(T.IDT[32:64, 128 * c:128 * c + 128], float(c), "IDT1")
            cp(T.IDT[0:32, 128 * c:128 * c + 128], T.IF[0:32, 64:192], "IF", "IDT0")
        cts("tRF", "lo2", 2.0, "x120", A.mult, A.add)
        cts("wRF", "b2", 15.0, 1.0, A.mult, A.add)
        cts("tKP", "x112", "h3", None, A.add)
        cts("tNG", "b4", 64.0, "h3", A.mult, A.add)
        cts("bD", "b3", 144.0, -144.0, A.mult, A.add)
        ts(T.EQ[:, 0:2], IF(0, 2), col("b0"), None, A.is_equal, None, "IF cb0", "EQ")
        cts("hb", "lo2", 2.5, -14.0, A.is_lt, A.mult)
        cts("i74", "j", 7.0, 4.0, A.is_equal, A.mult)
        cts("mid", "a2", 3.0, None, A.is_equal)
        cts("bh", "a2", 2.5, "hb", A.is_lt, A.mult)
        for e in range(2):
            onehot(blk(T.NG, e, 136), IF(-8, 128), "IF", "tNG", T.EQ[:, e:e + 1], "NG")
            onehot(blk(T.KP, e, 136), IF(-8, 128), "IF", "tKP", T.EQ[:, e:e + 1], "KP")
        onehot(T.RF[:], IF(-1, 128), "IF", "tRF", "wRF", "RF")
        line(T.BB[:], IF(0, 16), "i74", "bh", "IF", "BB")
        for u in range(4):
            ts(blk(T.EU, u, 128), T.RE[:], float(-u), None, A.is_equal, None, "RE0 RE1", "EU")

    def b_number(banks):
        for bank in banks:
            mm([(P[bank][:], [(T.IDL[0:96, :], T.IDT[0:96, :])])], "IDL0 IDT0 IDT1", "P%d" % bank, True, False)

    def b_cells(o, banks):
        for u, bank in enumerate(banks):
            b = 4 * o + u
            mm([(P[bank][:], [(blk(T.EU, u, 128), blk(T.LC, o, 512))])], "EU LC%d" % o, "P%d" % bank, False, True)
            if u % 2:
                ts(blk(T.B, b + 1, 512), P[bank][:], T.BB[:, b:b + 1], 0.0, A.add, A.max, "P%d BB" % bank, "B%d" % b)
            else:
                act(blk(T.B, b + 1, 512), P[bank][:], F.Relu, "P%d BB" % bank, "B%d" % b, bias=T.BB[:, b:b + 1])

    def halves():
        ts(T.KI[:, 0:512], T.KS[:, 0:512], 127, None, A.bitwise_and, None, "KS", "KI")
        ts(T.KB[:, 0:512], T.KS[:, 0:512], 2.0 ** -7, 143.504, A.mult, A.add, "KS", "KB0")
        cp(T.KB[:, 640:1152], T.KI[:, 0:512], "KI", "KB1")
        ts(T.NN[:, 128:256], T.NN[:, 0:128], 0.0, None, A.min, None, "N0", "NN")

    def lists_out():
        for o in peers:
            cp(T.KU[:, 160 * o:160 * o + 128], blk(T.KS, o, 128), "KS", "KU")
        ts(T.KI[:, 512:640], T.KS[:, 512:640], 127, None, A.bitwise_and, None, "KN", "KJ")
        ts(T.KB[:, 512:640], T.KS[:, 512:640], 2.0 ** -7, 143.504, A.mult, A.add, "KN", "KB2")
        ts(T.NF[:, 0:128], T.KI[:, 512:640], 64.0, -144.0, A.mult, A.add, "KJ", "NF0")
        cp(T.KL[:, rank::4], blk(T.KS, rank, 128), "KS", "KL")
        tt(T.NF[:, 128:256], T.NF[:, 0:128], T.KB[:, 512:640], A.add, "NF0 KB2", "NF1")
        for o in peers:
            cp(T.KU[:, 160 * o + 128:160 * o + 160], blk(T.NF, 4 + o, 32), "NF1", "KU")
        send(lambda o: blk(T.KU, o, 160), lambda o: blk(T.LK, o, 160), "ak", "KU")
        arrival("LK", "ak", peers)

    def d_kids(o):
        more_mm([(P[4 + o][:, 128 * e + x:128 * e + 128:2], T.NG[rows(o), 136 * e + 8 - 8 * x:136 * e + 136 - 8 * x], T.NN[rows(o), 128 + x:256:2])
                 for x in range(2) for e in range(2)], "NG NN", "P%d" % (4 + o), False, True)
        more_mm([(blk(P[4 + o], e, 128), T.KP[:, 136 * e + 8 - 8 * x:136 * e + 136 - 8 * x], T.KB[:, 640 * x + 128 * o:640 * x + 128 * o + 128])
                 for x in range(2) for e in range(2)], "KP KB0 KB1", "P%d" % (4 + o), True)
        act(blk(T.DS, o, 256), P[4 + o][:, 0:256], F.Identity, "P%d cbD" % (4 + o), "DS%d" % o, bias=col("bD"))

    at = lambda o, a, n_: T.D[a:a + n_, 512 + S * o:512 + S * o + S]

    def window(o, x, src, r, w, groups):
        dma("y", [(at(o, 16 * a + 8 * x, 8), src(slice(64 * (a % 2), 64 * (a % 2) + 64))) for a in groups], r, w)

    def d_pairs(o, bank):
        mm([(P[bank][:, 0:256], [(T.RF[:, 1 - h:129 - h], blk(T.LC, 2 * o + h, 256)) for h in range(2)])], "RF LC%d" % o, "P%d" % bank)
        act(blk(T.PT, o, 256), P[bank][:, 0:256], F.Copy, "P%d" % bank, "PT%d" % o)
        window(o, 0, lambda q: T.PT[q, 256 * o:256 * o + 256], "GO PT%d" % o, "Dp%d" % o, range(2))

    def kids_out():
        send(lambda o: blk(T.DS, o, 256), lambda o: T.DLD[o], "ad%d" % rank, " ".join("DS%d" % o for o in peers))
        for o in peers:
            arrival("DLD%d" % o, "ad%d" % o, [o])
        issued("GO")
        window(rank, 1, lambda q: T.DS[q, 256 * rank:256 * rank + 256], "GO DS%d" % rank, "Dw%d" % rank, range(2))

    def d_copies():
        dma("y", [(at(rank, 32 * y, 32), at(rank, 0, 32)) for y in range(1, 4)], "Dw%d Dp%d" % (rank, rank), "Dw%d Dp%d" % (rank, rank))
        for o in (far[0], near_[0], far[1]):
            dma("y", [(at(o, 16 * a, 8), at(o, 16 * (a % 2), 8)) for a in range(2, 8)], "Dp%d" % o, "Dp%d" % o)
        for o in srcs[1:]:
            window(o, 1, lambda q: T.DLD[o, q, :], "DLD%d" % o, "Dw%d" % o, range(8))

    def painted():
        for x in range(4):
            for s in range(2):
                c0 = 144 * x + 12 + 64 * s
                paint(T.NI[:, c0:c0 + 64], [[1, 4], [1000, 4], [-8, 4]], -(64 * s + 32 * (x // 2) + 4 * (x % 2) + 3), 1.0, "NI")
        for s in range(2):
            for x in range(2):
                paint(T.GW[:, 104 + 16 * s + x:112 + 16 * s:2], [[16, 4]], -(64 * s + 55 - 4 * x), 1.0, "GW")
        for x in range(2):
            paint(T.RY[:], [[-16, 8], [1000, 2], [-2, 8]], -x, (1.0, 16.0)[x], "RY", x == 0)
        iota(T.CA[:], [[0, 32], [-1, 4]], 4, 0, "CA")
        for c0, row, w in ((0, 7, 512.0), (1, 3, 512.0), (1, 11, -1024.0), (129, 8, 512.0), (129, 9, -512.0)):
            paint(T.WX[:, c0:c0 + 127:16], [[-16, 8]], -row, w, "WX")
        for jj, c0 in enumerate((0, 64, 192)):
            iota(T.MR[:, c0:c0 + 64 * (jj + 1)], [[0, 4], [1, 16 * (jj + 1)]], -16 * jj, 0, "MR")
        paint(T.M2[:], [[-16, 8], [0, 16]], -15, 1.0, "M2", True, A.is_gt)
        paint(T.RT[:], [[0, 4], [1, 32]], 0, 1.0, "RT", True, A.is_equal, 0)
        paint(T.M2[:], [[-1, 128]], 0, 0.0, "M2", False, A.is_gt)
        paint(T.M2[:], [[-1, 128]], 0, 1024.0, "M2")
        for c0, ws in ((0, (1.0, 64.0)), (136, (128.0, 1.0))):
            for x in range(2):
                paint(T.KR[:, c0 + 3:c0 + 131:4], [[-16, 2], [2, 4], [-32, 4]], -14 - x, ws[x], "KR")
        paint(T.RB[:], [[-32, 4], [0, 4], [-1, 32]], 0, 1.0, "RB", True)
        for rd in range(RO):
            fill_g(T.TL[:, TW * (N * rd + rank) + 48:TW * (N * rd + rank + 1)], 0, "TL~")
        fill_g(T.WR[:], 0, "WR")
        for t, key in ((T.SK, "SK"), (T.UY, "UY"), (T.UZ, "UZ")):
            fill_g(t[:], 0, key)
        for r in range(N):
            paint(T.WR[:, 224 * r + 96:224 * r + 128], [[-1, 32]], -32 * r, 1.0, "WR")
        for x in range(2):
            paint(T.SK[:, 0::4], [[-16, 8], [-2, 4]], -8 - x, (128.0, 1.0)[x], "SK")
            paint(T.UZ[:, x::2], [[-16, 8], [-1, 8]], 0, (-16.0, 1.0)[x], "UZ")
        paint(T.UY[:, 0::2], [[-16, 8], [-1, 8]], 0, 1.0, "UY")

    def painted_last():
        fill_g(T.NO[:], 0, "NO")
        fill_g(T.ZT[:], 0, "ZT~")
        fill_g(blk(T.ZL, rank, 8), 0, "ZL~")
        for r in range(N):
            for s in range(2):
                c0 = 176 * r + 36 + 64 * s
                paint(T.NO[:, c0:c0 + 32], [[-1, 4], [1000, 2], [16, 4]], -(64 * s + 48 + 4 * r), 1.0, "NO")

    def weights():
        ts(T.RG[:], IF(0, 128), 1.0 / 16, 143.53, A.mult, A.add, "IF", "RG")
        ts(T.RC[:, 0:16], IF(0, 16), 0.25, 143.6, A.mult, A.add, "IF", "RC0")
        cts("g144", "x112", 1.0 / 16, 144.0, A.mult, A.add)
        for x, (lo, hi, bit) in enumerate((("a2", "b5", "b1"), ("lo2", "b4", "b0"))):
            cts("n%d" % x, hi, 3.0, lo, A.mult, A.subtract)
            cts("d%d" % x, lo, bit, hi, A.subtract, A.subtract)
        ts(T.TM[:, 48:64], T.RC[:, 0:16], -4.0, 720.0, A.mult, A.add, "RC0", "TM1")
        onehot(T.OB[:], T.RG[:], "RG", "g144", 1.0, "OB")
        cts("wh", "bh", -1.0, 2.0 ** -13, A.is_lt, A.mult)
        tt(T.RC[:, 16:32], T.TM[:, 48:64], IF(0, 16), A.add, "TM1 IF", "RC")
        for x in range(2):
            cts("x%d" % x, "d%d" % x, "mid", "n%d" % x, A.mult, A.add)
        cts("wm", "mid", "wh", None, A.subtract)
        ts(T.WJ[:, 0:1], T.WI[:, 0:1], 6, None, A.logical_shift_right, None, "WI", "WJ")
        ts(T.WJ[:, 1:2], T.WI[:, 0:1], 63, None, A.bitwise_and, None, "WI", "WJ")
        for x in range(2):
            ts(blk(T.TM, x, 16), blk(T.RC, x, 16), col("x%d" % x), -146.0, A.add, A.add, "RC0 RC cx%d" % x, "TM0")
        ts(col("whi"), T.WJ[:, 0:1], 64.0, None, A.mult, None, "WJ", "cwhi")
        cp(col("wlo"), T.WJ[:, 1:2], "WJ", "cwlo")
        tt(T.TM[:, 32:64], T.TM[:, 0:32], T.TM[:, 0:32], A.mult, "TM0", "TM1")
        cts("s8", "j", 7.5, EQW, A.is_lt, A.mult)
        cts("s10", "j", 10.0, 48 * EQW, A.is_equal, A.mult)
        tt(T.TM[:, 0:16], T.TM[:, 32:48], T.TM[:, 48:64], A.add, "TM1", "TM0")
        cts("s11", "j", 10.5, -16 * EQW, A.is_lt, A.mult)
        cts("r0", "j", 0.0, None, A.is_equal)
        ts(T.TM[:, 32:48], T.TM[:, 0:16], 2.5, col("wh"), A.is_lt, A.mult, "TM0 cwh", "TM1")
        ts(T.TM[:, 48:64], T.TM[:, 0:16], 0.0, col("wm"), A.is_equal, A.mult, "TM0 cwm", "TM1")
        cts("r1", "j", 1.0, 512.0, A.is_equal, A.mult)
        cts("s9", "s10", "s11", None, A.add)
        for s in range(2):
            h = slice(64 * s, 64 * s + 64)
            tt(T.AU[h, 96 + 16 * s:112 + 16 * s], T.TM[h, 32:48], T.TM[h, 48:64], A.add, "TM1 AU", "AU1")
        cts("k0", "r0", 0.25, None, A.mult)
        cts("wS", "s9", "b3", "s8", A.mult, A.add)
        for o in range(N):
            cts("u%d" % o, "r0", 512.0 * (64 + o), 65536.0, A.mult, A.add)
        cts("wkey", "r1", 2.0 ** -18, "k0", A.mult, A.add)
        for o in range(N):
            line(T.CT[:, o::4], IF(0, 48), "r1", "u%d" % o, "IF", "CT")
        dma("y", [(blk(T.CW, x, 192), T.CT[:]) for x in range(RO)], "CT", "CW")
        for n_, c in enumerate(("whi", "wlo", "wS", "wkey")):
            line(T.LW[:, 144 * n_ + 15:144 * n_ + 143:16], T.OB[:, 0::16], c, 0.0, "OB LW", "LW%d" % n_)
        cts("mb3", "b3", -1.0, None, A.mult)
        onehot(T.SH[:], IF(0, 128), "IF", "p", 1.0, "SH")

    def late_constants(n_):
        if n_ == 0:
            ms(T.RS[:], 0.0, "RS0")
            ms(T.E[:], WON, "E")
            ms(T.DP[:], 1e6, "DP0")
        if n_ == 1:
            cts("jd", "j", -1.0, 2048.0, A.mult, A.add)
            cts("big", "r1", 65536.0, "b3", A.add, A.add)
            ms(T.RS[:, 0::48], WON, "RS", "RS0")
            cts("ju", "j", 8704.0, None, A.add)
            cts("jx", "j", float(S * (rank + 1)), None, A.add)
        if n_ == 2:
            ms(T.TS[:], 0.0, "TS~")
            line(T.OWN[:], IF(-32, 0), 16.0, "j", "IF", "OWN")
            line(T.DP[:, 0::4], IF(0, 32), -16.0, "jd", "IF DP0", "DP")
            line(T.BC[:], T.OB[:], "wkey", 0.0, "OB", "BC")
            line(T.UC[:], IF(0, 48), 16.0, "ju", "IF", "UC")
            line(T.XD[:], IF(0, 16), 16.0, "jx", "IF", "XD")
            cts("bY", "b0", -2448.0, 2304.0, A.mult, A.add)
        if n_ == 3:
            ts(T.MK[:], T.MR[:], col("j"), 16384.0, A.is_ge, A.mult, "MR cj", "MK")

    def first_outputs():
        cp(T.KF[:], T.KS[:, 0:512], "KS", "put KF")
        dma("y", [(T.YC[:, 0:S], T.cells[:])], alld, "WY")
        dma("y", [(T.YK[16 * q:16 * q + 16:4, 0:S], T.KF[64 * (q % 2):64 * (q % 2) + 64, 128 * (q // 2):128 * (q // 2) + 128]) for q in range(8)], "KF", "WK")

    def lists():
        for o in peers:
            cp(T.KL[:, o::4], T.LK[:, 160 * o:160 * o + 128], "LK", "KL")
        for o in peers:
            cp(blk(T.NF, 4 + o, 32), T.LK[:, 160 * o + 128:160 * o + 160], "LK", "NF1")

    def table_cc():
        act(T.CC[:, 0:4096], T.B[:, 512:8704].indirect(T.KL[:, 0:256]), F.Copy, allb + " KL", "CC0", gathers=True)
        cp(T.CC[:, 4096:6144], T.B[:, 512:8704].indirect(T.KL[:, 256:384]), allb + " KL", "CC1", gathers=True)
        mm([(P[7][:, 64 * (x % 2) + x // 2:64 * (x % 2) + 64:2], [(T.NI[:, 144 * x + 12 - 4 * r:144 * x + 140 - 4 * r], blk(T.NF, 4 + r, 32)) for r in range(N)])
            for x in range(4)], "NI NF1", "P7")
        cp(T.CC[:, 6144:8192], T.B[:, 512:8704].indirect(T.KL[:, 384:512]), allb + " KL", "CC2", gathers=True)
        cp(T.PL[:], P[7][:, 0:128], "P7", "PL")

    half = lambda k, a: T.G[:, 1024 * k + a:1024 * k + 1024:16]

    def gather(k, both=False):
        if both:
            cp(blk(T.G, 2 * k, 512), T.CC[:, 0:8192].indirect(blk(T.PL, 2 * k, 32)), allc + " PL", "Gv%d" % k, gathers=True)
            act(blk(T.G, 2 * k + 1, 512), T.CC[:, 0:8192].indirect(blk(T.PL, 2 * k + 1, 32)), F.Copy, allc + " PL", "G%d" % k, gathers=True)
        else:
            act(blk(T.G, k, 1024), T.CC[:, 0:8192].indirect(blk(T.PL, k, 64)), F.Copy, allc + " PL", "G%d Gv%d" % (k, k), gathers=True)

    def near(k):
        mm([(P[k][:, i:256:4], [(T.AU[:, 96 - 32 * r:224 - 32 * r], half(k, 4 * r + i)) for r in range(N)]) for i in range(4)],
           "AU1 G%d Gv%d" % (k, k), "P%da" % k)

    def life_a(k):
        act(T.AB[:, k:512:2], P[k][:, 0:256], F.Relu, "P%da" % k, "Aa%d" % k, bias=-(1.0 + 2.0 ** -10))

    def life_b(k):
        ts(T.AB[:, 512 + k::2], P[k][:, 0:256], 2.0 ** -12, 15.0, A.is_equal, A.mult, "P%da" % k, "Ab%d" % k)

    def life_s(k):
        act(T.UA[:], P[k][:, 0:256], F.Abs, "P%da" % k, "UA", scale=8192.0, bias=-2.0)
        life_a(k)
        act(T.AB[:, 512 + k::2], T.UA[:], F.Relu, "UA", "Ab%d" % k, scale=-15.0, bias=15.0)

    def hash_mm(k):
        mm([(P[2][:, 0:64], [(chain(n_, i), T.AB[:, i::16]) for i in range(k, 16, 2) for n_ in range(2)])],
           "LW0 LW1 Aa0 Ab0" + (" Aa1 Ab1" if k else ""), "P2a", k == 0, k == 1)

    def rec_kids(k):
        more_mm([(P[3][:, 2 * i + k::8], T.GW[:, 96 - 32 * r:224 - 32 * r], half(k, 4 * r + i)) for i in range(4) for r in range(N)],
                "GW G%d Gv%d" % (k, k), "P3", k == 1, k == 0)

    def rec_copy():
        act(REC, P[3][:], F.Copy, "P3", "REC")

    def rec_pairs():
        mm([(P[5][:], [(T.RY[:], T.AB[:, 0:512]), (T.RY[:], T.AB[:, 512:1024])])], "RY Aa0 Aa1 Ab0 Ab1", "P5")

    def rec_out():
        act(T.RX[:], P[5][:], F.Identity, "P5 cmb3", "RX", bias=col("mb3"))

    H, H1, OO, TI, B0 = (blk(T.HI, x, 32) for x in range(5))
    DH, TF = blk(T.HF, 0, 32), blk(T.HF, 1, 32)

    def hash_out():
        act(TF, P[2][:, 0:32], F.Copy, "P2a", "TF")

    def hash_sum():
        tt(TI, TF, P[2][:, 32:64], A.add, "TF P2a", "TI")

    def hash_ops():
        ts(B0, TI, 1, None, A.bitwise_and, None, "TI", "B0")
        ts(H, TI, 8191, None, A.bitwise_and, None, "TI", "H")
        ts(DH, B0, 2.0, -1.0, A.mult, A.add, "B0", "DH")
        cp(T.HL[:, 0:32], H, "H", "HL0")
        tt(H1, H, DH, A.subtract, "H DH", "H1")
        cp(T.HL[:, 32:64], H1, "H1", "HL1")

    c32 = lambda x: blk(T.CL, x, 32)
    S0, S1 = P[6][:, 0:32], P[7][:, 0:32]

    def look():
        act(T.WG[:], T.B[:, 512:8704].indirect(T.HL[:, 0:32]), F.Copy, allb + " HL0", "WG", gathers=True)
        mm([(P[2][:, 256:384], [(ID, T.CA[:])])], "SH CA", "P2b", True, False)
        mm([(P[5][:], [(ID, T.RX[:]), (ID, REC)])], "SH RX REC", "P5", True, False)
        mm([(P[5][:], [(blk(T.WX, 0, 128), T.WG[:])])], "WX WG", "P5", False, False)
        for x in range(2):
            tt(blk(T.DD, x, 512), T.D[:, 512:8704].indirect(blk(T.HL, x, 32)), T.RX[:], A.not_equal, "D %s RX HL%d" % (alld, x), "DD%d" % x, True)
            mm([((S0, S1)[x], [(chain(2, i), T.DD[:, 512 * x + i:512 * x + 512:16]) for i in range(16)])], "LW2 DD%d" % x, "P%da" % (6 + x))
        mm([(P[5][:], [(blk(T.WX, 1, 128), T.DD[:, 0:512])])], "WX DD0", "P5", False, True)
        act(T.RQ[:], P[5][:], F.Identity, "P5 cbig", "RQ", bias=col("big"))

    def flags():
        tt(c32(3), H, S0, A.subtract, "P6a H", "C3")
        ts(c32(0), S0, -1.0, 24.5 * EQW, A.mult, A.add, "P6a", "C0")
        ts(OO, TI, 11, 3, A.logical_shift_right, A.bitwise_and, "TI", "OO")
        tt(c32(4), c32(3), T.OWN[:], A.max, "C3 OWN", "C4")
        tt(c32(5), S1, c32(0), A.subtract, "P7a C0", "C5")
        tt(c32(8), H1, S1, A.subtract, "P7a H1", "C8")
        tt(c32(6), c32(5), OO, A.min, "C5 OO", "C6")
        tt(c32(7), S0, c32(8), A.min, "P6a C8", "C7")
        for o in range(N):
            ts(blk(T.FB, o, 32), c32(6), float(o), 4.0, A.is_equal, A.mult, "C6", "FB")
        tt(c32(9), c32(7), c32(4), A.max, "C7 C4", "C9")
        more_mm([(P[2][:, 256 + o:384:4], T.M2[:], blk(T.FB, o, 32)) for o in range(N)], "M2 FB", "P2b")
        scan(T.RR[:], T.RT[:], T.FB[:], 0.0, A.mult, A.subtract, "RT FB", "RR")
        more_mm([(P[2][:, 256 + o:384:4], T.OB[:], blk(T.RR, o, 32)) for o in range(N)], "OB RR", "P2b", True)
        ts(T.AT[:], c32(9), 512.0, None, A.add, None, "C9", "AT")
        act(T.PG[:], T.D[:, 0:8704].indirect(T.AT[:]), F.Copy, "D REC AT", "PG", gathers=True)
        mm([(P[7][:, 64:448], [(ID, T.MK[:])])], "SH MK", "P7b", True, False)
        scan(T.SQ[:], T.DP[:], P[2][:, 256:384], 1e6, A.min, A.max, "DP P2b", "SQ")
        ts(T.OL[:], T.SQ[:, 3::4], -1.0, 4096.0, A.mult, A.add, "SQ", "OL")

    def pointers(rd):
        kr = 136 if rd == RO - 1 else 0
        mm([(P[6][:, 128 + 64 * k:192 + 64 * k], [(T.KR[:, kr + 3 - i:kr + 131 - i], T.PG[:, 2 * i + k::8]) for i in range(4)]) for k in range(2)],
           "KR PG", "P6b")

    def nodes_out():
        act(T.PN[:], P[6][:, 128:256], F.Copy, "P6b", "PN")
        for r in range(N):
            mm([(blk(P[3], r, 32), [(T.NO[:, 176 * r + 36 - 32 * x - 4 * k:176 * r + 164 - 32 * x - 4 * k], T.PN[:, 64 * k + x:64 * k + 64:2])
                                    for x in range(2) for k in range(2)])], "NO PN", "P3")
        act(T.NS[:], P[3][:, 0:128], F.Copy, "P3", "NS")
        send(lambda o: blk(T.NS, o, 32), lambda o: blk(T.NL, o, 32), "an", "NS")
        arrival("NL", "an", peers)
        dma("y", [(T.ynodes[rows(rank), :], blk(T.NS, rank, 32))], "NS", "yn0")

    def mine(rd, o, a, b):
        c0 = TW * (N * rd + o)
        return (T.TL if o == rank else T.TS)[:, c0 + a:c0 + b]

    tri = lambda o, jj: P[7][:, 64 + (0, 64, 192)[jj] + 16 * (jj + 1) * o:64 + (0, 64, 192)[jj] + 16 * (jj + 1) * (o + 1)]

    def compact(rd):
        w0 = 192 * (RO - 1 - rd)
        if rd < RO - 1:
            cp(T.CW[:, w0:w0 + 2560].indirect(T.OL[:, 0:16]), T.RQ[:, 0:256], "OL RQ", "CW", scatters=True)
            cp(T.PL[:], P[6][:, 128:256], "P6b", "PL")
            cp(T.CW[:, w0:w0 + 2560].indirect(T.OL[:, 16:32]), T.RQ[:, 256:512], "OL RQ CW", "CW", scatters=True)
        else:
            cp(T.CW[:, w0:w0 + 2560].indirect(T.OL[:]), T.RQ[:], "OL RQ", "CW", scatters=True)
        for o in range(N):
            cp(blk(T.HX, o, 48), T.CW[:, w0 + o:w0 + 192:4], "CW", "HX%d" % o)
            more_mm([(tri(o, jj), T.BC[:], T.HX[:, 48 * o:48 * o + 16 * (jj + 1)]) for jj in range(3)], "BC HX%d" % o, "P7b", o == N - 1)
        mm([(P[7][:, 480:492], [(chain(3, i), T.HX[:, i::16]) for i in range(16)])], "LW3 HX0 HX1 HX2 HX3", "P7c")
        for o in range(N):
            tt(mine(rd, o, 0, 48), T.CW[:, w0 + o:w0 + 192:4], blk(T.HX, o, 48), A.subtract, "CW HX%d TS~" % o, "LO")

    def all_mm(rd, k):
        mm([(P[4 + k][:, 192 * x + 48 * o:192 * x + 48 * o + 48], [(blk(T.RB, 2 * k + x, 128), mine(rd, o, 0, 48))])
            for x in range(2) for o in range(N)], "RB LO", "P%d" % (4 + k))

    def all_out(k):
        act(blk(T.RL, k, 384), P[4 + k][:, 0:384], F.Copy, "P%d" % (4 + k), "RL%d" % k)

    def keys():
        cp(T.KC[:, 0:24:2], P[7][:, 480:492], "P7c", "KC0")

    def equal():
        for o in range(N):
            for jj in range(3):
                n_ = 3 * o + jj
                ts(T.E[:, 48 * n_:48 * n_ + 16 * (jj + 1)], tri(o, jj), P[7][:, 480 + n_:481 + n_], WON, A.not_equal, A.mult, "P7b P7c", "E")
        tt(T.KC[:, 1:24:2], P[7][:, 480:492], T.KC[:, 0:24:2], A.subtract, "P7c KC0", "KC1")
        scan(T.ZS[:], T.RS[:], T.E[:], WON, A.min, A.max, "RS E", "ZS")

    spread = lambda t, c: [(P[6][:, 256 + 12 * r:268 + 12 * r], blk(T.RB, r, 128), t[:, c]) for r in range(N)]

    def winners(x):
        if x == 0:
            more_mm(spread(T.KC, slice(0, 24, 2)), "RB KC0", "P6c", False, True)
        else:
            more_mm(spread(T.KC, slice(1, 24, 2)), "RB KC1", "P6c")
            more_mm(spread(T.ZS, slice(47, 576, 48)), "RB ZS", "P6c", True)

    def targets():
        tt(T.AF[:], P[6][:, 256:304], T.UC[:], A.min, "P6c UC", "AF")
        cp(T.AL[:], T.AF[:], "AF", "AL")

    def update(r):
        cp(T.D[:, 512:512 + DW].indirect(blk(T.AL, r, 12)), blk(T.RL, r, 192), "AL D RL%d" % (r // 2), "D", scatters=True)

    def parcel(rd):
        last = rd == RO - 1
        for o in [] if last else peers + [rank]:
            move("g", mine(rd, o, 48, 54), T.KC[:, 6 * o:6 * o + 6], "KC0 KC1 TS~ TL~", "OK%d" % (o == rank))
            move("g", mine(rd, o, 54, 57), T.ZS[:, 144 * o + 47:144 * o + 144:48], "ZS TS~ TL~", "OK%d" % (o == rank))
        send(lambda o: blk(T.TS, N * rd + o, TW), lambda o: blk(T.TL, N * rd + o, TW), "ar%d" % rd, "LO" if last else "LO OK0")
        for o in peers:
            arrival("TL%d%d" % (rd, o), "ar%d" % rd, peers)
        wrote["TL%d%d" % (rd, rank)], wrote["LO%d" % rd] = wrote["TL~" if last else "OK1"], wrote["LO"]

    mark = lambda o, a: (T.ZL if o == rank else T.ZT)[:, 8 * o + a:8 * o + a + 3]

    def marks():
        for o in peers + [rank]:
            move("s", mark(o, 4), T.KC[:, 6 * o + 1:6 * o + 6:2], "KC1 ZT~ ZL~", "ZK%d" % (o == rank))
            tt(mark(o, 0), T.KC[:, 6 * o:6 * o + 6:2], T.ZS[:, 144 * o + 47:144 * o + 144:48], A.add, "KC0 ZS ZT~ ZL~", "ZT%d" % (o == rank))
        send(lambda o: blk(T.ZT, o, 8), lambda o: blk(T.ZL, o, 8), "al%d" % rank, "ZT0 ZK0")
        for o in peers:
            arrival("ZL%d" % o, "al%d" % o, [o])
        wrote["ZL%d" % rank] = wrote["ZT1"]

    def marks_in():
        for d in srcs:
            more_mm([(P[3][:, 480 + 4 * r:484 + 4 * r], shift(r, d), T.ZL[:, 8 * d + a:8 * d + a + 4])
                     for r in range(N) for a in (0, 4)], "WR ZK1 ZL%d" % d, "P3b", d == srcs[-1], d == srcs[0])

    def regroup(rd):
        for d in srcs:
            more_mm([(blk(P[4], r, TW), shift(r, d), blk(T.TL, N * rd + d, TW)) for r in range(N)],
                    "WR LO%d TL%d%d" % (rd, rd, d), "P4a", d == srcs[-1], d == srcs[0])
        act(T.VT[:], P[4][:, 0:N * TW], F.Copy, "P4a", "VT")
        act(T.VA[:], P[4][:, 0:N * TW], F.Identity, "P4a", "VA", scale=1.0 / 16, bias=143.53)

    def unpack(rd):
        if rd < RO - 1:
            mm([(P[3][:, 480 + 4 * r:484 + 4 * r], [(ID, T.VT[:, TW * r + a:TW * r + b:st]) for a, b, st in ((48, 56, 2), (49, 57, 2), (54, 58, 1))])
                for r in range(N)], "SH VT", "P3b")
        mm([(P[0][:, 256:512], [(T.UY[:], T.VT[:]), (T.UZ[:], T.VA[:])])], "UY UZ VT VA", "P0b")
        mm([(P[1][:, 256:512], [(T.SK[:], T.VT[:])])], "SK VT", "P1b")
        act(blk(T.RBY, rd, N * TW), P[0][:, 256:512], F.Identity, "P0b cbY", "ry RBY%d" % rd, bias=col("bY"))
        act(blk(T.RBK, rd, N * TW), P[1][:, 256:512], F.Copy, "P1b", "rk RBK%d" % rd)

    def slots(rd):
        tt(T.XF[:], P[3][:, 480:496], T.XD[:], A.min, "P3b XD", "XF")
        ts(blk(T.XL, rd, 16), T.XF[:], float(-S * rank), None, A.add, None, "XF", "xl XL%d" % rd)
        todo.extend((rd, r, key) for r in reversed(range(N)) for key in "YK")

    def place(n_, name="put"):
        for rd, r, key in todo[:n_]:
            win, src, c0 = T.YC if key == "Y" else T.YK, T["RB" + key], TW * (N * rd + r)
            cp(win[:, 0:YW].indirect(T.XL[:, 16 * rd + 4 * r:16 * rd + 4 * r + 3]), src[:, c0:c0 + 48],
               "XL%d RB%s%d W%s" % (rd, key, rd, key), name + " W" + key, scatters=True)
        del todo[:n_]
    todo = []

    def stores():
        todo.sort(key=lambda x: x[2] == "K")
        place(2 * N, "end")
        dma("y", [(T.ynodes[rows(o), :], blk(T.NL, o, 32)) for o in peers], "NL", "yn")
        dma("y", [(T.ycells[:], T.YC[:, 0:S])], "WY", "yc")
        dma("s", [(T.ykids[:], T.YK[0::4, 0:S])], "WK", "yk")

    pin("", (loads,), (cells_out,), (first_constants,), (b_number, range(4)), (halves,), (d_kids, far[0]), (d_kids, far[1]), (d_kids, near_[0]),
        (d_kids, rank), (lists_out,), (kids_out,), (painted,), (d_pairs, rank, 4), (b_cells, rank, range(4)), (b_number, (4, 5, 6, 7, 0, 1, 2, 3)),
        (weights,), (b_cells, far[0], range(4, 8)), (b_cells, near_[0], range(4)), (b_number, range(4, 8)), (b_cells, far[1], range(4, 8)),
        (d_pairs, far[0], 0), (d_pairs, near_[0], 1), (d_pairs, far[1], 2), (d_copies,), (lists,), (table_cc,),
        (gather, 0, True), (gather, 1, True), (near, 0), (near, 1), (late_constants, 0), (life_a, 0), (life_b, 0), (late_constants, 1), (life_b, 1),
        (life_a, 1), (hash_mm, 0), (rec_kids, 0), (hash_mm, 1), (rec_pairs,), (rec_kids, 1), (late_constants, 2), (hash_out,), (rec_out,),
        (rec_copy,), (hash_sum,), (late_constants, 3), (hash_ops,))

    for rd in range(RO - 1):
        owner = [(regroup, rd - 1), (unpack, rd - 1), (slots, rd - 1)] if rd else [(first_outputs,)]
        pin(ROUND, (look,), (flags,), (place, 2), (pointers, rd), *owner, (compact, rd), (gather, 0), (gather, 1), (near, 0), (all_mm, rd, 1), (keys,),
            (winners, 0), (equal,), (life_a, 0), (all_out, 1), (near, 1), (winners, 1), (life_b, 0), (targets,), (life_s, 1),
            (all_mm, rd, 0), (hash_mm, 0), (update, 3), (all_out, 0), (hash_mm, 1), (hash_out,), (update, 2), (rec_pairs,), (rec_out,),
            (hash_sum,), (rec_kids, 0), (rec_kids, 1), (rec_copy,), (update, 1), (hash_ops,), (update, 0), (parcel, rd))
        if rd == 0:
            pin("", (painted_last,))

    rd = RO - 1
    pin(LAST, (look,), (flags,), (place, 2), (pointers, rd), (regroup, rd - 1), (unpack, rd - 1), (slots, rd - 1), (compact, rd), (parcel, rd), (keys,),
        (equal,), (marks,), (nodes_out,), (place, 22), (regroup, rd), (unpack, rd), (marks_in,), (slots, rd), (stores,))

    last_of = {}
    queue = {e: [me for first, at_, me in sorted(pinned) if jobs[me]["e"] == e] for e in "vstgya"}
    start, free, used = {}, {e: 0.0 for e in queue}, {}
    count, seen, total, user = {}, {e: {} for e in Q}, {}, {}

    def need(e, tok):
        if seen[e].get(tok[0], 0) < tok[1]:
            Q[e].wait_ge(T.sem[tok[0]], tok[1])
            seen[e][tok[0]] = tok[1]

    def earliest(me):
        j = jobs[me]
        if any(i not in start for i in j["pre"]):
            return 1e12
        return max([free[j["e"]]] + [start[i] + jobs[i]["ns"] + (jobs[i]["late"] + jobs[i]["busy"] + HOP) * sem for i, sem in j["pre"].items()]
                   + [t + HOP for b in j["banks"] for x, t in used.get(b, {}).items() if x != j["e"]])
    for _ in jobs:
        t, e = min((earliest(q[0]), e) for e, q in queue.items() if q)
        me = queue[e].pop(0)
        j = jobs[me]
        start[me], free[e] = t, t + j["ns"]
        if e != "a":
            for i, sem in j["pre"].items():
                if sem and jobs[i]["kind"] != "rem":
                    need(e, jobs[i]["tok"])
            for b in sorted(j["banks"]):
                for x, tok in user.setdefault(b, {}).items():
                    if x != e:
                        need(e, tok)
            ins = j["fn"]()
            if j["kind"] == "c":
                count[e] = count.get(e, 0) + 1
                ins.then_inc(T.sem["e" + e], 1)
                j["tok"] = ("e" + e, count[e])
            for b in j["banks"]:
                user[b][e], used.setdefault(b, {})[e] = j["tok"], free[e]
        total[j["tok"][0]] = j["tok"][1]
    for sem, n_ in total.items():
        need("g", (sem, n_))
